import numpy as np, ml_dtypes
CORES = [10,34,74,98]
N = 4
BF = ml_dtypes.bfloat16
W, E, B, C, RO, NC = 2048, 1024, 256, 12, 3, 32
def group(rng, noise, good, mode, proto):
    n = W // NC; mem = rng.permutation(W).reshape(NC, n); cl = np.zeros(W, np.int64); cl[mem] = np.arange(NC)[:, None]
    x = np.minimum(np.maximum(proto[:, cl] + rng.integers(-noise, noise + 1, (16, W)), 0), 63)
    nx = rng.integers(0, NC, (16, NC))
    if mode == 1: nx[:] = np.arange(NC)
    if mode == 2: nx[:] = cl[0]
    if mode == 3: nx[:] = cl[W - 1]
    l = mem[nx[:, cl], rng.integers(0, n, (16, W))]
    if mode == 1: l[:] = np.arange(W)
    if mode == 2: l[:] = 0
    if mode == 3: l[:] = W - 1
    i = np.zeros((16, E), np.int64); q = rng.integers(0, NC, E)
    for k in range(16):
        i[k] = mem[q, rng.integers(0, n, E)]
        if k < 15:
            go = nx[k, q]; q = np.where(good[k], go, (go + rng.integers(1, NC, E)) % NC)
    return x, i, l
def parts(rng, style):
    x = np.zeros((N, 8, 16, W), np.int64); i = np.zeros((N, 8, 16, E), np.int64); l = np.zeros((N, 8, 16, W), np.int64)
    for a in range(N):
        for g in range(8):
            noise = int(rng.integers(1, 4)); mode = 0; proto = rng.integers(0, 64, (16, NC))
            good = rng.random((15, E)) < rng.choice(np.array([0.2, 0.6, 0.8, 0.95, 1.0]), E)
            if style == "ties": noise = 0; proto = 16 + 8 * rng.integers(0, 2, (16, NC))
            if style == "corners":
                noise = 0; mode = (a + g) % 4; n = rng.choice(np.array([0, 1, C - 1, C, C + 1, 15]), E)
                good = np.argsort(np.argsort(rng.random((15, E)), axis=0), axis=0) < n
            x[a, g], i[a, g], l[a, g] = group(rng, noise, good, mode, proto)
    t = np.stack([rng.integers(20, 70, (N, 8, 16)), rng.integers(200, 420, (N, 8, 16))], axis=-1)
    return x, rng.integers(0, 64, (N, 8, 16, E)), i, l, rng.integers(0, 64, (N, 8, 16, B)), rng.integers(0, 256, (N, 8, 16, 1)), rng.integers(0, 2048, (N, 8, 16, 2)), t
def pack(x, gs, i, l, z, w, h, t):
    def bf(v): return np.ascontiguousarray(v.reshape(N, 128, -1)).astype(np.float32).astype(BF)
    def whole(v): return np.ascontiguousarray(v.reshape(N, 128, -1)).astype(np.int32)
    return {"xc": bf(x), "gi": bf(gs), "ix": whole(i), "lk": whole(l), "zc": bf(z), "wt": whole(w), "hk": whole(h), "th": whole(t)}
def ends(rng, lo, hi, shape, share):
    v = np.where(rng.random(shape) < 0.5, lo, hi)
    return np.where(rng.random(shape) < share, v, rng.integers(lo, hi + 1, shape))
def records(rng, n):
    k = rng.integers(0, 3, (N, 8, 1, n))
    return np.where(k == 0, 0, np.where(k == 1, 63, ends(rng, 0, 63, (N, 8, 16, n), 1.0)))
def full(rng, p):
    u = rng.permutation(4096); f, k = np.unique(((u * u >> 5) + p * u) & (E - 1), return_index=True)
    return u[rng.permutation(k)[:B]]
def setup_inputs(rng):
    return pack(*parts(rng, "plain"))
def setup_inputs_ties(rng):
    x, gs, i, l, z, w, h, t = parts(rng, "ties")
    gs = 16 + 8 * rng.integers(0, 2, gs.shape); z = 16 + 8 * rng.integers(0, 2, z.shape)
    t = rng.choice(np.array([56, 63, 64, 65, 72]), t.shape)
    for a in range(N):
        for g in (6, 7):
            v = (256, 257, 259, 513, 515, 767, 1005, 1007)[(a + g) & 7]; base = int(rng.integers(0, 1008 - v))
            m = rng.permutation(W); low = np.flatnonzero(m < W // 2); high = np.flatnonzero(m >= W // 2)
            size = base + np.where(m < W // 2, 0, v + (rng.random(W) < 0.3).astype(np.int64))
            x[a, g] = (size >> 4) + (np.arange(16)[:, None] < (size & 15)).astype(np.int64)
            i[a, g] = low[rng.integers(0, W // 2, (16, E))]; l[a, g] = high[rng.integers(0, W // 2, (16, W))]
            t[a, g, :, 0] = v; t[a, g, :, 1] = 1008
    return pack(x, gs, i, l, z, w, h, t)
def setup_inputs_corners(rng):
    x, gs, i, l, z, w, h, t = parts(rng, "corners")
    for a in range(N):
        for g in range(8):
            kind = (3 * a + g) % 4
            if kind == 0: w[a, g] = 255
            if kind == 1: w[a, g] = 255 * rng.integers(0, 2, (16, 1))
            if kind == 2: w[a, g] = 0; w[a, g, 15] = 1
            t[a, g, :, 0] = (0, 1, 40, 0, 0, 1008, 40, 1)[(a + g) % 8]
            t[a, g, :, 1] = rng.choice(np.array([0, 340, 1008]), 16)
            h[a, g] = np.where(rng.random((16, 2)) < 0.4, 2047 * rng.integers(0, 2, (16, 2)), h[a, g])
    k = rng.integers(0, 4, (N, 8, 1, B)); z = np.where(k == 0, 0, np.where(k == 1, 63, z))
    k = rng.integers(0, 4, (N, 8, 1, E)); gs = np.where(k == 0, 0, np.where(k == 1, 63, gs))
    i = np.where(rng.random((N, 8, 1, E)) < 0.1, (W - 1) * rng.integers(0, 2, (N, 8, 1, E)), i)
    return pack(x, gs, i, l, z, w, h, t)
def setup_inputs_crowd(rng):
    x, gs, i, l, z, w, h, t = parts(rng, "plain")
    w[:, 0::4] = 0; w[:, 0::4, 5] = 1; z[:, 0::4, 5] = rng.integers(0, 6, (N, 2, B)); h[:, 0::4, :, 0] = 0
    i[:, 1] = rng.choice(np.array([0, 1, W // 2, W - 2, W - 1]), (N, 16, E)); gs[:, 1] = 30
    w[:, 2] = 0
    z[:, 3] = z[:, 3][..., rng.integers(0, 3, B)]
    for a in range(N):
        for g in (5, 6, 7):
            w[a, g] = 0; w[a, g, 0] = 1; w[a, g, 1] = 64; gs[a, g] = 0
            p = int(h[a, g, 0, 0]); u = full(rng, p)
            if g == 5: u[B // 2:] = u[:B // 2]
            z[a, g, 0] = u & 63; z[a, g, 1] = u >> 6
            e = ((u * u >> 5) + p * u) & (E - 1)
            if g == 5:
                side = rng.random(B // 2) < 0.5; side[0] = True; side[1] = False; near = np.concatenate([side, ~side])
                x[a, g] = rng.integers(16, 25, (16, W)); i[a, g] = rng.integers(0, W, (16, E))
                z[a, g, 2:] = np.where(near, rng.integers(16, 25, (14, B)), rng.integers(56, 64, (14, B)))
                t[a, g, :, 0] = 0; t[a, g, :, 1] = rng.integers(206, 448, 16)
            if g == 6:
                o = rng.permutation(W); i[a, g][:, e] = o[(np.arange(16)[:, None] % (W // B)) * B + np.arange(B)]
                t[a, g, :, 0] = 0
            if g == 7: t[a, g, :, 0] = 1008
    t[2, :, :, 0] = 0
    gs[2, 3] = 30; c = int(rng.integers(0, W)); u = np.add.reduce(w[2, 3] * z[2, 3], axis=0) & 4095
    e = ((u * u >> 5) + h[2, 3, 0, 0] * u) & (E - 1)
    i[2, 3][:, e] = c; l[2, 3][:, c] = c
    return pack(x, gs, i, l, z, w, h, t)
def setup_inputs_spread(rng):
    x, gs, i, l, z, w, h, t = parts(rng, "plain")
    x = x >> rng.integers(0, 7, (N, 8, 1, W)); gs = gs >> rng.integers(0, 7, (N, 8, 1, E)); z = z >> rng.integers(0, 7, (N, 8, 1, B))
    i[:, ::2] = (W * rng.random((N, 4, 16, E)) ** 3).astype(np.int64); l[:, ::4] = (W * rng.random((N, 2, 16, W)) ** 3).astype(np.int64)
    w = np.exp2(8 * rng.random(w.shape)).astype(np.int64); h = np.exp2(11 * rng.random(h.shape)).astype(np.int64)
    t = np.minimum(np.exp2(10.2 * rng.random(t.shape)).astype(np.int64), 1008)
    return pack(x, gs, i, l, z, np.minimum(w, 255), np.minimum(h, 2047), t)
def setup_inputs_ends(rng):
    x = records(rng, W); gs = records(rng, E); z = records(rng, B)
    x[:, 0::2, :, 0] = 63; x[:, 0::2, :, W - 1] = 0; x[:, 1::2, :, 0] = 0; x[:, 1::2, :, W - 1] = 63
    i = ends(rng, 0, W - 1, (N, 8, 16, E), 0.75); l = ends(rng, 0, W - 1, (N, 8, 16, W), 0.75)
    w = ends(rng, 0, 255, (N, 8, 16, 1), 0.75); w[:, 7] = 255
    h = ends(rng, 0, 2047, (N, 8, 16, 2), 0.8); t = ends(rng, 0, 1008, (N, 8, 16, 2), 1.0)
    t[0, :, :, 0] = 1008; a = N - 1; t[a, 7, :, 0] = 0
    i[0, 5] = W - 1; l[0, 5, :, W - 1] = 0
    t[1, :, :, 0] = 1008; t[1, 6, :, 0] = 0
    w[1, 6] = 0; w[1, 6, 15] = 255; z[1, 6, 15] = 0; z[1, 6, 15, B - 1] = 63; h[1, 6, :, 0] = 2047 * rng.integers(0, 2, 16)
    i[1, 6] = W - 1; i[1, 6, :, 0] = 0; l[1, 6, :, 0] = 0; l[1, 6, :, W - 1] = 0
    v = z[a, 7]; v[:, B - 1] = 63; v[:, B - 2] = 0; v[15, B - 2] = 63; v[:, B - 3] = 0; v[:4, B - 3] = 63; v[4, B - 3] = 5
    h[a, 7, 0, 0] = 2047; h[a, 7, 1, 0] = 0; h[a, 7, 15, 1] = 2047
    h[a, 7, 15, 0] = ((E - 1 - (3777 * 3777 >> 5)) * pow(3777, -1, E)) % E
    c = ((3088 * 3088 >> 5) + h[a, 7, :, 0] * 3088) & (E - 1)
    gs[a, 7][:, c] = 0; gs[a, 7, :, E - 1] = v[:, B - 2]
    i[a, 7, :, c[1]] = 0; i[a, 7, :, c[0]] = W - 1; i[a, 7, :8, E - 1] = 0; i[a, 7, 8:, E - 1] = W - 1
    l[a, 7, :, 0] = 0; l[a, 7, :, W - 1] = 0
    return pack(x, gs, i, l, z, w, h, t)
def check_inputs(d):
    bad = []
    for k, lo, hi in (("xc", 0, 63), ("gi", 0, 63), ("ix", 0, W - 1), ("lk", 0, W - 1), ("zc", 0, 63), ("wt", 0, 255), ("hk", 0, 2047), ("th", 0, 1008)):
        v = np.asarray(d[k]).astype(np.float64)
        if not np.all((v >= lo) & (v <= hi) & (v == np.floor(v))): bad.append("range of " + k)
    return bad
def reference(xc, gi, ix, lk, zc, wt, hk, th):
    def cut(v): return np.asarray(v).astype(np.float32).astype(np.int64).reshape(N, 8, 16, -1)
    X, G, I, L, Z, w, h, t = cut(xc), cut(gi), cut(ix), cut(lk), cut(zc), cut(wt), cut(hk), cut(th)
    A = np.zeros(N, np.int64); lane = np.arange(B)
    for rnd in range(RO):
        count = np.zeros(N, np.int64)
        for a in range(N):
            r = (a - rnd) % N
            for g in range(8):
                z = Z[r, g]
                u = np.add.reduce(w[a, g] * z, axis=0) & 4095
                em = ((u * u >> 5) + h[a, g, :, 0:1] * u + A[a]) & (E - 1)
                d = np.add.reduce(np.abs(G[a, g][:, em] - z[:, None, :]), axis=0)
                e = em[np.argmin(d, axis=0), lane]
                J = I[a, g][:, e]
                x = X[a, g][:, J]
                y = X[a, g][:, np.take_along_axis(L[a, g], J, 1)]
                s = np.add.reduce(np.abs(y[:, :15] - x[:, 1:]), axis=0)
                far = np.add.reduce(np.abs(x - z[:, None, :]), axis=0)
                rec = np.add.reduce((s <= t[a, g, :15, 0:1]).astype(np.int64), axis=0) >= C
                fresh = ((u * u >> 4) + h[a, g, :, 1:2] * u) & (W - 1)
                col = np.where(rec[None, :] | (far > t[a, g, :, 1:2]), fresh, J)
                ks = np.argmax(s, axis=0)
                f, first = np.unique(e, return_index=True)
                I[a, g][:, f] = col[:, first]
                if rnd < RO - 1:
                    o = first[rec[first]]; G[a, g][:, e[o]] = z[:, o]
                q = np.flatnonzero(~rec); c, one = np.unique(J[ks[q], q], return_index=True); q = q[one]
                L[a, g][ks[q], c] = J[ks[q] + 1, q]
                count[a] += np.count_nonzero(rec)
                Z[r, g] = (z + np.maximum.reduce(x, axis=1)) >> 1
        A = count
    return {"yz": Z.reshape(N, 128, B).astype(np.float32).astype(BF), "yi": I.reshape(N, 128, E).astype(np.float32), "yl": L.reshape(N, 128, W).astype(np.float32)}

@@ -1,0 +1,647 @@
+import numpy as np
+from concourse.mybir import AluOpType as A, AxisListType, ActivationFunctionType as F
+
+BIG = 1.0e9
+OFF24 = 16777216.0
+CYC = 0.8333
+GAT, SCA, WAKE, FIX = 1.56, 3.8, 70.0, 20.0
+SCRATCH, SIZES = {}, {}
+TWO = ("bfloat16", "float16", "uint16")
+
+
+def _buf(name, cols, dtype, where="sbuf"):
+    SCRATCH[name] = (where, [128, cols], dtype)
+
+
+for _n, _c, _d in (
+        ("xb", 2048, "bfloat16"), ("G", 1280, "bfloat16"), ("ixi", 1024, "int32"), ("I", 1280, "float32"),
+        ("lki", 2048, "int32"), ("L", 2304, "float32"),
+        ("wti", 1, "int32"), ("hki", 2, "int32"), ("thi", 2, "int32"),
+        ("z0", 256, "bfloat16"), ("z1", 256, "bfloat16"), ("z2", 256, "bfloat16"), ("z3", 256, "bfloat16"),
+        ("zs0", 256, "bfloat16"), ("zs1", 256, "bfloat16"), ("zs2", 256, "bfloat16"), ("zt", 256, "bfloat16"),
+        ("pI", 1, "int32"), ("p16i", 1, "int32"), ("pgi", 1, "int32"), ("pf", 1, "float32"), ("p16", 1, "float32"),
+        ("pg", 1, "float32"), ("pz", 1, "float32"), ("colA", 1, "float32"), ("colB", 1, "float32"), ("k15", 1, "float32"),
+        ("wf", 1, "float32"), ("hf", 2, "float32"), ("tf", 2, "float32"),
+        ("dI", 144, "int32"), ("cI", 144, "int32"), ("gI", 128, "int32"), ("g8I", 16, "int32"), ("rI", 256, "int32"),
+        ("dgI", 128, "int32"), ("duI", 16, "int32"), ("r15I", 256, "int32"),
+        ("IW", 136, "float16"), ("IB", 136, "bfloat16"), ("INB", 136, "bfloat16"), ("BB", 128, "bfloat16"), ("BH", 128, "float16"),
+        ("BLK", 16, "bfloat16"), ("Q16", 8, "float16"), ("MK", 256, "float16"), ("ZB", 144, "bfloat16"),
+        ("SEL", 2048, "float16"), ("KM", 16, "float32"), ("CD", 128, "bfloat16"), ("CS", 256, "bfloat16"),
+        ("ONB", 128, "bfloat16"), ("ONH", 128, "float16"), ("MMIN", 128, "float32"), ("MMAX", 256, "float32"),
+        ("MR", 2048, "bfloat16"), ("OFFR", 8, "uint16"), ("pk1", 1, "float32"), ("pk2", 1, "float32"), ("pk3", 1, "float32"),
+        ("PICK", 2, "uint16"), ("DUE", 16, "float32"), ("DUJ", 16, "float32"), ("DM", 2176, "bfloat16"), ("OWN", 16, "bfloat16"),
+        ("RPR", 128, "float16"), ("RPJ", 128, "float16"), ("RPt", 128, "float16"), ("RPN", 128, "float16"), ("RPK", 128, "float16"),
+        ("dgA", 128, "float16"), ("THR", 128, "float32"), ("Wb", 128, "bfloat16"),
+        ("W8", 8, "bfloat16"), ("ZQ", 200, "float16"), ("PM_0", 128, "float16"), ("PM_1", 128, "float16"), ("PQ_0", 128, "float16"), ("PQ_1", 128, "float16"),
+        ("C0", 256, "bfloat16"), ("BL2", 16, "bfloat16"), ("BLN", 16, "bfloat16"), ("CDi", 128, "bfloat16"), ("CSi", 256, "bfloat16"),
+        ("ui", 16, "int32"), ("uu", 16, "int32"), ("UQ", 48, "int32"), ("UH", 48, "float16"), ("RLu", 128, "float16"), ("em", 256, "int32"), ("emu", 256, "uint16"), ("emh", 256, "float16"),
+        ("sh4", 256, "int32"), ("vi", 256, "int32"), ("vJ", 256, "float32"), ("Jf", 256, "float32"), ("Jh", 256, "float16"),
+        ("zx0", 4096, "bfloat16"), ("zx1", 4096, "bfloat16"), ("e_rq", 16, "float32"), ("Y", 256, "float16"), ("Er", 256, "float16"),
+        ("far", 256, "float32"), ("ch", 256, "float32"), ("tmp", 256, "float32"), ("RL", 256, "float16"), ("RJh", 256, "float16"),
+        ("mj", 256, "float32"), ("scj", 256, "float32"), ("EQE", 2176, "bfloat16"), ("DUPE", 2176, "bfloat16"),
+        ("EQJ", 2176, "bfloat16"), ("DUPJ", 2176, "bfloat16"), ("fl", 16, "float32"), ("of1", 16, "float32"), ("of2", 16, "float32"),
+        ("nr", 16, "float32"), ("og1", 16, "float32"), ("og2", 16, "float32"), ("flJ", 16, "float32"), ("oj1", 16, "float32"),
+        ("oj2", 16, "float32"), ("oj3", 16, "float32"), ("oEu", 16, "uint16"), ("oGu", 16, "uint16"), ("oJu", 16, "uint16"),
+        ("Lold", 256, "float32"), ("mk", 256, "float32"), ("t1", 256, "float32"), ("t2", 256, "float32"), ("Ac", 1, "float32")):
+    _buf(_n, _c, _d)
+for _h in "01":
+    for _n, _c, _d in (("DG", 2048, "bfloat16"), ("AG", 2048, "bfloat16"), ("x", 2064, "bfloat16"), ("Lg", 2048, "float16"), ("mx", 2048, "bfloat16"),
+                       ("Dy", 2048, "bfloat16"), ("Ay", 2048, "bfloat16"), ("Af", 2048, "bfloat16"), ("km", 128, "float32"),
+                       ("ei", 8, "int32"), ("ej", 8, "int32"), ("ME", 128, "float16"), ("eu", 8, "uint16"), ("Ju", 128, "uint16"), ("nu", 128, "uint16"),
+                       ("le", 128, "bfloat16"), ("cs", 128, "bfloat16"), ("sm", 256, "float32"), ("si", 16, "int32"), ("sj", 24, "int32"), ("QT", 32, "float16")):
+        _buf(_n + "_" + _h, _c, _d)
+for _b in range(8):
+    _buf("b%d" % _b, 512, "float32", "psum")
+PLACE = {}
+_pack = {}
+for _n in sorted(SCRATCH):
+    _w, _s, _d = SCRATCH[_n]
+    if _w == "sbuf" and _n not in ("xb", "G", "I", "L", "ixi", "lki", "z0", "z1", "z2", "z3", "zs0", "zs1", "zs2") and _s[1] < 2000:
+        _o = _pack.get(_d, 0)
+        PLACE[_n] = ("k_" + _d, _o)
+        _pack[_d] = _o + (_s[1] + 31) // 32 * 32
+    else:
+        PLACE[_n] = (_n, 0)
+DTYPE = {_n: SCRATCH[_n][2] for _n in SCRATCH}
+for _n in list(SCRATCH):
+    if PLACE[_n][0] != _n:
+        del SCRATCH[_n]
+for _d in _pack:
+    _buf("k_" + _d, _pack[_d], _d)
+SEMAPHORES = ["qv", "qs", "qt", "qg", "loc", "arr1", "arr2", "arr3"] + ["d%d" % i for i in range(16)]
+
+
+def R(buf, a=0, b=None, step=1, p=128):
+    if b is None:
+        b = a + 1
+    return (buf, a, b, step, p)
+
+
+def width(r):
+    return (r[2] - r[1] + r[3] - 1) // r[3]
+
+
+def clash(r, s):
+    if r[0] != s[0] or r[1] >= s[2] or s[1] >= r[2]:
+        return False
+    return not (r[3] == s[3] and r[3] > 1 and (r[1] - s[1]) % r[3] != 0)
+
+
+class IndOp(tuple):
+    pass
+
+
+def ind(win, off):
+    return IndOp((win, off))
+
+
+def build(rank, opt):
+    ops, loaded = [], [0.0]
+
+    def add(q, kind, calls, reads, writes, cost, lat=0.0, **kw):
+        ops.append(dict(q=q, kind=kind, calls=calls, reads=reads, writes=writes, cost=cost, lat=lat, i=len(ops), **kw))
+
+    def flat(x):
+        if isinstance(x, IndOp):
+            return [x[0], x[1]]
+        return [x] if isinstance(x, tuple) else []
+
+    def small(rs):
+        return all(DTYPE[r[0]] in TWO for r in rs)
+
+    def price(n, half=False, mult=1.0):
+        return max(64.0, n * (0.5 if half else 1.0) * mult) * CYC + FIX
+
+    def V(name, out, *args):
+        full = [x for x in args if isinstance(x, tuple)]
+        rd = [y for x in full for y in flat(x)]
+        wr = flat(out)[:1]
+        if isinstance(out, IndOp):
+            rd = rd + [out[1]]
+            n = width(out[1]) * 16
+            c = 50 + n * SCA * CYC
+        elif any(isinstance(x, IndOp) for x in full):
+            c = 50 + width(out) * GAT * CYC
+        elif name == "tensor_tensor":
+            ps = any(x[0][0] == "b" and len(x[0]) == 2 for x in full)
+            c = price(width(out), False, 1.0 if ps else 2.0)
+        elif name == "tensor_reduce":
+            c = price(width(args[0]))
+        else:
+            c = price(width(out), small([out] + [x for x in full if width(x) > 1]))
+        add("v", name, [(out,) + args], rd, wr, c)
+
+    def VM(name, items):
+        if not items:
+            return
+        n0 = len(ops)
+        for it in items:
+            V(name, *it)
+        got = ops[n0:]
+        del ops[n0:]
+        add("v", name, [o["calls"][0] for o in got], [r for o in got for r in o["reads"]], [r for o in got for r in o["writes"]], sum(o["cost"] for o in got))
+
+    def S(out, in_, func, bias=None, scale=None):
+        c = (65 + width(out) * GAT * CYC) if isinstance(in_, IndOp) else width(out) * CYC + 60
+        rd = flat(in_) + [x for x in (bias, scale) if isinstance(x, tuple)]
+        add("s", "activation", [(out, in_, func, bias, scale)], rd, [out], c)
+
+    def P(items):
+        c = 0.0
+        for o, l, r, a, b in items:
+            f32 = DTYPE[l[0]] == "float32"
+            c += max(min(64, width(l)), width(r)) * (4 if f32 else 1) * CYC + 5
+        rd, wr = [], []
+        for o, l, r, a, b in items:
+            for x in (l, r):
+                if x not in rd:
+                    rd.append(x)
+            if o not in wr:
+                wr.append(o)
+        add("t", "matmul", items, rd, wr, c)
+
+    def iota(out, pattern, base, cm):
+        add("g", "iota", [(out, pattern, base, cm)], [], [out], 130 + 2 * width(out) * CYC)
+
+    def dma(q, out, in_, nbytes, sem):
+        rd = [in_] if isinstance(in_, tuple) else []
+        wr = [out] if isinstance(out, tuple) else []
+        loaded[0] += nbytes * 128 / 200.0 if wr else 0.0
+        add(q, "dma", [(out, in_)], rd, wr, 60, 2000 + (loaded[0] if wr else nbytes * 128 / 200.0), sem=sem)
+
+    dma("y", R("z0", 0, 256), "zc", 512, "d0")
+    dma("s", R("wti", 0, 1), "wt", 4, "d1")
+    dma("s", R("hki", 0, 2), "hk", 8, "d2")
+    dma("y", R("G", 0, 1024), "gi", 2048, "d3")
+    dma("y", R("ixi", 0, 1024), "ix", 4096, "d4")
+    dma("y", R("xb", 0, 2048), "xc", 4096, "d5")
+    dma("s", R("thi", 0, 2), "th", 8, "d6")
+    dma("y", R("lki", 0, 2048), "lk", 8192, "d7")
+    iota(R("pI", 0, 1), [[0, 1]], 0, 1)
+    iota(R("gI", 0, 128), [[1, 8], [0, 16]], 0, 0)
+    iota(R("dI", 0, 144), [[1, 144]], 0, -1)
+    iota(R("g8I", 0, 16), [[0, 2], [1, 8]], 0, 0)
+    iota(R("rI", 0, 256), [[0, 16], [1, 16]], 0, 0)
+    iota(R("cI", 0, 144), [[1, 144]], 0, 0)
+    iota(R("r15I", 0, 256), [[0, 16], [-1, 16]], 15, 0)
+    iota(R("duI", 0, 16), [[16, 16]], 0, 0)
+    iota(R("dgI", 0, 128), [[1, 8], [0, 16]], 0, -1)
+    c1 = lambda b: R(b, 0, 1)
+    ts, tt, tc = "tensor_scalar", "tensor_tensor", "tensor_copy"
+    V(ts, c1("pgi"), c1("pI"), 4, None, A.arith_shift_right)
+    V(tc, c1("pg"), c1("pgi"))
+    V(tc, c1("wf"), c1("wti"))
+    V(ts, R("W8", 0, 8), R("g8I", 0, 8), c1("pg"), c1("wf"), A.is_equal, A.mult)
+    V(tc, R("hf", 0, 2), R("hki", 0, 2))
+    V("memset", R("ZQ", 0, 200), 0.0)
+    V(ts, R("ZQ", 48, 56), R("g8I", 0, 8), c1("pg"), None, A.is_equal)
+    V(ts, R("ZQ", 152, 160), R("g8I", 0, 8), c1("pg"), 0.0625, A.is_equal, A.mult)
+    V(ts, R("BH", 0, 128), R("gI", 0, 128), c1("pg"), None, A.is_equal)
+    V(ts, c1("p16i"), c1("pI"), 15, None, A.bitwise_and)
+    V(tc, c1("p16"), c1("p16i"))
+    V(tc, c1("pf"), c1("pI"))
+    V(ts, R("IW", 0, 136), R("dI", 0, 136), 4.0, None, A.is_equal)
+    V(ts, R("BLK", 0, 16), R("g8I", 0, 16), c1("pg"), 32768.0, A.is_equal, A.mult)
+    V(ts, R("Q16", 0, 8), R("g8I", 0, 8), c1("pg"), None, A.is_equal)
+    V(ts, R("MK", 0, 256), R("rI", 0, 256), c1("p16"), None, A.is_equal)
+    V(tc, R("OFFR", 0, 8), R("g8I", 0, 8))
+    V(ts, c1("colA"), c1("pf"), 64.0, 32.0, A.is_ge, A.mult)
+    V(ts, c1("colB"), c1("pf"), 64.0, -262144.0, A.is_lt, A.mult)
+    V("memset", R("ONB", 0, 128), 1.0)
+    V(ts, R("CD", 0, 128), R("rI", 0, 128), c1("colA"), c1("colB"), A.mult, A.add)
+    V(ts, R("mj", 0, 256), R("rI", 0, 256), 0.0, 2 * BIG, A.is_equal, A.mult)
+    V(ts, R("MMIN", 0, 128), R("mj", 0, 128), -BIG, None, A.add)
+    V("memset", c1("pz"), 0.0)
+
+    def factors(j, name, at):
+        V(ts, R("dgA", 0, 128), R("IW", 4, 132), R("hf", j, j + 1), None, A.mult)
+        for h in (0, 1):
+            o = R("b4", 128 + 128 * h, 256 + 128 * h, 1, 48)
+            P([(o, R("ZQ", 48 - 8 * h, 96 - 8 * h), R("dgA", 0, 128), True, False), (o, R("ZQ", at - 8 * h, at + 48 - 8 * h), R("BH", 0, 128), False, True)])
+            S(R(name + str(h), 0, 128, 1, 48), o, F.Copy)
+    factors(0, "PM_", 120)
+    if any(opt["rg"]):
+        V("memset", R("C0", 0, 256), -131072.0)
+        V(ts, R("BL2", 0, 16), R("BLK", 0, 16), 2.0, None, A.mult)
+        V(ts, R("BLN", 0, 16), R("BLK", 0, 16), -1.0, None, A.mult)
+        V(ts, R("CDi", 0, 128), R("rI", 0, 128), c1("colA"), None, A.mult)
+
+    def load_names():
+        V(tc, R("I", 0, 1024), R("ixi", 0, 1024))
+
+    def load_links():
+        V("memset", R("L", 2048, 2304), 0.0)
+        S(R("L", 0, 1024), R("lki", 0, 1024), F.Copy)
+        S(R("L", 1024, 2048), R("lki", 1024, 2048), F.Copy)
+
+    def late_constants():
+        V(ts, R("IB", 0, 136), R("dI", 0, 136), 4.0, None, A.is_equal)
+        V(ts, R("INB", 0, 136), R("dI", 0, 136), 4.0, -1.0, A.is_equal, A.mult)
+        V(ts, R("KM", 0, 16), R("rI", 0, 16), c1("p16"), None, A.is_equal)
+        for k in range(16):
+            S(R("SEL", 128 * k, 128 * k + 128), R("IW", 4, 132), F.Copy, None, R("KM", k, k + 1))
+        V("memset", R("MR", 0, 2048), 1.0)
+        V("memset", R("MR", 0, 2048, 16), 0.0)
+        V("memset", R("x_0", 2048, 2064), 0.0)
+        V("memset", R("x_1", 2048, 2064), 0.0)
+        V(ts, c1("pk3"), c1("pg"), 16.0, 15.0, A.mult, A.add)
+        V(ts, R("ZB", 0, 144), R("cI", 0, 144), c1("pk3"), None, A.is_equal)
+        V(ts, R("CS", 0, 256), R("r15I", 0, 256), c1("colA"), c1("colB"), A.mult, A.add)
+        V(ts, R("MMAX", 0, 256), R("mj", 0, 256), -1.0, BIG, A.mult, A.add)
+        V(tc, R("tf", 0, 2), R("thi", 0, 2))
+        V("memset", R("ONH", 0, 128), 1.0)
+        V(ts, R("dgA", 0, 128), R("IW", 4, 132), R("tf", 0, 1), None, A.mult)
+        P([(R("b4", 0, 128), R("ONH", 0, 128), R("dgA", 0, 128), True, True)])
+        V(ts, R("THR", 0, 128), R("b4", 0, 128), 32768.0, 32768.0 - OFF24, A.mult, A.add)
+        V("memset", R("THR", 15, 128, 16), -2.0e7)
+        factors(1, "PQ_", 136)
+        if not any(opt["rg"]):
+            V("memset", R("C0", 0, 256), -131072.0)
+            V(ts, R("BL2", 0, 16), R("BLK", 0, 16), 2.0, None, A.mult)
+            V(ts, R("BLN", 0, 16), R("BLK", 0, 16), -1.0, None, A.mult)
+        V(ts, R("CSi", 0, 256), R("r15I", 0, 256), c1("colA"), None, A.mult)
+        V(ts, c1("pk1"), c1("p16"), 8.0, 24.0, A.mult, A.add)
+        V(tt, c1("pk2"), c1("pk1"), c1("p16"), A.mult)
+        V(ts, R("PICK", 0, 1), c1("pk2"), 15.0, None, A.add)
+        V(ts, R("DUE", 0, 16), R("duI", 0, 16), c1("p16"), 1024.0, A.add, A.add)
+        V(ts, R("DUJ", 0, 16), R("duI", 0, 16), c1("p16"), 2048.0, A.add, A.add)
+        V("memset", R("DM", 0, 2176), 1.0)
+        V(ts, R("OWN", 0, 16), R("rI", 0, 16), c1("p16"), 1.0, A.is_equal, A.add)
+        for q in range(16):
+            e = 8 * (q + 1) * (q + 2)
+            S(R("DM", e - 16, e), R("OWN", 0, 16), F.Copy)
+        for q in range(16):
+            s = 8 * q * (q + 1)
+            S(R("DM", s, s + 1), c1("pz"), F.Copy)
+        V(ts, c1("k15"), c1("p16"), -1.0, 15.0, A.mult, A.add)
+        V(ts, R("RPR", 0, 128), R("dgI", 0, 128), 0.0, None, A.is_equal)
+        V(ts, R("RPt", 0, 128), R("dgI", 0, 128), 0.0, 4096.0, A.is_equal, A.mult)
+        V(ts, R("RPJ", 0, 128), R("dgI", 0, 128), -8.0, None, A.is_equal)
+        V(tt, R("RPJ", 0, 128), R("RPJ", 0, 128), R("RPt", 0, 128), A.add)
+        V(ts, R("RPN", 0, 128), R("dgI", 0, 128), -16.0, None, A.is_equal)
+        V(ts, R("RPK", 0, 128), R("dgI", 0, 128), -24.0, None, A.is_equal)
+
+    def dedupe(row, col, cw, eq, du, fl):
+        items = []
+        for q in range(16):
+            s, n = 8 * q * (q + 1), 16 * (q + 1)
+            items.append((R(eq, s, s + n), R(row, 0, n), cw(q), None, A.is_equal))
+        for a in range(0, 16, 4):
+            VM(ts, items[a:a + 4])
+        V("tensor_tensor_scan", R(du, 0, 2176), R("DM", 0, 2176), R(eq, 0, 2176), 0.0, A.mult, A.max)
+        V(ts, R(fl, 0, 16), ind(R(du, 0, 2176), R("PICK", 0, 1)), -1.0, None, A.add)
+
+    def size(relu, out, in_):
+        if relu:
+            V(ts, out, in_, 0.0, None, A.max)
+        else:
+            S(out, in_, F.Abs)
+
+    def keys(relu, K, n, m, d, a, con, coni, payload):
+        if relu:
+            P([(R(K, 0, n), R("ONB", 0, 128), R("C0", 0, n), True, False)] +
+              [(R(K, k, n, 16), R(d, k, 2048, 16), R("BLN", 0, n // 16), False, False) for k in range(m)])
+            P([(R(K, k, n, 16), R(a, k, 2048, 16), R("BL2", 0, n // 16), False, False) for k in range(m)] +
+              [(R(K, 0, n), R("ONB", 0, 128), R(coni, 0, n), False, False)] +
+              [(o, l, r, False, i == len(payload) - 1) for i, (o, l, r) in enumerate(payload)])
+        else:
+            P([(R(K, 0, n), R("ONB", 0, 128), R(con, 0, n), True, False)] + [(o, l, r, False, False) for o, l, r in payload])
+            P([(R(K, k, n, 16), R(a, k, 2048, 16), R("BLK", 0, n // 16), False, k == m - 1) for k in range(m)])
+
+    I16, IB, INB = R("IW", 4, 132), R("IB", 4, 132), R("INB", 4, 132)
+    ISH = R("IW", 5, 133)
+    for t in range(3):
+        z = "z%d" % t
+        P([(R("b0", 8 * h, 8 * h + 8), R(z, 128 * h, 128 * h + 128), R("W8", 0, 8), True, True) for h in (0, 1)])
+        V(tc, R("ui", 0, 16), R("b0", 0, 16))
+        V(ts, R("ui", 0, 16), R("ui", 0, 16), 4095, None, A.bitwise_and)
+        V(tt, R("uu", 0, 16), R("ui", 0, 16), R("ui", 0, 16), A.mult)
+        V(ts, R("UQ", 0, 16), R("ui", 0, 16), 2047, None, A.bitwise_and)
+        V(ts, R("UQ", 16, 32), R("uu", 0, 16), 4, 2047, A.arith_shift_right, A.bitwise_and)
+        V(ts, R("UQ", 32, 48), R("uu", 0, 16), 5, 1023, A.arith_shift_right, A.bitwise_and)
+        V(tc, R("UH", 0, 48), R("UQ", 0, 48))
+        P([(R("b0", 128, 256, 1, 48), R("UH", 0, 48), I16, True, True)])
+        S(R("RLu", 0, 128, 1, 48), R("b0", 128, 256, 1, 48), F.Copy)
+        P([(R("b0", 256 + 128 * h, 384 + 128 * h), R("PM_%d" % h, 0, 128, 1, 48), R("RLu", 0, 128, 1, 48), True, True) for h in (0, 1)])
+        if t == 0:
+            V(tc, R("em", 0, 256), R("b0", 256, 512))
+        else:
+            V(ts, R("em", 0, 256), R("b0", 256, 512), c1("Ac"), None, A.add)
+        V(ts, R("em", 0, 256), R("em", 0, 256), 1023, None, A.bitwise_and)
+        V(tc, R("emu", 0, 256), R("em", 0, 256))
+        nz = opt["zv"][t]
+        zx = "zx%d" % (t % 2)
+        VM(tc, [(R(zx, m, 4096, 16), R(z, 0, 256)) for m in range(nz)])
+        for m in range(nz, 16):
+            S(R(zx, m, 4096, 16), R(z, 0, 256), F.Copy)
+        V(tc, R("emh", 0, 256), R("emu", 0, 256))
+        for h in (0, 1):
+            H, K = "_%d" % h, "b%d" % (2 + h)
+            ch = opt["gchunk"]
+            w = 2048 // ch
+            for c in range(ch):
+                V(tt, R("DG" + H, w * c, w * c + w), ind(R("G", 0, 1024), R("emu", 128 * h + w // 16 * c, 128 * h + w // 16 * (c + 1))),
+                  R(zx, 2048 * h + w * c, 2048 * h + w * c + w), A.subtract)
+                size(opt["rg"][h], R("AG" + H, w * c, w * c + w), R("DG" + H, w * c, w * c + w))
+            keys(opt["rg"][h], K, 128, 16, "DG" + H, "AG" + H, "CD", "CDi", [(R(K, 0, 128), R("emh", 128 * h, 128 * h + 128), I16)])
+        if t == 0:
+            load_names()
+        for h in (0, 1):
+            H, K = "_%d" % h, "b%d" % (2 + h)
+            V("tensor_tensor_scan", R("km" + H, 0, 128), R("MMIN", 0, 128), R(K, 0, 128), 0.0, A.max, A.min)
+            V(tc, R("ei" + H, 0, 8), R("km" + H, 15, 128, 16))
+            V(ts, R("ej" + H, 0, 8), R("ei" + H, 0, 8), 1023, None, A.bitwise_and)
+            V(tt, R("ME" + H, 0, 128), ind(R("ej" + H, 0, 8), R("OFFR", 0, 8)), R("MK", 0, 128), A.mult)
+            P([(R("b7", 8 * h, 8 * h + 8), R("ME" + H, 0, 128), R("Q16", 0, 8), True, True)])
+            V(tc, R("eu" + H, 0, 8), R("b7", 8 * h, 8 * h + 8))
+            V(tc, R("Ju" + H, 0, 128), ind(R("I", 0, 1024), R("eu" + H, 0, 8)))
+            V(tc, R("Jh", 128 * h, 128 * h + 128), R("Ju" + H, 0, 128))
+            V(tc, R("e_rq", 8 * h, 8 * h + 8), R("eu" + H, 0, 8))
+            P([(R("b7", 256 + 128 * h, 384 + 128 * h), R("ME" + H, 0, 128), I16, True, True)])
+        if t == 0:
+            late_constants()
+            load_links()
+        for h in (0, 1):
+            H, K = "_%d" % h, "b%d" % (2 + h)
+            lk = ind(R("L", 0, 2048), R("Ju" + H, 0, 128))
+            xg = ind(R("xb", 0, 2048), R("Ju" + H, 0, 128))
+            if opt["lv"][h]:
+                V(tc, R("Lg" + H, 0, 2048), lk)
+            else:
+                S(R("Lg" + H, 0, 2048), lk, F.Copy)
+            if opt["xv"][h]:
+                V(tc, R("x" + H, 0, 2048), xg)
+            else:
+                S(R("x" + H, 0, 2048), xg, F.Copy)
+            P([(R("b6", 128 * h, 128 * h + 128), R("SEL", 128 * k, 128 * k + 128), R("Lg" + H, k, 2048, 16), k == 0, k == 15) for k in range(16)])
+            V(tc, R("nu" + H, 0, 128), R("b6", 128 * h, 128 * h + 128))
+            yc = opt["ychunk"]
+            w = 2048 // yc
+            for c in range(yc):
+                V(tt, R("Dy" + H, w * c, w * c + w), ind(R("xb", 0, 2048), R("nu" + H, w // 16 * c, w // 16 * (c + 1))), R("x" + H, w * c + 1, w * c + w + 1), A.subtract)
+                size(opt["ry"][h], R("Ay" + H, w * c, w * c + w), R("Dy" + H, w * c, w * c + w))
+            V("tensor_tensor_scan", R("mx" + H, 0, 2048), R("MR", 0, 2048), R("x" + H, 0, 2048), 0.0, A.mult, A.max)
+        P([(R("b6", 256 + 128 * h, 384 + 128 * h), IB, R(z, 128 * h, 128 * h + 128), True, False) if a == 0 else
+           (R("b6", 256 + 128 * h, 384 + 128 * h), IB, R("mx_%d" % h, 15, 2048, 16), False, True) for h in (0, 1) for a in (0, 1)])
+        S(R("zt", 0, 256), R("b6", 256, 512), F.Copy, 127.75, 0.5)
+        V(ts, R("zs%d" % t, 0, 256), R("zt", 0, 256), -128.0, None, A.add)
+        add("g", "remote", [(t,)], [R("zs%d" % t, 0, 256)], [R("z%d" % (t + 1), 0, 256)], 300, 4000)
+        S(R("Y", 0, 256), R("b7", 256, 512), F.Copy)
+        P([(R("b7", 256, 512), R("BH", 0, 128), R("Y", 0, 256), True, True)])
+        S(R("Er", 0, 256), R("b7", 256, 512), F.Copy)
+        dedupe("Er", None, lambda q: R("e_rq", q, q + 1), "EQE", "DUPE", "fl")
+        V(tt, R("of1", 0, 16), R("fl", 0, 16), R("DUE", 0, 16), A.mult)
+        V(tt, R("of2", 0, 16), R("of1", 0, 16), R("e_rq", 0, 16), A.max)
+        V(tc, R("oEu", 0, 16), R("of2", 0, 16))
+        P([(R("b0", 256 + 128 * h, 384 + 128 * h), R("PQ_%d" % h, 0, 128, 1, 48), R("RLu", 0, 128, 1, 48), True, True) for h in (0, 1)])
+        V(tc, R("vi", 0, 256), R("b0", 256, 512))
+        V(ts, R("vi", 0, 256), R("vi", 0, 256), 2047, None, A.bitwise_and)
+        S(R("Jf", 0, 256), R("Jh", 0, 256), F.Copy)
+        VJ = R("b3", 256, 512)
+        P([(R("b2", 256, 512), I16, R("Jh", 0, 256), True, True)])
+        V(tt, VJ, R("vi", 0, 256), R("b2", 256, 512), A.subtract)
+        for h in (0, 1):
+            H, K = "_%d" % h, "b%d" % (2 + h)
+            J = R("Jh", 128 * h, 128 * h + 128)
+            keys(opt["ry"][h], K, 256, 15, "Dy" + H, "Ay" + H, "CS", "CSi", [(R(K, 0, 128), J, I16), (R(K, 128, 256), J, ISH)])
+            V(tt, R("le" + H, 0, 128), R(K, 0, 128), R("THR", 0, 128), A.is_lt)
+            V("tensor_tensor_scan", R("sm" + H, 0, 256), R("MMAX", 0, 256), R(K, 0, 256), 0.0, A.min, A.max)
+            V("tensor_tensor_scan", R("cs" + H, 0, 128), R("MR", 0, 128), R("le" + H, 0, 128), 0.0, A.mult, A.add)
+            V(tc, R("si" + H, 0, 16), R("sm" + H, 15, 256, 16))
+            V(ts, R("QT" + H, 0, 8), R("cs" + H, 15, 128, 16), 11.5, None, A.is_gt)
+            V(ts, R("sj" + H, 0, 16), R("si" + H, 0, 16), 2047, None, A.bitwise_and)
+            V(ts, R("sj" + H, 16, 24), R("si" + H, 0, 8), 11, 15, A.arith_shift_right, A.bitwise_and)
+            V(tc, R("QT" + H, 8, 32), R("sj" + H, 0, 24))
+            P([(R("b7", 128, 256, 1, 32), R("QT" + H, 0, 32), I16, True, True)])
+            S(R("RL", 128 * h, 128 * h + 128, 1, 32), R("b7", 128, 256, 1, 32), F.Copy)
+        if t < 2:
+            P([(R("b7", 16, 24), R("ONH", 0, 128), R("QT_0", 0, 8), True, False), (R("b7", 16, 24), R("ONH", 0, 128), R("QT_1", 0, 8), False, True)])
+            V("tensor_reduce", c1("Ac"), R("b7", 16, 24), "X", A.add)
+        RL = R("RL", 0, 256, 1, 32)
+        P([(R("b6", 256, 512), R("RPJ", 0, 128, 1, 32), RL, True, True)])
+        V(tt, R("mj", 0, 256), R("b6", 256, 512), R("MK", 0, 256), A.mult)
+        S(R("RJh", 0, 256), R("b6", 256, 512), F.Copy)
+        P([(R("b6", 0, 256), R("RPN", 0, 128, 1, 32), RL, True, True), (R("b6", 256, 512), R("RPK", 0, 128, 1, 32), RL, True, True)])
+        V("tensor_tensor_scan", R("scj", 0, 256), R("MR", 0, 256), R("mj", 0, 256), 0.0, A.mult, A.add)
+        JJ = R("scj", 15, 256, 16)
+        if t < 2:
+            V(ts, R("nr", 0, 16), JJ, 4095.5, None, A.is_lt)
+            V(tt, R("og1", 0, 16), R("nr", 0, 16), R("DUE", 0, 16), A.mult)
+            V(tt, R("og2", 0, 16), R("og1", 0, 16), R("of2", 0, 16), A.max)
+            V(tc, R("oGu", 0, 16), R("og2", 0, 16))
+            V(tc, ind(R("G", 0, 1280), R("oGu", 0, 16)), R(z, 0, 256))
+        for h in (0, 1):
+            H = "_%d" % h
+            for c in range(4):
+                B = "b%d" % (4 + c % 2)
+                P([(R(B, 0, 512), IB, R("x" + H, 512 * c, 512 * c + 512), True, False),
+                   (R(B, 0, 512), INB, R(zx, 2048 * h + 512 * c, 2048 * h + 512 * c + 512), False, True)])
+                S(R("Af" + H, 512 * c, 512 * c + 512), R(B, 0, 512), F.Abs)
+            P([(R("b1", 128 * h, 128 * h + 128), R("ZB", 15 - k, 143 - k), R("Af" + H, k, 2048, 16), k == 0, k == 15) for k in range(16)])
+            V(ts, R("far", 128 * h, 128 * h + 128), R("b1", 128 * h, 128 * h + 128), R("tf", 1, 2), None, A.is_gt)
+        P([(R("b1", 256, 512), R("RPR", 0, 128, 1, 32), RL, True, True)])
+        V(tt, R("ch", 0, 256), R("b1", 256, 512), R("far", 0, 256), A.max)
+        V(tt, R("tmp", 0, 256), R("ch", 0, 256), VJ, A.mult)
+        V(tt, ind(R("I", 0, 1280), R("oEu", 0, 16)), R("tmp", 0, 256), R("Jf", 0, 256), A.add)
+        if t == 2:
+            dma("y", "yi", R("I", 0, 1024), 4096, "d8")
+        dedupe("RJh", None, lambda q: R("scj", 16 * q + 15, 16 * q + 16), "EQJ", "DUPJ", "flJ")
+        V(tt, R("oj1", 0, 16), R("flJ", 0, 16), R("DUJ", 0, 16), A.mult)
+        V(tt, R("oj2", 0, 16), R("oj1", 0, 16), JJ, A.max)
+        V(tt, R("oj3", 0, 16), R("oj2", 0, 16), R("DUJ", 0, 16), A.min)
+        V(tc, R("oJu", 0, 16), R("oj3", 0, 16))
+        S(R("Lold", 0, 256), ind(R("L", 0, 2304), R("oJu", 0, 16)), F.Copy)
+        V(ts, R("mk", 0, 256), R("b6", 256, 512), c1("k15"), None, A.is_equal)
+        V(tt, R("b6", 0, 256), R("b6", 0, 256), R("Lold", 0, 256), A.subtract)
+        V(tt, R("t2", 0, 256), R("b6", 0, 256), R("mk", 0, 256), A.mult)
+        V(tt, ind(R("L", 0, 2304), R("oJu", 0, 16)), R("t2", 0, 256), R("Lold", 0, 256), A.add)
+    dma("s", "yz", R("z3", 0, 256), 512, "d9")
+    dma("y", "yl", R("L", 0, 2048), 8192, "d10")
+    return ops
+
+
+def bank(r):
+    return r[0] if r[0][0] == "b" and len(r[0]) == 2 else None
+
+
+def edges(ops):
+    touched, pre = {}, []
+    for o in ops:
+        e = {}
+        for w, rs in ((True, o["writes"]), (False, o["reads"])):
+            for r in rs:
+                key = PLACE[r[0]][0] if False else r[0]
+                for (j, s, sw) in touched.get(key, []):
+                    same = ops[j]["q"] == o["q"]
+                    if bank(r):
+                        if not same:
+                            e[j] = True
+                        elif o["q"] == "t":
+                            e.setdefault(j, False)
+                        elif (w or sw) and clash(r, s):
+                            e[j] = e.get(j, False) or bool(sw)
+                    elif (w or sw) and clash(r, s):
+                        need = True if not same else (sw or ops[j]["kind"] == "dma")
+                        e[j] = e.get(j, False) or bool(need)
+        pre.append(e)
+        for w, rs in ((True, o["writes"]), (False, o["reads"])):
+            for r in rs:
+                touched.setdefault(r[0], []).append((o["i"], r, w))
+    return pre
+
+
+def label(o):
+    r = (o["writes"] or o["reads"])[0]
+    return o["q"] + r[0] + ("@%d" % r[1] if r[0][0] == "b" else "")
+
+
+def schedule(ops, pre, bias):
+    n = len(ops)
+    succ = [[] for _ in range(n)]
+    for i in range(n):
+        for j in pre[i]:
+            succ[j].append(i)
+    rankv = [0.0] * n
+    for i in range(n - 1, -1, -1):
+        o = ops[i]
+        b = 0.0
+        for k in succ[i]:
+            b = max(b, rankv[k] + (WAKE if pre[k][i] else 0.0))
+        rankv[i] = b + o["cost"] + o["lat"]
+    rankv = [rankv[i] + bias.get(label(ops[i]), 0.0) for i in range(n)]
+    left = [len(pre[i]) for i in range(n)]
+    ready = [0.0] * n
+    free = {}
+    avail = [i for i in range(n) if left[i] == 0]
+    order, start = [], [0.0] * n
+    while avail:
+        best = None
+        for i in avail:
+            s = max(ready[i], free.get(ops[i]["q"], 0.0))
+            key = (s, -rankv[i])
+            if best is None or key < best[0]:
+                best = (key, i)
+        s0, q = best[0][0], ops[best[1]]["q"]
+        i = best[1]
+        for k in avail:
+            if ops[k]["q"] == q and max(ready[k], free.get(q, 0.0)) <= s0 + 40 and rankv[k] > rankv[i]:
+                i = k
+        s = max(ready[i], free.get(q, 0.0))
+        avail.remove(i)
+        start[i] = s
+        free[q] = s + ops[i]["cost"]
+        order.append(i)
+        fin = s + ops[i]["cost"] + ops[i]["lat"]
+        for k in succ[i]:
+            ready[k] = max(ready[k], fin + (WAKE if pre[k][i] else 0.0) if pre[k][i] else s)
+            left[k] -= 1
+            if left[k] == 0:
+                avail.append(k)
+    return order, start
+
+
+URGE = """
+vmk:-5 vDUPE:-1 vb6@0:-10 tb1@0:-16 vCS:31 sAy_1:-8 vONH:-16 vmx_0:-6 vI:-11 ve_rq:8 vp16i:9 szx1:-5 vx_1:13 vQ16:15 vUQ:-19 sAf_1:-8 vpk1:-21 vDUE:7 vDUPJ:-4 vmx_1:-5 vMMIN:-9 vBLK:8 tb6@256:25 szx0:-16 tb6@0:29 sAy_0:-4 vle_0:1 vch:6 tb5@0:4 vkm_0:17 vDy_1:-2 vk15:12 voEu:-19 sDM:2 vJh:4 vsi_0:5 vRPR:13 vp16:8 shki:-7 vRPN:13 vej_0:-5 vvi:4 vEQE:1 vL:6 gz1:2 yG:-15 vIW:-4 vsm_1:4 vpk3:4 yixi:3 vle_1:2 vOWN:-8 vsi_1:9 vsj_1:-1 yL:23 tb4@0:-5 gduI:7 vzs0:-3 sAG_1:1 vDG_0:-6 yxb:4 vzx0:-14 vZQ:-10 vemh:-1 vtf:-11 ylki:-12 vzs2:-11 gdI:2 tb7@16:-9 vej_1:2 vzx1:-1 vZB:1 vKM:2 sRL:3 vG:4 vMMAX:5 tb6@128:16 vDG_1:-5 vME_1:-4 vscj:-5 vUH:-10 gz3:-9 vBLN:-6 yz0:-4 vsj_0:1 vpk2:4 vPICK:2 sL:4 vnu_1:7 sJf:1 vONB:3 vEQJ:5 veu_0:9 voJu:-3 vx_0:-4 vW8:9 vINB:-1 voj3:2 vRPK:-3 vOFFR:8 gr15I:-1 vJu_0:-4 vCD:-6 voj2:-5 vt2:1 vDy_0:6 tb4@256:6 vIB:-6 tb1@128:6 vQT_1:-1 sx_0:3 tb7@128:3 grI:-7 sPQ_1:3 vTHR:-4 vDM:-1 sz3:-8 veu_1:-4 vfl:1 vdgA:-3 vuu:-1 vAc:5 vcs_1:-1 vME_0:-3 tb2@256:-10 szt:1 voj1:1 vmj:-1 vnr:-2 gdgI:3 sEr:6 vwf:-1 sLg_0:-3 vMK:3 gz2:3 gcI:3 sRLu:-5 sRJh:3 vzs1:-1 tb0@0:5 vog2:-3 sthi:-5 vkm_1:1 ggI:8 vof1:5 sAG_0:-1 tb7@8:-3 sLold:1
+"""
+OPT = {"gchunk": 1, "ychunk": 4, "lv": (0, 0), "xv": (0, 1), "zv": (0, 0, 0), "rg": (0, 0), "ry": (0, 0),
+       "bias": {w.split(":")[0]: 500.0 * int(w.split(":")[1]) for w in URGE.split()}}
+PLAN = {}
+
+
+def rank_program(g, core, T, topo):
+    rank = T.rank_of(core)
+    if rank is None:
+        return
+    if "ops" not in PLAN:
+        PLAN["ops"] = build(rank, OPT)
+        PLAN["pre"] = edges(PLAN["ops"])
+        PLAN["order"], PLAN["start"] = schedule(PLAN["ops"], PLAN["pre"], OPT["bias"])
+    ops, pre = PLAN["ops"], PLAN["pre"]
+    nxt = T.cores[(rank + 1) % len(T.cores)]
+    home = T.cores[(rank + 2) % len(T.cores)]
+    queue = {"v": g.vector, "s": g.scalar, "t": g.tensor, "g": g, "y": g.sync}
+    qsem = {"v": "qv", "s": "qs", "t": "qt", "g": "qg"}
+    count = {}
+    seen = {q: {} for q in queue}
+    done = {}
+
+    def ap(r):
+        if isinstance(r, IndOp):
+            return ap(r[0]).indirect(ap(r[1]))
+        name, off = PLACE[r[0]]
+        a, b, st, p = r[1] + off, r[2] + off, r[3], r[4]
+        t = T[name]
+        if st == 1:
+            return t[:, a:b] if p == 128 else t[0:p, a:b]
+        return t[:, a:b:st]
+
+    def arg(x):
+        return ap(x) if isinstance(x, tuple) else x
+
+    place = {i: n for n, i in enumerate(PLAN["order"])}
+    for i in PLAN["order"]:
+        o = ops[i]
+        q, eng = o["q"], queue[o["q"]]
+        known = seen[q]
+        for j in sorted(pre[i], key=lambda j: -place[j]):
+            if not pre[i][j]:
+                continue
+            sem, val, kn = done[j]
+            if known.get(sem, 0) < val:
+                eng.wait_ge(T.sem[sem], val)
+                for k in kn:
+                    known[k] = max(known.get(k, 0), kn[k])
+                known[sem] = max(known.get(sem, 0), val)
+        if o["kind"] == "dma":
+            out, in_ = o["calls"][0]
+            out = ap(out) if isinstance(out, tuple) else T[out][:]
+            in_ = ap(in_) if isinstance(in_, tuple) else T[in_][:]
+            eng.dma_start(out, in_).then_inc(T.sem[o["sem"]], 16)
+            done[i] = (o["sem"], 16, dict(known))
+            count[o["sem"]] = 16
+            continue
+        if o["kind"] == "remote":
+            t = o["calls"][0][0]
+            dst = nxt if t < 2 else home
+            rid, pid, _e = topo.addr(dst)
+            g.remote_dma(T["z%d" % (t + 1)][:], T["zs%d" % t][:], T.sem["arr%d" % (t + 1)], T.sem["loc"], pid, rid, topo.mask(core, dst))
+            m = len(topo.engines(core, dst))
+            src = T.cores[(rank - 1) % len(T.cores)] if t < 2 else T.cores[(rank - 2) % len(T.cores)]
+            count["loc"] = count.get("loc", 0) + m
+            done[i] = ("arr%d" % (t + 1), len(topo.engines(src, core)), {})
+            continue
+        sem = qsem[q]
+        for c in o["calls"]:
+            if o["kind"] == "matmul":
+                ins = g.tensor.matmul(ap(c[0]), ap(c[1]), ap(c[2]), c[3], c[4])
+            elif o["kind"] == "activation":
+                kw = {}
+                if c[3] is not None:
+                    kw["bias"] = arg(c[3])
+                if c[4] is not None:
+                    kw["scale"] = arg(c[4])
+                ins = g.scalar.activation(ap(c[0]), ap(c[1]), c[2], **kw)
+            elif o["kind"] == "iota":
+                ins = g.iota(ap(c[0]), c[1], c[2], c[3])
+            else:
+                x = [arg(y) for y in c]
+                k = o["kind"]
+                if k == "tensor_copy":
+                    ins = g.vector.tensor_copy(*x)
+                elif k == "tensor_scalar":
+                    ins = g.vector.tensor_scalar(*x)
+                elif k == "tensor_tensor":
+                    ins = g.vector.tensor_tensor(*x)
+                elif k == "tensor_tensor_scan":
+                    ins = g.vector.tensor_tensor_scan(*x)
+                elif k == "tensor_reduce":
+                    ins = g.vector.tensor_reduce(x[0], x[1], AxisListType.X, x[3])
+                else:
+                    ins = g.vector.memset(*x)
+            ins.then_inc(T.sem[sem], 1)
+            count[sem] = count.get(sem, 0) + 1
+        kn = dict(known)
+        kn[sem] = count[sem]
+        done[i] = (sem, count[sem], kn)
+    for sem in sorted(count):
+        g.wait_ge(T.sem[sem], count[sem])

@@ -1,57 +1,54 @@
 import numpy as np
+from concourse.bass import DstId, RemoteDMATransfer
 from concourse.mybir import AluOpType as A, AxisListType, ActivationFunctionType as F
 
 BIG = 1.0e9
 OFF24 = 16777216.0
 CYC = 0.8333
-GAT, SCA, WAKE, FIX = 1.56, 3.8, 70.0, 20.0
-SCRATCH, SIZES = {}, {}
+GAT, SCA, WAKE, FIX, SFIX = 1.56, 3.8, 90.0, 20.0, 120.0
+DLAT, DRATE, RLAT, FLAT, RCOST = 1500.0, 200.0, 5000.0, 12000.0, 800.0
+SCRATCH = {}
 TWO = ("bfloat16", "float16", "uint16")
+SEG = (0, 16, 48, 96)
 
 
 def _buf(name, cols, dtype, where="sbuf"):
     SCRATCH[name] = (where, [128, cols], dtype)
 
 
+_B, _H, _F, _I, _U = "bfloat16", "float16", "float32", "int32", "uint16"
 for _n, _c, _d in (
-        ("xb", 2048, "bfloat16"), ("G", 1280, "bfloat16"), ("ixi", 1024, "int32"), ("I", 1280, "float32"),
-        ("lki", 2048, "int32"), ("L", 2304, "float32"),
-        ("wti", 1, "int32"), ("hki", 2, "int32"), ("thi", 2, "int32"),
-        ("z0", 256, "bfloat16"), ("z1", 256, "bfloat16"), ("z2", 256, "bfloat16"), ("z3", 256, "bfloat16"),
-        ("zs0", 256, "bfloat16"), ("zs1", 256, "bfloat16"), ("zs2", 256, "bfloat16"), ("zt", 256, "bfloat16"),
-        ("pI", 1, "int32"), ("p16i", 1, "int32"), ("pgi", 1, "int32"), ("pf", 1, "float32"), ("p16", 1, "float32"),
-        ("pg", 1, "float32"), ("pz", 1, "float32"), ("colA", 1, "float32"), ("colB", 1, "float32"), ("k15", 1, "float32"),
-        ("wf", 1, "float32"), ("hf", 2, "float32"), ("tf", 2, "float32"),
-        ("dI", 144, "int32"), ("cI", 144, "int32"), ("gI", 128, "int32"), ("g8I", 16, "int32"), ("rI", 256, "int32"),
-        ("dgI", 128, "int32"), ("duI", 16, "int32"), ("r15I", 256, "int32"),
-        ("IW", 136, "float16"), ("IB", 136, "bfloat16"), ("INB", 136, "bfloat16"), ("BB", 128, "bfloat16"), ("BH", 128, "float16"),
-        ("BLK", 16, "bfloat16"), ("Q16", 8, "float16"), ("MK", 256, "float16"), ("ZB", 144, "bfloat16"),
-        ("SEL", 2048, "float16"), ("KM", 16, "float32"), ("CD", 128, "bfloat16"), ("CS", 256, "bfloat16"),
-        ("ONB", 128, "bfloat16"), ("ONH", 128, "float16"), ("MMIN", 128, "float32"), ("MMAX", 256, "float32"),
-        ("MR", 2048, "bfloat16"), ("OFFR", 8, "uint16"), ("pk1", 1, "float32"), ("pk2", 1, "float32"), ("pk3", 1, "float32"),
-        ("PICK", 2, "uint16"), ("DUE", 16, "float32"), ("DUJ", 16, "float32"), ("DM", 2176, "bfloat16"), ("OWN", 16, "bfloat16"),
-        ("RPR", 128, "float16"), ("RPJ", 128, "float16"), ("RPt", 128, "float16"), ("RPN", 128, "float16"), ("RPK", 128, "float16"),
-        ("dgA", 128, "float16"), ("THR", 128, "float32"), ("Wb", 128, "bfloat16"),
-        ("W8", 8, "bfloat16"), ("ZQ", 200, "float16"), ("PM_0", 128, "float16"), ("PM_1", 128, "float16"), ("PQ_0", 128, "float16"), ("PQ_1", 128, "float16"),
-        ("C0", 256, "bfloat16"), ("BL2", 16, "bfloat16"), ("BLN", 16, "bfloat16"), ("CDi", 128, "bfloat16"), ("CSi", 256, "bfloat16"),
-        ("ui", 16, "int32"), ("uu", 16, "int32"), ("UQ", 48, "int32"), ("UH", 48, "float16"), ("RLu", 128, "float16"), ("em", 256, "int32"), ("emu", 256, "uint16"), ("emh", 256, "float16"),
-        ("sh4", 256, "int32"), ("vi", 256, "int32"), ("vJ", 256, "float32"), ("Jf", 256, "float32"), ("Jh", 256, "float16"),
-        ("zx0", 4096, "bfloat16"), ("zx1", 4096, "bfloat16"), ("e_rq", 16, "float32"), ("Y", 256, "float16"), ("Er", 256, "float16"),
-        ("far", 256, "float32"), ("ch", 256, "float32"), ("tmp", 256, "float32"), ("RL", 256, "float16"), ("RJh", 256, "float16"),
-        ("mj", 256, "float32"), ("scj", 256, "float32"), ("EQE", 2176, "bfloat16"), ("DUPE", 2176, "bfloat16"),
-        ("EQJ", 2176, "bfloat16"), ("DUPJ", 2176, "bfloat16"), ("fl", 16, "float32"), ("of1", 16, "float32"), ("of2", 16, "float32"),
-        ("nr", 16, "float32"), ("og1", 16, "float32"), ("og2", 16, "float32"), ("flJ", 16, "float32"), ("oj1", 16, "float32"),
-        ("oj2", 16, "float32"), ("oj3", 16, "float32"), ("oEu", 16, "uint16"), ("oGu", 16, "uint16"), ("oJu", 16, "uint16"),
-        ("Lold", 256, "float32"), ("mk", 256, "float32"), ("t1", 256, "float32"), ("t2", 256, "float32"), ("Ac", 1, "float32")):
+        ("xb", 2048, _B), ("G", 1088, _B), ("ixi", 1024, _I), ("I", 1088, _F), ("lki", 2048, _I), ("L", 2112, _F),
+        ("wti", 1, _I), ("hki", 2, _I), ("thi", 2, _I),
+        ("z0", 256, _B), ("z1", 256, _B), ("z2", 256, _B), ("z3", 256, _B),
+        ("zs0", 256, _B), ("zs1", 256, _B), ("zs2", 256, _B), ("zt", 256, _B),
+        ("pI", 1, _I), ("p16i", 1, _I), ("pgi", 1, _I), ("pf", 1, _F), ("p16", 1, _F), ("pg", 1, _F), ("colA", 1, _F), ("colB", 1, _F),
+        ("k15", 1, _F), ("wf", 1, _F), ("hf", 2, _F), ("tf", 2, _F), ("q2i", 1, _I), ("bI", 1, _I), ("pk1", 1, _F), ("pk2", 1, _F), ("pk3", 1, _F),
+        ("pk4", 1, _F), ("dI", 144, _B), ("cI", 144, _B), ("gI", 128, _B), ("g8I", 16, _I), ("rI", 128, _B), ("dg4", 128, _B), ("duI", 16, _I),
+        ("r15I", 128, _B), ("slI", 16, _B), ("qrel", 160, _B), ("dcol", 160, _B), ("SM", 320, _B),
+        ("IW", 136, _H), ("IB", 136, _B), ("INB", 136, _B), ("BHn", 128, _H), ("BLK", 8, _B), ("Q16", 8, _H), ("MK", 128, _H), ("ZB", 144, _B),
+        ("SEL", 2048, _H), ("KM", 16, _F), ("CD", 128, _B), ("CS", 128, _B), ("ONB", 128, _B), ("ONn", 128, _H), ("MMIN", 128, _F), ("OF15", 8, _U), ("nrx", 256, _H),
+        ("MMAX", 128, _F), ("MR", 2048, _B), ("OFFR", 8, _U), ("PK", 2, _U), ("DUE", 16, _F), ("DUn", 16, _H),
+        ("RPn", 128, _H), ("RPc", 128, _H), ("RPJ", 128, _H), ("RPt", 128, _H), ("RPK", 128, _H), ("SLW", 16, _H), ("I4n", 128, _H),
+        ("E2", 320, _H), ("EC", 640, _H), ("TR", 320, _H), ("Ju16", 16, _U), ("dgA", 128, _H), ("dgB", 128, _H), ("dgC", 128, _H), ("THR", 128, _F),
+        ("W8", 8, _B), ("ZQ", 328, _H), ("PM_0", 128, _H), ("PM_1", 128, _H), ("PQ_0", 128, _H), ("PQ_1", 128, _H),
+        ("ui", 16, _I), ("uu", 16, _I), ("UQ", 48, _I), ("UH", 48, _H), ("RLu", 128, _H), ("em", 256, _I), ("emu", 256, _U), ("emh", 256, _H),
+        ("vi", 256, _I), ("Jf", 256, _F), ("Jh", 256, _H), ("zx0", 4096, _B), ("zx1", 4096, _B), ("Y", 256, _H), ("eu", 16, _U),
+        ("ch", 256, _F), ("tmp", 256, _F), ("RL", 256, _H), ("WT", 256, _H), ("AdE", 640, _B), ("AdJ", 640, _B), ("msE", 640, _B), ("msJ", 640, _B),
+        ("aE", 16, _F), ("tE", 16, _F), ("oE", 16, _F), ("oEu", 16, _U), ("aJ", 16, _F), ("tJ", 16, _F), ("oJ", 16, _F), ("oJu", 16, _U),
+        ("dz", 256, _B), ("tg", 256, _B), ("le", 256, _B), ("cs", 256, _B), ("sm", 256, _F), ("si", 16, _I), ("SJ", 32, _I), ("QT", 64, _H),
+        ("Lold", 256, _F), ("mk", 256, _F), ("t2", 256, _F), ("Nc", 1, _F), ("fT", 256, _H), ("BBn", 128, _B), ("BL1", 8, _B), ("BL2", 8, _B),
+        ("BKn", 8, _B), ("BK2", 8, _B), ("zT", 128, _B), ("EN", 2048, _B)):
     _buf(_n, _c, _d)
+for _t in "012":
+    for _h in "01":
+        _buf("M" + _t + _h, 2048, _B)
 for _h in "01":
-    for _n, _c, _d in (("DG", 2048, "bfloat16"), ("AG", 2048, "bfloat16"), ("x", 2064, "bfloat16"), ("Lg", 2048, "float16"), ("mx", 2048, "bfloat16"),
-                       ("Dy", 2048, "bfloat16"), ("Ay", 2048, "bfloat16"), ("Af", 2048, "bfloat16"), ("km", 128, "float32"),
-                       ("ei", 8, "int32"), ("ej", 8, "int32"), ("ME", 128, "float16"), ("eu", 8, "uint16"), ("Ju", 128, "uint16"), ("nu", 128, "uint16"),
-                       ("le", 128, "bfloat16"), ("cs", 128, "bfloat16"), ("sm", 256, "float32"), ("si", 16, "int32"), ("sj", 24, "int32"), ("QT", 32, "float16")):
+    for _n, _c, _d in (("DG", 2048, _B), ("AG", 2048, _B), ("x", 2064, _B), ("Lg", 2048, _H), ("mx", 2048, _B), ("Dy", 2048, _B), ("Ay", 2048, _B),
+                       ("km", 128, _F), ("ei", 8, _I), ("ej", 8, _I), ("ME", 128, _H), ("Ju", 128, _U), ("nu", 128, _U)):
         _buf(_n + "_" + _h, _c, _d)
 for _b in range(8):
-    _buf("b%d" % _b, 512, "float32", "psum")
+    _buf("b%d" % _b, 512, _F, "psum")
 PLACE = {}
 _pack = {}
 for _n in sorted(SCRATCH):
@@ -62,13 +59,14 @@ for _n in sorted(SCRATCH):
         _pack[_d] = _o + (_s[1] + 31) // 32 * 32
     else:
         PLACE[_n] = (_n, 0)
+PLACE["lk"] = ("lk", 0)
 DTYPE = {_n: SCRATCH[_n][2] for _n in SCRATCH}
 for _n in list(SCRATCH):
     if PLACE[_n][0] != _n:
         del SCRATCH[_n]
 for _d in _pack:
     _buf("k_" + _d, _pack[_d], _d)
-SEMAPHORES = ["qv", "qs", "qt", "qg", "loc", "arr1", "arr2", "arr3"] + ["d%d" % i for i in range(16)]
+SEMAPHORES = ["qv", "qs", "qt", "qg", "loc"] + [s + str(i) for s in ("arr", "fa", "fb") for i in range(6)] + ["d%d" % i for i in range(16)]
 
 
 def R(buf, a=0, b=None, step=1, p=128):
@@ -87,6 +85,10 @@ def clash(r, s):
     return not (r[3] == s[3] and r[3] > 1 and (r[1] - s[1]) % r[3] != 0)
 
 
+def bank(r):
+    return r[0] if r[0][0] == "b" and len(r[0]) == 2 and r[0][1].isdigit() else None
+
+
 class IndOp(tuple):
     pass
 
@@ -95,8 +97,8 @@ def ind(win, off):
     return IndOp((win, off))
 
 
-def build(rank, opt):
-    ops, loaded = [], [0.0]
+def build(opt):
+    ops = []
 
     def add(q, kind, calls, reads, writes, cost, lat=0.0, **kw):
         ops.append(dict(q=q, kind=kind, calls=calls, reads=reads, writes=writes, cost=cost, lat=lat, i=len(ops), **kw))
@@ -118,41 +120,35 @@ def build(rank, opt):
         wr = flat(out)[:1]
         if isinstance(out, IndOp):
             rd = rd + [out[1]]
-            n = width(out[1]) * 16
-            c = 50 + n * SCA * CYC
+            c = 50 + width(out[1]) * 16 * SCA * CYC
         elif any(isinstance(x, IndOp) for x in full):
             c = 50 + width(out) * GAT * CYC
         elif name == "tensor_tensor":
-            ps = any(x[0][0] == "b" and len(x[0]) == 2 for x in full)
-            c = price(width(out), False, 1.0 if ps else 2.0)
+            c = price(width(out), False, 1.0 if any(bank(x) for x in full) else 2.0)
         elif name == "tensor_reduce":
             c = price(width(args[0]))
         else:
             c = price(width(out), small([out] + [x for x in full if width(x) > 1]))
         add("v", name, [(out,) + args], rd, wr, c)
 
-    def VM(name, items):
-        if not items:
-            return
-        n0 = len(ops)
-        for it in items:
-            V(name, *it)
-        got = ops[n0:]
-        del ops[n0:]
-        add("v", name, [o["calls"][0] for o in got], [r for o in got for r in o["reads"]], [r for o in got for r in o["writes"]], sum(o["cost"] for o in got))
-
     def S(out, in_, func, bias=None, scale=None):
-        c = (65 + width(out) * GAT * CYC) if isinstance(in_, IndOp) else width(out) * CYC + 60
+        c = SFIX + width(out) * CYC * (GAT if isinstance(in_, IndOp) else 1.0)
         rd = flat(in_) + [x for x in (bias, scale) if isinstance(x, tuple)]
         add("s", "activation", [(out, in_, func, bias, scale)], rd, [out], c)
 
+    def C(eng, out, in_):
+        if eng == "v":
+            V("tensor_copy", out, in_)
+        elif eng == "s":
+            S(out, in_, F.Copy)
+        else:
+            add("g", "select", [(out, in_)], [in_], [out], 170 + 2 * width(out) * CYC)
+
     def P(items):
         c = 0.0
-        for o, l, r, a, b in items:
-            f32 = DTYPE[l[0]] == "float32"
-            c += max(min(64, width(l)), width(r)) * (4 if f32 else 1) * CYC + 5
         rd, wr = [], []
         for o, l, r, a, b in items:
+            c += max(min(64, width(l)), width(r)) * CYC + 5
             for x in (l, r):
                 if x not in rd:
                     rd.append(x)
@@ -160,14 +156,16 @@ def build(rank, opt):
                 wr.append(o)
         add("t", "matmul", items, rd, wr, c)
 
+    def group(items):
+        P([(o, l, r, i == 0, i == len(items) - 1) for i, (o, l, r) in enumerate(items)])
+
     def iota(out, pattern, base, cm):
         add("g", "iota", [(out, pattern, base, cm)], [], [out], 130 + 2 * width(out) * CYC)
 
     def dma(q, out, in_, nbytes, sem):
         rd = [in_] if isinstance(in_, tuple) else []
         wr = [out] if isinstance(out, tuple) else []
-        loaded[0] += nbytes * 128 / 200.0 if wr else 0.0
-        add(q, "dma", [(out, in_)], rd, wr, 60, 2000 + (loaded[0] if wr else nbytes * 128 / 200.0), sem=sem)
+        add(q, "dma", [(out, in_)], rd, wr, 60, DLAT + nbytes * 128 / DRATE, sem=sem, nbytes=nbytes * 128)
 
     dma("y", R("z0", 0, 256), "zc", 512, "d0")
     dma("s", R("wti", 0, 1), "wt", 4, "d1")
@@ -176,120 +174,110 @@ def build(rank, opt):
     dma("y", R("ixi", 0, 1024), "ix", 4096, "d4")
     dma("y", R("xb", 0, 2048), "xc", 4096, "d5")
     dma("s", R("thi", 0, 2), "th", 8, "d6")
-    dma("y", R("lki", 0, 2048), "lk", 8192, "d7")
+    dma("y", R("lki", 0, 1024), R("lk", 0, 1024), 4096, "d7")
+    dma("y", R("lki", 1024, 2048), R("lk", 1024, 2048), 4096, "d11")
     iota(R("pI", 0, 1), [[0, 1]], 0, 1)
-    iota(R("gI", 0, 128), [[1, 8], [0, 16]], 0, 0)
-    iota(R("dI", 0, 144), [[1, 144]], 0, -1)
     iota(R("g8I", 0, 16), [[0, 2], [1, 8]], 0, 0)
-    iota(R("rI", 0, 256), [[0, 16], [1, 16]], 0, 0)
-    iota(R("cI", 0, 144), [[1, 144]], 0, 0)
-    iota(R("r15I", 0, 256), [[0, 16], [-1, 16]], 15, 0)
-    iota(R("duI", 0, 16), [[16, 16]], 0, 0)
-    iota(R("dgI", 0, 128), [[1, 8], [0, 16]], 0, -1)
+    iota(R("dI", 0, 144), [[1, 144]], 0, -1)
+    iota(R("gI", 0, 128), [[1, 8], [0, 16]], 0, 0)
+    iota(R("rI", 0, 128), [[0, 8], [1, 16]], 0, 0)
+    iota(R("r15I", 0, 128), [[0, 8], [-1, 16]], 15, 0)
+    iota(R("duI", 0, 16), [[0, 4], [-16, 4]], 0, 0)
+    iota(R("dg4", 0, 128), [[4, 8], [0, 16]], 0, -1)
+    iota(R("slI", 0, 16), [[1, 2], [4, 8]], 0, -1)
+    for q in range(4):
+        a, n = SEG[q], 16 * (q + 1)
+        iota(R("qrel", a, a + n), [[0, n]], q, 0)
+        iota(R("dcol", a, a + n), [[1, n]], -16 * q, 0)
+        iota(R("SM", a, a + n), [[-1, n]], 1, 0)
+    iota(R("MR", 0, 2048), [[0, 128], [64, 16]], 0, 0)
     c1 = lambda b: R(b, 0, 1)
-    ts, tt, tc = "tensor_scalar", "tensor_tensor", "tensor_copy"
+    ts, tt, tc, scan = "tensor_scalar", "tensor_tensor", "tensor_copy", "tensor_tensor_scan"
+    I16, IB, ISH = R("IW", 4, 132), R("IB", 4, 132), R("IW", 5, 133)
     V(ts, c1("pgi"), c1("pI"), 4, None, A.arith_shift_right)
     V(tc, c1("pg"), c1("pgi"))
     V(tc, c1("wf"), c1("wti"))
     V(ts, R("W8", 0, 8), R("g8I", 0, 8), c1("pg"), c1("wf"), A.is_equal, A.mult)
     V(tc, R("hf", 0, 2), R("hki", 0, 2))
-    V("memset", R("ZQ", 0, 200), 0.0)
+    V("memset", R("ZQ", 0, 328), 0.0)
     V(ts, R("ZQ", 48, 56), R("g8I", 0, 8), c1("pg"), None, A.is_equal)
-    V(ts, R("ZQ", 152, 160), R("g8I", 0, 8), c1("pg"), 0.0625, A.is_equal, A.mult)
-    V(ts, R("BH", 0, 128), R("gI", 0, 128), c1("pg"), None, A.is_equal)
+    V(ts, R("ZQ", 152, 160), R("g8I", 0, 8), c1("pg"), -0.0625, A.is_equal, A.mult)
+    V(ts, R("BHn", 0, 128), R("gI", 0, 128), c1("pg"), -1.0, A.is_equal, A.mult)
     V(ts, c1("p16i"), c1("pI"), 15, None, A.bitwise_and)
     V(tc, c1("p16"), c1("p16i"))
     V(tc, c1("pf"), c1("pI"))
     V(ts, R("IW", 0, 136), R("dI", 0, 136), 4.0, None, A.is_equal)
-    V(ts, R("BLK", 0, 16), R("g8I", 0, 16), c1("pg"), 32768.0, A.is_equal, A.mult)
+    V(ts, R("BLK", 0, 8), R("g8I", 0, 8), c1("pg"), 32768.0, A.is_equal, A.mult)
     V(ts, R("Q16", 0, 8), R("g8I", 0, 8), c1("pg"), None, A.is_equal)
-    V(ts, R("MK", 0, 256), R("rI", 0, 256), c1("p16"), None, A.is_equal)
+    V(ts, R("MK", 0, 128), R("rI", 0, 128), c1("p16"), None, A.is_equal)
     V(tc, R("OFFR", 0, 8), R("g8I", 0, 8))
     V(ts, c1("colA"), c1("pf"), 64.0, 32.0, A.is_ge, A.mult)
     V(ts, c1("colB"), c1("pf"), 64.0, -262144.0, A.is_lt, A.mult)
     V("memset", R("ONB", 0, 128), 1.0)
     V(ts, R("CD", 0, 128), R("rI", 0, 128), c1("colA"), c1("colB"), A.mult, A.add)
-    V(ts, R("mj", 0, 256), R("rI", 0, 256), 0.0, 2 * BIG, A.is_equal, A.mult)
-    V(ts, R("MMIN", 0, 128), R("mj", 0, 128), -BIG, None, A.add)
-    V("memset", c1("pz"), 0.0)
+    V(ts, R("MMIN", 0, 128), R("rI", 0, 128), 0.0, BIG, A.is_equal, A.mult)
 
-    def factors(j, name, at):
-        V(ts, R("dgA", 0, 128), R("IW", 4, 132), R("hf", j, j + 1), None, A.mult)
+    def factors(j, name, at, dg):
+        V(ts, R(dg, 0, 128), I16, R("hf", j, j + 1), None, A.mult)
         for h in (0, 1):
-            o = R("b4", 128 + 128 * h, 256 + 128 * h, 1, 48)
-            P([(o, R("ZQ", 48 - 8 * h, 96 - 8 * h), R("dgA", 0, 128), True, False), (o, R("ZQ", at - 8 * h, at + 48 - 8 * h), R("BH", 0, 128), False, True)])
+            o = R("b%d" % (4 + h), 128 * j, 128 * j + 128, 1, 48)
+            group([(o, R("ZQ", 48 - 8 * h, 96 - 8 * h), R(dg, 0, 128)), (o, R("ZQ", at - 8 * h, at + 48 - 8 * h), R("BHn", 0, 128))])
             S(R(name + str(h), 0, 128, 1, 48), o, F.Copy)
-    factors(0, "PM_", 120)
-    if any(opt["rg"]):
-        V("memset", R("C0", 0, 256), -131072.0)
-        V(ts, R("BL2", 0, 16), R("BLK", 0, 16), 2.0, None, A.mult)
-        V(ts, R("BLN", 0, 16), R("BLK", 0, 16), -1.0, None, A.mult)
-        V(ts, R("CDi", 0, 128), R("rI", 0, 128), c1("colA"), None, A.mult)
-
-    def load_names():
-        V(tc, R("I", 0, 1024), R("ixi", 0, 1024))
-
-    def load_links():
-        V("memset", R("L", 2048, 2304), 0.0)
-        S(R("L", 0, 1024), R("lki", 0, 1024), F.Copy)
-        S(R("L", 1024, 2048), R("lki", 1024, 2048), F.Copy)
-
-    def late_constants():
-        V(ts, R("IB", 0, 136), R("dI", 0, 136), 4.0, None, A.is_equal)
-        V(ts, R("INB", 0, 136), R("dI", 0, 136), 4.0, -1.0, A.is_equal, A.mult)
-        V(ts, R("KM", 0, 16), R("rI", 0, 16), c1("p16"), None, A.is_equal)
-        for k in range(16):
-            S(R("SEL", 128 * k, 128 * k + 128), R("IW", 4, 132), F.Copy, None, R("KM", k, k + 1))
-        V("memset", R("MR", 0, 2048), 1.0)
-        V("memset", R("MR", 0, 2048, 16), 0.0)
-        V("memset", R("x_0", 2048, 2064), 0.0)
-        V("memset", R("x_1", 2048, 2064), 0.0)
-        V(ts, c1("pk3"), c1("pg"), 16.0, 15.0, A.mult, A.add)
-        V(ts, R("ZB", 0, 144), R("cI", 0, 144), c1("pk3"), None, A.is_equal)
-        V(ts, R("CS", 0, 256), R("r15I", 0, 256), c1("colA"), c1("colB"), A.mult, A.add)
-        V(ts, R("MMAX", 0, 256), R("mj", 0, 256), -1.0, BIG, A.mult, A.add)
-        V(tc, R("tf", 0, 2), R("thi", 0, 2))
-        V("memset", R("ONH", 0, 128), 1.0)
-        V(ts, R("dgA", 0, 128), R("IW", 4, 132), R("tf", 0, 1), None, A.mult)
-        P([(R("b4", 0, 128), R("ONH", 0, 128), R("dgA", 0, 128), True, True)])
-        V(ts, R("THR", 0, 128), R("b4", 0, 128), 32768.0, 32768.0 - OFF24, A.mult, A.add)
-        V("memset", R("THR", 15, 128, 16), -2.0e7)
-        factors(1, "PQ_", 136)
-        if not any(opt["rg"]):
-            V("memset", R("C0", 0, 256), -131072.0)
-            V(ts, R("BL2", 0, 16), R("BLK", 0, 16), 2.0, None, A.mult)
-            V(ts, R("BLN", 0, 16), R("BLK", 0, 16), -1.0, None, A.mult)
-        V(ts, R("CSi", 0, 256), R("r15I", 0, 256), c1("colA"), None, A.mult)
-        V(ts, c1("pk1"), c1("p16"), 8.0, 24.0, A.mult, A.add)
-        V(tt, c1("pk2"), c1("pk1"), c1("p16"), A.mult)
-        V(ts, R("PICK", 0, 1), c1("pk2"), 15.0, None, A.add)
-        V(ts, R("DUE", 0, 16), R("duI", 0, 16), c1("p16"), 1024.0, A.add, A.add)
-        V(ts, R("DUJ", 0, 16), R("duI", 0, 16), c1("p16"), 2048.0, A.add, A.add)
-        V("memset", R("DM", 0, 2176), 1.0)
-        V(ts, R("OWN", 0, 16), R("rI", 0, 16), c1("p16"), 1.0, A.is_equal, A.add)
-        for q in range(16):
-            e = 8 * (q + 1) * (q + 2)
-            S(R("DM", e - 16, e), R("OWN", 0, 16), F.Copy)
-        for q in range(16):
-            s = 8 * q * (q + 1)
-            S(R("DM", s, s + 1), c1("pz"), F.Copy)
-        V(ts, c1("k15"), c1("p16"), -1.0, 15.0, A.mult, A.add)
-        V(ts, R("RPR", 0, 128), R("dgI", 0, 128), 0.0, None, A.is_equal)
-        V(ts, R("RPt", 0, 128), R("dgI", 0, 128), 0.0, 4096.0, A.is_equal, A.mult)
-        V(ts, R("RPJ", 0, 128), R("dgI", 0, 128), -8.0, None, A.is_equal)
-        V(tt, R("RPJ", 0, 128), R("RPJ", 0, 128), R("RPt", 0, 128), A.add)
-        V(ts, R("RPN", 0, 128), R("dgI", 0, 128), -16.0, None, A.is_equal)
-        V(ts, R("RPK", 0, 128), R("dgI", 0, 128), -24.0, None, A.is_equal)
-
-    def dedupe(row, col, cw, eq, du, fl):
-        items = []
-        for q in range(16):
-            s, n = 8 * q * (q + 1), 16 * (q + 1)
-            items.append((R(eq, s, s + n), R(row, 0, n), cw(q), None, A.is_equal))
-        for a in range(0, 16, 4):
-            VM(ts, items[a:a + 4])
-        V("tensor_tensor_scan", R(du, 0, 2176), R("DM", 0, 2176), R(eq, 0, 2176), 0.0, A.mult, A.max)
-        V(ts, R(fl, 0, 16), ind(R(du, 0, 2176), R("PICK", 0, 1)), -1.0, None, A.add)
+    factors(0, "PM_", 120, "dgA")
+    factors(1, "PQ_", 136, "dgB")
+    C(opt["icv"], R("I", 0, 1024), R("ixi", 0, 1024))
+    for c in range(2):
+        C(opt["lcv"][c], R("L", 1024 * c, 1024 * c + 1024), R("lki", 1024 * c, 1024 * c + 1024))
+    V(ts, R("IB", 0, 136), R("dI", 0, 136), 4.0, None, A.is_equal)
+    V(ts, R("BBn", 0, 128), R("gI", 0, 128), c1("pg"), -1.0, A.is_equal, A.mult)
+    V(ts, R("BL1", 0, 8), R("g8I", 0, 8), c1("pg"), -1.0, A.is_equal, A.mult)
+    V(ts, R("BL2", 0, 8), R("g8I", 0, 8), c1("pg"), 2.0, A.is_equal, A.mult)
+    V(ts, R("KM", 0, 16), R("rI", 0, 16), c1("p16"), None, A.is_equal)
+    for k in range(16):
+        if k < opt["selv"]:
+            V(ts, R("SEL", 128 * k, 128 * k + 128), I16, R("KM", k, k + 1), None, A.mult)
+        else:
+            S(R("SEL", 128 * k, 128 * k + 128), I16, F.Copy, None, R("KM", k, k + 1))
+    V("memset", R("x_0", 2048, 2064), 0.0)
+    V("memset", R("x_1", 2048, 2064), 0.0)
+    V(ts, R("CS", 0, 128), R("r15I", 0, 128), c1("colA"), c1("colB"), A.mult, A.add)
+    V(ts, R("MMAX", 0, 128), R("rI", 0, 128), 0.0, -BIG, A.is_equal, A.mult)
+    V(tc, R("tf", 0, 2), R("thi", 0, 2))
+    V("memset", R("ONn", 0, 128), -1.0)
+    V(ts, R("dgC", 0, 128), I16, R("tf", 0, 1), None, A.mult)
+    group([(R("b4", 256, 384), R("ONn", 0, 128), R("dgC", 0, 128))])
+    V(ts, R("THR", 0, 128), R("b4", 256, 384), -32768.0, 32768.0 - OFF24, A.mult, A.add)
+    V("memset", R("THR", 15, 128, 16), -2.0e7)
+    V(ts, c1("q2i"), c1("pI"), 3, None, A.bitwise_and)
+    V(ts, c1("bI"), c1("p16i"), 2, None, A.arith_shift_right)
+    V(ts, c1("pk1"), c1("q2i"), 8.0, 8.0, A.mult, A.add)
+    V(ts, c1("pk2"), c1("q2i"), 2.0, c1("pk1"), A.add, A.mult)
+    V(ts, c1("pk4"), c1("bI"), 160.0, c1("pk2"), A.mult, A.add)
+    V(ts, R("PK", 0, 1), c1("pk4"), -1.0, None, A.add)
+    V(ts, R("DUn", 0, 16), R("duI", 0, 16), c1("p16"), None, A.subtract)
+    V(ts, R("DUE", 0, 16), R("DUn", 0, 16), -1.0, 1024.0, A.mult, A.add)
+    V(ts, c1("k15"), c1("p16"), -1.0, 15.0, A.mult, A.add)
+    V(ts, R("RPc", 0, 128), R("dg4", 0, 128), -1.0, -4096.0, A.is_equal, A.mult)
+    V(ts, R("RPt", 0, 128), R("dg4", 0, 128), 0.0, -1.0, A.is_equal, A.mult)
+    V(tt, R("RPJ", 0, 128), R("RPt", 0, 128), R("RPc", 0, 128), A.subtract)
+    V(ts, R("RPK", 0, 128), R("dg4", 0, 128), -2.0, None, A.is_equal)
+    V(ts, R("SLW", 0, 16), R("slI", 0, 16), 0.0, None, A.is_equal)
+    V(ts, R("I4n", 0, 128), R("dI", 0, 128), 0.0, -4096.0, A.is_equal, A.mult)
+    V(ts, R("OF15", 0, 8), R("g8I", 0, 8), 16.0, 15.0, A.mult, A.add)
+    for b in range(2):
+        V(ts, R("E2", 160 * b, 160 * b + 160), R("qrel", 0, 160), 4.0 * b, c1("pg"), A.add, A.is_equal)
+    for b in range(4):
+        V(ts, R("EC", 160 * b, 160 * b + 160), R("qrel", 0, 160), 4.0 * b, c1("pf"), A.add, A.is_equal)
+    for b in range(2):
+        V(ts, R("TR", 160 * b, 160 * b + 160), R("dcol", 0, 160), c1("pf"), 16384.0, A.is_ge, A.mult)
+    V(tc, R("SM", 160, 320), R("SM", 0, 160))
+    V("memset", R("QT", 3, 64, 4), 0.0)
+    if any(opt["rg"] + opt["ry"]):
+        V(ts, R("BKn", 0, 8), R("BLK", 0, 8), -1.0, None, A.mult)
+        V(ts, R("BK2", 0, 8), R("BLK", 0, 8), 2.0, None, A.mult)
+    if any(e.strip("v") for r in opt["ge"] for e in r):
+        iota(R("EN", 0, 2048), [[1, 128], [0, 16]], 0, -1)
+        V(ts, R("EN", 0, 2048), R("EN", 0, 2048), 0.0, -1.0, A.is_equal, A.mult)
 
     def size(relu, out, in_):
         if relu:
@@ -297,21 +285,34 @@ def build(rank, opt):
         else:
             S(out, in_, F.Abs)
 
-    def keys(relu, K, n, m, d, a, con, coni, payload):
+    def keys(relu, K, m, d, a, con, payload):
+        o = R(K, 0, 128)
         if relu:
-            P([(R(K, 0, n), R("ONB", 0, 128), R("C0", 0, n), True, False)] +
-              [(R(K, k, n, 16), R(d, k, 2048, 16), R("BLN", 0, n // 16), False, False) for k in range(m)])
-            P([(R(K, k, n, 16), R(a, k, 2048, 16), R("BL2", 0, n // 16), False, False) for k in range(m)] +
-              [(R(K, 0, n), R("ONB", 0, 128), R(coni, 0, n), False, False)] +
-              [(o, l, r, False, i == len(payload) - 1) for i, (o, l, r) in enumerate(payload)])
+            P([(o, R("ONB", 0, 128), R(con, 0, 128), True, False)] + [(R(K, k, 128, 16), R(d, k, 2048, 16), R("BKn", 0, 8), False, False) for k in range(m)])
+            P([(R(K, k, 128, 16), R(a, k, 2048, 16), R("BK2", 0, 8), False, False) for k in range(m)] + [(o, payload, I16, False, True)])
         else:
-            P([(R(K, 0, n), R("ONB", 0, 128), R(con, 0, n), True, False)] + [(o, l, r, False, False) for o, l, r in payload])
-            P([(R(K, k, n, 16), R(a, k, 2048, 16), R("BLK", 0, n // 16), False, k == m - 1) for k in range(m)])
+            P([(o, R("ONB", 0, 128), R(con, 0, 128), True, False), (o, payload, I16, False, False)])
+            P([(R(K, k, 128, 16), R(a, k, 2048, 16), R("BLK", 0, 8), False, k == m - 1) for k in range(m)])
 
-    I16, IB, INB = R("IW", 4, 132), R("IB", 4, 132), R("INB", 4, 132)
-    ISH = R("IW", 5, 133)
+    def earlier(h, own, spread, pick, row, p, Ad, ms, bias):
+        D = "b%d" % (4 + h)
+        items = [(R(D, 0, 320), R("MK", 0, 128, 1, 16), R("TR", 0, 320, 1, 16), True, False)]
+        for b in (0, 1):
+            for q in range(4):
+                a, n, l = 160 * b + SEG[q], 16 * (q + 1), 128 * h + 64 * b
+                items.append((R(D, a, a + n), pick, R(row, l, l + n, 1, p), False, False))
+        P(items)
+        P([(R(D, 0, 320), own, spread, False, True)])
+        S(R(Ad, 320 * h, 320 * h + 320), R(D, 0, 320), F.Abs, bias)
+        V(scan, R(ms, 320 * h, 320 * h + 320), R("SM", 0, 320), R(Ad, 320 * h, 320 * h + 320), 0.0, A.max, A.min)
+
+    def scatter(table, n, off, a, b):
+        for k in (3, 2, 1, 0):
+            V(tt, ind(R(table, 0, n), R(off, 4 * k, 4 * k + 4)), R(a, 64 * k, 64 * k + 64), R(b, 64 * k, 64 * k + 64), A.add)
+
     for t in range(3):
         z = "z%d" % t
+        zx = "zx%d" % (t % 2)
         P([(R("b0", 8 * h, 8 * h + 8), R(z, 128 * h, 128 * h + 128), R("W8", 0, 8), True, True) for h in (0, 1)])
         V(tc, R("ui", 0, 16), R("b0", 0, 16))
         V(ts, R("ui", 0, 16), R("ui", 0, 16), 4095, None, A.bitwise_and)
@@ -320,148 +321,160 @@ def build(rank, opt):
         V(ts, R("UQ", 16, 32), R("uu", 0, 16), 4, 2047, A.arith_shift_right, A.bitwise_and)
         V(ts, R("UQ", 32, 48), R("uu", 0, 16), 5, 1023, A.arith_shift_right, A.bitwise_and)
         V(tc, R("UH", 0, 48), R("UQ", 0, 48))
-        P([(R("b0", 128, 256, 1, 48), R("UH", 0, 48), I16, True, True)])
+        group([(R("b0", 128, 256, 1, 48), R("UH", 0, 48), I16)])
         S(R("RLu", 0, 128, 1, 48), R("b0", 128, 256, 1, 48), F.Copy)
         P([(R("b0", 256 + 128 * h, 384 + 128 * h), R("PM_%d" % h, 0, 128, 1, 48), R("RLu", 0, 128, 1, 48), True, True) for h in (0, 1)])
         if t == 0:
-            V(tc, R("em", 0, 256), R("b0", 256, 512))
+            C(opt["em"], R("em", 0, 256), R("b0", 256, 512))
+        elif opt["em"] == "v":
+            V(ts, R("em", 0, 256), R("b0", 256, 512), c1("Nc"), None, A.add)
         else:
-            V(ts, R("em", 0, 256), R("b0", 256, 512), c1("Ac"), None, A.add)
+            S(R("em", 0, 256), R("b0", 256, 512), F.Identity, c1("Nc"))
         V(ts, R("em", 0, 256), R("em", 0, 256), 1023, None, A.bitwise_and)
-        V(tc, R("emu", 0, 256), R("em", 0, 256))
-        nz = opt["zv"][t]
-        zx = "zx%d" % (t % 2)
-        VM(tc, [(R(zx, m, 4096, 16), R(z, 0, 256)) for m in range(nz)])
-        for m in range(nz, 16):
-            S(R(zx, m, 4096, 16), R(z, 0, 256), F.Copy)
-        V(tc, R("emh", 0, 256), R("emu", 0, 256))
+        C(opt["emu"], R("emu", 0, 256), R("em", 0, 256))
+        C(opt["emh"], R("emh", 0, 256), R("emu", 0, 256) if opt["emh"] == "v" else R("em", 0, 256))
+        for h in (0, 1):
+            for m, eng in enumerate(opt["zx"][t][h]):
+                if eng.islower():
+                    C(eng, R(zx, 2048 * h + m, 2048 * h + 2048, 16), R(z, 128 * h, 128 * h + 128))
+                elif h == 0:
+                    C(eng.lower(), R(zx, m, 4096, 16), R(z, 0, 256))
         for h in (0, 1):
             H, K = "_%d" % h, "b%d" % (2 + h)
-            ch = opt["gchunk"]
-            w = 2048 // ch
-            for c in range(ch):
-                V(tt, R("DG" + H, w * c, w * c + w), ind(R("G", 0, 1024), R("emu", 128 * h + w // 16 * c, 128 * h + w // 16 * (c + 1))),
-                  R(zx, 2048 * h + w * c, 2048 * h + w * c + w), A.subtract)
-                size(opt["rg"][h], R("AG" + H, w * c, w * c + w), R("DG" + H, w * c, w * c + w))
-            keys(opt["rg"][h], K, 128, 16, "DG" + H, "AG" + H, "CD", "CDi", [(R(K, 0, 128), R("emh", 128 * h, 128 * h + 128), I16)])
-        if t == 0:
-            load_names()
-        for h in (0, 1):
-            H, K = "_%d" % h, "b%d" % (2 + h)
-            V("tensor_tensor_scan", R("km" + H, 0, 128), R("MMIN", 0, 128), R(K, 0, 128), 0.0, A.max, A.min)
+            w = 2048 // opt["gch"]
+            if opt["ge"][t][h].strip("v"):
+                group([(R("b0", 128, 256), R(z, 128 * h, 128 * h + 128), IB)])
+                S(R("zT", 0, 128), R("b0", 128, 256), F.Copy)
+            for c in range(opt["gch"]):
+                got = ind(R("G", 0, 1024), R("emu", 128 * h + w // 16 * c, 128 * h + w // 16 * (c + 1)))
+                if opt["ge"][t][h][c] == "v":
+                    V(tt, R("DG" + H, w * c, w * c + w), got, R(zx, 2048 * h + w * c, 2048 * h + w * c + w), A.subtract)
+                    size(opt["rg"][h], R("AG" + H, w * c, w * c + w), R("DG" + H, w * c, w * c + w))
+                else:
+                    C(opt["ge"][t][h][c].lower(), R("DG" + H, w * c, w * c + w), got)
+                    for a in range(w * c, w * c + w, 512):
+                        o = R("b%d" % (4 + a // 512 % 2), 0, 512)
+                        group([(o, IB, R("DG" + H, a, a + 512)), (o, R("zT", 0, 128), R("EN", a, a + 512))])
+                        S(R("AG" + H, a, a + 512), o, F.Abs)
+            keys(opt["rg"][h], K, 16, "DG" + H, "AG" + H, "CD", R("emh", 128 * h, 128 * h + 128))
+            V(scan, R("km" + H, 0, 128), R("MMIN", 0, 128), R(K, 0, 128), 0.0, A.add, A.min)
             V(tc, R("ei" + H, 0, 8), R("km" + H, 15, 128, 16))
             V(ts, R("ej" + H, 0, 8), R("ei" + H, 0, 8), 1023, None, A.bitwise_and)
             V(tt, R("ME" + H, 0, 128), ind(R("ej" + H, 0, 8), R("OFFR", 0, 8)), R("MK", 0, 128), A.mult)
-            P([(R("b7", 8 * h, 8 * h + 8), R("ME" + H, 0, 128), R("Q16", 0, 8), True, True)])
-            V(tc, R("eu" + H, 0, 8), R("b7", 8 * h, 8 * h + 8))
-            V(tc, R("Ju" + H, 0, 128), ind(R("I", 0, 1024), R("eu" + H, 0, 8)))
-            V(tc, R("Jh", 128 * h, 128 * h + 128), R("Ju" + H, 0, 128))
-            V(tc, R("e_rq", 8 * h, 8 * h + 8), R("eu" + H, 0, 8))
-            P([(R("b7", 256 + 128 * h, 384 + 128 * h), R("ME" + H, 0, 128), I16, True, True)])
-        if t == 0:
-            late_constants()
-            load_links()
-        for h in (0, 1):
-            H, K = "_%d" % h, "b%d" % (2 + h)
-            lk = ind(R("L", 0, 2048), R("Ju" + H, 0, 128))
-            xg = ind(R("xb", 0, 2048), R("Ju" + H, 0, 128))
-            if opt["lv"][h]:
-                V(tc, R("Lg" + H, 0, 2048), lk)
-            else:
-                S(R("Lg" + H, 0, 2048), lk, F.Copy)
-            if opt["xv"][h]:
-                V(tc, R("x" + H, 0, 2048), xg)
-            else:
-                S(R("x" + H, 0, 2048), xg, F.Copy)
-            P([(R("b6", 128 * h, 128 * h + 128), R("SEL", 128 * k, 128 * k + 128), R("Lg" + H, k, 2048, 16), k == 0, k == 15) for k in range(16)])
-            V(tc, R("nu" + H, 0, 128), R("b6", 128 * h, 128 * h + 128))
-            yc = opt["ychunk"]
-            w = 2048 // yc
-            for c in range(yc):
-                V(tt, R("Dy" + H, w * c, w * c + w), ind(R("xb", 0, 2048), R("nu" + H, w // 16 * c, w // 16 * (c + 1))), R("x" + H, w * c + 1, w * c + w + 1), A.subtract)
-                size(opt["ry"][h], R("Ay" + H, w * c, w * c + w), R("Dy" + H, w * c, w * c + w))
-            V("tensor_tensor_scan", R("mx" + H, 0, 2048), R("MR", 0, 2048), R("x" + H, 0, 2048), 0.0, A.mult, A.max)
-        P([(R("b6", 256 + 128 * h, 384 + 128 * h), IB, R(z, 128 * h, 128 * h + 128), True, False) if a == 0 else
-           (R("b6", 256 + 128 * h, 384 + 128 * h), IB, R("mx_%d" % h, 15, 2048, 16), False, True) for h in (0, 1) for a in (0, 1)])
-        S(R("zt", 0, 256), R("b6", 256, 512), F.Copy, 127.75, 0.5)
-        V(ts, R("zs%d" % t, 0, 256), R("zt", 0, 256), -128.0, None, A.add)
-        add("g", "remote", [(t,)], [R("zs%d" % t, 0, 256)], [R("z%d" % (t + 1), 0, 256)], 300, 4000)
-        S(R("Y", 0, 256), R("b7", 256, 512), F.Copy)
-        P([(R("b7", 256, 512), R("BH", 0, 128), R("Y", 0, 256), True, True)])
-        S(R("Er", 0, 256), R("b7", 256, 512), F.Copy)
-        dedupe("Er", None, lambda q: R("e_rq", q, q + 1), "EQE", "DUPE", "fl")
-        V(tt, R("of1", 0, 16), R("fl", 0, 16), R("DUE", 0, 16), A.mult)
-        V(tt, R("of2", 0, 16), R("of1", 0, 16), R("e_rq", 0, 16), A.max)
-        V(tc, R("oEu", 0, 16), R("of2", 0, 16))
-        P([(R("b0", 256 + 128 * h, 384 + 128 * h), R("PQ_%d" % h, 0, 128, 1, 48), R("RLu", 0, 128, 1, 48), True, True) for h in (0, 1)])
-        V(tc, R("vi", 0, 256), R("b0", 256, 512))
-        V(ts, R("vi", 0, 256), R("vi", 0, 256), 2047, None, A.bitwise_and)
-        S(R("Jf", 0, 256), R("Jh", 0, 256), F.Copy)
-        VJ = R("b3", 256, 512)
-        P([(R("b2", 256, 512), I16, R("Jh", 0, 256), True, True)])
-        V(tt, VJ, R("vi", 0, 256), R("b2", 256, 512), A.subtract)
-        for h in (0, 1):
-            H, K = "_%d" % h, "b%d" % (2 + h)
-            J = R("Jh", 128 * h, 128 * h + 128)
-            keys(opt["ry"][h], K, 256, 15, "Dy" + H, "Ay" + H, "CS", "CSi", [(R(K, 0, 128), J, I16), (R(K, 128, 256), J, ISH)])
-            V(tt, R("le" + H, 0, 128), R(K, 0, 128), R("THR", 0, 128), A.is_lt)
-            V("tensor_tensor_scan", R("sm" + H, 0, 256), R("MMAX", 0, 256), R(K, 0, 256), 0.0, A.min, A.max)
-            V("tensor_tensor_scan", R("cs" + H, 0, 128), R("MR", 0, 128), R("le" + H, 0, 128), 0.0, A.mult, A.add)
-            V(tc, R("si" + H, 0, 16), R("sm" + H, 15, 256, 16))
-            V(ts, R("QT" + H, 0, 8), R("cs" + H, 15, 128, 16), 11.5, None, A.is_gt)
-            V(ts, R("sj" + H, 0, 16), R("si" + H, 0, 16), 2047, None, A.bitwise_and)
-            V(ts, R("sj" + H, 16, 24), R("si" + H, 0, 8), 11, 15, A.arith_shift_right, A.bitwise_and)
-            V(tc, R("QT" + H, 8, 32), R("sj" + H, 0, 24))
-            P([(R("b7", 128, 256, 1, 32), R("QT" + H, 0, 32), I16, True, True)])
-            S(R("RL", 128 * h, 128 * h + 128, 1, 32), R("b7", 128, 256, 1, 32), F.Copy)
-        if t < 2:
-            P([(R("b7", 16, 24), R("ONH", 0, 128), R("QT_0", 0, 8), True, False), (R("b7", 16, 24), R("ONH", 0, 128), R("QT_1", 0, 8), False, True)])
-            V("tensor_reduce", c1("Ac"), R("b7", 16, 24), "X", A.add)
-        RL = R("RL", 0, 256, 1, 32)
-        P([(R("b6", 256, 512), R("RPJ", 0, 128, 1, 32), RL, True, True)])
-        V(tt, R("mj", 0, 256), R("b6", 256, 512), R("MK", 0, 256), A.mult)
-        S(R("RJh", 0, 256), R("b6", 256, 512), F.Copy)
-        P([(R("b6", 0, 256), R("RPN", 0, 128, 1, 32), RL, True, True), (R("b6", 256, 512), R("RPK", 0, 128, 1, 32), RL, True, True)])
-        V("tensor_tensor_scan", R("scj", 0, 256), R("MR", 0, 256), R("mj", 0, 256), 0.0, A.mult, A.add)
-        JJ = R("scj", 15, 256, 16)
-        if t < 2:
-            V(ts, R("nr", 0, 16), JJ, 4095.5, None, A.is_lt)
-            V(tt, R("og1", 0, 16), R("nr", 0, 16), R("DUE", 0, 16), A.mult)
-            V(tt, R("og2", 0, 16), R("og1", 0, 16), R("of2", 0, 16), A.max)
-            V(tc, R("oGu", 0, 16), R("og2", 0, 16))
-            V(tc, ind(R("G", 0, 1280), R("oGu", 0, 16)), R(z, 0, 256))
+            group([(R("b7", 8 * h, 8 * h + 8), R("ME" + H, 0, 128), R("Q16", 0, 8))])
+            V(tc, R("eu", 8 * h, 8 * h + 8), R("b7", 8 * h, 8 * h + 8))
+            V(tc, R("Ju" + H, 0, 128), ind(R("I", 0, 1024), R("eu", 8 * h, 8 * h + 8)))
+            C(opt["jh"], R("Jh", 128 * h, 128 * h + 128), R("Ju" + H, 0, 128))
+            group([(R("b7", 256 + 128 * h, 384 + 128 * h), R("ME" + H, 0, 128), I16)])
         for h in (0, 1):
             H = "_%d" % h
-            for c in range(4):
-                B = "b%d" % (4 + c % 2)
-                P([(R(B, 0, 512), IB, R("x" + H, 512 * c, 512 * c + 512), True, False),
-                   (R(B, 0, 512), INB, R(zx, 2048 * h + 512 * c, 2048 * h + 512 * c + 512), False, True)])
-                S(R("Af" + H, 512 * c, 512 * c + 512), R(B, 0, 512), F.Abs)
-            P([(R("b1", 128 * h, 128 * h + 128), R("ZB", 15 - k, 143 - k), R("Af" + H, k, 2048, 16), k == 0, k == 15) for k in range(16)])
-            V(ts, R("far", 128 * h, 128 * h + 128), R("b1", 128 * h, 128 * h + 128), R("tf", 1, 2), None, A.is_gt)
-        P([(R("b1", 256, 512), R("RPR", 0, 128, 1, 32), RL, True, True)])
-        V(tt, R("ch", 0, 256), R("b1", 256, 512), R("far", 0, 256), A.max)
+            w = 2048 // opt["xch"]
+            for c in range(opt["xch"]):
+                C(opt["xe"][t][h][c], R("x" + H, w * c, w * c + w), ind(R("xb", 0, 2048), R("Ju" + H, w // 16 * c, w // 16 * (c + 1))))
+            w = 2048 // opt["lch"]
+            n = w // 16
+            for c in range(opt["lch"]):
+                C("s", R("Lg" + H, w * c, w * c + w), ind(R("L", 0, 2048), R("Ju" + H, n * c, n * c + n)))
+                o = R("b6", 128 * h + n * c, 128 * h + n * c + n)
+                group([(o, R("SEL", 128 * k, 128 * k + 128), R("Lg" + H, w * c + k, w * c + w, 16)) for k in range(16)])
+                C(opt["nu"], R("nu" + H, n * c, n * c + n), o)
+            w = 2048 // opt["ych"]
+            for c in range(opt["ych"]):
+                V(tt, R("Dy" + H, w * c, w * c + w), ind(R("xb", 0, 2048), R("nu" + H, w // 16 * c, w // 16 * (c + 1))), R("x" + H, w * c + 1, w * c + w + 1), A.subtract)
+                size(opt["ry"][h], R("Ay" + H, w * c, w * c + w), R("Dy" + H, w * c, w * c + w))
+            V(scan, R("mx" + H, 0, 2048), R("MR", 0, 2048), R("x" + H, 0, 2048), 0.0, A.min, A.max)
+            o = R("b%d" % (4 + h), 320, 448)
+            group([(o, IB, R(z, 128 * h, 128 * h + 128)), (o, IB, R("mx" + H, 15, 2048, 16))])
+            S(R("zt", 128 * h, 128 * h + 128), o, F.Copy, 127.75, 0.5)
+            parts = [(128 * h, 128 * h + 128)] if opt["split"][t] else [(0, 256)] if h == 1 else []
+            for a, b in parts:
+                V(ts, R("zs%d" % t, a, b), R("zt", a, b), -128.0, None, A.add)
+                add("g", "remote", [(t, a, b, "arr%d" % (2 * t + h))], [R("zs%d" % t, a, b)], [R("z%d" % (t + 1), a, b)], RCOST, RLAT)
+        V(tt, R("aE", 0, 16), R("b7", 0, 16), R("DUE", 0, 16), A.subtract)
+        S(R("Y", 0, 256), R("b7", 256, 512), F.Copy)
+        for h in (0, 1):
+            earlier(h, R("ME_%d" % h, 0, 128), R("E2", 0, 320), R("BHn", 0, 128), "Y", 128, "AdE", "msE", None)
+        V(tt, R("tE", 0, 16), ind(R("msE", 0, 640), R("PK", 0, 1)), R("aE", 0, 16), A.mult)
+        V(tt, R("oE", 0, 16), R("tE", 0, 16), R("DUE", 0, 16), A.add)
+        V(tc, R("oEu", 0, 16), R("oE", 0, 16))
+        if t < 2:
+            V(tt, R("dz", 0, 256), ind(R("G", 0, 1024), R("eu", 0, 16)), R(z, 0, 256), A.subtract)
+        P([(R("b0", 256 + 128 * h, 384 + 128 * h), R("PQ_%d" % h, 0, 128, 1, 48), R("RLu", 0, 128, 1, 48), True, True) for h in (0, 1)])
+        C(opt["vi"], R("vi", 0, 256), R("b0", 256, 512))
+        V(ts, R("vi", 0, 256), R("vi", 0, 256), 2047, None, A.bitwise_and)
+        C(opt["jf"], R("Jf", 0, 256), R("Jh", 0, 256))
+        VJ = R("b2", 256, 512)
+        group([(R("b3", 256, 512), I16, R("Jh", 0, 256))])
+        V(tt, VJ, R("vi", 0, 256), R("b3", 256, 512), A.subtract)
+        for h in (0, 1):
+            H, K = "_%d" % h, "b%d" % (2 + h)
+            l = (128 * h, 128 * h + 128)
+            keys(opt["ry"][h], K, 15, "Dy" + H, "Ay" + H, "CS", R("Jh", *l))
+            V(tt, R("le", *l), R(K, 0, 128), R("THR", 0, 128), A.is_lt)
+            V(scan, R("cs", *l), R("MR", 0, 128), R("le", *l), 0.0, A.min, A.add)
+            V(ts, R("nrx", *l), ind(R("cs", *l), R("OF15", 0, 8)), 11.5, None, A.is_lt)
+            if t < 2:
+                group([(R("b6", *l), R("nrx", *l), I16)])
+                V(tt, R("tg", *l), R("b6", *l), R("dz", *l), A.mult)
+            V(scan, R("sm", *l), R("MMAX", 0, 128), R(K, 0, 128), 0.0, A.add, A.max)
+        V(tc, R("QT", 1, 64, 4), R("nrx", 0, 256, 16))
+        V(tc, R("si", 0, 16), R("sm", 15, 256, 16))
+        V(ts, R("SJ", 0, 32, 2), R("si", 0, 16), 2047, None, A.bitwise_and)
+        V(ts, R("SJ", 1, 32, 2), R("si", 0, 16), 11, 15, A.arith_shift_right, A.bitwise_and)
+        V(tc, R("QT", 0, 64, 2), R("SJ", 0, 32))
+        if t < 2:
+            group([(R("b7", 16, 24), R("ONn", 0, 128), R("nrx", 128 * h, 128 * h + 128, 16)) for h in (0, 1)])
+            V("tensor_reduce", c1("Nc"), R("b7", 16, 24), "X", A.add)
+        P([(R("b7", 256 + 128 * h, 384 + 128 * h, 1, 32), R("QT", 32 * h, 32 * h + 32), I16, True, True) for h in (0, 1)])
+        RL = R("RL", 0, 256, 1, 32)
+        S(RL, R("b7", 256, 512, 1, 32), F.Copy)
+        if t < 2:
+            scatter("G", 1088, "oEu", "tg", z)
+        P([(R("b1", 0, 256), R("ZQ", 200, 328), R("Jh", 0, 256), True, False)] +
+          [(R("b1", 128 * h, 128 * h + 128), R(z, 128 * h, 128 * h + 128), R("BBn", 0, 128), False, False) for h in (0, 1)])
+        for h in (0, 1):
+            X, M = "x_%d" % h, "M%d%d" % (t, h)
+            add("g", "fold", [(R(M, 0, 2048), R(X, 0, 2048), R(zx, 2048 * h, 2048 * h + 2048), 2 * t + h)],
+                [R(X, 0, 2048), R(zx, 2048 * h, 2048 * h + 2048)], [R(M, 0, 2048)], RCOST, FLAT)
+        for src, by in (("x_%d", "BL1"), ("M%d%%d" % t, "BL2")):
+            for h in (0, 1):
+                for k0 in (0, 8):
+                    P([(R("b1", 128 * h + k, 128 * h + 128, 16), R(src % h, k, 2048, 16), R(by, 0, 8), False, by == "BL2" and h == 1 and k == 15)
+                       for k in range(k0, k0 + 8)])
+        S(R("fT", 0, 256), R("b1", 0, 256), F.Copy)
+        for h in (0, 1):
+            o = R("b1", 256 + 128 * h, 384 + 128 * h)
+            group([(o, R("fT", 128 * h, 128 * h + 128), I16), (o, R("nrx", 128 * h, 128 * h + 128), R("I4n", 0, 128))])
+        V(ts, R("ch", 0, 256), R("b1", 256, 512), 4096.0, R("tf", 1, 2), A.add, A.is_gt)
         V(tt, R("tmp", 0, 256), R("ch", 0, 256), VJ, A.mult)
-        V(tt, ind(R("I", 0, 1280), R("oEu", 0, 16)), R("tmp", 0, 256), R("Jf", 0, 256), A.add)
+        scatter("I", 1088, "oEu", "tmp", "Jf")
         if t == 2:
             dma("y", "yi", R("I", 0, 1024), 4096, "d8")
-        dedupe("RJh", None, lambda q: R("scj", 16 * q + 15, 16 * q + 16), "EQJ", "DUPJ", "flJ")
-        V(tt, R("oj1", 0, 16), R("flJ", 0, 16), R("DUJ", 0, 16), A.mult)
-        V(tt, R("oj2", 0, 16), R("oj1", 0, 16), JJ, A.max)
-        V(tt, R("oj3", 0, 16), R("oj2", 0, 16), R("DUJ", 0, 16), A.min)
-        V(tc, R("oJu", 0, 16), R("oj3", 0, 16))
-        S(R("Lold", 0, 256), ind(R("L", 0, 2304), R("oJu", 0, 16)), F.Copy)
+        P([(R("b7", 64 + r, 320, 16, 16), R("RL", r, 256, 16, 32), R("SLW", 0, 16, 1, 32), True, True) for r in range(16)])
+        S(R("WT", 0, 256, 1, 16), R("b7", 64, 320, 1, 16), F.Copy)
+        o = R("b7", 32, 48)
+        group([(o, R("WT", 0, 128, 1, 16), R("IW", 4, 20, 1, 16)), (o, R("WT", 128, 256, 1, 16), R("I4n", 0, 16, 1, 16)), (o, I16, R("DUn", 0, 16))])
+        group([(R("b7", 48, 64), R("WT", 0, 128, 1, 16), R("IW", 4, 20, 1, 16))])
+        V(ts, R("aJ", 0, 16), o, 2048.0, 0.0, A.add, A.min)
+        V(tc, R("Ju16", 0, 16), R("b7", 48, 64))
+        for h in (0, 1):
+            earlier(h, R("WT", 0, 128, 1, 16), R("EC", 320 * h, 320 * h + 320, 1, 16), R("RPJ", 0, 128, 1, 32), "RL", 32, "AdJ", "msJ", -4096.0)
+        V(tt, R("tJ", 0, 16), ind(R("msJ", 0, 640), R("PK", 0, 1)), R("aJ", 0, 16), A.mult)
+        V(tt, R("oJ", 0, 16), R("tJ", 0, 16), R("DUn", 0, 16), A.subtract)
+        V(ts, R("oJu", 0, 16), R("oJ", 0, 16), 2048.0, None, A.add)
+        S(R("Lold", 0, 256), ind(R("L", 0, 2048), R("Ju16", 0, 16)), F.Copy)
+        group([(R("b6", 256, 512), R("RPK", 0, 128, 1, 32), RL)])
         V(ts, R("mk", 0, 256), R("b6", 256, 512), c1("k15"), None, A.is_equal)
+        group([(R("b6", 0, 256), ISH, R("Jh", 0, 256))])
         V(tt, R("b6", 0, 256), R("b6", 0, 256), R("Lold", 0, 256), A.subtract)
         V(tt, R("t2", 0, 256), R("b6", 0, 256), R("mk", 0, 256), A.mult)
-        V(tt, ind(R("L", 0, 2304), R("oJu", 0, 16)), R("t2", 0, 256), R("Lold", 0, 256), A.add)
+        scatter("L", 2112, "oJu", "t2", "Lold")
     dma("s", "yz", R("z3", 0, 256), 512, "d9")
     dma("y", "yl", R("L", 0, 2048), 8192, "d10")
     return ops
 
 
-def bank(r):
-    return r[0] if r[0][0] == "b" and len(r[0]) == 2 else None
+SPAN = ("b1", "b2", "b3", "b4", "b5")
 
 
 def edges(ops):
@@ -470,19 +483,13 @@ def edges(ops):
         e = {}
         for w, rs in ((True, o["writes"]), (False, o["reads"])):
             for r in rs:
-                key = PLACE[r[0]][0] if False else r[0]
-                for (j, s, sw) in touched.get(key, []):
+                for (j, s, sw) in touched.get(r[0], []):
                     same = ops[j]["q"] == o["q"]
-                    if bank(r):
-                        if not same:
-                            e[j] = True
-                        elif o["q"] == "t":
+                    if same and o["q"] == "t" and bank(r):
+                        if r[0] in SPAN or clash(r, s):
                             e.setdefault(j, False)
-                        elif (w or sw) and clash(r, s):
-                            e[j] = e.get(j, False) or bool(sw)
                     elif (w or sw) and clash(r, s):
-                        need = True if not same else (sw or ops[j]["kind"] == "dma")
-                        e[j] = e.get(j, False) or bool(need)
+                        e[j] = e.get(j, False) or bool(not same or sw or ops[j]["lat"] > 0)
         pre.append(e)
         for w, rs in ((True, o["writes"]), (False, o["reads"])):
             for r in rs:
@@ -490,75 +497,210 @@ def edges(ops):
     return pre
 
 
-def label(o):
-    r = (o["writes"] or o["reads"])[0]
-    return o["q"] + r[0] + ("@%d" % r[1] if r[0][0] == "b" else "")
+def tails(ops, pre, extra=None):
+    n = len(ops)
+    best = [0.0] * n
+    tail = [0.0] * n
+    for i in range(n - 1, -1, -1):
+        tail[i] = best[i] + ops[i]["cost"] + ops[i]["lat"]
+        for j in pre[i]:
+            best[j] = max(best[j], tail[i] + (WAKE if pre[i][j] else -ops[j]["lat"]))
+    return tail
 
 
-def schedule(ops, pre, bias):
+def schedule(ops, pre, urge, slack=40.0):
     n = len(ops)
     succ = [[] for _ in range(n)]
     for i in range(n):
         for j in pre[i]:
             succ[j].append(i)
-    rankv = [0.0] * n
-    for i in range(n - 1, -1, -1):
-        o = ops[i]
-        b = 0.0
-        for k in succ[i]:
-            b = max(b, rankv[k] + (WAKE if pre[k][i] else 0.0))
-        rankv[i] = b + o["cost"] + o["lat"]
-    rankv = [rankv[i] + bias.get(label(ops[i]), 0.0) for i in range(n)]
-    left = [len(pre[i]) for i in range(n)]
-    ready = [0.0] * n
-    free = {}
+    banks = [sorted(set(bank(r) for r in o["reads"] + o["writes"] if bank(r))) for o in ops]
+    waits = [dict(e) for e in pre]
+    left = [len(e) for e in pre]
+    ready, start, fin = [0.0] * n, [0.0] * n, [0.0] * n
+    free, last, pipe = {}, {}, 0.0
     avail = [i for i in range(n) if left[i] == 0]
-    order, start = [], [0.0] * n
+    order = []
+
+    def can(i):
+        s = max(ready[i], free.get(ops[i]["q"], 0.0))
+        for b in banks[i]:
+            for q, j in last.get(b, {}).items():
+                if q != ops[i]["q"]:
+                    s = max(s, fin[j] + WAKE)
+        return s
+
     while avail:
-        best = None
-        for i in avail:
-            s = max(ready[i], free.get(ops[i]["q"], 0.0))
-            key = (s, -rankv[i])
-            if best is None or key < best[0]:
-                best = (key, i)
-        s0, q = best[0][0], ops[best[1]]["q"]
-        i = best[1]
-        for k in avail:
-            if ops[k]["q"] == q and max(ready[k], free.get(q, 0.0)) <= s0 + 40 and rankv[k] > rankv[i]:
+        at = {i: can(i) for i in avail}
+        i = min(avail, key=lambda k: (at[k], -urge[k]))
+        q, s0 = ops[i]["q"], at[i]
+        mine = [k for k in avail if ops[k]["q"] == q]
+        for k in mine:
+            if at[k] <= s0 + slack and urge[k] > urge[i]:
                 i = k
-        s = max(ready[i], free.get(q, 0.0))
+        for k in mine:
+            if at[k] < at[i] + ops[i]["cost"] and urge[k] - urge[i] > 4 * (at[k] - at[i]) + ops[k]["cost"] and at[k] - at[i] < 0.25 * ops[i]["cost"]:
+                i = k
+        o, s = ops[i], at[i]
         avail.remove(i)
+        for b in banks[i]:
+            for p, j in last.setdefault(b, {}).items():
+                if p != q:
+                    waits[i][j] = True
+            last[b][q] = i
         start[i] = s
-        free[q] = s + ops[i]["cost"]
+        free[q] = s + o["cost"]
+        fin[i] = s + o["cost"] + o["lat"]
+        if o["kind"] == "dma":
+            pipe = fin[i] = max(s + o["cost"] + DLAT, pipe) + o["nbytes"] / DRATE
         order.append(i)
-        fin = s + ops[i]["cost"] + ops[i]["lat"]
         for k in succ[i]:
-            ready[k] = max(ready[k], fin + (WAKE if pre[k][i] else 0.0) if pre[k][i] else s)
+            ready[k] = max(ready[k], fin[i] + WAKE if pre[k][i] else s)
             left[k] -= 1
             if left[k] == 0:
                 avail.append(k)
-    return order, start
+    return order, waits, start, max(fin)
 
 
-URGE = """
-vmk:-5 vDUPE:-1 vb6@0:-10 tb1@0:-16 vCS:31 sAy_1:-8 vONH:-16 vmx_0:-6 vI:-11 ve_rq:8 vp16i:9 szx1:-5 vx_1:13 vQ16:15 vUQ:-19 sAf_1:-8 vpk1:-21 vDUE:7 vDUPJ:-4 vmx_1:-5 vMMIN:-9 vBLK:8 tb6@256:25 szx0:-16 tb6@0:29 sAy_0:-4 vle_0:1 vch:6 tb5@0:4 vkm_0:17 vDy_1:-2 vk15:12 voEu:-19 sDM:2 vJh:4 vsi_0:5 vRPR:13 vp16:8 shki:-7 vRPN:13 vej_0:-5 vvi:4 vEQE:1 vL:6 gz1:2 yG:-15 vIW:-4 vsm_1:4 vpk3:4 yixi:3 vle_1:2 vOWN:-8 vsi_1:9 vsj_1:-1 yL:23 tb4@0:-5 gduI:7 vzs0:-3 sAG_1:1 vDG_0:-6 yxb:4 vzx0:-14 vZQ:-10 vemh:-1 vtf:-11 ylki:-12 vzs2:-11 gdI:2 tb7@16:-9 vej_1:2 vzx1:-1 vZB:1 vKM:2 sRL:3 vG:4 vMMAX:5 tb6@128:16 vDG_1:-5 vME_1:-4 vscj:-5 vUH:-10 gz3:-9 vBLN:-6 yz0:-4 vsj_0:1 vpk2:4 vPICK:2 sL:4 vnu_1:7 sJf:1 vONB:3 vEQJ:5 veu_0:9 voJu:-3 vx_0:-4 vW8:9 vINB:-1 voj3:2 vRPK:-3 vOFFR:8 gr15I:-1 vJu_0:-4 vCD:-6 voj2:-5 vt2:1 vDy_0:6 tb4@256:6 vIB:-6 tb1@128:6 vQT_1:-1 sx_0:3 tb7@128:3 grI:-7 sPQ_1:3 vTHR:-4 vDM:-1 sz3:-8 veu_1:-4 vfl:1 vdgA:-3 vuu:-1 vAc:5 vcs_1:-1 vME_0:-3 tb2@256:-10 szt:1 voj1:1 vmj:-1 vnr:-2 gdgI:3 sEr:6 vwf:-1 sLg_0:-3 vMK:3 gz2:3 gcI:3 sRLu:-5 sRJh:3 vzs1:-1 tb0@0:5 vog2:-3 sthi:-5 vkm_1:1 ggI:8 vof1:5 sAG_0:-1 tb7@8:-3 sLold:1
-"""
-OPT = {"gchunk": 1, "ychunk": 4, "lv": (0, 0), "xv": (0, 1), "zv": (0, 0, 0), "rg": (0, 0), "ry": (0, 0),
-       "bias": {w.split(":")[0]: 500.0 * int(w.split(":")[1]) for w in URGE.split()}}
+def fit(seq, lags, uses):
+    start, busy = {}, {}
+    for i in seq:
+        s = max([0.0] + [start[j] + d for j, d in lags[i].items()])
+        moved = True
+        while moved:
+            moved = False
+            for res, off, n, who in uses[i]:
+                taken = busy.setdefault(res, [])
+                k = max(0, before(taken, s + off) - 2)
+                while k < len(taken) and taken[k][0] < s + off + n - 1e-6:
+                    if s + off < taken[k][1] - 1e-6 and (who is None or who != taken[k][2]):
+                        s, moved = taken[k][1] - off, len(uses[i]) > 1
+                    k += 1
+        start[i] = s
+        for res, off, n, who in uses[i]:
+            busy[res].insert(before(busy[res], s + off), (s + off, s + off + n, who))
+    return start
+
+
+def before(taken, s):
+    lo, hi = 0, len(taken)
+    while lo < hi:
+        mid = (lo + hi) // 2
+        if taken[mid][0] < s:
+            lo = mid + 1
+        else:
+            hi = mid
+    return lo
+
+
+def schedule(ops, pre, passes, seed):
+    n = len(ops)
+    span = [o["cost"] + o["lat"] for o in ops]
+    banks = [sorted(set(bank(r) for r in o["reads"] + o["writes"] if bank(r))) for o in ops]
+    fwd = [{j: (span[j] + WAKE if w else ops[j]["cost"]) for j, w in pre[i].items()} for i in range(n)]
+    bwd = [{} for _ in range(n)]
+    for i in range(n):
+        for j, d in fwd[i].items():
+            bwd[j][i] = d - span[j] + span[i]
+    ahead, back = [], []
+    for i, o in enumerate(ops):
+        u = [(o["q"], 0.0, o["cost"], None)] + [(b, 0.0, o["cost"] + WAKE, o["q"]) for b in banks[i]]
+        if o["kind"] == "dma":
+            u.append(("engines", o["cost"] + DLAT, o["lat"] - DLAT, None))
+        ahead.append(u)
+        back.append([(res, span[i] - off - m, m, who) for res, off, m, who in u])
+
+    def ordered(key, lags, way):
+        key = list(key)
+        for i in way:
+            key[i] = max([key[i]] + [key[j] + 1e-3 for j in lags[i]])
+        return sorted(range(n), key=lambda i: key[i])
+
+    tail = [0.0] * n
+    for i in range(n - 1, -1, -1):
+        tail[i] = max([span[i]] + [tail[k] + fwd[k][i] for k in bwd[i]])
+
+    def pack(key):
+        start = fit(ordered(key, fwd, range(n)), fwd, ahead)
+        late = fit(ordered([-start[i] - span[i] for i in range(n)], bwd, range(n - 1, -1, -1)), bwd, back)
+        key = [-late[i] - span[i] for i in range(n)]
+        start = fit(ordered(key, fwd, range(n)), fwd, ahead)
+        return max(start[i] + span[i] for i in range(n)), start, key
+
+    rng = np.random.default_rng(seed)
+    names = [(o["q"],) + (o["writes"] or o["reads"])[0][:2] for o in ops]
+    now = best = pack([-tail[i] for i in range(n)])
+    for k in range(passes):
+        key = list(now[2]) if k % 2 else [now[1][i] for i in range(n)]
+        if k % 3 == 0:
+            at, wide, by = key[rng.integers(n)], rng.choice((3000, 8000)), rng.choice((300, 1000, 2500))
+            key = [x + by * rng.normal() if abs(x - at) < wide else x for x in key]
+        elif k % 3 == 1:
+            some, by = [names[i] for i in rng.integers(n, size=rng.choice((1, 2, 4)))], 3000 * rng.normal()
+            key = [key[i] + by if names[i] in some else key[i] for i in range(n)]
+        else:
+            for i in rng.integers(n, size=rng.choice((1, 3, 8))):
+                key[i] += 3000 * rng.normal()
+        new = pack(key)
+        if new[0] < now[0] - 200.0 * (1 - k / passes) * np.log(rng.random()):
+            now = new
+            if new[0] < best[0]:
+                best = new
+    end, start = best[:2]
+    order = sorted(range(n), key=lambda i: (start[i], i))
+    waits, last = [dict(e) for e in pre], {}
+    for i in order:
+        for b in banks[i]:
+            for q, j in last.setdefault(b, {}).items():
+                if q != ops[i]["q"]:
+                    waits[i][j] = True
+            last[b][ops[i]["q"]] = i
+    return order, waits, start, end
+
+
+OPT = {"ge": (("vv", "vv"), ("vv", "Vs"), ("vv", "Vs")), "rg": (0, 0), "ry": (0, 0), "gch": 2, "ych": 2, "lch": 2, "xch": 2, "xe": (("ss", "vs"),) * 3, "emh": "g", "jh": "g", "em": "s", "emu": "v", "vi": "v", "nu": "v", "jf": "g", "icv": "s", "lcv": "gs", "selv": 16,
+       "split": (1, 1, 0), "zx": (("V" * 12 + "S" * 4,) * 2, ("g" * 12 + "v" * 4, "g" * 16), ("g" * 12 + "v" * 4, "g" * 16))}
 PLAN = {}
 
 
+def plan(opt, passes=4000, seed=0):
+    ops = build(opt)
+    pre = edges(ops)
+    order, waits, start, end = schedule(ops, pre, passes, seed)
+    return ops, order, waits, start, end
+
+
+def helper(core, T, topo):
+    return [c for c in topo.cores_of(core) if c not in T.cores and topo.die(c) == topo.die(core)][0]
+
+
+def spare(core, T, topo):
+    near = topo.engines(core, helper(core, T, topo))
+    far = topo.engines(core, T.cores[(T.rank_of(core) + 1) % len(T.cores)])
+    use = [e for e in near if e not in far] or near
+    return sum(1 << e for e in use), len(use)
+
+
+def hand_back(g, core, owner, T, topo):
+    rid, pid, _e = topo.addr(owner)
+    folds = [PLAN["ops"][i]["calls"][0] for i in PLAN["order"] if PLAN["ops"][i]["kind"] == "fold"]
+    for out, a, b, k in folds:
+        g.wait_ge(T.sem["fa%d" % k], spare(owner, T, topo)[1])
+        g.remote_dma(T[out[0]][:], T[out[0]][:], T.sem["fb%d" % k], T.sem["loc"], pid, rid, topo.mask(core, owner))
+    g.wait_ge(T.sem["loc"], len(folds) * len(topo.engines(core, owner)))
+
+
 def rank_program(g, core, T, topo):
+    if "ops" not in PLAN:
+        PLAN["ops"], PLAN["order"], PLAN["waits"] = plan(OPT)[:3]
     rank = T.rank_of(core)
     if rank is None:
+        for owner in T.cores:
+            if helper(owner, T, topo) == core:
+                hand_back(g, core, owner, T, topo)
         return
-    if "ops" not in PLAN:
-        PLAN["ops"] = build(rank, OPT)
-        PLAN["pre"] = edges(PLAN["ops"])
-        PLAN["order"], PLAN["start"] = schedule(PLAN["ops"], PLAN["pre"], OPT["bias"])
-    ops, pre = PLAN["ops"], PLAN["pre"]
-    nxt = T.cores[(rank + 1) % len(T.cores)]
-    home = T.cores[(rank + 2) % len(T.cores)]
+    ops, pre = PLAN["ops"], PLAN["waits"]
+    n = len(T.cores)
     queue = {"v": g.vector, "s": g.scalar, "t": g.tensor, "g": g, "y": g.sync}
     qsem = {"v": "qv", "s": "qs", "t": "qt", "g": "qg"}
     count = {}
@@ -570,15 +712,14 @@ def rank_program(g, core, T, topo):
             return ap(r[0]).indirect(ap(r[1]))
         name, off = PLACE[r[0]]
         a, b, st, p = r[1] + off, r[2] + off, r[3], r[4]
-        t = T[name]
         if st == 1:
-            return t[:, a:b] if p == 128 else t[0:p, a:b]
-        return t[:, a:b:st]
+            return T[name][:, a:b] if p == 128 else T[name][0:p, a:b]
+        return T[name][:, a:b:st] if p == 128 else T[name][0:p, a:b:st]
 
     def arg(x):
         return ap(x) if isinstance(x, tuple) else x
 
-    place = {i: n for n, i in enumerate(PLAN["order"])}
+    place = {i: k for k, i in enumerate(PLAN["order"])}
     for i in PLAN["order"]:
         o = ops[i]
         q, eng = o["q"], queue[o["q"]]
@@ -601,31 +742,45 @@ def rank_program(g, core, T, topo):
             count[o["sem"]] = 16
             continue
         if o["kind"] == "remote":
-            t = o["calls"][0][0]
-            dst = nxt if t < 2 else home
+            t, a, b, sem = o["calls"][0]
+            step = 1 if t < 2 else 2
+            dst, src = T.cores[(rank + step) % n], T.cores[(rank - step) % n]
             rid, pid, _e = topo.addr(dst)
-            g.remote_dma(T["z%d" % (t + 1)][:], T["zs%d" % t][:], T.sem["arr%d" % (t + 1)], T.sem["loc"], pid, rid, topo.mask(core, dst))
-            m = len(topo.engines(core, dst))
-            src = T.cores[(rank - 1) % len(T.cores)] if t < 2 else T.cores[(rank - 2) % len(T.cores)]
+            g.remote_dma(T["z%d" % (t + 1)][:, a:b], T["zs%d" % t][:, a:b], T.sem[sem], T.sem["loc"], pid, rid, topo.mask(core, dst))
+            count["loc"] = count.get("loc", 0) + len(topo.engines(core, dst))
+            done[i] = (sem, len(topo.engines(src, core)), {})
+            continue
+        if o["kind"] == "fold":
+            out, a, b, k = o["calls"][0]
+            relay = helper(core, T, topo)
+            rid, pid, _e = topo.addr(relay)
+            mask, m = spare(core, T, topo)
+            g.remote_dma_fused([RemoteDMATransfer(dst_ids=[DstId(rid=rid, pnc=pid)], dma_engine_mask=mask, remote_sem=T.sem["fa%d" % k],
+                                                  srcs=[ap(a), ap(b)], dsts=[ap(out)], alu_op=2)], local_sem=T.sem["loc"])
             count["loc"] = count.get("loc", 0) + m
-            done[i] = ("arr%d" % (t + 1), len(topo.engines(src, core)), {})
+            done[i] = ("fb%d" % k, len(topo.engines(relay, core)), dict(known))
             continue
         sem = qsem[q]
         for c in o["calls"]:
-            if o["kind"] == "matmul":
+            k = o["kind"]
+            if k == "matmul":
                 ins = g.tensor.matmul(ap(c[0]), ap(c[1]), ap(c[2]), c[3], c[4])
-            elif o["kind"] == "activation":
+            elif k == "activation":
                 kw = {}
                 if c[3] is not None:
                     kw["bias"] = arg(c[3])
                 if c[4] is not None:
                     kw["scale"] = arg(c[4])
                 ins = g.scalar.activation(ap(c[0]), ap(c[1]), c[2], **kw)
-            elif o["kind"] == "iota":
-                ins = g.iota(ap(c[0]), c[1], c[2], c[3])
+            elif k == "iota":
+                if DTYPE[c[0][0]] == "int32":
+                    ins = g.iota(ap(c[0]), c[1], c[2], c[3])
+                else:
+                    ins = g.iota(ap(c[0]), c[1], c[2], c[3], allow_small_or_imprecise_dtypes=True)
+            elif k == "select":
+                ins = g.affine_select(ap(c[0]), ap(c[1]), [[0, width(c[0])]], A.is_ge, 0.0, 0, 0)
             else:
                 x = [arg(y) for y in c]
-                k = o["kind"]
                 if k == "tensor_copy":
                     ins = g.vector.tensor_copy(*x)
                 elif k == "tensor_scalar":

@@ -1,12 +1,11 @@
+import math
 import numpy as np
 from concourse.bass import DstId, RemoteDMATransfer
 from concourse.mybir import AluOpType as A, AxisListType, ActivationFunctionType as F
 
 BIG = 1.0e9
-OFF24 = 16777216.0
-CYC = 0.8333
-GAT, SCA, WAKE, FIX, SFIX = 1.56, 3.8, 90.0, 20.0, 120.0
-DLAT, DRATE, RLAT, FLAT, RCOST = 1500.0, 200.0, 5000.0, 12000.0, 800.0
+CYC, GAT, SCA, WAKE, FIX, SFIX, TCYC = 0.8333, 1.56, 3.8, 130.0, 20.0, 80.0, 0.5
+DLAT, DRATE, RLAT, FLAT, RCOST = 1600.0, 200.0, 3800.0, 9500.0, 500.0
 SCRATCH = {}
 TWO = ("bfloat16", "float16", "uint16")
 SEG = (0, 16, 48, 96)
@@ -23,56 +22,52 @@ for _n, _c, _d in (
         ("z0", 256, _B), ("z1", 256, _B), ("z2", 256, _B), ("z3", 256, _B),
         ("zs0", 256, _B), ("zs1", 256, _B), ("zs2", 256, _B), ("zt", 256, _B),
         ("pI", 1, _I), ("p16i", 1, _I), ("pgi", 1, _I), ("pf", 1, _F), ("p16", 1, _F), ("pg", 1, _F), ("colA", 1, _F), ("colB", 1, _F),
-        ("k15", 1, _F), ("wf", 1, _F), ("hf", 2, _F), ("tf", 2, _F), ("q2i", 1, _I), ("bI", 1, _I), ("pk1", 1, _F), ("pk2", 1, _F), ("pk3", 1, _F),
-        ("pk4", 1, _F), ("dI", 144, _B), ("cI", 144, _B), ("gI", 128, _B), ("g8I", 16, _I), ("rI", 128, _B), ("dg4", 128, _B), ("duI", 16, _I),
-        ("r15I", 128, _B), ("slI", 16, _B), ("qrel", 160, _B), ("dcol", 160, _B), ("SM", 320, _B),
-        ("IW", 136, _H), ("IB", 136, _B), ("INB", 136, _B), ("BHn", 128, _H), ("BLK", 8, _B), ("Q16", 8, _H), ("MK", 128, _H), ("ZB", 144, _B),
-        ("SEL", 2048, _H), ("KM", 16, _F), ("CD", 128, _B), ("CS", 128, _B), ("ONB", 128, _B), ("ONn", 128, _H), ("MMIN", 128, _F), ("OF15", 8, _U), ("nrx", 256, _H),
-        ("MMAX", 128, _F), ("MR", 2048, _B), ("OFFR", 8, _U), ("PK", 2, _U), ("DUE", 16, _F), ("DUn", 16, _H),
-        ("RPn", 128, _H), ("RPc", 128, _H), ("RPJ", 128, _H), ("RPt", 128, _H), ("RPK", 128, _H), ("SLW", 16, _H), ("I4n", 128, _H),
-        ("E2", 320, _H), ("EC", 640, _H), ("TR", 320, _H), ("Ju16", 16, _U), ("dgA", 128, _H), ("dgB", 128, _H), ("dgC", 128, _H), ("THR", 128, _F),
-        ("W8", 8, _B), ("ZQ", 328, _H), ("PM_0", 128, _H), ("PM_1", 128, _H), ("PQ_0", 128, _H), ("PQ_1", 128, _H),
-        ("ui", 16, _I), ("uu", 16, _I), ("UQ", 48, _I), ("UH", 48, _H), ("RLu", 128, _H), ("em", 256, _I), ("emu", 256, _U), ("emh", 256, _H),
-        ("vi", 256, _I), ("Jf", 256, _F), ("Jh", 256, _H), ("zx0", 4096, _B), ("zx1", 4096, _B), ("Y", 256, _H), ("eu", 16, _U),
-        ("ch", 256, _F), ("tmp", 256, _F), ("RL", 256, _H), ("WT", 256, _H), ("AdE", 640, _B), ("AdJ", 640, _B), ("msE", 640, _B), ("msJ", 640, _B),
-        ("aE", 16, _F), ("tE", 16, _F), ("oE", 16, _F), ("oEu", 16, _U), ("aJ", 16, _F), ("tJ", 16, _F), ("oJ", 16, _F), ("oJu", 16, _U),
-        ("dz", 256, _B), ("tg", 256, _B), ("le", 256, _B), ("cs", 256, _B), ("sm", 256, _F), ("si", 16, _I), ("SJ", 32, _I), ("QT", 64, _H),
-        ("Lold", 256, _F), ("mk", 256, _F), ("t2", 256, _F), ("Nc", 1, _F), ("fT", 256, _H), ("BBn", 128, _B), ("BL1", 8, _B), ("BL2", 8, _B),
-        ("BKn", 8, _B), ("BK2", 8, _B), ("zT", 128, _B), ("EN", 2048, _B)):
+        ("k15", 1, _F), ("wf", 1, _F), ("hI", 4, _I), ("hf", 4, _F), ("tf", 2, _F), ("q2i", 1, _I), ("bI", 1, _I), ("pk1", 1, _F),
+        ("pk2", 1, _F), ("pk4", 1, _F), ("m15", 1, _F), ("acol", 1, _F), ("dI", 144, _B), ("gI", 128, _B), ("g8I", 16, _I),
+        ("rI", 128, _B), ("dg4", 128, _B), ("duI", 16, _I), ("r15I", 128, _B), ("slI", 16, _B), ("qrel", 160, _B), ("dcol", 160, _B),
+        ("SM", 320, _B), ("IW", 136, _H), ("IB", 136, _B), ("In", 128, _H), ("I1n", 128, _H), ("I4n", 128, _H), ("Ih", 128, _H), ("Ic", 128, _H), ("BHn", 128, _H),
+        ("BBn", 128, _B), ("BLK", 16, _B), ("BKn", 16, _B), ("BK2", 16, _B), ("BL1", 8, _B), ("BL2", 8, _B), ("Q16", 8, _H),
+        ("MK", 128, _H), ("SEL", 2048, _H), ("EN", 2048, _B), ("MR", 2048, _B), ("CD", 128, _H), ("CS", 256, _H), ("ON64", 128, _H),
+        ("ONn", 128, _H), ("ONk", 128, _H), ("MMIN", 128, _F), ("MMAX", 128, _F), ("OFFR", 8, _U), ("OF15", 8, _U), ("PK", 4, _U), ("DUE", 16, _F),
+        ("DUn", 16, _H), ("RPc", 128, _H), ("RPJ", 128, _H), ("RPt", 128, _H), ("RPK", 128, _H), ("SLW", 16, _H), ("E2", 320, _H),
+        ("EC", 640, _H), ("TR", 320, _H), ("dg0", 128, _H), ("dg1", 128, _H), ("dg2", 128, _H), ("dg3", 128, _H), ("W8", 8, _B),
+        ("ZQ", 528, _H), ("PM_0", 128, _H), ("PM_1", 128, _H), ("PQ_0", 128, _H), ("PQ_1", 128, _H),
+        ("ui", 16, _I), ("uu", 16, _I), ("UQ", 64, _I), ("UH", 66, _H), ("RLu", 128, _H), ("q1", 256, _H), ("q2", 256, _H),
+        ("emu", 256, _U), ("emh", 256, _H), ("Nc", 1, _F), ("Nb", 1, _F), ("zx0", 4096, _B), ("zx1", 4096, _B), ("zT", 256, _B),
+        ("eu", 16, _U), ("Jf", 256, _F), ("Jh", 256, _H), ("Y", 256, _H), ("AdE", 640, _B), ("msE", 640, _B), ("aE", 16, _F),
+        ("tE", 16, _F), ("oE", 16, _F), ("oEu", 16, _U), ("dz", 256, _B), ("tg", 256, _B), ("le", 256, _B), ("cs", 256, _B),
+        ("nrx", 256, _H), ("sm", 256, _F), ("si", 16, _I), ("SJ", 32, _I), ("QT", 64, _H), ("RL", 256, _H), ("WT", 512, _H),
+        ("AdJ", 640, _B), ("msJ", 640, _B), ("aJ", 24, _F), ("tJ", 32, _F), ("oJ", 16, _F), ("oJu", 16, _U), ("Ju16", 16, _U),
+        ("fT", 256, _H), ("ch", 256, _F), ("tmp", 256, _F), ("Lold", 256, _F), ("Lo16", 256, _H), ("mk", 256, _F), ("t2", 256, _F)):
     _buf(_n, _c, _d)
-for _t in "012":
-    for _h in "01":
-        _buf("M" + _t + _h, 2048, _B)
 for _h in "01":
-    for _n, _c, _d in (("DG", 2048, _B), ("AG", 2048, _B), ("x", 2064, _B), ("Lg", 2048, _H), ("mx", 2048, _B), ("Dy", 2048, _B), ("Ay", 2048, _B),
-                       ("km", 128, _F), ("ei", 8, _I), ("ej", 8, _I), ("ME", 128, _H), ("Ju", 128, _U), ("nu", 128, _U)):
+    for _n, _c, _d in (("DG", 2048, _B), ("AG", 2048, _B), ("x", 2064, _B), ("Lg", 2048, _H), ("mx", 2048, _B), ("Dy", 2048, _B),
+                       ("Ay", 2048, _B), ("km", 128, _F), ("ei", 8, _I), ("ej", 8, _I), ("ME", 128, _H), ("Ju", 128, _U), ("nu", 128, _U),
+                       ("M0", 2048, _B), ("M1", 2048, _B), ("M2", 2048, _B)):
         _buf(_n + "_" + _h, _c, _d)
 for _b in range(8):
     _buf("b%d" % _b, 512, _F, "psum")
-PLACE = {}
+PLACE = {_n: (_n, 0) for _n in ("lk", "zc", "yz")}
 _pack = {}
 for _n in sorted(SCRATCH):
     _w, _s, _d = SCRATCH[_n]
-    if _w == "sbuf" and _n not in ("xb", "G", "I", "L", "ixi", "lki", "z0", "z1", "z2", "z3", "zs0", "zs1", "zs2") and _s[1] < 2000:
+    if _w == "sbuf" and _n not in ("G", "I", "ixi", "z0", "z1", "z2", "z3", "zs0", "zs1", "zs2") and _s[1] < 2000:
         _o = _pack.get(_d, 0)
         PLACE[_n] = ("k_" + _d, _o)
         _pack[_d] = _o + (_s[1] + 31) // 32 * 32
     else:
         PLACE[_n] = (_n, 0)
-PLACE["lk"] = ("lk", 0)
 DTYPE = {_n: SCRATCH[_n][2] for _n in SCRATCH}
 for _n in list(SCRATCH):
     if PLACE[_n][0] != _n:
         del SCRATCH[_n]
 for _d in _pack:
     _buf("k_" + _d, _pack[_d], _d)
-SEMAPHORES = ["qv", "qs", "qt", "qg", "loc"] + [s + str(i) for s in ("arr", "fa", "fb") for i in range(6)] + ["d%d" % i for i in range(16)]
+SEMAPHORES = ["qv", "qs", "qt", "qg", "loc"] + [s + str(i) for s in ("arr", "fa", "fb") for i in range(6)] + ["d%d" % i for i in range(14)]
 
 
-def R(buf, a=0, b=None, step=1, p=128):
-    if b is None:
-        b = a + 1
-    return (buf, a, b, step, p)
+def R(buf, a=0, b=None, step=1, p=128, p0=0):
+    return (buf, a, a + 1 if b is None else b, step, p, p0)
 
 
 def width(r):
@@ -98,10 +93,12 @@ def ind(win, off):
 
 
 def build(opt):
-    ops = []
+    ops, now = [], [-1]
 
     def add(q, kind, calls, reads, writes, cost, lat=0.0, **kw):
-        ops.append(dict(q=q, kind=kind, calls=calls, reads=reads, writes=writes, cost=cost, lat=lat, i=len(ops), **kw))
+        r = (writes or reads)[0]
+        ops.append(dict(q=q, kind=kind, calls=calls, reads=reads, writes=writes, cost=cost, lat=lat, i=len(ops), t=now[0],
+                        name="%s%s@%d" % (q, r[0], r[1]), turns=opt["turns"], **kw))
 
     def flat(x):
         if isinstance(x, IndOp):
@@ -136,19 +133,22 @@ def build(opt):
         rd = flat(in_) + [x for x in (bias, scale) if isinstance(x, tuple)]
         add("s", "activation", [(out, in_, func, bias, scale)], rd, [out], c)
 
+    def select(out, in_, pattern, base, cm):
+        add("g", "select", [(out, in_, pattern, base, cm)], [in_], [out], 170 + 2 * width(out) * CYC)
+
     def C(eng, out, in_):
         if eng == "v":
             V("tensor_copy", out, in_)
         elif eng == "s":
             S(out, in_, F.Copy)
         else:
-            add("g", "select", [(out, in_)], [in_], [out], 170 + 2 * width(out) * CYC)
+            select(out, in_, [[0, width(out)]], 0, 0)
 
     def P(items):
         c = 0.0
         rd, wr = [], []
         for o, l, r, a, b in items:
-            c += max(min(64, width(l)), width(r)) * CYC + 5
+            c += max(min(64, width(l)), width(r)) * TCYC + 5
             for x in (l, r):
                 if x not in rd:
                     rd.append(x)
@@ -165,9 +165,10 @@ def build(opt):
     def dma(q, out, in_, nbytes, sem):
         rd = [in_] if isinstance(in_, tuple) else []
         wr = [out] if isinstance(out, tuple) else []
-        add(q, "dma", [(out, in_)], rd, wr, 60, DLAT + nbytes * 128 / DRATE, sem=sem, nbytes=nbytes * 128)
+        add(q, "dma", [(out, in_)], rd, wr, 60, DLAT + nbytes * 128 / DRATE, sem=sem, nbytes=nbytes * 128, hold=nbytes * 128 / DRATE if nbytes > 32 else 0)
 
-    dma("y", R("z0", 0, 256), "zc", 512, "d0")
+    dma("y", R("z0", 0, 128), R("zc", 128, 256), 256, "d0")
+    dma("s", R("z0", 128, 256), R("zc", 0, 128), 256, "d12")
     dma("s", R("wti", 0, 1), "wt", 4, "d1")
     dma("s", R("hki", 0, 2), "hk", 8, "d2")
     dma("y", R("G", 0, 1024), "gi", 2048, "d3")
@@ -190,41 +191,58 @@ def build(opt):
         iota(R("qrel", a, a + n), [[0, n]], q, 0)
         iota(R("dcol", a, a + n), [[1, n]], -16 * q, 0)
         iota(R("SM", a, a + n), [[-1, n]], 1, 0)
-    iota(R("MR", 0, 2048), [[0, 128], [64, 16]], 0, 0)
+    for a in range(0, 2048, 512):
+        iota(R("MR", a, a + 512), [[0, 512]], 1, 0)
+        select(R("SEL", a, a + 512), R("MR", a, a + 512), [[-256, 4], [-16, 8], [255, 16]], -2 * a, 1)
+        select(R("EN", a, a + 512), R("MR", a, a + 512), [[1, 32], [0, 16]], a // 16, -1)
     c1 = lambda b: R(b, 0, 1)
     ts, tt, tc, scan = "tensor_scalar", "tensor_tensor", "tensor_copy", "tensor_tensor_scan"
     I16, IB, ISH = R("IW", 4, 132), R("IB", 4, 132), R("IW", 5, 133)
+    In, I1n, I4n = R("In", 0, 128), R("I1n", 0, 128), R("I4n", 0, 128)
+    V("memset", R("MR", 0, 2048, 16), 0.0)
     V(ts, c1("pgi"), c1("pI"), 4, None, A.arith_shift_right)
     V(tc, c1("pg"), c1("pgi"))
     V(tc, c1("wf"), c1("wti"))
     V(ts, R("W8", 0, 8), R("g8I", 0, 8), c1("pg"), c1("wf"), A.is_equal, A.mult)
-    V(tc, R("hf", 0, 2), R("hki", 0, 2))
-    V("memset", R("ZQ", 0, 328), 0.0)
-    V(ts, R("ZQ", 48, 56), R("g8I", 0, 8), c1("pg"), None, A.is_equal)
-    V(ts, R("ZQ", 152, 160), R("g8I", 0, 8), c1("pg"), -0.0625, A.is_equal, A.mult)
+    for j, (col, bits) in enumerate(((0, 31), (0, 992), (1, 63), (1, 1984))):
+        V(ts, R("hI", j, j + 1), R("hki", col, col + 1), bits, None, A.bitwise_and)
+    V(tc, R("hf", 0, 4), R("hI", 0, 4))
+    V("memset", R("ZQ", 0, 528), 0.0)
+    V(ts, R("ZQ", 72, 80), R("g8I", 0, 8), c1("pg"), None, A.is_equal)
+    V(ts, R("ZQ", 200, 208), R("g8I", 0, 8), c1("pg"), -0.0625, A.is_equal, A.mult)
+    V("memset", R("ZQ", 320, 321), 1088.0)
+    V("memset", R("ZQ", 392, 393), 2176.0)
+    V("memset", R("UH", 64, 66), 1024.0)
     V(ts, R("BHn", 0, 128), R("gI", 0, 128), c1("pg"), -1.0, A.is_equal, A.mult)
     V(ts, c1("p16i"), c1("pI"), 15, None, A.bitwise_and)
     V(tc, c1("p16"), c1("p16i"))
     V(tc, c1("pf"), c1("pI"))
     V(ts, R("IW", 0, 136), R("dI", 0, 136), 4.0, None, A.is_equal)
     V(ts, R("BLK", 0, 8), R("g8I", 0, 8), c1("pg"), 32768.0, A.is_equal, A.mult)
+    V(ts, R("BLK", 8, 16), R("g8I", 0, 8), c1("pg"), None, A.is_equal)
     V(ts, R("Q16", 0, 8), R("g8I", 0, 8), c1("pg"), None, A.is_equal)
     V(ts, R("MK", 0, 128), R("rI", 0, 128), c1("p16"), None, A.is_equal)
     V(tc, R("OFFR", 0, 8), R("g8I", 0, 8))
-    V(ts, c1("colA"), c1("pf"), 64.0, 32.0, A.is_ge, A.mult)
-    V(ts, c1("colB"), c1("pf"), 64.0, -262144.0, A.is_lt, A.mult)
-    V("memset", R("ONB", 0, 128), 1.0)
+    V(ts, c1("colA"), c1("pf"), 64.0, 0.5, A.is_ge, A.mult)
+    V(ts, c1("colB"), c1("pf"), 64.0, -4096.0, A.is_lt, A.mult)
+    V("memset", R("ON64", 0, 128), 64.0)
     V(ts, R("CD", 0, 128), R("rI", 0, 128), c1("colA"), c1("colB"), A.mult, A.add)
     V(ts, R("MMIN", 0, 128), R("rI", 0, 128), 0.0, BIG, A.is_equal, A.mult)
+    amp = 1.0 if opt["nrx"] == "s" else 2.0
+    for name, by in ((In, -1.0), (I1n, -1024.0), (I4n, -2048.0 * amp), (R("Ih", 0, 128), 0.5 * amp), (R("Ic", 0, 128), 1.0 / 128)):
+        V(ts, name, R("dI", 0, 128), 0.0, by, A.is_equal, A.mult)
 
-    def factors(j, name, at, dg):
-        V(ts, R(dg, 0, 128), I16, R("hf", j, j + 1), None, A.mult)
+    def factors(j, name, square, const):
+        for i in (2 * j, 2 * j + 1):
+            V(ts, R("dg%d" % i, 0, 128), I16, R("hf", i, i + 1), None, A.mult)
         for h in (0, 1):
-            o = R("b%d" % (4 + h), 128 * j, 128 * j + 128, 1, 48)
-            group([(o, R("ZQ", 48 - 8 * h, 96 - 8 * h), R(dg, 0, 128)), (o, R("ZQ", at - 8 * h, at + 48 - 8 * h), R("BHn", 0, 128))])
-            S(R(name + str(h), 0, 128, 1, 48), o, F.Copy)
-    factors(0, "PM_", 120, "dgA")
-    factors(1, "PQ_", 136, "dgB")
+            o = R("b%d" % (4 + h), 128 * j, 128 * j + 128, 1, 65)
+            rows = ((72 - 8 * h, R("dg%d" % (2 * j), 0, 128)), (24 - 8 * h, R("dg%d" % (2 * j + 1), 0, 128)),
+                    (200 - square - 8 * h, R("BHn", 0, 128)), (const - 64, I16))
+            group([(o, R("ZQ", a, a + 65), r) for a, r in rows])
+            S(R(name + str(h), 0, 128, 1, 65), o, F.Copy)
+    factors(0, "PM_", 32, 320)
+    factors(1, "PQ_", 16, 392)
     C(opt["icv"], R("I", 0, 1024), R("ixi", 0, 1024))
     for c in range(2):
         C(opt["lcv"][c], R("L", 1024 * c, 1024 * c + 1024), R("lki", 1024 * c, 1024 * c + 1024))
@@ -232,22 +250,18 @@ def build(opt):
     V(ts, R("BBn", 0, 128), R("gI", 0, 128), c1("pg"), -1.0, A.is_equal, A.mult)
     V(ts, R("BL1", 0, 8), R("g8I", 0, 8), c1("pg"), -1.0, A.is_equal, A.mult)
     V(ts, R("BL2", 0, 8), R("g8I", 0, 8), c1("pg"), 2.0, A.is_equal, A.mult)
-    V(ts, R("KM", 0, 16), R("rI", 0, 16), c1("p16"), None, A.is_equal)
-    for k in range(16):
-        if k < opt["selv"]:
-            V(ts, R("SEL", 128 * k, 128 * k + 128), I16, R("KM", k, k + 1), None, A.mult)
-        else:
-            S(R("SEL", 128 * k, 128 * k + 128), I16, F.Copy, None, R("KM", k, k + 1))
     V("memset", R("x_0", 2048, 2064), 0.0)
     V("memset", R("x_1", 2048, 2064), 0.0)
     V(ts, R("CS", 0, 128), R("r15I", 0, 128), c1("colA"), c1("colB"), A.mult, A.add)
     V(ts, R("MMAX", 0, 128), R("rI", 0, 128), 0.0, -BIG, A.is_equal, A.mult)
     V(tc, R("tf", 0, 2), R("thi", 0, 2))
-    V("memset", R("ONn", 0, 128), -1.0)
-    V(ts, R("dgC", 0, 128), I16, R("tf", 0, 1), None, A.mult)
-    group([(R("b4", 256, 384), R("ONn", 0, 128), R("dgC", 0, 128))])
-    V(ts, R("THR", 0, 128), R("b4", 256, 384), -32768.0, 32768.0 - OFF24, A.mult, A.add)
-    V("memset", R("THR", 15, 128, 16), -2.0e7)
+    V("memset", R("ONn", 0, 128), -0.5 * amp)
+    V("memset", R("ONk", 0, 128), -0.5 * amp / 1024)
+    V("memset", R("b0", 32, 33), -0.5 + 2.0 ** -12)
+    V(ts, c1("m15"), c1("p16"), 15.0, -1.0 / 64, A.is_lt, A.mult)
+    V(ts, c1("acol"), c1("tf"), 1.5, c1("m15"), A.add, A.mult)
+    V(ts, c1("acol"), c1("acol"), 1.0 / 64, None, A.add)
+    V(ts, R("CS", 128, 256), I16, c1("acol"), None, A.mult)
     V(ts, c1("q2i"), c1("pI"), 3, None, A.bitwise_and)
     V(ts, c1("bI"), c1("p16i"), 2, None, A.arith_shift_right)
     V(ts, c1("pk1"), c1("q2i"), 8.0, 8.0, A.mult, A.add)
@@ -257,27 +271,25 @@ def build(opt):
     V(ts, R("DUn", 0, 16), R("duI", 0, 16), c1("p16"), None, A.subtract)
     V(ts, R("DUE", 0, 16), R("DUn", 0, 16), -1.0, 1024.0, A.mult, A.add)
     V(ts, c1("k15"), c1("p16"), -1.0, 15.0, A.mult, A.add)
-    V(ts, R("RPc", 0, 128), R("dg4", 0, 128), -1.0, -4096.0, A.is_equal, A.mult)
+    V(ts, R("RPc", 0, 128), R("dg4", 0, 128), -1.0, -2048.0 * amp, A.is_equal, A.mult)
     V(ts, R("RPt", 0, 128), R("dg4", 0, 128), 0.0, -1.0, A.is_equal, A.mult)
     V(tt, R("RPJ", 0, 128), R("RPt", 0, 128), R("RPc", 0, 128), A.subtract)
     V(ts, R("RPK", 0, 128), R("dg4", 0, 128), -2.0, None, A.is_equal)
     V(ts, R("SLW", 0, 16), R("slI", 0, 16), 0.0, None, A.is_equal)
-    V(ts, R("I4n", 0, 128), R("dI", 0, 128), 0.0, -4096.0, A.is_equal, A.mult)
     V(ts, R("OF15", 0, 8), R("g8I", 0, 8), 16.0, 15.0, A.mult, A.add)
     for b in range(2):
         V(ts, R("E2", 160 * b, 160 * b + 160), R("qrel", 0, 160), 4.0 * b, c1("pg"), A.add, A.is_equal)
+        V(ts, R("TR", 160 * b, 160 * b + 160), R("dcol", 0, 160), c1("pf"), 16384.0, A.is_ge, A.mult)
     for b in range(4):
         V(ts, R("EC", 160 * b, 160 * b + 160), R("qrel", 0, 160), 4.0 * b, c1("pf"), A.add, A.is_equal)
-    for b in range(2):
-        V(ts, R("TR", 160 * b, 160 * b + 160), R("dcol", 0, 160), c1("pf"), 16384.0, A.is_ge, A.mult)
     V(tc, R("SM", 160, 320), R("SM", 0, 160))
     V("memset", R("QT", 3, 64, 4), 0.0)
     if any(opt["rg"] + opt["ry"]):
-        V(ts, R("BKn", 0, 8), R("BLK", 0, 8), -1.0, None, A.mult)
-        V(ts, R("BK2", 0, 8), R("BLK", 0, 8), 2.0, None, A.mult)
-    if any(e.strip("v") for r in opt["ge"] for e in r):
-        iota(R("EN", 0, 2048), [[1, 128], [0, 16]], 0, -1)
-        V(ts, R("EN", 0, 2048), R("EN", 0, 2048), 0.0, -1.0, A.is_equal, A.mult)
+        V(ts, R("BKn", 0, 16), R("BLK", 0, 16), -1.0, None, A.mult)
+        V(ts, R("BK2", 0, 16), R("BLK", 0, 16), 2.0, None, A.mult)
+    if any(opt["apart"]):
+        V(ts, R("PK", 2, 3), c1("pk4"), -1.0, 319.0, A.add, A.min)
+        V("memset", R("aJ", 16, 24), 0.0)
 
     def size(relu, out, in_):
         if relu:
@@ -285,14 +297,17 @@ def build(opt):
         else:
             S(out, in_, F.Abs)
 
-    def keys(relu, K, m, d, a, con, payload):
-        o = R(K, 0, 128)
+    def keys(relu, K, n, m, d, a, con, payload, cuts):
+        def sums(src, by, lo, hi, last):
+            P([(R(K, k, n, 16, hi, lo), R(src, 16 * lo + k, 16 * hi, 16), R(by, 0, n // 16), False, last and k == m - 1) for k in range(m)])
+        pay = (R(K, 0, 128), payload, I16, False, relu)
+        P([(R(K, 0, n), R("ON64", 0, 128), R(con, 0, n), True, False)] + ([] if relu else [pay]))
+        for lo, hi in cuts:
+            if relu:
+                sums(d, "BKn", lo, hi, False)
+            sums(a, "BK2" if relu else "BLK", lo, hi, not relu)
         if relu:
-            P([(o, R("ONB", 0, 128), R(con, 0, 128), True, False)] + [(R(K, k, 128, 16), R(d, k, 2048, 16), R("BKn", 0, 8), False, False) for k in range(m)])
-            P([(R(K, k, 128, 16), R(a, k, 2048, 16), R("BK2", 0, 8), False, False) for k in range(m)] + [(o, payload, I16, False, True)])
-        else:
-            P([(o, R("ONB", 0, 128), R(con, 0, 128), True, False), (o, payload, I16, False, False)])
-            P([(R(K, k, 128, 16), R(a, k, 2048, 16), R("BLK", 0, 8), False, k == m - 1) for k in range(m)])
+            P([pay])
 
     def earlier(h, own, spread, pick, row, p, Ad, ms, bias):
         D = "b%d" % (4 + h)
@@ -307,32 +322,48 @@ def build(opt):
         V(scan, R(ms, 320 * h, 320 * h + 320), R("SM", 0, 320), R(Ad, 320 * h, 320 * h + 320), 0.0, A.max, A.min)
 
     def scatter(table, n, off, a, b):
-        for k in (3, 2, 1, 0):
+        for k in (1, 0, 3, 2):
             V(tt, ind(R(table, 0, n), R(off, 4 * k, 4 * k + 4)), R(a, 64 * k, 64 * k + 64), R(b, 64 * k, 64 * k + 64), A.add)
+            ops[-1]["name"] = "v%s@%d" % (table, k)
 
+    def cuts(s):
+        out, lo = [], 0
+        for w in s.split():
+            out.append((lo, lo + int(w[:-1]), w[-1]))
+            lo = out[-1][1]
+        return out
+
+    DOWN = -0.5 + 2.0 ** -12
+    RLu = R("RLu", 0, 128, 1, 65)
     for t in range(3):
+        now[0] = t
         z = "z%d" % t
         zx = "zx%d" % (t % 2)
         P([(R("b0", 8 * h, 8 * h + 8), R(z, 128 * h, 128 * h + 128), R("W8", 0, 8), True, True) for h in (0, 1)])
-        V(tc, R("ui", 0, 16), R("b0", 0, 16))
+        C(opt["ui"][t], R("ui", 0, 16), R("b0", 0, 16))
         V(ts, R("ui", 0, 16), R("ui", 0, 16), 4095, None, A.bitwise_and)
         V(tt, R("uu", 0, 16), R("ui", 0, 16), R("ui", 0, 16), A.mult)
         V(ts, R("UQ", 0, 16), R("ui", 0, 16), 2047, None, A.bitwise_and)
+        V(ts, R("UQ", 48, 64), R("ui", 0, 16), 31, None, A.bitwise_and)
         V(ts, R("UQ", 16, 32), R("uu", 0, 16), 4, 2047, A.arith_shift_right, A.bitwise_and)
         V(ts, R("UQ", 32, 48), R("uu", 0, 16), 5, 1023, A.arith_shift_right, A.bitwise_and)
-        V(tc, R("UH", 0, 48), R("UQ", 0, 48))
-        group([(R("b0", 128, 256, 1, 48), R("UH", 0, 48), I16)])
-        S(R("RLu", 0, 128, 1, 48), R("b0", 128, 256, 1, 48), F.Copy)
-        P([(R("b0", 256 + 128 * h, 384 + 128 * h), R("PM_%d" % h, 0, 128, 1, 48), R("RLu", 0, 128, 1, 48), True, True) for h in (0, 1)])
+        C(opt["ui"][t], R("UH", 0, 64), R("UQ", 0, 64))
+        group([(R("b0", 128, 256, 1, 65), R("UH", 0, 65), I16)])
+        S(RLu, R("b0", 128, 256, 1, 65), F.Copy)
+        P([(R("b0", 256 + 128 * h, 384 + 128 * h), R("PM_%d" % h, 0, 128, 1, 65), RLu, True, True) for h in (0, 1)])
         if t == 0:
-            C(opt["em"], R("em", 0, 256), R("b0", 256, 512))
-        elif opt["em"] == "v":
-            V(ts, R("em", 0, 256), R("b0", 256, 512), c1("Nc"), None, A.add)
+            S(R("q1", 0, 256), R("b0", 256, 512), F.Copy, DOWN, 1.0 / 1024)
         else:
-            S(R("em", 0, 256), R("b0", 256, 512), F.Identity, c1("Nc"))
-        V(ts, R("em", 0, 256), R("em", 0, 256), 1023, None, A.bitwise_and)
-        C(opt["emu"], R("emu", 0, 256), R("em", 0, 256))
-        C(opt["emh"], R("emh", 0, 256), R("emu", 0, 256) if opt["emh"] == "v" else R("em", 0, 256))
+            S(R("q1", 0, 256), R("b0", 256, 512), F.Identity, c1("Nb"), 1.0 / 1024)
+        P([(R("b3", 256, 512), I1n, R("q1", 0, 256), True, False)] +
+          [(R("b3", 256 + 128 * h, 384 + 128 * h), R("PM_%d" % h, 0, 128, 1, 65), RLu, False, h == 1) for h in (0, 1)])
+        if t == 0:
+            C(opt["emu"], R("emu", 0, 256), R("b3", 256, 512))
+        elif opt["emu"] == "v":
+            V(ts, R("emu", 0, 256), R("b3", 256, 512), c1("Nc"), None, A.add)
+        else:
+            S(R("emu", 0, 256), R("b3", 256, 512), F.Identity, c1("Nc"))
+        C(opt["emh"], R("emh", 0, 256), R("emu", 0, 256))
         for h in (0, 1):
             for m, eng in enumerate(opt["zx"][t][h]):
                 if eng.islower():
@@ -341,53 +372,49 @@ def build(opt):
                     C(eng.lower(), R(zx, m, 4096, 16), R(z, 0, 256))
         for h in (0, 1):
             H, K = "_%d" % h, "b%d" % (2 + h)
-            w = 2048 // opt["gch"]
-            if opt["ge"][t][h].strip("v"):
+            parts = cuts(opt["ge"][t][h])
+            if any(e != "v" for a, b, e in parts):
                 group([(R("b0", 128, 256), R(z, 128 * h, 128 * h + 128), IB)])
-                S(R("zT", 0, 128), R("b0", 128, 256), F.Copy)
-            for c in range(opt["gch"]):
-                got = ind(R("G", 0, 1024), R("emu", 128 * h + w // 16 * c, 128 * h + w // 16 * (c + 1)))
-                if opt["ge"][t][h][c] == "v":
-                    V(tt, R("DG" + H, w * c, w * c + w), got, R(zx, 2048 * h + w * c, 2048 * h + w * c + w), A.subtract)
-                    size(opt["rg"][h], R("AG" + H, w * c, w * c + w), R("DG" + H, w * c, w * c + w))
+                S(R("zT", 128 * h, 128 * h + 128), R("b0", 128, 256), F.Copy, None, -1.0)
+            for a, b, e in parts:
+                got, d = ind(R("G", 0, 1024), R("emu", 128 * h + a, 128 * h + b)), R("DG" + H, 16 * a, 16 * b)
+                if e == "v":
+                    V(tt, d, got, R(zx, 2048 * h + 16 * a, 2048 * h + 16 * b), A.subtract)
+                    size(opt["rg"][h], R("AG" + H, 16 * a, 16 * b), d)
                 else:
-                    C(opt["ge"][t][h][c].lower(), R("DG" + H, w * c, w * c + w), got)
-                    for a in range(w * c, w * c + w, 512):
-                        o = R("b%d" % (4 + a // 512 % 2), 0, 512)
-                        group([(o, IB, R("DG" + H, a, a + 512)), (o, R("zT", 0, 128), R("EN", a, a + 512))])
-                        S(R("AG" + H, a, a + 512), o, F.Abs)
-            keys(opt["rg"][h], K, 16, "DG" + H, "AG" + H, "CD", R("emh", 128 * h, 128 * h + 128))
+                    C(e.lower(), d, got)
+                    for c in range(16 * a, 16 * b, 512):
+                        o = R("b%d" % (4 + c // 512 % 2), 0, 512)
+                        group([(o, IB, R("DG" + H, c, c + 512)), (o, R("zT", 128 * h, 128 * h + 128), R("EN", c, c + 512))])
+                        S(R("AG" + H, c, c + 512), o, F.Abs)
+            keys(opt["rg"][h], K, 128, 16, "DG" + H, "AG" + H, "CD", R("emh", 128 * h, 128 * h + 128), opt["gk"][h])
             V(scan, R("km" + H, 0, 128), R("MMIN", 0, 128), R(K, 0, 128), 0.0, A.add, A.min)
             V(tc, R("ei" + H, 0, 8), R("km" + H, 15, 128, 16))
             V(ts, R("ej" + H, 0, 8), R("ei" + H, 0, 8), 1023, None, A.bitwise_and)
             V(tt, R("ME" + H, 0, 128), ind(R("ej" + H, 0, 8), R("OFFR", 0, 8)), R("MK", 0, 128), A.mult)
             group([(R("b7", 8 * h, 8 * h + 8), R("ME" + H, 0, 128), R("Q16", 0, 8))])
-            V(tc, R("eu", 8 * h, 8 * h + 8), R("b7", 8 * h, 8 * h + 8))
+            C(opt["eu"], R("eu", 8 * h, 8 * h + 8), R("b7", 8 * h, 8 * h + 8))
             V(tc, R("Ju" + H, 0, 128), ind(R("I", 0, 1024), R("eu", 8 * h, 8 * h + 8)))
             C(opt["jh"], R("Jh", 128 * h, 128 * h + 128), R("Ju" + H, 0, 128))
             group([(R("b7", 256 + 128 * h, 384 + 128 * h), R("ME" + H, 0, 128), I16)])
         for h in (0, 1):
             H = "_%d" % h
-            w = 2048 // opt["xch"]
-            for c in range(opt["xch"]):
-                C(opt["xe"][t][h][c], R("x" + H, w * c, w * c + w), ind(R("xb", 0, 2048), R("Ju" + H, w // 16 * c, w // 16 * (c + 1))))
-            w = 2048 // opt["lch"]
-            n = w // 16
-            for c in range(opt["lch"]):
-                C("s", R("Lg" + H, w * c, w * c + w), ind(R("L", 0, 2048), R("Ju" + H, n * c, n * c + n)))
-                o = R("b6", 128 * h + n * c, 128 * h + n * c + n)
-                group([(o, R("SEL", 128 * k, 128 * k + 128), R("Lg" + H, w * c + k, w * c + w, 16)) for k in range(16)])
-                C(opt["nu"], R("nu" + H, n * c, n * c + n), o)
-            w = 2048 // opt["ych"]
-            for c in range(opt["ych"]):
-                V(tt, R("Dy" + H, w * c, w * c + w), ind(R("xb", 0, 2048), R("nu" + H, w // 16 * c, w // 16 * (c + 1))), R("x" + H, w * c + 1, w * c + w + 1), A.subtract)
-                size(opt["ry"][h], R("Ay" + H, w * c, w * c + w), R("Dy" + H, w * c, w * c + w))
-            V(scan, R("mx" + H, 0, 2048), R("MR", 0, 2048), R("x" + H, 0, 2048), 0.0, A.min, A.max)
+            for a, b, e in cuts(opt["xe"][t][h]):
+                C(e, R("x" + H, 16 * a, 16 * b), ind(R("xb", 0, 2048), R("Ju" + H, a, b)))
+            for a, b, e in cuts(opt["le"][t][h]):
+                C(e, R("Lg" + H, 16 * a, 16 * b), ind(R("L", 0, 2048), R("Ju" + H, a, b)))
+                o = R("b6", 128 * h + a, 128 * h + b)
+                group([(o, R("SEL", 128 * k, 128 * k + 128), R("Lg" + H, 16 * a + k, 16 * b, 16)) for k in range(16)])
+                C(opt["nu"], R("nu" + H, a, b), o)
+            for a, b in opt["yk"][h]:
+                d = R("Dy" + H, 16 * a, 16 * b)
+                V(tt, d, ind(R("xb", 0, 2048), R("nu" + H, a, b)), R("x" + H, 16 * a + 1, 16 * b + 1), A.subtract)
+                size(opt["ry"][h], R("Ay" + H, 16 * a, 16 * b), d)
+            V(scan, R("mx" + H, 0, 2048), R("MR", 0, 2048), R("x" + H, 0, 2048), 0.0, A.mult, A.max)
             o = R("b%d" % (4 + h), 320, 448)
             group([(o, IB, R(z, 128 * h, 128 * h + 128)), (o, IB, R("mx" + H, 15, 2048, 16))])
             S(R("zt", 128 * h, 128 * h + 128), o, F.Copy, 127.75, 0.5)
-            parts = [(128 * h, 128 * h + 128)] if opt["split"][t] else [(0, 256)] if h == 1 else []
-            for a, b in parts:
+            for a, b in [(128 * h, 128 * h + 128)] if opt["split"][t] else [(0, 256)] if h == 1 else []:
                 V(ts, R("zs%d" % t, a, b), R("zt", a, b), -128.0, None, A.add)
                 add("g", "remote", [(t, a, b, "arr%d" % (2 * t + h))], [R("zs%d" % t, a, b)], [R("z%d" % (t + 1), a, b)], RCOST, RLAT)
         V(tt, R("aE", 0, 16), R("b7", 0, 16), R("DUE", 0, 16), A.subtract)
@@ -396,80 +423,101 @@ def build(opt):
             earlier(h, R("ME_%d" % h, 0, 128), R("E2", 0, 320), R("BHn", 0, 128), "Y", 128, "AdE", "msE", None)
         V(tt, R("tE", 0, 16), ind(R("msE", 0, 640), R("PK", 0, 1)), R("aE", 0, 16), A.mult)
         V(tt, R("oE", 0, 16), R("tE", 0, 16), R("DUE", 0, 16), A.add)
-        V(tc, R("oEu", 0, 16), R("oE", 0, 16))
+        C(opt["oeu"], R("oEu", 0, 16), R("oE", 0, 16))
         if t < 2:
             V(tt, R("dz", 0, 256), ind(R("G", 0, 1024), R("eu", 0, 16)), R(z, 0, 256), A.subtract)
-        P([(R("b0", 256 + 128 * h, 384 + 128 * h), R("PQ_%d" % h, 0, 128, 1, 48), R("RLu", 0, 128, 1, 48), True, True) for h in (0, 1)])
-        C(opt["vi"], R("vi", 0, 256), R("b0", 256, 512))
-        V(ts, R("vi", 0, 256), R("vi", 0, 256), 2047, None, A.bitwise_and)
+        P([(R("b0", 256 + 128 * h, 384 + 128 * h), R("PQ_%d" % h, 0, 128, 1, 65), RLu, True, True) for h in (0, 1)])
+        S(R("q2", 0, 256), R("b0", 256, 512), F.Copy, DOWN, 1.0 / 2048)
         C(opt["jf"], R("Jf", 0, 256), R("Jh", 0, 256))
         VJ = R("b2", 256, 512)
-        group([(R("b3", 256, 512), I16, R("Jh", 0, 256))])
-        V(tt, VJ, R("vi", 0, 256), R("b3", 256, 512), A.subtract)
+        P([(VJ, I1n, R("q2", 0, 256), True, False), (VJ, I1n, R("q2", 0, 256), False, False)] +
+          [(R("b2", 256 + 128 * h, 384 + 128 * h), R("PQ_%d" % h, 0, 128, 1, 65), RLu, False, False) for h in (0, 1)] +
+          [(VJ, In, R("Jh", 0, 256), False, True)])
         for h in (0, 1):
             H, K = "_%d" % h, "b%d" % (2 + h)
             l = (128 * h, 128 * h + 128)
-            keys(opt["ry"][h], K, 15, "Dy" + H, "Ay" + H, "CS", R("Jh", *l))
-            V(tt, R("le", *l), R(K, 0, 128), R("THR", 0, 128), A.is_lt)
-            V(scan, R("cs", *l), R("MR", 0, 128), R("le", *l), 0.0, A.min, A.add)
-            V(ts, R("nrx", *l), ind(R("cs", *l), R("OF15", 0, 8)), 11.5, None, A.is_lt)
+            keys(opt["ry"][h], K, 256, 15, "Dy" + H, "Ay" + H, "CS", R("Jh", *l), opt["yk"][h])
+            if opt["sign"] == "s":
+                S(R("le", *l), R(K, 128, 256), F.Sign)
+            else:
+                V(ts, R("le", *l), R(K, 128, 256), 0.0, None, A.is_gt)
+            V(scan, R("cs", *l), R("MR", 0, 128), R("le", *l), 0.0, A.mult, A.add)
+            edge = -7.0 if opt["sign"] == "s" else 4.5
+            if opt["nrx"] == "s":
+                S(R("nrx", *l), ind(R("cs", *l), R("OF15", 0, 8)), F.Sign, -edge)
+            else:
+                V(ts, R("nrx", *l), ind(R("cs", *l), R("OF15", 0, 8)), edge, 0.5, A.is_gt, A.subtract)
             if t < 2:
-                group([(R("b6", *l), R("nrx", *l), I16)])
+                group([(R("b6", *l), R("ON64", 0, 128), R("Ic", 0, 128)), (R("b6", *l), R("nrx", *l), R("Ih", 0, 128))])
                 V(tt, R("tg", *l), R("b6", *l), R("dz", *l), A.mult)
             V(scan, R("sm", *l), R("MMAX", 0, 128), R(K, 0, 128), 0.0, A.add, A.max)
-        V(tc, R("QT", 1, 64, 4), R("nrx", 0, 256, 16))
-        V(tc, R("si", 0, 16), R("sm", 15, 256, 16))
-        V(ts, R("SJ", 0, 32, 2), R("si", 0, 16), 2047, None, A.bitwise_and)
-        V(ts, R("SJ", 1, 32, 2), R("si", 0, 16), 11, 15, A.arith_shift_right, A.bitwise_and)
-        V(tc, R("QT", 0, 64, 2), R("SJ", 0, 32))
         if t < 2:
-            group([(R("b7", 16, 24), R("ONn", 0, 128), R("nrx", 128 * h, 128 * h + 128, 16)) for h in (0, 1)])
-            V("tensor_reduce", c1("Nc"), R("b7", 16, 24), "X", A.add)
-        P([(R("b7", 256 + 128 * h, 384 + 128 * h, 1, 32), R("QT", 32 * h, 32 * h + 32), I16, True, True) for h in (0, 1)])
-        RL = R("RL", 0, 256, 1, 32)
-        S(RL, R("b7", 256, 512, 1, 32), F.Copy)
-        if t < 2:
+            for a, by in ((24, "ONk"), (16, "ONn")):
+                group([(R("b0", a, a + 8), R(by, 0, 128), R("nrx", 128 * h, 128 * h + 128, 16)) for h in (0, 1)])
+            V("tensor_reduce", c1("Nb"), R("b0", 24, 33), "X", A.add)
+            V("tensor_reduce", c1("Nc"), R("b0", 16, 24), "X", A.add)
             scatter("G", 1088, "oEu", "tg", z)
-        P([(R("b1", 0, 256), R("ZQ", 200, 328), R("Jh", 0, 256), True, False)] +
-          [(R("b1", 128 * h, 128 * h + 128), R(z, 128 * h, 128 * h + 128), R("BBn", 0, 128), False, False) for h in (0, 1)])
+        folded = [h for h in (0, 1) if opt["fold"][t][h]]
+        P([(R("b1", 0, 256), R("ZQ", 400, 528), R("Jh", 0, 256), True, False)] +
+          [(R("b1", 128 * h, 128 * h + 128), R(z, 128 * h, 128 * h + 128), R("BBn", 0, 128), False, False) for h in folded])
         for h in (0, 1):
-            X, M = "x_%d" % h, "M%d%d" % (t, h)
-            add("g", "fold", [(R(M, 0, 2048), R(X, 0, 2048), R(zx, 2048 * h, 2048 * h + 2048), 2 * t + h)],
-                [R(X, 0, 2048), R(zx, 2048 * h, 2048 * h + 2048)], [R(M, 0, 2048)], RCOST, FLAT)
-        for src, by in (("x_%d", "BL1"), ("M%d%%d" % t, "BL2")):
-            for h in (0, 1):
-                for k0 in (0, 8):
-                    P([(R("b1", 128 * h + k, 128 * h + 128, 16), R(src % h, k, 2048, 16), R(by, 0, 8), False, by == "BL2" and h == 1 and k == 15)
-                       for k in range(k0, k0 + 8)])
+            X, M, Z = R("x_%d" % h, 0, 2048), R("M%d_%d" % (t, h), 0, 2048), R(zx, 2048 * h, 2048 * h + 2048)
+            if h in folded:
+                add("g", "fold", [(M, X, Z, 2 * t + h)], [X, Z], [M], RCOST, FLAT)
+                continue
+            for c in range(0, 2048, 512):
+                o = R("b0", 0, 512)
+                group([(o, IB, R(X[0], c, c + 512)), (o, R("zT", 128 * h, 128 * h + 128), R("EN", c, c + 512))])
+                S(R(M[0], c, c + 512), o, F.Abs)
+        terms = [("x_%d" % h, h, R("BL1", 0, 8)) for h in folded]
+        terms += [("M%d_%d" % (t, h), h, R("BL2", 0, 8) if h in folded else R("BLK", 8, 16)) for h in (0, 1)]
+        for src, h, by in terms:
+            P([(R("b1", 128 * h + k, 128 * h + 128, 16), R(src, k, 2048, 16), by, False, src == terms[-1][0] and k == 15) for k in range(16)])
         S(R("fT", 0, 256), R("b1", 0, 256), F.Copy)
         for h in (0, 1):
             o = R("b1", 256 + 128 * h, 384 + 128 * h)
-            group([(o, R("fT", 128 * h, 128 * h + 128), I16), (o, R("nrx", 128 * h, 128 * h + 128), R("I4n", 0, 128))])
-        V(ts, R("ch", 0, 256), R("b1", 256, 512), 4096.0, R("tf", 1, 2), A.add, A.is_gt)
+            group([(o, R("fT", 128 * h, 128 * h + 128), I16), (o, R("nrx", 128 * h, 128 * h + 128), I4n)])
+        V(ts, R("ch", 0, 256), R("b1", 256, 512), 2048.0, R("tf", 1, 2), A.add, A.is_gt)
         V(tt, R("tmp", 0, 256), R("ch", 0, 256), VJ, A.mult)
         scatter("I", 1088, "oEu", "tmp", "Jf")
         if t == 2:
             dma("y", "yi", R("I", 0, 1024), 4096, "d8")
-        P([(R("b7", 64 + r, 320, 16, 16), R("RL", r, 256, 16, 32), R("SLW", 0, 16, 1, 32), True, True) for r in range(16)])
-        S(R("WT", 0, 256, 1, 16), R("b7", 64, 320, 1, 16), F.Copy)
-        o = R("b7", 32, 48)
-        group([(o, R("WT", 0, 128, 1, 16), R("IW", 4, 20, 1, 16)), (o, R("WT", 128, 256, 1, 16), R("I4n", 0, 16, 1, 16)), (o, I16, R("DUn", 0, 16))])
-        group([(R("b7", 48, 64), R("WT", 0, 128, 1, 16), R("IW", 4, 20, 1, 16))])
-        V(ts, R("aJ", 0, 16), o, 2048.0, 0.0, A.add, A.min)
-        V(tc, R("Ju16", 0, 16), R("b7", 48, 64))
-        for h in (0, 1):
-            earlier(h, R("WT", 0, 128, 1, 16), R("EC", 320 * h, 320 * h + 320, 1, 16), R("RPJ", 0, 128, 1, 32), "RL", 32, "AdJ", "msJ", -4096.0)
-        V(tt, R("tJ", 0, 16), ind(R("msJ", 0, 640), R("PK", 0, 1)), R("aJ", 0, 16), A.mult)
-        V(tt, R("oJ", 0, 16), R("tJ", 0, 16), R("DUn", 0, 16), A.subtract)
-        V(ts, R("oJu", 0, 16), R("oJ", 0, 16), 2048.0, None, A.add)
-        S(R("Lold", 0, 256), ind(R("L", 0, 2048), R("Ju16", 0, 16)), F.Copy)
-        group([(R("b6", 256, 512), R("RPK", 0, 128, 1, 32), RL)])
-        V(ts, R("mk", 0, 256), R("b6", 256, 512), c1("k15"), None, A.is_equal)
-        group([(R("b6", 0, 256), ISH, R("Jh", 0, 256))])
-        V(tt, R("b6", 0, 256), R("b6", 0, 256), R("Lold", 0, 256), A.subtract)
-        V(tt, R("t2", 0, 256), R("b6", 0, 256), R("mk", 0, 256), A.mult)
+        for h0, h1 in ((0, 1), (1, 2)) if opt["apart"][t] else ((0, 2),):
+            n, a, b, w = 8 * (h1 - h0), 128 * h0, 128 * h1, 256 * h0
+            C(opt["qt"][0], R("QT", 32 * h0 + 1, 32 * h1, 4), R("nrx", a, b, 16))
+            C(opt["qt"][1], R("si", 8 * h0, 8 * h1), R("sm", a + 15, b, 16))
+            V(ts, R("SJ", 16 * h0, 16 * h1, 2), R("si", 8 * h0, 8 * h1), 2047, None, A.bitwise_and)
+            V(ts, R("SJ", 16 * h0 + 1, 16 * h1, 2), R("si", 8 * h0, 8 * h1), 11, 15, A.arith_shift_right, A.bitwise_and)
+            C(opt["qt"][2], R("QT", 32 * h0, 32 * h1, 2), R("SJ", 16 * h0, 16 * h1))
+            P([(R("b7", 256 + 128 * h, 384 + 128 * h, 1, 32), R("QT", 32 * h, 32 * h + 32), I16, True, True) for h in range(h0, h1)])
+            RL = R("RL", a, b, 1, 32)
+            S(RL, R("b7", 256 + a, 256 + b, 1, 32), F.Copy)
+            P([(R("b7", 64 + r, 320, 16, n), R("RL", a + r, b, 16, 32), R("SLW", 0, 16, 1, 32), True, True) for r in range(16)])
+            S(R("WT", w, w + 256, 1, n), R("b7", 64, 320, 1, n), F.Copy)
+            WJ, o = R("WT", w, w + 128, 1, n), R("b7", 32 + 8 * h0, 32 + 8 * h1)
+            group([(o, WJ, R("IW", 4, 4 + n, 1, n)), (o, R("WT", w + 128, w + 256, 1, n), R("I4n", 0, n, 1, n)), (o, I16, R("DUn", 8 * h0, 8 * h1))])
+            group([(R("b7", 48 + 8 * h0, 48 + 8 * h1), WJ, R("IW", 4, 4 + n, 1, n))])
+            V(ts, R("aJ", 8 * h0, 8 * h1), o, 0.0, None, A.min)
+            C(opt["ju16"], R("Ju16", 8 * h0, 8 * h1), R("b7", 48 + 8 * h0, 48 + 8 * h1))
+            for h in range(h0, h1):
+                earlier(h, WJ, R("EC", 320 * (h - h0), 320 * (h - h0) + 320, 1, n), R("RPJ", 0, 128, 1, 32), "RL", 32, "AdJ", "msJ", -2048.0)
+            pk = 2 if n == 8 else 0
+            V(tt, R("tJ", 16 * h0, 16 * h0 + 16), ind(R("msJ", 320 * h0, 320 * h1), R("PK", pk, pk + 1)), R("aJ", 8 * h0, 8 * h0 + 16), A.mult)
+            V(tt, R("oJ", 8 * h0, 8 * h1), R("tJ", 16 * h0, 16 * h0 + n), R("DUn", 8 * h0, 8 * h1), A.subtract)
+            V(ts, R("oJu", 8 * h0, 8 * h1), R("oJ", 8 * h0, 8 * h1), 2048.0, None, A.add)
+            S(R("Lold", a, b), ind(R("L", 0, 2048), R("Ju16", 8 * h0, 8 * h1)), F.Copy)
+            group([(R("b6", 256 + a, 256 + b), R("RPK", 0, 128, 1, 32), RL)])
+            V(ts, R("mk", a, b), R("b6", 256 + a, 256 + b), c1("k15"), None, A.is_equal)
+            if opt["lo16"][t] == "v":
+                group([(R("b6", a, b), ISH, R("Jh", a, b))])
+                V(tt, R("b6", a, b), R("b6", a, b), R("Lold", a, b), A.subtract)
+            else:
+                C(opt["lo16"][t], R("Lo16", a, b), R("Lold", a, b))
+                group([(R("b6", a, b), ISH, R("Jh", a, b)), (R("b6", a, b), In, R("Lo16", a, b))])
+            V(tt, R("t2", a, b), R("b6", a, b), R("mk", a, b), A.mult)
         scatter("L", 2112, "oJu", "t2", "Lold")
-    dma("s", "yz", R("z3", 0, 256), 512, "d9")
+    dma("y", R("yz", 0, 128), R("z3", 128, 256), 256, "d9")
+    dma("y", R("yz", 128, 256), R("z3", 0, 128), 256, "d13")
     dma("y", "yl", R("L", 0, 2048), 8192, "d10")
     return ops
 
@@ -494,92 +542,29 @@ def edges(ops):
         for w, rs in ((True, o["writes"]), (False, o["reads"])):
             for r in rs:
                 touched.setdefault(r[0], []).append((o["i"], r, w))
+    where = {(o["t"], o["name"]): o["i"] for o in ops}
+    for t in range(3):
+        for turn in ops[0]["turns"][t]:
+            got = [where[t, w] for w in turn.split() if (t, w) in where]
+            for j, i in zip(got, got[1:]):
+                pre[i].setdefault(j, False)
     return pre
 
 
-def tails(ops, pre, extra=None):
-    n = len(ops)
-    best = [0.0] * n
-    tail = [0.0] * n
-    for i in range(n - 1, -1, -1):
-        tail[i] = best[i] + ops[i]["cost"] + ops[i]["lat"]
-        for j in pre[i]:
-            best[j] = max(best[j], tail[i] + (WAKE if pre[i][j] else -ops[j]["lat"]))
-    return tail
-
-
-def schedule(ops, pre, urge, slack=40.0):
-    n = len(ops)
-    succ = [[] for _ in range(n)]
-    for i in range(n):
-        for j in pre[i]:
-            succ[j].append(i)
-    banks = [sorted(set(bank(r) for r in o["reads"] + o["writes"] if bank(r))) for o in ops]
-    waits = [dict(e) for e in pre]
-    left = [len(e) for e in pre]
-    ready, start, fin = [0.0] * n, [0.0] * n, [0.0] * n
-    free, last, pipe = {}, {}, 0.0
-    avail = [i for i in range(n) if left[i] == 0]
-    order = []
-
-    def can(i):
-        s = max(ready[i], free.get(ops[i]["q"], 0.0))
-        for b in banks[i]:
-            for q, j in last.get(b, {}).items():
-                if q != ops[i]["q"]:
-                    s = max(s, fin[j] + WAKE)
-        return s
-
-    while avail:
-        at = {i: can(i) for i in avail}
-        i = min(avail, key=lambda k: (at[k], -urge[k]))
-        q, s0 = ops[i]["q"], at[i]
-        mine = [k for k in avail if ops[k]["q"] == q]
-        for k in mine:
-            if at[k] <= s0 + slack and urge[k] > urge[i]:
-                i = k
-        for k in mine:
-            if at[k] < at[i] + ops[i]["cost"] and urge[k] - urge[i] > 4 * (at[k] - at[i]) + ops[k]["cost"] and at[k] - at[i] < 0.25 * ops[i]["cost"]:
-                i = k
-        o, s = ops[i], at[i]
-        avail.remove(i)
-        for b in banks[i]:
-            for p, j in last.setdefault(b, {}).items():
-                if p != q:
-                    waits[i][j] = True
-            last[b][q] = i
-        start[i] = s
-        free[q] = s + o["cost"]
-        fin[i] = s + o["cost"] + o["lat"]
-        if o["kind"] == "dma":
-            pipe = fin[i] = max(s + o["cost"] + DLAT, pipe) + o["nbytes"] / DRATE
-        order.append(i)
-        for k in succ[i]:
-            ready[k] = max(ready[k], fin[i] + WAKE if pre[k][i] else s)
-            left[k] -= 1
-            if left[k] == 0:
-                avail.append(k)
-    return order, waits, start, max(fin)
-
-
-def fit(seq, lags, uses):
-    start, busy = {}, {}
-    for i in seq:
-        s = max([0.0] + [start[j] + d for j, d in lags[i].items()])
-        moved = True
-        while moved:
-            moved = False
-            for res, off, n, who in uses[i]:
-                taken = busy.setdefault(res, [])
-                k = max(0, before(taken, s + off) - 2)
-                while k < len(taken) and taken[k][0] < s + off + n - 1e-6:
-                    if s + off < taken[k][1] - 1e-6 and (who is None or who != taken[k][2]):
-                        s, moved = taken[k][1] - off, len(uses[i]) > 1
-                    k += 1
-        start[i] = s
-        for res, off, n, who in uses[i]:
-            busy[res].insert(before(busy[res], s + off), (s + off, s + off + n, who))
-    return start
+def sequence(pre):
+    seq, seen = [], set()
+    for i in range(len(pre)):
+        todo = [i]
+        while todo:
+            left = [j for j in pre[todo[-1]] if j not in seen]
+            if left:
+                todo.append(left[0])
+            elif todo[-1] not in seen:
+                seen.add(todo[-1])
+                seq.append(todo.pop())
+            else:
+                todo.pop()
+    return seq
 
 
 def before(taken, s):
@@ -591,6 +576,35 @@ def before(taken, s):
         else:
             hi = mid
     return lo
+
+
+def fit(seq, lags, uses):
+    start, busy = [0.0] * len(seq), {}
+    for i in seq:
+        s = 0.0
+        for j, d in lags[i].items():
+            if start[j] + d > s:
+                s = start[j] + d
+        moved = True
+        while moved:
+            moved = False
+            for res, off, n, who in uses[i]:
+                taken = busy.setdefault(res, [])
+                if not taken or taken[-1][1] <= s + off:
+                    continue
+                k = max(0, before(taken, s + off) - 2)
+                while k < len(taken) and taken[k][0] < s + off + n - 1e-6:
+                    if s + off < taken[k][1] - 1e-6 and (who is None or who != taken[k][2]):
+                        s, moved = taken[k][1] - off, len(uses[i]) > 1
+                    k += 1
+        start[i] = s
+        for res, off, n, who in uses[i]:
+            taken = busy[res]
+            if not taken or taken[-1][0] <= s + off:
+                taken.append((s + off, s + off + n, who))
+            else:
+                taken.insert(before(taken, s + off), (s + off, s + off + n, who))
+    return start
 
 
 def schedule(ops, pre, passes, seed):
@@ -605,48 +619,62 @@ def schedule(ops, pre, passes, seed):
     ahead, back = [], []
     for i, o in enumerate(ops):
         u = [(o["q"], 0.0, o["cost"], None)] + [(b, 0.0, o["cost"] + WAKE, o["q"]) for b in banks[i]]
-        if o["kind"] == "dma":
-            u.append(("engines", o["cost"] + DLAT, o["lat"] - DLAT, None))
+        if o.get("hold"):
+            u.append(("engines", o["cost"] + DLAT, o["hold"], None))
         ahead.append(u)
         back.append([(res, span[i] - off - m, m, who) for res, off, m, who in u])
 
     def ordered(key, lags, way):
         key = list(key)
         for i in way:
-            key[i] = max([key[i]] + [key[j] + 1e-3 for j in lags[i]])
+            for j in lags[i]:
+                if key[j] >= key[i]:
+                    key[i] = key[j] + 1e-3
         return sorted(range(n), key=lambda i: key[i])
 
+    def early(key):
+        start = fit(ordered(key, fwd, seq), fwd, ahead)
+        end = max(start[i] + span[i] for i in range(n))
+        return end + 0.3 * sum(start[i] for i in long) / len(long), end, start, key
+
+    def late(start):
+        s = fit(ordered([-start[i] - span[i] for i in range(n)], bwd, seq[::-1]), bwd, back)
+        return [-s[i] - span[i] for i in range(n)]
+
+    def move(key, i, by):
+        todo = [(i, key[i] + by)]
+        key[i] = max(key[i], key[i] + by)
+        while todo:
+            i, at = todo.pop()
+            if key[i] > at:
+                key[i] = at
+                todo += [(j, at - 1e-2) for j in fwd[i]]
+
+    seq = sequence(pre)
+    long = [i for i in range(n) if ops[i]["cost"] > 800 and ops[i]["q"] in "vs"]
+    alike = {}
+    for o in ops:
+        alike.setdefault(o["name"], []).append(o["i"])
     tail = [0.0] * n
-    for i in range(n - 1, -1, -1):
+    for i in seq[::-1]:
         tail[i] = max([span[i]] + [tail[k] + fwd[k][i] for k in bwd[i]])
-
-    def pack(key):
-        start = fit(ordered(key, fwd, range(n)), fwd, ahead)
-        late = fit(ordered([-start[i] - span[i] for i in range(n)], bwd, range(n - 1, -1, -1)), bwd, back)
-        key = [-late[i] - span[i] for i in range(n)]
-        start = fit(ordered(key, fwd, range(n)), fwd, ahead)
-        return max(start[i] + span[i] for i in range(n)), start, key
-
-    rng = np.random.default_rng(seed)
-    names = [(o["q"],) + (o["writes"] or o["reads"])[0][:2] for o in ops]
-    now = best = pack([-tail[i] for i in range(n)])
-    for k in range(passes):
-        key = list(now[2]) if k % 2 else [now[1][i] for i in range(n)]
-        if k % 3 == 0:
-            at, wide, by = key[rng.integers(n)], rng.choice((3000, 8000)), rng.choice((300, 1000, 2500))
-            key = [x + by * rng.normal() if abs(x - at) < wide else x for x in key]
-        elif k % 3 == 1:
-            some, by = [names[i] for i in rng.integers(n, size=rng.choice((1, 2, 4)))], 3000 * rng.normal()
-            key = [key[i] + by if names[i] in some else key[i] for i in range(n)]
+    dice = np.random.default_rng(seed).random((passes, 3, 7)).tolist()
+    now = best = early(late(early([-x for x in tail])[2]))
+    for k, d in enumerate(dice):
+        if d[0][0] < 0.05:
+            key = late(now[2])
         else:
-            for i in rng.integers(n, size=rng.choice((1, 3, 8))):
-                key[i] += 3000 * rng.normal()
-        new = pack(key)
-        if new[0] < now[0] - 200.0 * (1 - k / passes) * np.log(rng.random()):
+            key = list(now[3]) if d[0][1] < 0.7 else [now[2][i] for i in range(n)]
+            for a in d[:(1, 1, 2, 3)[int(4 * d[1][0])]]:
+                i = long[int(a[2] * len(long))] if a[3] < 0.3 else int(a[2] * n)
+                for j in alike[ops[i]["name"]] if a[4] < 0.4 else [i]:
+                    move(key, j, (600, 2000, 6000)[int(3 * a[5])] * (2 * a[6] - 1) * abs(2 * a[6] - 1))
+        new = early(key)
+        if new[0] < now[0] - (5 + 120.0 * (1 - k / passes)) * math.log(d[2][0]):
             now = new
-            if new[0] < best[0]:
+            if new[1] < best[1]:
                 best = new
-    end, start = best[:2]
+    end, start = best[1:3]
     order = sorted(range(n), key=lambda i: (start[i], i))
     waits, last = [dict(e) for e in pre], {}
     for i in order:
@@ -658,12 +686,15 @@ def schedule(ops, pre, passes, seed):
     return order, waits, start, end
 
 
-OPT = {"ge": (("vv", "vv"), ("vv", "Vs"), ("vv", "Vs")), "rg": (0, 0), "ry": (0, 0), "gch": 2, "ych": 2, "lch": 2, "xch": 2, "xe": (("ss", "vs"),) * 3, "emh": "g", "jh": "g", "em": "s", "emu": "v", "vi": "v", "nu": "v", "jf": "g", "icv": "s", "lcv": "gs", "selv": 16,
-       "split": (1, 1, 0), "zx": (("V" * 12 + "S" * 4,) * 2, ("g" * 12 + "v" * 4, "g" * 16), ("g" * 12 + "v" * 4, "g" * 16))}
+HALVES = ((0, 64), (64, 128))
+OPT = {"turns": ((), (), ("vI@2 vL@1",)), "ge": (("64v 64v", "64v 64s"), ("64v 64v", "64V 64s"), ("64v 64v", "64V 64s")), "gk": (HALVES, HALVES), "rg": (0, 0),
+       "xe": (("64s 64s", "96v 32s"),) * 3, "le": (("64s 64s", "64s 64s"),) * 3, "yk": (HALVES, ((0, 64), (64, 96), (96, 128))), "ry": (0, 0),
+       "emu": "s", "emh": "g", "eu": "v", "jh": "g", "jf": "g", "nu": "v", "sign": "s", "nrx": "v", "qt": "gss", "ui": "vss", "oeu": "g", "fold": ((1, 1), (1, 1), (1, 1)), "ju16": "v", "lo16": "ggv", "icv": "s", "lcv": "gs",
+       "split": (1, 1, 0), "apart": (0, 0, 1), "zx": (("V" * 12 + "S" * 4,) * 2, ("g" * 12 + "v" * 4, "g" * 16), ("g" * 12 + "v" * 4, "g" * 16))}
 PLAN = {}
 
 
-def plan(opt, passes=4000, seed=0):
+def plan(opt, passes=12000, seed=0):
     ops = build(opt)
     pre = edges(ops)
     order, waits, start, end = schedule(ops, pre, passes, seed)
@@ -677,7 +708,7 @@ def helper(core, T, topo):
 def spare(core, T, topo):
     near = topo.engines(core, helper(core, T, topo))
     far = topo.engines(core, T.cores[(T.rank_of(core) + 1) % len(T.cores)])
-    use = [e for e in near if e not in far] or near
+    use = near
     return sum(1 << e for e in use), len(use)
 
 
@@ -711,10 +742,10 @@ def rank_program(g, core, T, topo):
         if isinstance(r, IndOp):
             return ap(r[0]).indirect(ap(r[1]))
         name, off = PLACE[r[0]]
-        a, b, st, p = r[1] + off, r[2] + off, r[3], r[4]
+        a, b, st, p, p0 = r[1] + off, r[2] + off, r[3], r[4], r[5]
         if st == 1:
-            return T[name][:, a:b] if p == 128 else T[name][0:p, a:b]
-        return T[name][:, a:b:st] if p == 128 else T[name][0:p, a:b:st]
+            return T[name][:, a:b] if p - p0 == 128 else T[name][p0:p, a:b]
+        return T[name][:, a:b:st] if p - p0 == 128 else T[name][p0:p, a:b:st]
 
     def arg(x):
         return ap(x) if isinstance(x, tuple) else x
@@ -722,7 +753,7 @@ def rank_program(g, core, T, topo):
     place = {i: k for k, i in enumerate(PLAN["order"])}
     for i in PLAN["order"]:
         o = ops[i]
-        q, eng = o["q"], queue[o["q"]]
+        q, eng, k = o["q"], queue[o["q"]], o["kind"]
         known = seen[q]
         for j in sorted(pre[i], key=lambda j: -place[j]):
             if not pre[i][j]:
@@ -730,10 +761,10 @@ def rank_program(g, core, T, topo):
             sem, val, kn = done[j]
             if known.get(sem, 0) < val:
                 eng.wait_ge(T.sem[sem], val)
-                for k in kn:
-                    known[k] = max(known.get(k, 0), kn[k])
+                for s in kn:
+                    known[s] = max(known.get(s, 0), kn[s])
                 known[sem] = max(known.get(sem, 0), val)
-        if o["kind"] == "dma":
+        if k == "dma":
             out, in_ = o["calls"][0]
             out = ap(out) if isinstance(out, tuple) else T[out][:]
             in_ = ap(in_) if isinstance(in_, tuple) else T[in_][:]
@@ -741,7 +772,7 @@ def rank_program(g, core, T, topo):
             done[i] = (o["sem"], 16, dict(known))
             count[o["sem"]] = 16
             continue
-        if o["kind"] == "remote":
+        if k == "remote":
             t, a, b, sem = o["calls"][0]
             step = 1 if t < 2 else 2
             dst, src = T.cores[(rank + step) % n], T.cores[(rank - step) % n]
@@ -750,21 +781,20 @@ def rank_program(g, core, T, topo):
             count["loc"] = count.get("loc", 0) + len(topo.engines(core, dst))
             done[i] = (sem, len(topo.engines(src, core)), {})
             continue
-        if o["kind"] == "fold":
-            out, a, b, k = o["calls"][0]
+        if k == "fold":
+            out, a, b, f = o["calls"][0]
             relay = helper(core, T, topo)
             rid, pid, _e = topo.addr(relay)
             mask, m = spare(core, T, topo)
-            g.remote_dma_fused([RemoteDMATransfer(dst_ids=[DstId(rid=rid, pnc=pid)], dma_engine_mask=mask, remote_sem=T.sem["fa%d" % k],
+            g.remote_dma_fused([RemoteDMATransfer(dst_ids=[DstId(rid=rid, pnc=pid)], dma_engine_mask=mask, remote_sem=T.sem["fa%d" % f],
                                                   srcs=[ap(a), ap(b)], dsts=[ap(out)], alu_op=2)], local_sem=T.sem["loc"])
             count["loc"] = count.get("loc", 0) + m
-            done[i] = ("fb%d" % k, len(topo.engines(relay, core)), dict(known))
+            done[i] = ("fb%d" % f, len(topo.engines(relay, core)), dict(known))
             continue
         sem = qsem[q]
         for c in o["calls"]:
-            k = o["kind"]
             if k == "matmul":
-                ins = g.tensor.matmul(ap(c[0]), ap(c[1]), ap(c[2]), c[3], c[4])
+                ins = g.tensor.matmul(ap(c[0]), ap(c[1]), ap(c[2]), bool(c[3]), bool(c[4]))
             elif k == "activation":
                 kw = {}
                 if c[3] is not None:
@@ -778,7 +808,7 @@ def rank_program(g, core, T, topo):
                 else:
                     ins = g.iota(ap(c[0]), c[1], c[2], c[3], allow_small_or_imprecise_dtypes=True)
             elif k == "select":
-                ins = g.affine_select(ap(c[0]), ap(c[1]), [[0, width(c[0])]], A.is_ge, 0.0, 0, 0)
+                ins = g.affine_select(ap(c[0]), ap(c[1]), c[2], A.is_equal, 0.0, c[3], c[4])
             else:
                 x = [arg(y) for y in c]
                 if k == "tensor_copy":

@@ -5,7 +5,7 @@ from concourse.mybir import AluOpType as A, AxisListType, ActivationFunctionType
 
 BIG = 1.0e9
 CYC, GAT, SCA, WAKE, FIX, SFIX, TCYC = 0.8333, 1.56, 3.8, 130.0, 20.0, 80.0, 0.5
-DLAT, DRATE, RLAT, FLAT, RCOST = 1600.0, 200.0, 3800.0, 9500.0, 500.0
+DLAT, DRATE, RLAT, FLAT0, FLAT1, RCOST = 1600.0, 200.0, 3800.0, 3500.0, 3.0, 500.0
 SCRATCH = {}
 TWO = ("bfloat16", "float16", "uint16")
 SEG = (0, 16, 48, 96)
@@ -36,13 +36,13 @@ for _n, _c, _d in (
         ("emu", 256, _U), ("emh", 256, _H), ("Nc", 1, _F), ("Nb", 1, _F), ("zx0", 4096, _B), ("zx1", 4096, _B), ("zT", 256, _B),
         ("eu", 16, _U), ("Jf", 256, _F), ("Jh", 256, _H), ("Y", 256, _H), ("AdE", 640, _B), ("msE", 640, _B), ("aE", 16, _F),
         ("tE", 16, _F), ("oE", 16, _F), ("oEu", 16, _U), ("dz", 256, _B), ("tg", 256, _B), ("le", 256, _B), ("cs", 256, _B),
-        ("nrx", 256, _H), ("sm", 256, _F), ("si", 16, _I), ("SJ", 32, _I), ("QT", 64, _H), ("RL", 256, _H), ("WT", 512, _H),
+        ("nrx", 256, _H), ("sm", 256, _I), ("SJ", 32, _I), ("QT", 64, _H), ("RL", 256, _H), ("WT", 512, _H),
         ("AdJ", 640, _B), ("msJ", 640, _B), ("aJ", 24, _F), ("tJ", 32, _F), ("oJ", 16, _F), ("oJu", 16, _U), ("Ju16", 16, _U),
         ("fT", 256, _H), ("ch", 256, _F), ("tmp", 256, _F), ("Lold", 256, _F), ("Lo16", 256, _H), ("mk", 256, _F), ("t2", 256, _F)):
     _buf(_n, _c, _d)
 for _h in "01":
     for _n, _c, _d in (("DG", 2048, _B), ("AG", 2048, _B), ("x", 2064, _B), ("Lg", 2048, _H), ("mx", 2048, _B), ("Dy", 2048, _B),
-                       ("Ay", 2048, _B), ("km", 128, _F), ("ei", 8, _I), ("ej", 8, _I), ("ME", 128, _H), ("Ju", 128, _U), ("nu", 128, _U),
+                       ("Ay", 2048, _B), ("km", 128, _I), ("ej", 8, _I), ("ME", 128, _H), ("Ju", 128, _U), ("nu", 128, _U),
                        ("M0", 2048, _B), ("M1", 2048, _B), ("M2", 2048, _B)):
         _buf(_n + "_" + _h, _c, _d)
 for _b in range(8):
@@ -63,7 +63,7 @@ for _n in list(SCRATCH):
         del SCRATCH[_n]
 for _d in _pack:
     _buf("k_" + _d, _pack[_d], _d)
-SEMAPHORES = ["qv", "qs", "qt", "qg", "loc"] + [s + str(i) for s in ("arr", "fa", "fb") for i in range(6)] + ["d%d" % i for i in range(14)]
+SEMAPHORES = ["qv", "qs", "qt", "qg", "loc"] + ["arr%d" % i for i in range(6)] + [s + str(i) for s in ("fa", "fb") for i in range(18)] + ["d%d" % i for i in range(14)]
 
 
 def R(buf, a=0, b=None, step=1, p=128, p0=0):
@@ -297,13 +297,19 @@ def build(opt):
         else:
             S(out, in_, F.Abs)
 
-    def keys(relu, K, n, m, d, a, con, payload, cuts):
-        def sums(src, by, lo, hi, last):
-            P([(R(K, k, n, 16, hi, lo), R(src, 16 * lo + k, 16 * hi, 16), R(by, 0, n // 16), False, last and k == m - 1) for k in range(m)])
+    def fold(out, a, b):
+        add("g", "fold", [(out, a, b, sum(o["kind"] == "fold" for o in ops))], [a, b], [out], RCOST, FLAT0 + FLAT1 * width(out))
+
+    def keys(relu, K, n, m, d, a, con, payload, cuts, nxt=None):
+        def sums(src, by, lo, hi, last, shift=0):
+            P([(R(K, k, n, 16, hi, lo), R(src, 16 * lo + k + shift, 16 * hi + shift, 16), R(by, 0, n // 16), False, last and k == m - 1) for k in range(m)])
         pay = (R(K, 0, 128), payload, I16, False, relu)
         P([(R(K, 0, n), R("ON64", 0, 128), R(con, 0, n), True, False)] + ([] if relu else [pay]))
+        for lo, hi in cuts if relu == 2 else ():
+            sums(nxt, "BKn", lo, hi, False, 1)
+            sums(d, "BKn", lo, hi, False)
         for lo, hi in cuts:
-            if relu:
+            if relu == 1:
                 sums(d, "BKn", lo, hi, False)
             sums(a, "BK2" if relu else "BLK", lo, hi, not relu)
         if relu:
@@ -389,8 +395,7 @@ def build(opt):
                         S(R("AG" + H, c, c + 512), o, F.Abs)
             keys(opt["rg"][h], K, 128, 16, "DG" + H, "AG" + H, "CD", R("emh", 128 * h, 128 * h + 128), opt["gk"][h])
             V(scan, R("km" + H, 0, 128), R("MMIN", 0, 128), R(K, 0, 128), 0.0, A.add, A.min)
-            V(tc, R("ei" + H, 0, 8), R("km" + H, 15, 128, 16))
-            V(ts, R("ej" + H, 0, 8), R("ei" + H, 0, 8), 1023, None, A.bitwise_and)
+            V(ts, R("ej" + H, 0, 8), R("km" + H, 15, 128, 16), 1023, None, A.bitwise_and)
             V(tt, R("ME" + H, 0, 128), ind(R("ej" + H, 0, 8), R("OFFR", 0, 8)), R("MK", 0, 128), A.mult)
             group([(R("b7", 8 * h, 8 * h + 8), R("ME" + H, 0, 128), R("Q16", 0, 8))])
             C(opt["eu"], R("eu", 8 * h, 8 * h + 8), R("b7", 8 * h, 8 * h + 8))
@@ -407,9 +412,13 @@ def build(opt):
                 group([(o, R("SEL", 128 * k, 128 * k + 128), R("Lg" + H, 16 * a + k, 16 * b, 16)) for k in range(16)])
                 C(opt["nu"], R("nu" + H, a, b), o)
             for a, b in opt["yk"][h]:
-                d = R("Dy" + H, 16 * a, 16 * b)
-                V(tt, d, ind(R("xb", 0, 2048), R("nu" + H, a, b)), R("x" + H, 16 * a + 1, 16 * b + 1), A.subtract)
-                size(opt["ry"][h], R("Ay" + H, 16 * a, 16 * b), d)
+                d, got, nxt = R("Dy" + H, 16 * a, 16 * b), ind(R("xb", 0, 2048), R("nu" + H, a, b)), R("x" + H, 16 * a + 1, 16 * b + 1)
+                if opt["ry"][h] == 2:
+                    C("v", d, got)
+                    fold(R("Ay" + H, 16 * a, 16 * b), d, nxt)
+                else:
+                    V(tt, d, got, nxt, A.subtract)
+                    size(opt["ry"][h], R("Ay" + H, 16 * a, 16 * b), d)
             V(scan, R("mx" + H, 0, 2048), R("MR", 0, 2048), R("x" + H, 0, 2048), 0.0, A.mult, A.max)
             o = R("b%d" % (4 + h), 320, 448)
             group([(o, IB, R(z, 128 * h, 128 * h + 128)), (o, IB, R("mx" + H, 15, 2048, 16))])
@@ -436,7 +445,7 @@ def build(opt):
         for h in (0, 1):
             H, K = "_%d" % h, "b%d" % (2 + h)
             l = (128 * h, 128 * h + 128)
-            keys(opt["ry"][h], K, 256, 15, "Dy" + H, "Ay" + H, "CS", R("Jh", *l), opt["yk"][h])
+            keys(opt["ry"][h], K, 256, 15, "Dy" + H, "Ay" + H, "CS", R("Jh", *l), opt["sk"][h], "x" + H)
             if opt["sign"] == "s":
                 S(R("le", *l), R(K, 128, 256), F.Sign)
             else:
@@ -463,7 +472,9 @@ def build(opt):
         for h in (0, 1):
             X, M, Z = R("x_%d" % h, 0, 2048), R("M%d_%d" % (t, h), 0, 2048), R(zx, 2048 * h, 2048 * h + 2048)
             if h in folded:
-                add("g", "fold", [(M, X, Z, 2 * t + h)], [X, Z], [M], RCOST, FLAT)
+                w = 2048 // opt["fold"][t][h]
+                for c in range(0, 2048, w):
+                    fold(R(M[0], c, c + w), R(X[0], c, c + w), R(zx, 2048 * h + c, 2048 * h + c + w))
                 continue
             for c in range(0, 2048, 512):
                 o = R("b0", 0, 512)
@@ -477,17 +488,17 @@ def build(opt):
         for h in (0, 1):
             o = R("b1", 256 + 128 * h, 384 + 128 * h)
             group([(o, R("fT", 128 * h, 128 * h + 128), I16), (o, R("nrx", 128 * h, 128 * h + 128), I4n)])
-        V(ts, R("ch", 0, 256), R("b1", 256, 512), 2048.0, R("tf", 1, 2), A.add, A.is_gt)
-        V(tt, R("tmp", 0, 256), R("ch", 0, 256), VJ, A.mult)
+        for a, b in ((0, 128), (128, 256)) if opt["apart"][t] else ((0, 256),):
+            V(ts, R("ch", a, b), R("b1", 256 + a, 256 + b), 2048.0, R("tf", 1, 2), A.add, A.is_gt)
+            V(tt, R("tmp", a, b), R("ch", a, b), R("b2", 256 + a, 256 + b), A.mult)
         scatter("I", 1088, "oEu", "tmp", "Jf")
         if t == 2:
             dma("y", "yi", R("I", 0, 1024), 4096, "d8")
         for h0, h1 in ((0, 1), (1, 2)) if opt["apart"][t] else ((0, 2),):
             n, a, b, w = 8 * (h1 - h0), 128 * h0, 128 * h1, 256 * h0
             C(opt["qt"][0], R("QT", 32 * h0 + 1, 32 * h1, 4), R("nrx", a, b, 16))
-            C(opt["qt"][1], R("si", 8 * h0, 8 * h1), R("sm", a + 15, b, 16))
-            V(ts, R("SJ", 16 * h0, 16 * h1, 2), R("si", 8 * h0, 8 * h1), 2047, None, A.bitwise_and)
-            V(ts, R("SJ", 16 * h0 + 1, 16 * h1, 2), R("si", 8 * h0, 8 * h1), 11, 15, A.arith_shift_right, A.bitwise_and)
+            V(ts, R("SJ", 16 * h0, 16 * h1, 2), R("sm", a + 15, b, 16), 2047, None, A.bitwise_and)
+            V(ts, R("SJ", 16 * h0 + 1, 16 * h1, 2), R("sm", a + 15, b, 16), 11, 15, A.arith_shift_right, A.bitwise_and)
             C(opt["qt"][2], R("QT", 32 * h0, 32 * h1, 2), R("SJ", 16 * h0, 16 * h1))
             P([(R("b7", 256 + 128 * h, 384 + 128 * h, 1, 32), R("QT", 32 * h, 32 * h + 32), I16, True, True) for h in range(h0, h1)])
             RL = R("RL", a, b, 1, 32)
@@ -545,7 +556,8 @@ def edges(ops):
     where = {(o["t"], o["name"]): o["i"] for o in ops}
     for t in range(3):
         for turn in ops[0]["turns"][t]:
-            got = [where[t, w] for w in turn.split() if (t, w) in where]
+            got = [(t - w.count("<"), w.strip("<")) for w in turn.split()]
+            got = [where[w] for w in got if w in where]
             for j, i in zip(got, got[1:]):
                 pre[i].setdefault(j, False)
     return pre
@@ -686,15 +698,141 @@ def schedule(ops, pre, passes, seed):
     return order, waits, start, end
 
 
+def fit(seq, lags, uses, tail=None, limit=None, old=None):
+    n, k0 = len(seq), 0
+    if old:
+        while k0 < n and seq[k0] == old[0][k0]:
+            k0 += 1
+        k0 = min(k0, n - 1) // 32 * 32
+        start, marks = list(old[1]), old[2][:k0 // 32]
+        busy = [list(x) for x in old[2][k0 // 32]]
+    else:
+        start, marks, busy = [0.0] * n, [], [[] for _ in range(16)]
+    for k in range(k0, n):
+        if k % 32 == 0:
+            marks.append([list(x) for x in busy])
+        i, s = seq[k], 0.0
+        for j, d in lags[i]:
+            if start[j] + d > s:
+                s = start[j] + d
+        moved = True
+        while moved:
+            moved = False
+            for res, off, m, who in uses[i]:
+                taken = busy[res]
+                if taken and taken[-1][1] > s + off:
+                    for a, b, other in taken[max(0, before(taken, s + off) - 2):]:
+                        if a >= s + off + m - 1e-6:
+                            break
+                        if s + off < b - 1e-6 and who != other:
+                            s, moved = b - off, len(uses[i]) > 1
+        if limit and s + tail[i] > limit:
+            return None
+        start[i] = s
+        for res, off, m, who in uses[i]:
+            taken = busy[res]
+            if not taken or taken[-1][0] <= s + off:
+                taken.append((s + off, s + off + m, who))
+            else:
+                taken.insert(before(taken, s + off), (s + off, s + off + m, who))
+    return seq, start, marks
+
+
+def schedule(ops, pre, passes, seed, heat=100.0):
+    n = len(ops)
+    span = [o["cost"] + o["lat"] for o in ops]
+    banks = [sorted(set(bank(r) for r in o["reads"] + o["writes"] if bank(r))) for o in ops]
+    lag = [{j: (span[j] + WAKE if w else ops[j]["cost"]) for j, w in pre[i].items()} for i in range(n)]
+    fwd = [[(j, d) for j, d in lag[i].items() if not any(lag[k].get(j, -1e9) + e >= d for k, e in lag[i].items())] for i in range(n)]
+    bwd = [[] for _ in range(n)]
+    for i in range(n):
+        for j, d in fwd[i]:
+            bwd[j].append((i, d - span[j] + span[i]))
+    ahead, back = [], []
+    for i, o in enumerate(ops):
+        u = [(8 + "vstgy".index(o["q"]), 0.0, o["cost"], i)] + [(int(b[1]), 0.0, o["cost"] + WAKE, o["q"]) for b in banks[i]]
+        if o.get("hold"):
+            u.append((13, o["cost"] + DLAT, o["hold"], i))
+        ahead.append(u)
+        back.append([(res, span[i] - off - m, m, who) for res, off, m, who in u])
+
+    def mend(key, lags, way):
+        for i in way:
+            for j, d in lags[i]:
+                if key[j] >= key[i]:
+                    key[i] = key[j] + 1e-3
+        return key
+
+    def early(key, limit=None, old=None):
+        got = fit(sorted(range(n), key=lambda i: key[i]), fwd, ahead, tail, limit, old)
+        if got:
+            end = max(s + w for s, w in zip(got[1], span))
+            return end + 0.3 * sum(got[1][i] for i in long) / len(long), end, got, key
+
+    def late(start):
+        key = mend([-start[i] - span[i] for i in range(n)], bwd, seq[::-1])
+        s = fit(sorted(range(n), key=lambda i: key[i]), bwd, back)[1]
+        return mend([-s[i] - span[i] for i in range(n)], fwd, seq)
+
+    def move(key, i, by):
+        todo, sign, lags = [(i, key[i] + by)], (1 if by > 0 else -1), (bwd if by > 0 else fwd)
+        while todo:
+            i, at = todo.pop()
+            if sign * key[i] < sign * at:
+                key[i] = at
+                todo += [(j, at + sign * 1e-2) for j, d in lags[i]]
+
+    seq = sequence(pre)
+    long = [i for i in range(n) if ops[i]["cost"] > 800 and ops[i]["q"] in "vs"]
+    alike = {}
+    for o in ops:
+        alike.setdefault(o["name"], []).append(o["i"])
+    tail = [0.0] * n
+    for i in seq[::-1]:
+        tail[i] = max([span[i]] + [tail[k] + d + span[i] - span[k] for k, d in bwd[i]])
+    dice = np.random.default_rng(seed).random((passes, 3, 7)).tolist()
+    now = best = early(late(early(mend([-x for x in tail], fwd, seq))[2][1]))
+    for k, d in enumerate(dice):
+        if d[0][0] < 0.03:
+            key = late(now[2][1])
+        else:
+            key = list(now[3]) if d[0][1] < 0.8 else mend(list(now[2][1]), fwd, seq)
+            for a in d[:(1, 1, 2, 3)[int(4 * d[1][0])]]:
+                i = long[int(a[2] * len(long))] if a[3] < 0.3 else int(a[2] * n)
+                for j in alike[ops[i]["name"]] if a[4] < 0.3 else [i]:
+                    move(key, j, (600, 2000, 6000)[int(3 * a[5])] * (2 * a[6] - 1) * abs(2 * a[6] - 1))
+        more = -(5 + heat * (1 - k / passes)) * math.log(d[2][0])
+        new = early(key, now[1] + more + 300, now[2])
+        if new and new[0] < now[0] + more:
+            now = new
+            if new[1] < best[1]:
+                best = new
+    end, start = best[1], best[2][1]
+    order = sorted(range(n), key=lambda i: (start[i], i))
+    waits, last = [dict(e) for e in pre], {}
+    for i in order:
+        for b in banks[i]:
+            for q, j in last.setdefault(b, {}).items():
+                if q != ops[i]["q"]:
+                    waits[i][j] = True
+            last[b][ops[i]["q"]] = i
+    return order, waits, start, end
+
+
 HALVES = ((0, 64), (64, 128))
-OPT = {"turns": ((), (), ("vI@2 vL@1",)), "ge": (("64v 64v", "64v 64s"), ("64v 64v", "64V 64s"), ("64v 64v", "64V 64s")), "gk": (HALVES, HALVES), "rg": (0, 0),
-       "xe": (("64s 64s", "96v 32s"),) * 3, "le": (("64s 64s", "64s 64s"),) * 3, "yk": (HALVES, ((0, 64), (64, 96), (96, 128))), "ry": (0, 0),
-       "emu": "s", "emh": "g", "eu": "v", "jh": "g", "jf": "g", "nu": "v", "sign": "s", "nrx": "v", "qt": "gss", "ui": "vss", "oeu": "g", "fold": ((1, 1), (1, 1), (1, 1)), "ju16": "v", "lo16": "ggv", "icv": "s", "lcv": "gs",
-       "split": (1, 1, 0), "apart": (0, 0, 1), "zx": (("V" * 12 + "S" * 4,) * 2, ("g" * 12 + "v" * 4, "g" * 16), ("g" * 12 + "v" * 4, "g" * 16))}
+WHOLE = ((0, 128),)
+S_TURN = "sAG_1@1536 sx_0@0 sx_0@1024 sLg_0@0 sLg_0@1024 sLg_1@0 sLg_1@1024 sAy_0@0 sAy_0@1024 sAy_1@0 sAy_1@1024 sAy_1@1536"
+V_TURN = "vDG_0@0 vDG_0@1024 vJu_0@0 vJu_1@0 vx_1@0 vDy_0@0 vDy_0@1024 vDy_1@0 vDy_1@1024 vDy_1@1536"
+OPT = {"turns": ((V_TURN,), (S_TURN, V_TURN), (S_TURN, V_TURN, "vI@2 vL@1")),
+       "ge": (("64v 64v", "64s 64v"), ("64v 64v", "64s 64s"), ("64v 64v", "64s 64s")), "gk": (WHOLE, WHOLE), "rg": (1, 0),
+       "xe": (("64s 64s", "64v 64v"),) * 3, "le": (("64s 64s", "64s 64s"),) * 3, "yk": (HALVES, ((0, 64), (64, 96), (96, 128))), "ry": (0, 0),
+       "sk": (WHOLE, ((0, 96), (96, 128))),
+       "emu": "s", "emh": "g", "eu": "v", "jh": "g", "jf": "g", "nu": "v", "sign": "s", "nrx": "s", "qt": "gss", "ui": "vss", "oeu": "g", "fold": ((1, 1), (1, 1), (1, 2)), "ju16": "v", "lo16": "ggv", "icv": "s", "lcv": "gs",
+       "split": (1, 1, 0), "apart": (0, 0, 1), "zx": (("V" * 12 + "S" * 4,) * 2, ("g" * 13 + "v" * 3, "g" * 16), ("g" * 13 + "v" * 3, "g" * 16))}
 PLAN = {}
 
 
-def plan(opt, passes=12000, seed=0):
+def plan(opt, passes=28000, seed=2):
     ops = build(opt)
     pre = edges(ops)
     order, waits, start, end = schedule(ops, pre, passes, seed)
@@ -717,7 +855,7 @@ def hand_back(g, core, owner, T, topo):
     folds = [PLAN["ops"][i]["calls"][0] for i in PLAN["order"] if PLAN["ops"][i]["kind"] == "fold"]
     for out, a, b, k in folds:
         g.wait_ge(T.sem["fa%d" % k], spare(owner, T, topo)[1])
-        g.remote_dma(T[out[0]][:], T[out[0]][:], T.sem["fb%d" % k], T.sem["loc"], pid, rid, topo.mask(core, owner))
+        g.remote_dma(T[out[0]][:, out[1]:out[2]], T[out[0]][:, out[1]:out[2]], T.sem["fb%d" % k], T.sem["loc"], pid, rid, topo.mask(core, owner))
     g.wait_ge(T.sem["loc"], len(folds) * len(topo.engines(core, owner)))
 
 

@@ -1,7 +1,7 @@
 import math
 import numpy as np
 from concourse.bass import DstId, RemoteDMATransfer
-from concourse.mybir import AluOpType as A, AxisListType, ActivationFunctionType as F
+from concourse.mybir import AluOpType as A, ActivationFunctionType as F
 
 BIG = 1.0e9
 CYC, GAT, SCA, WAKE, FIX, SFIX, TCYC = 0.8333, 1.56, 3.8, 130.0, 20.0, 80.0, 0.5
@@ -25,20 +25,22 @@ for _n, _c, _d in (
         ("k15", 1, _F), ("wf", 1, _F), ("hI", 4, _I), ("hf", 4, _F), ("tf", 2, _F), ("q2i", 1, _I), ("bI", 1, _I), ("pk1", 1, _F),
         ("pk2", 1, _F), ("pk4", 1, _F), ("m15", 1, _F), ("acol", 1, _F), ("dI", 144, _B), ("gI", 128, _B), ("g8I", 16, _I),
         ("rI", 128, _B), ("dg4", 128, _B), ("duI", 16, _I), ("r15I", 128, _B), ("slI", 16, _B), ("qrel", 160, _B), ("dcol", 160, _B),
-        ("SM", 320, _B), ("IW", 136, _H), ("IB", 136, _B), ("In", 128, _H), ("I1n", 128, _H), ("I4n", 128, _H), ("Ih", 128, _H), ("Ic", 128, _H), ("BHn", 128, _H),
-        ("BBn", 128, _B), ("BLK", 16, _B), ("BKn", 16, _B), ("BK2", 16, _B), ("BL1", 8, _B), ("BL2", 8, _B), ("Q16", 8, _H),
-        ("MK", 128, _H), ("SEL", 2048, _H), ("EN", 2048, _B), ("MR", 2048, _B), ("CD", 128, _H), ("CS", 256, _H), ("ON64", 128, _H),
-        ("ONn", 128, _H), ("ONk", 128, _H), ("MMIN", 128, _F), ("MMAX", 128, _F), ("OFFR", 8, _U), ("OF15", 8, _U), ("PK", 4, _U), ("DUE", 16, _F),
-        ("DUn", 16, _H), ("RPc", 128, _H), ("RPJ", 128, _H), ("RPt", 128, _H), ("RPK", 128, _H), ("SLW", 16, _H), ("E2", 320, _H),
-        ("EC", 640, _H), ("TR", 320, _H), ("dg0", 128, _H), ("dg1", 128, _H), ("dg2", 128, _H), ("dg3", 128, _H), ("W8", 8, _B),
-        ("ZQ", 528, _H), ("PM_0", 128, _H), ("PM_1", 128, _H), ("PQ_0", 128, _H), ("PQ_1", 128, _H),
+        ("SM", 320, _B), ("IW", 136, _H), ("IB", 136, _B), ("In", 128, _H), ("I1n", 128, _H), ("I2n", 128, _H), ("Ih", 128, _H),
+        ("Ic", 128, _H), ("BHn", 128, _H), ("BBn", 128, _B), ("BLK", 16, _B), ("BKn", 16, _B), ("BK2", 16, _B), ("BL1", 8, _B),
+        ("BL2", 8, _B), ("Q16", 8, _H), ("MK", 128, _H), ("SEL", 2048, _H), ("EN", 2048, _B), ("MR", 2048, _B), ("CD", 128, _H),
+        ("CS", 256, _H), ("ON64", 128, _H), ("ONn", 128, _H), ("ONk", 128, _H), ("MMIN", 128, _F), ("MMAX", 128, _F), ("OFFR", 8, _U),
+        ("OF15", 8, _U), ("OFF2", 8, _U), ("PK", 4, _U), ("DUE", 16, _F), ("DUn", 16, _H), ("DUJ", 16, _F), ("RPJ", 128, _H),
+        ("TS", 320, _H), ("RPK", 128, _H), ("SLW", 16, _H), ("E2", 320, _H), ("EC", 640, _H), ("TR", 320, _H), ("dg0", 128, _H),
+        ("dg1", 128, _H), ("dg2", 128, _H), ("dg3", 128, _H), ("W8", 8, _B), ("ZQ", 528, _H), ("PM_0", 128, _H), ("PM_1", 128, _H),
+        ("PQ_0", 128, _H), ("PQ_1", 128, _H),
         ("ui", 16, _I), ("uu", 16, _I), ("UQ", 64, _I), ("UH", 66, _H), ("RLu", 128, _H), ("q1", 256, _H), ("q2", 256, _H),
-        ("emu", 256, _U), ("emh", 256, _H), ("Nc", 1, _F), ("Nb", 1, _F), ("zx0", 4096, _B), ("zx1", 4096, _B), ("zT", 256, _B),
-        ("eu", 16, _U), ("Jf", 256, _F), ("Jh", 256, _H), ("Y", 256, _H), ("AdE", 640, _B), ("msE", 640, _B), ("aE", 16, _F),
-        ("tE", 16, _F), ("oE", 16, _F), ("oEu", 16, _U), ("dz", 256, _B), ("tg", 256, _B), ("le", 256, _B), ("cs", 256, _B),
-        ("nrx", 256, _H), ("sm", 256, _I), ("SJ", 32, _I), ("QT", 64, _H), ("RL", 256, _H), ("WT", 512, _H),
-        ("AdJ", 640, _B), ("msJ", 640, _B), ("aJ", 24, _F), ("tJ", 32, _F), ("oJ", 16, _F), ("oJu", 16, _U), ("Ju16", 16, _U),
-        ("fT", 256, _H), ("ch", 256, _F), ("tmp", 256, _F), ("Lold", 256, _F), ("Lo16", 256, _H), ("mk", 256, _F), ("t2", 256, _F)):
+        ("emu", 256, _U), ("emh", 256, _H), ("Nc", 1, _F), ("Nb", 1, _F), ("Ncx", 9, _F), ("Nbx", 9, _F), ("zx0", 4096, _B),
+        ("zx1", 4096, _B), ("zT", 128, _B), ("eu", 16, _U), ("Jf", 256, _F), ("Jh", 256, _H), ("Y", 256, _H), ("AdE", 640, _B),
+        ("msE", 640, _B), ("aE", 16, _F), ("tE", 16, _F), ("oE", 16, _F), ("oEu", 16, _U), ("dz", 256, _B), ("tg", 256, _B),
+        ("le", 256, _B), ("cs", 256, _B), ("nrx", 256, _H), ("sm", 256, _I), ("SJ", 32, _I), ("QT", 64, _H), ("RL", 256, _H),
+        ("WT", 512, _H), ("AdJ", 640, _B), ("msJ", 640, _B), ("aJ", 24, _F), ("tJ", 32, _F), ("oJ", 16, _F), ("oJu", 16, _U),
+        ("Ju16", 16, _U), ("fT", 256, _H), ("ch", 256, _F), ("tmp", 256, _F), ("Lold", 256, _F), ("Lo16", 256, _H), ("mk", 256, _F),
+        ("t2", 256, _F)):
     _buf(_n, _c, _d)
 for _h in "01":
     for _n, _c, _d in (("DG", 2048, _B), ("AG", 2048, _B), ("x", 2064, _B), ("Lg", 2048, _H), ("mx", 2048, _B), ("Dy", 2048, _B),
@@ -63,7 +65,19 @@ for _n in list(SCRATCH):
         del SCRATCH[_n]
 for _d in _pack:
     _buf("k_" + _d, _pack[_d], _d)
-SEMAPHORES = ["qv", "qs", "qt", "qg", "loc"] + ["arr%d" % i for i in range(6)] + [s + str(i) for s in ("fa", "fb") for i in range(18)] + ["d%d" % i for i in range(14)]
+SEMAPHORES = (["qv", "qs", "qt", "qg", "loc"] + ["arr%d" % i for i in range(6)] + [s + str(i) for s in ("fa", "fb") for i in range(10)]
+              + ["d%d" % i for i in range(15)])
+
+LOADS = "<yz0@0 <yG@0 <yixi@0 <yxb@0 <ylki@0 <ylki@1024 <ylki@1536"
+S_TURN = ("sDG_1@0 sDG_1@1024 sAG_1@0 sAG_1@512 sAG_1@1024 sAG_1@1536 sx_0@0 sx_0@1024 sLg_0@0 sLg_0@1024 sLg_1@0 sLg_1@1024 "
+          "sAy_0@0 sAy_0@1024 sAy_1@0 sAy_1@1024 sAy_1@1536")
+V_TURN = "vDG_0@0 vDG_0@1024 vJu_0@0 vJu_1@0 vx_1@0 vDy_0@0 vDy_0@1024 vDy_1@0 vDy_1@1024 vDy_1@1536"
+Z_TURN = "vx_1@0 vmx_0@0 vx_1@1024 vmx_1@0 vDy_0@0"
+TURNS = ((LOADS, S_TURN, V_TURN, Z_TURN), (S_TURN, V_TURN, Z_TURN),
+         (S_TURN, V_TURN + " vmx_1@0", "vI@2 vL@1", "vzs2@0 vzs2@128 vI@3"))
+HALVES = ((0, 64), (64, 128))
+LAST = ((0, 64), (64, 96), (96, 128))
+FOLDS = ((1, 2), (1, 2), (2, 2))
 
 
 def R(buf, a=0, b=None, step=1, p=128, p0=0):
@@ -92,46 +106,38 @@ def ind(win, off):
     return IndOp((win, off))
 
 
-def build(opt):
+def build():
     ops, now = [], [-1]
 
     def add(q, kind, calls, reads, writes, cost, lat=0.0, **kw):
         r = (writes or reads)[0]
         ops.append(dict(q=q, kind=kind, calls=calls, reads=reads, writes=writes, cost=cost, lat=lat, i=len(ops), t=now[0],
-                        name="%s%s@%d" % (q, r[0], r[1]), turns=opt["turns"], **kw))
+                        name="%s%s@%d" % (q, r[0], r[1]), **kw))
 
     def flat(x):
         if isinstance(x, IndOp):
             return [x[0], x[1]]
         return [x] if isinstance(x, tuple) else []
 
-    def small(rs):
-        return all(DTYPE[r[0]] in TWO for r in rs)
-
-    def price(n, half=False, mult=1.0):
-        return max(64.0, n * (0.5 if half else 1.0) * mult) * CYC + FIX
-
     def V(name, out, *args):
         full = [x for x in args if isinstance(x, tuple)]
         rd = [y for x in full for y in flat(x)]
-        wr = flat(out)[:1]
         if isinstance(out, IndOp):
             rd = rd + [out[1]]
             c = 50 + width(out[1]) * 16 * SCA * CYC
         elif any(isinstance(x, IndOp) for x in full):
             c = 50 + width(out) * GAT * CYC
         elif name == "tensor_tensor":
-            c = price(width(out), False, 1.0 if any(bank(x) for x in full) else 2.0)
-        elif name == "tensor_reduce":
-            c = price(width(args[0]))
+            c = max(64.0, width(out) * (1.0 if any(bank(x) for x in full) else 2.0)) * CYC + FIX
         else:
-            c = price(width(out), small([out] + [x for x in full if width(x) > 1]))
-        add("v", name, [(out,) + args], rd, wr, c)
+            half = all(DTYPE[r[0]] in TWO for r in [out] + [x for x in full if width(x) > 1])
+            c = max(64.0, width(out) * (0.5 if half else 1.0)) * CYC + FIX
+        add("v", name, [(out,) + args], rd, flat(out)[:1], c)
 
-    def S(out, in_, func, bias=None, scale=None):
-        c = SFIX + width(out) * CYC * (GAT if isinstance(in_, IndOp) else 1.0)
+    def S(out, in_, func, bias=None, scale=None, total=None):
+        c = SFIX + width(out) * CYC * (GAT if isinstance(in_, IndOp) else 1.0) + (20 if total else 0)
         rd = flat(in_) + [x for x in (bias, scale) if isinstance(x, tuple)]
-        add("s", "activation", [(out, in_, func, bias, scale)], rd, [out], c)
+        add("s", "activation", [(out, in_, func, bias, scale, total)], rd, [out] + flat(total), c)
 
     def select(out, in_, pattern, base, cm):
         add("g", "select", [(out, in_, pattern, base, cm)], [in_], [out], 170 + 2 * width(out) * CYC)
@@ -165,7 +171,10 @@ def build(opt):
     def dma(q, out, in_, nbytes, sem):
         rd = [in_] if isinstance(in_, tuple) else []
         wr = [out] if isinstance(out, tuple) else []
-        add(q, "dma", [(out, in_)], rd, wr, 60, DLAT + nbytes * 128 / DRATE, sem=sem, nbytes=nbytes * 128, hold=nbytes * 128 / DRATE if nbytes > 32 else 0)
+        add(q, "dma", [(out, in_)], rd, wr, 60, DLAT + nbytes * 128 / DRATE, sem=sem, hold=nbytes * 128 / DRATE if nbytes > 32 else 0)
+
+    def fill(out, value):
+        S(out, R("ZQ", 400, 400 + width(out)), F.Copy, value)
 
     dma("y", R("z0", 0, 128), R("zc", 128, 256), 256, "d0")
     dma("s", R("z0", 128, 256), R("zc", 0, 128), 256, "d12")
@@ -176,7 +185,8 @@ def build(opt):
     dma("y", R("xb", 0, 2048), "xc", 4096, "d5")
     dma("s", R("thi", 0, 2), "th", 8, "d6")
     dma("y", R("lki", 0, 1024), R("lk", 0, 1024), 4096, "d7")
-    dma("y", R("lki", 1024, 2048), R("lk", 1024, 2048), 4096, "d11")
+    dma("y", R("lki", 1024, 1536), R("lk", 1024, 1536), 2048, "d11")
+    dma("y", R("lki", 1536, 2048), R("lk", 1536, 2048), 2048, "d14")
     iota(R("pI", 0, 1), [[0, 1]], 0, 1)
     iota(R("g8I", 0, 16), [[0, 2], [1, 8]], 0, 0)
     iota(R("dI", 0, 144), [[1, 144]], 0, -1)
@@ -192,13 +202,13 @@ def build(opt):
         iota(R("dcol", a, a + n), [[1, n]], -16 * q, 0)
         iota(R("SM", a, a + n), [[-1, n]], 1, 0)
     for a in range(0, 2048, 512):
-        iota(R("MR", a, a + 512), [[0, 512]], 1, 0)
+        V("memset", R("MR", a, a + 512), 1.0)
         select(R("SEL", a, a + 512), R("MR", a, a + 512), [[-256, 4], [-16, 8], [255, 16]], -2 * a, 1)
         select(R("EN", a, a + 512), R("MR", a, a + 512), [[1, 32], [0, 16]], a // 16, -1)
     c1 = lambda b: R(b, 0, 1)
     ts, tt, tc, scan = "tensor_scalar", "tensor_tensor", "tensor_copy", "tensor_tensor_scan"
     I16, IB, ISH = R("IW", 4, 132), R("IB", 4, 132), R("IW", 5, 133)
-    In, I1n, I4n = R("In", 0, 128), R("I1n", 0, 128), R("I4n", 0, 128)
+    In, I1n, I2n = R("In", 0, 128), R("I1n", 0, 128), R("I2n", 0, 128)
     V("memset", R("MR", 0, 2048, 16), 0.0)
     V(ts, c1("pgi"), c1("pI"), 4, None, A.arith_shift_right)
     V(tc, c1("pg"), c1("pgi"))
@@ -210,9 +220,9 @@ def build(opt):
     V("memset", R("ZQ", 0, 528), 0.0)
     V(ts, R("ZQ", 72, 80), R("g8I", 0, 8), c1("pg"), None, A.is_equal)
     V(ts, R("ZQ", 200, 208), R("g8I", 0, 8), c1("pg"), -0.0625, A.is_equal, A.mult)
-    V("memset", R("ZQ", 320, 321), 1088.0)
-    V("memset", R("ZQ", 392, 393), 2176.0)
-    V("memset", R("UH", 64, 66), 1024.0)
+    fill(R("ZQ", 320, 321), 1088.0)
+    fill(R("ZQ", 392, 393), 2176.0)
+    fill(R("UH", 64, 66), 1024.0)
     V(ts, R("BHn", 0, 128), R("gI", 0, 128), c1("pg"), -1.0, A.is_equal, A.mult)
     V(ts, c1("p16i"), c1("pI"), 15, None, A.bitwise_and)
     V(tc, c1("p16"), c1("p16i"))
@@ -225,12 +235,13 @@ def build(opt):
     V(tc, R("OFFR", 0, 8), R("g8I", 0, 8))
     V(ts, c1("colA"), c1("pf"), 64.0, 0.5, A.is_ge, A.mult)
     V(ts, c1("colB"), c1("pf"), 64.0, -4096.0, A.is_lt, A.mult)
-    V("memset", R("ON64", 0, 128), 64.0)
+    fill(R("ON64", 0, 128), 64.0)
     V(ts, R("CD", 0, 128), R("rI", 0, 128), c1("colA"), c1("colB"), A.mult, A.add)
     V(ts, R("MMIN", 0, 128), R("rI", 0, 128), 0.0, BIG, A.is_equal, A.mult)
-    amp = 1.0 if opt["nrx"] == "s" else 2.0
-    for name, by in ((In, -1.0), (I1n, -1024.0), (I4n, -2048.0 * amp), (R("Ih", 0, 128), 0.5 * amp), (R("Ic", 0, 128), 1.0 / 128)):
+    for name, by in ((In, -1.0), (I1n, -1024.0)):
         V(ts, name, R("dI", 0, 128), 0.0, by, A.is_equal, A.mult)
+    for name, by in ((I2n, -2048.0), (R("Ih", 0, 128), 0.5), (R("Ic", 0, 128), 1.0 / 128)):
+        S(name, I16, F.Copy, None, by)
 
     def factors(j, name, square, const):
         for i in (2 * j, 2 * j + 1):
@@ -243,21 +254,22 @@ def build(opt):
             S(R(name + str(h), 0, 128, 1, 65), o, F.Copy)
     factors(0, "PM_", 32, 320)
     factors(1, "PQ_", 16, 392)
-    C(opt["icv"], R("I", 0, 1024), R("ixi", 0, 1024))
-    for c in range(2):
-        C(opt["lcv"][c], R("L", 1024 * c, 1024 * c + 1024), R("lki", 1024 * c, 1024 * c + 1024))
+    C("s", R("I", 0, 1024), R("ixi", 0, 1024))
+    for e, a, b in (("g", 0, 1024), ("g", 1024, 1536), ("s", 1536, 2048)):
+        C(e, R("L", a, b), R("lki", a, b))
     V(ts, R("IB", 0, 136), R("dI", 0, 136), 4.0, None, A.is_equal)
     V(ts, R("BBn", 0, 128), R("gI", 0, 128), c1("pg"), -1.0, A.is_equal, A.mult)
-    V(ts, R("BL1", 0, 8), R("g8I", 0, 8), c1("pg"), -1.0, A.is_equal, A.mult)
-    V(ts, R("BL2", 0, 8), R("g8I", 0, 8), c1("pg"), 2.0, A.is_equal, A.mult)
-    V("memset", R("x_0", 2048, 2064), 0.0)
-    V("memset", R("x_1", 2048, 2064), 0.0)
+    S(R("BL1", 0, 8), R("BLK", 8, 16), F.Copy, None, -1.0)
+    S(R("BL2", 0, 8), R("BLK", 8, 16), F.Copy, None, 2.0)
+    fill(R("x_0", 2048, 2064), 0.0)
+    fill(R("x_1", 2048, 2064), 0.0)
     V(ts, R("CS", 0, 128), R("r15I", 0, 128), c1("colA"), c1("colB"), A.mult, A.add)
     V(ts, R("MMAX", 0, 128), R("rI", 0, 128), 0.0, -BIG, A.is_equal, A.mult)
     V(tc, R("tf", 0, 2), R("thi", 0, 2))
-    V("memset", R("ONn", 0, 128), -0.5 * amp)
-    V("memset", R("ONk", 0, 128), -0.5 * amp / 1024)
-    V("memset", R("b0", 32, 33), -0.5 + 2.0 ** -12)
+    DOWN = -0.5 + 2.0 ** -12
+    fill(R("ONn", 0, 128), -0.5)
+    fill(R("ONk", 0, 128), -0.5 / 1024)
+    fill(R("b0", 32, 33), DOWN)
     V(ts, c1("m15"), c1("p16"), 15.0, -1.0 / 64, A.is_lt, A.mult)
     V(ts, c1("acol"), c1("tf"), 1.5, c1("m15"), A.add, A.mult)
     V(ts, c1("acol"), c1("acol"), 1.0 / 64, None, A.add)
@@ -271,60 +283,46 @@ def build(opt):
     V(ts, R("DUn", 0, 16), R("duI", 0, 16), c1("p16"), None, A.subtract)
     V(ts, R("DUE", 0, 16), R("DUn", 0, 16), -1.0, 1024.0, A.mult, A.add)
     V(ts, c1("k15"), c1("p16"), -1.0, 15.0, A.mult, A.add)
-    V(ts, R("RPc", 0, 128), R("dg4", 0, 128), -1.0, -2048.0 * amp, A.is_equal, A.mult)
-    V(ts, R("RPt", 0, 128), R("dg4", 0, 128), 0.0, -1.0, A.is_equal, A.mult)
-    V(tt, R("RPJ", 0, 128), R("RPt", 0, 128), R("RPc", 0, 128), A.subtract)
+    V(ts, R("DUJ", 0, 16), R("DUn", 0, 16), -1.0, 2048.0, A.mult, A.add)
+    V(ts, R("RPJ", 0, 128), R("dg4", 0, 128), 0.0, -1.0, A.is_equal, A.mult)
     V(ts, R("RPK", 0, 128), R("dg4", 0, 128), -2.0, None, A.is_equal)
     V(ts, R("SLW", 0, 16), R("slI", 0, 16), 0.0, None, A.is_equal)
     V(ts, R("OF15", 0, 8), R("g8I", 0, 8), 16.0, 15.0, A.mult, A.add)
     for b in range(2):
         V(ts, R("E2", 160 * b, 160 * b + 160), R("qrel", 0, 160), 4.0 * b, c1("pg"), A.add, A.is_equal)
         V(ts, R("TR", 160 * b, 160 * b + 160), R("dcol", 0, 160), c1("pf"), 16384.0, A.is_ge, A.mult)
+        V(ts, R("TS", 160 * b, 160 * b + 160), R("dcol", 0, 160), c1("pf"), -20480.0, A.is_equal, A.mult)
     for b in range(4):
         V(ts, R("EC", 160 * b, 160 * b + 160), R("qrel", 0, 160), 4.0 * b, c1("pf"), A.add, A.is_equal)
     V(tc, R("SM", 160, 320), R("SM", 0, 160))
-    V("memset", R("QT", 3, 64, 4), 0.0)
-    if any(opt["rg"] + opt["ry"]):
-        V(ts, R("BKn", 0, 16), R("BLK", 0, 16), -1.0, None, A.mult)
-        V(ts, R("BK2", 0, 16), R("BLK", 0, 16), 2.0, None, A.mult)
-    if any(opt["apart"]):
-        V(ts, R("PK", 2, 3), c1("pk4"), -1.0, 319.0, A.add, A.min)
-        V("memset", R("aJ", 16, 24), 0.0)
+    fill(R("QT", 1, 64, 2), 0.0)
+    S(R("BKn", 0, 16), R("BLK", 0, 16), F.Copy, None, -1.0)
+    S(R("BK2", 0, 16), R("BLK", 0, 16), F.Copy, None, 2.0)
+    V(ts, R("PK", 2, 3), c1("pk4"), -1.0, 319.0, A.add, A.min)
+    fill(R("aJ", 16, 24), 0.0)
+    V(ts, R("OFF2", 0, 8), R("g8I", 0, 8), 2.0, None, A.mult)
 
-    def size(relu, out, in_):
-        if relu:
-            V(ts, out, in_, 0.0, None, A.max)
-        else:
-            S(out, in_, F.Abs)
-
-    def fold(out, a, b):
-        add("g", "fold", [(out, a, b, sum(o["kind"] == "fold" for o in ops))], [a, b], [out], RCOST, FLAT0 + FLAT1 * width(out))
-
-    def keys(relu, K, n, m, d, a, con, payload, cuts, nxt=None):
-        def sums(src, by, lo, hi, last, shift=0):
-            P([(R(K, k, n, 16, hi, lo), R(src, 16 * lo + k + shift, 16 * hi + shift, 16), R(by, 0, n // 16), False, last and k == m - 1) for k in range(m)])
-        pay = (R(K, 0, 128), payload, I16, False, relu)
-        P([(R(K, 0, n), R("ON64", 0, 128), R(con, 0, n), True, False)] + ([] if relu else [pay]))
-        for lo, hi in cuts if relu == 2 else ():
-            sums(nxt, "BKn", lo, hi, False, 1)
-            sums(d, "BKn", lo, hi, False)
+    def keys(K, n, m, a, con, payload, cuts, d=None):
+        def sums(src, by, lo, hi, last):
+            P([(R(K, k, n, 16, hi, lo), R(src, 16 * lo + k, 16 * hi, 16), R(by, 0, n // 16), False, last and k == m - 1) for k in range(m)])
+        pay = (R(K, 0, 128), payload, I16, False, bool(d))
+        P([(R(K, 0, n), R("ON64", 0, 128), R(con, 0, n), True, False)] + ([] if d else [pay]))
         for lo, hi in cuts:
-            if relu == 1:
+            if d:
                 sums(d, "BKn", lo, hi, False)
-            sums(a, "BK2" if relu else "BLK", lo, hi, not relu)
-        if relu:
+            sums(a, "BK2" if d else "BLK", lo, hi, not d)
+        if d:
             P([pay])
 
-    def earlier(h, own, spread, pick, row, p, Ad, ms, bias):
+    def earlier(h, own, spread, pick, row, p, Ad, ms, links):
         D = "b%d" % (4 + h)
-        items = [(R(D, 0, 320), R("MK", 0, 128, 1, 16), R("TR", 0, 320, 1, 16), True, False)]
-        for b in (0, 1):
-            for q in range(4):
-                a, n, l = 160 * b + SEG[q], 16 * (q + 1), 128 * h + 64 * b
-                items.append((R(D, a, a + n), pick, R(row, l, l + n, 1, p), False, False))
-        P(items)
+        items = [(R(D, 0, 320), R("MK", 0, 128, 1, 16), R(c, 0, 320, 1, 16), c == "TR", False) for c in (("TR", "TS") if links else ("TR",))]
+        rows = [(160 * b + SEG[q], 16 * (q + 1), 64 * b) for b in (0, 1) for q in range(4)]
+        P(items + [(R(D, a, a + n), pick, R(row, 128 * h + l, 128 * h + l + n, 1, p), False, False) for a, n, l in rows])
+        if links:
+            P([(R(D, a, a + n), R("nrx", 128 * h, 128 * h + 128), R("I2n", l, l + n), False, False) for a, n, l in rows])
         P([(R(D, 0, 320), own, spread, False, True)])
-        S(R(Ad, 320 * h, 320 * h + 320), R(D, 0, 320), F.Abs, bias)
+        S(R(Ad, 320 * h, 320 * h + 320), R(D, 0, 320), F.Abs, 2048.0 if links else None)
         V(scan, R(ms, 320 * h, 320 * h + 320), R("SM", 0, 320), R(Ad, 320 * h, 320 * h + 320), 0.0, A.max, A.min)
 
     def scatter(table, n, off, a, b):
@@ -332,198 +330,167 @@ def build(opt):
             V(tt, ind(R(table, 0, n), R(off, 4 * k, 4 * k + 4)), R(a, 64 * k, 64 * k + 64), R(b, 64 * k, 64 * k + 64), A.add)
             ops[-1]["name"] = "v%s@%d" % (table, k)
 
-    def cuts(s):
-        out, lo = [], 0
-        for w in s.split():
-            out.append((lo, lo + int(w[:-1]), w[-1]))
-            lo = out[-1][1]
-        return out
-
-    DOWN = -0.5 + 2.0 ** -12
     RLu = R("RLu", 0, 128, 1, 65)
     for t in range(3):
         now[0] = t
-        z = "z%d" % t
-        zx = "zx%d" % (t % 2)
-        P([(R("b0", 8 * h, 8 * h + 8), R(z, 128 * h, 128 * h + 128), R("W8", 0, 8), True, True) for h in (0, 1)])
-        C(opt["ui"][t], R("ui", 0, 16), R("b0", 0, 16))
+        z, zx = "z%d" % t, "zx%d" % (t % 2)
+        half = lambda buf, h, at=0: R(buf, at + 128 * h, at + 128 * h + 128)
+        P([(R("b0", 8 * h, 8 * h + 8), half(z, h), R("W8", 0, 8), True, True) for h in (0, 1)])
+        C("s" if t else "v", R("ui", 0, 16), R("b0", 0, 16))
         V(ts, R("ui", 0, 16), R("ui", 0, 16), 4095, None, A.bitwise_and)
         V(tt, R("uu", 0, 16), R("ui", 0, 16), R("ui", 0, 16), A.mult)
         V(ts, R("UQ", 0, 16), R("ui", 0, 16), 2047, None, A.bitwise_and)
         V(ts, R("UQ", 48, 64), R("ui", 0, 16), 31, None, A.bitwise_and)
         V(ts, R("UQ", 16, 32), R("uu", 0, 16), 4, 2047, A.arith_shift_right, A.bitwise_and)
         V(ts, R("UQ", 32, 48), R("uu", 0, 16), 5, 1023, A.arith_shift_right, A.bitwise_and)
-        C(opt["ui"][t], R("UH", 0, 64), R("UQ", 0, 64))
+        C("s" if t else "v", R("UH", 0, 64), R("UQ", 0, 64))
         group([(R("b0", 128, 256, 1, 65), R("UH", 0, 65), I16)])
         S(RLu, R("b0", 128, 256, 1, 65), F.Copy)
-        P([(R("b0", 256 + 128 * h, 384 + 128 * h), R("PM_%d" % h, 0, 128, 1, 65), RLu, True, True) for h in (0, 1)])
-        if t == 0:
-            S(R("q1", 0, 256), R("b0", 256, 512), F.Copy, DOWN, 1.0 / 1024)
-        else:
-            S(R("q1", 0, 256), R("b0", 256, 512), F.Identity, c1("Nb"), 1.0 / 1024)
+        P([(half("b0", h, 256), R("PM_%d" % h, 0, 128, 1, 65), RLu, True, True) for h in (0, 1)])
+        S(R("q1", 0, 256), R("b0", 256, 512), F.Identity if t else F.Copy, c1("Nb") if t else DOWN, 1.0 / 1024)
         P([(R("b3", 256, 512), I1n, R("q1", 0, 256), True, False)] +
-          [(R("b3", 256 + 128 * h, 384 + 128 * h), R("PM_%d" % h, 0, 128, 1, 65), RLu, False, h == 1) for h in (0, 1)])
+          [(half("b3", h, 256), R("PM_%d" % h, 0, 128, 1, 65), RLu, False, h == 1) for h in (0, 1)])
+        S(R("emu", 0, 256), R("b3", 256, 512), F.Identity if t else F.Copy, c1("Nc") if t else None)
+        C("g", R("emh", 0, 256), R("emu", 0, 256))
         if t == 0:
-            C(opt["emu"], R("emu", 0, 256), R("b3", 256, 512))
-        elif opt["emu"] == "v":
-            V(ts, R("emu", 0, 256), R("b3", 256, 512), c1("Nc"), None, A.add)
+            for m in range(16):
+                C("v" if m < 11 else "s", R(zx, m, 4096, 16), R(z, 0, 256))
         else:
-            S(R("emu", 0, 256), R("b3", 256, 512), F.Identity, c1("Nc"))
-        C(opt["emh"], R("emh", 0, 256), R("emu", 0, 256))
-        for h in (0, 1):
-            for m, eng in enumerate(opt["zx"][t][h]):
-                if eng.islower():
-                    C(eng, R(zx, 2048 * h + m, 2048 * h + 2048, 16), R(z, 128 * h, 128 * h + 128))
-                elif h == 0:
-                    C(eng.lower(), R(zx, m, 4096, 16), R(z, 0, 256))
+            for h in (0, 1):
+                for m in range(16):
+                    C("s" if h == 0 and m >= 14 else "g", R(zx, 2048 * h + m, 2048 * h + 2048, 16), half(z, h))
         for h in (0, 1):
             H, K = "_%d" % h, "b%d" % (2 + h)
-            parts = cuts(opt["ge"][t][h])
-            if any(e != "v" for a, b, e in parts):
-                group([(R("b0", 128, 256), R(z, 128 * h, 128 * h + 128), IB)])
-                S(R("zT", 128 * h, 128 * h + 128), R("b0", 128, 256), F.Copy, None, -1.0)
-            for a, b, e in parts:
+            if h == 1:
+                group([(R("b0", 128, 256), half(z, h), IB)])
+                S(R("zT", 0, 128), R("b0", 128, 256), F.Copy, None, -1.0)
+            for a, b in HALVES:
                 got, d = ind(R("G", 0, 1024), R("emu", 128 * h + a, 128 * h + b)), R("DG" + H, 16 * a, 16 * b)
-                if e == "v":
-                    V(tt, d, got, R(zx, 2048 * h + 16 * a, 2048 * h + 16 * b), A.subtract)
-                    size(opt["rg"][h], R("AG" + H, 16 * a, 16 * b), d)
+                if h == 0:
+                    V(tt, d, got, R(zx, 16 * a, 16 * b), A.subtract)
+                    V(ts, R("AG" + H, 16 * a, 16 * b), d, 0.0, None, A.max)
                 else:
-                    C(e.lower(), d, got)
+                    S(d, got, F.Copy)
                     for c in range(16 * a, 16 * b, 512):
                         o = R("b%d" % (4 + c // 512 % 2), 0, 512)
-                        group([(o, IB, R("DG" + H, c, c + 512)), (o, R("zT", 128 * h, 128 * h + 128), R("EN", c, c + 512))])
+                        group([(o, IB, R("DG" + H, c, c + 512)), (o, R("zT", 0, 128), R("EN", c, c + 512))])
                         S(R("AG" + H, c, c + 512), o, F.Abs)
-            keys(opt["rg"][h], K, 128, 16, "DG" + H, "AG" + H, "CD", R("emh", 128 * h, 128 * h + 128), opt["gk"][h])
+            keys(K, 128, 16, "AG" + H, "CD", half("emh", h), ((0, 128),), None if h else "DG_0")
             V(scan, R("km" + H, 0, 128), R("MMIN", 0, 128), R(K, 0, 128), 0.0, A.add, A.min)
             V(ts, R("ej" + H, 0, 8), R("km" + H, 15, 128, 16), 1023, None, A.bitwise_and)
             V(tt, R("ME" + H, 0, 128), ind(R("ej" + H, 0, 8), R("OFFR", 0, 8)), R("MK", 0, 128), A.mult)
             group([(R("b7", 8 * h, 8 * h + 8), R("ME" + H, 0, 128), R("Q16", 0, 8))])
-            C(opt["eu"], R("eu", 8 * h, 8 * h + 8), R("b7", 8 * h, 8 * h + 8))
+            V(tc, R("eu", 8 * h, 8 * h + 8), R("b7", 8 * h, 8 * h + 8))
             V(tc, R("Ju" + H, 0, 128), ind(R("I", 0, 1024), R("eu", 8 * h, 8 * h + 8)))
-            C(opt["jh"], R("Jh", 128 * h, 128 * h + 128), R("Ju" + H, 0, 128))
-            group([(R("b7", 256 + 128 * h, 384 + 128 * h), R("ME" + H, 0, 128), I16)])
+            C("g", half("Jh", h), R("Ju" + H, 0, 128))
+            group([(half("b7", h, 256), R("ME" + H, 0, 128), I16)])
+        P([(half("b0", h, 256), R("PQ_%d" % h, 0, 128, 1, 65), RLu, True, True) for h in (0, 1)])
+        S(R("q2", 0, 256), R("b0", 256, 512), F.Copy, DOWN, 1.0 / 2048)
         for h in (0, 1):
             H = "_%d" % h
-            for a, b, e in cuts(opt["xe"][t][h]):
-                C(e, R("x" + H, 16 * a, 16 * b), ind(R("xb", 0, 2048), R("Ju" + H, a, b)))
-            for a, b, e in cuts(opt["le"][t][h]):
-                C(e, R("Lg" + H, 16 * a, 16 * b), ind(R("L", 0, 2048), R("Ju" + H, a, b)))
+            for a, b in HALVES:
+                C("sv"[h], R("x" + H, 16 * a, 16 * b), ind(R("xb", 0, 2048), R("Ju" + H, a, b)))
+            for a, b in HALVES:
+                S(R("Lg" + H, 16 * a, 16 * b), ind(R("L", 0, 2048), R("Ju" + H, a, b)), F.Copy)
                 o = R("b6", 128 * h + a, 128 * h + b)
                 group([(o, R("SEL", 128 * k, 128 * k + 128), R("Lg" + H, 16 * a + k, 16 * b, 16)) for k in range(16)])
-                C(opt["nu"], R("nu" + H, a, b), o)
-            for a, b in opt["yk"][h]:
-                d, got, nxt = R("Dy" + H, 16 * a, 16 * b), ind(R("xb", 0, 2048), R("nu" + H, a, b)), R("x" + H, 16 * a + 1, 16 * b + 1)
-                if opt["ry"][h] == 2:
-                    C("v", d, got)
-                    fold(R("Ay" + H, 16 * a, 16 * b), d, nxt)
-                else:
-                    V(tt, d, got, nxt, A.subtract)
-                    size(opt["ry"][h], R("Ay" + H, 16 * a, 16 * b), d)
-            V(scan, R("mx" + H, 0, 2048), R("MR", 0, 2048), R("x" + H, 0, 2048), 0.0, A.mult, A.max)
-            o = R("b%d" % (4 + h), 320, 448)
-            group([(o, IB, R(z, 128 * h, 128 * h + 128)), (o, IB, R("mx" + H, 15, 2048, 16))])
-            S(R("zt", 128 * h, 128 * h + 128), o, F.Copy, 127.75, 0.5)
-            for a, b in [(128 * h, 128 * h + 128)] if opt["split"][t] else [(0, 256)] if h == 1 else []:
-                V(ts, R("zs%d" % t, a, b), R("zt", a, b), -128.0, None, A.add)
-                add("g", "remote", [(t, a, b, "arr%d" % (2 * t + h))], [R("zs%d" % t, a, b)], [R("z%d" % (t + 1), a, b)], RCOST, RLAT)
+                V(tc, R("nu" + H, a, b), o)
+            for a, b in (HALVES, LAST)[h]:
+                d = R("Dy" + H, 16 * a, 16 * b)
+                V(tt, d, ind(R("xb", 0, 2048), R("nu" + H, a, b)), R("x" + H, 16 * a + 1, 16 * b + 1), A.subtract)
+                S(R("Ay" + H, 16 * a, 16 * b), d, F.Abs)
+            w = 2048 if t < 2 else 512
+            for c in range(0, 2048, w):
+                V(scan, R("mx" + H, c, c + w), R("MR", c, c + w), R("x" + H, c, c + w), 0.0, A.mult, A.max)
+            o = half("b0", h, 256)
+            group([(o, IB, half(z, h)), (o, IB, R("mx" + H, 15, 2048, 16))])
+            S(half("zt", h), o, F.Copy, 127.75, 0.5)
+            V(ts, half("zs%d" % t, h), half("zt", h), -128.0, None, A.add)
+            add("g", "remote", [(t, 128 * h, 128 * h + 128, "arr%d" % (2 * t + h))], [half("zs%d" % t, h)], [half("z%d" % (t + 1), h)], RCOST, RLAT)
         V(tt, R("aE", 0, 16), R("b7", 0, 16), R("DUE", 0, 16), A.subtract)
         S(R("Y", 0, 256), R("b7", 256, 512), F.Copy)
         for h in (0, 1):
-            earlier(h, R("ME_%d" % h, 0, 128), R("E2", 0, 320), R("BHn", 0, 128), "Y", 128, "AdE", "msE", None)
+            earlier(h, R("ME_%d" % h, 0, 128), R("E2", 0, 320), R("BHn", 0, 128), "Y", 128, "AdE", "msE", False)
         V(tt, R("tE", 0, 16), ind(R("msE", 0, 640), R("PK", 0, 1)), R("aE", 0, 16), A.mult)
         V(tt, R("oE", 0, 16), R("tE", 0, 16), R("DUE", 0, 16), A.add)
-        C(opt["oeu"], R("oEu", 0, 16), R("oE", 0, 16))
+        C("g", R("oEu", 0, 16), R("oE", 0, 16))
         if t < 2:
             V(tt, R("dz", 0, 256), ind(R("G", 0, 1024), R("eu", 0, 16)), R(z, 0, 256), A.subtract)
-        P([(R("b0", 256 + 128 * h, 384 + 128 * h), R("PQ_%d" % h, 0, 128, 1, 65), RLu, True, True) for h in (0, 1)])
-        S(R("q2", 0, 256), R("b0", 256, 512), F.Copy, DOWN, 1.0 / 2048)
-        C(opt["jf"], R("Jf", 0, 256), R("Jh", 0, 256))
+        C("g", R("Jf", 0, 256), R("Jh", 0, 256))
         VJ = R("b2", 256, 512)
         P([(VJ, I1n, R("q2", 0, 256), True, False), (VJ, I1n, R("q2", 0, 256), False, False)] +
-          [(R("b2", 256 + 128 * h, 384 + 128 * h), R("PQ_%d" % h, 0, 128, 1, 65), RLu, False, False) for h in (0, 1)] +
+          [(half("b2", h, 256), R("PQ_%d" % h, 0, 128, 1, 65), RLu, False, False) for h in (0, 1)] +
           [(VJ, In, R("Jh", 0, 256), False, True)])
         for h in (0, 1):
-            H, K = "_%d" % h, "b%d" % (2 + h)
-            l = (128 * h, 128 * h + 128)
-            keys(opt["ry"][h], K, 256, 15, "Dy" + H, "Ay" + H, "CS", R("Jh", *l), opt["sk"][h], "x" + H)
-            if opt["sign"] == "s":
-                S(R("le", *l), R(K, 128, 256), F.Sign)
-            else:
-                V(ts, R("le", *l), R(K, 128, 256), 0.0, None, A.is_gt)
-            V(scan, R("cs", *l), R("MR", 0, 128), R("le", *l), 0.0, A.mult, A.add)
-            edge = -7.0 if opt["sign"] == "s" else 4.5
-            if opt["nrx"] == "s":
-                S(R("nrx", *l), ind(R("cs", *l), R("OF15", 0, 8)), F.Sign, -edge)
-            else:
-                V(ts, R("nrx", *l), ind(R("cs", *l), R("OF15", 0, 8)), edge, 0.5, A.is_gt, A.subtract)
+            K = "b%d" % (2 + h)
+            keys(K, 256, 15, "Ay_%d" % h, "CS", half("Jh", h), (((0, 128),), ((0, 96), (96, 128)))[h])
+            S(half("le", h), R(K, 128, 256), F.Sign)
+            V(scan, half("cs", h), R("MR", 0, 128), half("le", h), 0.0, A.mult, A.add)
+            S(half("nrx", h), ind(half("cs", h), R("OF15", 0, 8)), F.Sign, 7.0)
             if t < 2:
-                group([(R("b6", *l), R("ON64", 0, 128), R("Ic", 0, 128)), (R("b6", *l), R("nrx", *l), R("Ih", 0, 128))])
-                V(tt, R("tg", *l), R("b6", *l), R("dz", *l), A.mult)
-            V(scan, R("sm", *l), R("MMAX", 0, 128), R(K, 0, 128), 0.0, A.add, A.max)
+                group([(half("b6", h), R("ON64", 0, 128), R("Ic", 0, 128)), (half("b6", h), half("nrx", h), R("Ih", 0, 128))])
+                V(tt, half("tg", h), half("b6", h), half("dz", h), A.mult)
+            V(scan, half("sm", h), R("MMAX", 0, 128), R(K, 0, 128), 0.0, A.add, A.max)
         if t < 2:
             for a, by in ((24, "ONk"), (16, "ONn")):
                 group([(R("b0", a, a + 8), R(by, 0, 128), R("nrx", 128 * h, 128 * h + 128, 16)) for h in (0, 1)])
-            V("tensor_reduce", c1("Nb"), R("b0", 24, 33), "X", A.add)
-            V("tensor_reduce", c1("Nc"), R("b0", 16, 24), "X", A.add)
+            for out, a, b in (("Nb", 24, 33), ("Nc", 16, 24)):
+                S(R(out + "x", 0, b - a), R("b0", a, b), F.Copy, None, None, c1(out))
             scatter("G", 1088, "oEu", "tg", z)
-        folded = [h for h in (0, 1) if opt["fold"][t][h]]
         P([(R("b1", 0, 256), R("ZQ", 400, 528), R("Jh", 0, 256), True, False)] +
-          [(R("b1", 128 * h, 128 * h + 128), R(z, 128 * h, 128 * h + 128), R("BBn", 0, 128), False, False) for h in folded])
+          [(half("b1", h), half(z, h), R("BBn", 0, 128), False, False) for h in (0, 1)])
         for h in (0, 1):
-            X, M, Z = R("x_%d" % h, 0, 2048), R("M%d_%d" % (t, h), 0, 2048), R(zx, 2048 * h, 2048 * h + 2048)
-            if h in folded:
-                w = 2048 // opt["fold"][t][h]
-                for c in range(0, 2048, w):
-                    fold(R(M[0], c, c + w), R(X[0], c, c + w), R(zx, 2048 * h + c, 2048 * h + c + w))
-                continue
-            for c in range(0, 2048, 512):
-                o = R("b0", 0, 512)
-                group([(o, IB, R(X[0], c, c + 512)), (o, R("zT", 128 * h, 128 * h + 128), R("EN", c, c + 512))])
-                S(R(M[0], c, c + 512), o, F.Abs)
-        terms = [("x_%d" % h, h, R("BL1", 0, 8)) for h in folded]
-        terms += [("M%d_%d" % (t, h), h, R("BL2", 0, 8) if h in folded else R("BLK", 8, 16)) for h in (0, 1)]
-        for src, h, by in terms:
-            P([(R("b1", 128 * h + k, 128 * h + 128, 16), R(src, k, 2048, 16), by, False, src == terms[-1][0] and k == 15) for k in range(16)])
+            w = 2048 // FOLDS[t][h]
+            for c in range(0, 2048, w):
+                M, X, Z = R("M%d_%d" % (t, h), c, c + w), R("x_%d" % h, c, c + w), R(zx, 2048 * h + c, 2048 * h + c + w)
+                add("g", "fold", [(M, X, Z, sum(o["kind"] == "fold" for o in ops))], [X, Z], [M], RCOST, FLAT0 + FLAT1 * w)
+        for src, by in (("x_%d", "BL1"), ("M%d_%%d" % t, "BL2")):
+            for h in (0, 1):
+                P([(R("b1", 128 * h + k, 128 * h + 128, 16), R(src % h, k, 2048, 16), R(by, 0, 8), False, by == "BL2" and h == 1 and k == 15)
+                   for k in range(16)])
         S(R("fT", 0, 256), R("b1", 0, 256), F.Copy)
         for h in (0, 1):
-            o = R("b1", 256 + 128 * h, 384 + 128 * h)
-            group([(o, R("fT", 128 * h, 128 * h + 128), I16), (o, R("nrx", 128 * h, 128 * h + 128), I4n)])
-        for a, b in ((0, 128), (128, 256)) if opt["apart"][t] else ((0, 256),):
+            group([(half("b1", h, 256), half("fT", h), I16), (half("b1", h, 256), half("nrx", h), I2n)])
+        for a, b in ((0, 256),) if t < 2 else ((0, 128), (128, 256)):
             V(ts, R("ch", a, b), R("b1", 256 + a, 256 + b), 2048.0, R("tf", 1, 2), A.add, A.is_gt)
             V(tt, R("tmp", a, b), R("ch", a, b), R("b2", 256 + a, 256 + b), A.mult)
         scatter("I", 1088, "oEu", "tmp", "Jf")
         if t == 2:
             dma("y", "yi", R("I", 0, 1024), 4096, "d8")
-        for h0, h1 in ((0, 1), (1, 2)) if opt["apart"][t] else ((0, 2),):
-            n, a, b, w = 8 * (h1 - h0), 128 * h0, 128 * h1, 256 * h0
-            C(opt["qt"][0], R("QT", 32 * h0 + 1, 32 * h1, 4), R("nrx", a, b, 16))
+        for h0, h1 in ((0, 2),) if t < 2 else ((0, 1), (1, 2)):
+            n, a, b = 8 * (h1 - h0), 128 * h0, 128 * h1
             V(ts, R("SJ", 16 * h0, 16 * h1, 2), R("sm", a + 15, b, 16), 2047, None, A.bitwise_and)
             V(ts, R("SJ", 16 * h0 + 1, 16 * h1, 2), R("sm", a + 15, b, 16), 11, 15, A.arith_shift_right, A.bitwise_and)
-            C(opt["qt"][2], R("QT", 32 * h0, 32 * h1, 2), R("SJ", 16 * h0, 16 * h1))
+            C("s" if t < 2 else "v", R("QT", 32 * h0, 32 * h1, 2), R("SJ", 16 * h0, 16 * h1))
             P([(R("b7", 256 + 128 * h, 384 + 128 * h, 1, 32), R("QT", 32 * h, 32 * h + 32), I16, True, True) for h in range(h0, h1)])
             RL = R("RL", a, b, 1, 32)
             S(RL, R("b7", 256 + a, 256 + b, 1, 32), F.Copy)
-            P([(R("b7", 64 + r, 320, 16, n), R("RL", a + r, b, 16, 32), R("SLW", 0, 16, 1, 32), True, True) for r in range(16)])
-            S(R("WT", w, w + 256, 1, n), R("b7", 64, 320, 1, n), F.Copy)
-            WJ, o = R("WT", w, w + 128, 1, n), R("b7", 32 + 8 * h0, 32 + 8 * h1)
-            group([(o, WJ, R("IW", 4, 4 + n, 1, n)), (o, R("WT", w + 128, w + 256, 1, n), R("I4n", 0, n, 1, n)), (o, I16, R("DUn", 8 * h0, 8 * h1))])
-            group([(R("b7", 48 + 8 * h0, 48 + 8 * h1), WJ, R("IW", 4, 4 + n, 1, n))])
-            V(ts, R("aJ", 8 * h0, 8 * h1), o, 0.0, None, A.min)
-            C(opt["ju16"], R("Ju16", 8 * h0, 8 * h1), R("b7", 48 + 8 * h0, 48 + 8 * h1))
+            o = R("b7", 48 + 8 * h0, 48 + 8 * h1)
+            if t == 2:
+                WJ, spread = R("WT", 256 * h0, 256 * h0 + 128), [R("E2", 0, 320)]
+                V(tt, WJ, ind(R("SJ", 16 * h0, 16 * h1), R("OFF2", 0, 8)), R("MK", 0, 128), A.mult)
+                group([(o, WJ, R("Q16", 0, 8))])
+            else:
+                WJ, spread = R("WT", 0, 128, 1, 16), [R("EC", 320 * h, 320 * h + 320, 1, 16) for h in (0, 1)]
+                P([(R("b7", 64 + r, 192, 16, 16), R("RL", r, 256, 16, 32), R("SLW", 0, 8, 1, 32), True, True) for r in range(16)])
+                S(WJ, R("b7", 64, 192, 1, 16), F.Copy)
+                group([(o, WJ, R("IW", 4, 20, 1, 16))])
+            V(tt, R("aJ", 8 * h0, 8 * h1), o, R("DUJ", 8 * h0, 8 * h1), A.subtract)
+            V(tc, R("Ju16", 8 * h0, 8 * h1), o)
             for h in range(h0, h1):
-                earlier(h, WJ, R("EC", 320 * (h - h0), 320 * (h - h0) + 320, 1, n), R("RPJ", 0, 128, 1, 32), "RL", 32, "AdJ", "msJ", -2048.0)
-            pk = 2 if n == 8 else 0
+                earlier(h, WJ, spread[h - h0], R("RPJ", 0, 128, 1, 32), "RL", 32, "AdJ", "msJ", True)
+            pk = 2 if t == 2 else 0
             V(tt, R("tJ", 16 * h0, 16 * h0 + 16), ind(R("msJ", 320 * h0, 320 * h1), R("PK", pk, pk + 1)), R("aJ", 8 * h0, 8 * h0 + 16), A.mult)
-            V(tt, R("oJ", 8 * h0, 8 * h1), R("tJ", 16 * h0, 16 * h0 + n), R("DUn", 8 * h0, 8 * h1), A.subtract)
-            V(ts, R("oJu", 8 * h0, 8 * h1), R("oJ", 8 * h0, 8 * h1), 2048.0, None, A.add)
+            V(tt, R("oJ", 8 * h0, 8 * h1), R("tJ", 16 * h0, 16 * h0 + n), R("DUJ", 8 * h0, 8 * h1), A.add)
+            V(tc, R("oJu", 8 * h0, 8 * h1), R("oJ", 8 * h0, 8 * h1))
             S(R("Lold", a, b), ind(R("L", 0, 2048), R("Ju16", 8 * h0, 8 * h1)), F.Copy)
             group([(R("b6", 256 + a, 256 + b), R("RPK", 0, 128, 1, 32), RL)])
             V(ts, R("mk", a, b), R("b6", 256 + a, 256 + b), c1("k15"), None, A.is_equal)
-            if opt["lo16"][t] == "v":
+            if t == 2:
                 group([(R("b6", a, b), ISH, R("Jh", a, b))])
                 V(tt, R("b6", a, b), R("b6", a, b), R("Lold", a, b), A.subtract)
             else:
-                C(opt["lo16"][t], R("Lo16", a, b), R("Lold", a, b))
+                C("g", R("Lo16", a, b), R("Lold", a, b))
                 group([(R("b6", a, b), ISH, R("Jh", a, b)), (R("b6", a, b), In, R("Lo16", a, b))])
             V(tt, R("t2", a, b), R("b6", a, b), R("mk", a, b), A.mult)
         scatter("L", 2112, "oJu", "t2", "Lold")
@@ -549,15 +516,15 @@ def edges(ops):
                             e.setdefault(j, False)
                     elif (w or sw) and clash(r, s):
                         e[j] = e.get(j, False) or bool(not same or sw or ops[j]["lat"] > 0)
+        o["clash"] = set(e) if o["q"] != "t" else set()
         pre.append(e)
         for w, rs in ((True, o["writes"]), (False, o["reads"])):
             for r in rs:
                 touched.setdefault(r[0], []).append((o["i"], r, w))
     where = {(o["t"], o["name"]): o["i"] for o in ops}
     for t in range(3):
-        for turn in ops[0]["turns"][t]:
-            got = [(t - w.count("<"), w.strip("<")) for w in turn.split()]
-            got = [where[w] for w in got if w in where]
+        for turn in TURNS[t]:
+            got = [where[t - w.count("<"), w.strip("<")] for w in turn.split()]
             for j, i in zip(got, got[1:]):
                 pre[i].setdefault(j, False)
     return pre
@@ -588,114 +555,6 @@ def before(taken, s):
         else:
             hi = mid
     return lo
-
-
-def fit(seq, lags, uses):
-    start, busy = [0.0] * len(seq), {}
-    for i in seq:
-        s = 0.0
-        for j, d in lags[i].items():
-            if start[j] + d > s:
-                s = start[j] + d
-        moved = True
-        while moved:
-            moved = False
-            for res, off, n, who in uses[i]:
-                taken = busy.setdefault(res, [])
-                if not taken or taken[-1][1] <= s + off:
-                    continue
-                k = max(0, before(taken, s + off) - 2)
-                while k < len(taken) and taken[k][0] < s + off + n - 1e-6:
-                    if s + off < taken[k][1] - 1e-6 and (who is None or who != taken[k][2]):
-                        s, moved = taken[k][1] - off, len(uses[i]) > 1
-                    k += 1
-        start[i] = s
-        for res, off, n, who in uses[i]:
-            taken = busy[res]
-            if not taken or taken[-1][0] <= s + off:
-                taken.append((s + off, s + off + n, who))
-            else:
-                taken.insert(before(taken, s + off), (s + off, s + off + n, who))
-    return start
-
-
-def schedule(ops, pre, passes, seed):
-    n = len(ops)
-    span = [o["cost"] + o["lat"] for o in ops]
-    banks = [sorted(set(bank(r) for r in o["reads"] + o["writes"] if bank(r))) for o in ops]
-    fwd = [{j: (span[j] + WAKE if w else ops[j]["cost"]) for j, w in pre[i].items()} for i in range(n)]
-    bwd = [{} for _ in range(n)]
-    for i in range(n):
-        for j, d in fwd[i].items():
-            bwd[j][i] = d - span[j] + span[i]
-    ahead, back = [], []
-    for i, o in enumerate(ops):
-        u = [(o["q"], 0.0, o["cost"], None)] + [(b, 0.0, o["cost"] + WAKE, o["q"]) for b in banks[i]]
-        if o.get("hold"):
-            u.append(("engines", o["cost"] + DLAT, o["hold"], None))
-        ahead.append(u)
-        back.append([(res, span[i] - off - m, m, who) for res, off, m, who in u])
-
-    def ordered(key, lags, way):
-        key = list(key)
-        for i in way:
-            for j in lags[i]:
-                if key[j] >= key[i]:
-                    key[i] = key[j] + 1e-3
-        return sorted(range(n), key=lambda i: key[i])
-
-    def early(key):
-        start = fit(ordered(key, fwd, seq), fwd, ahead)
-        end = max(start[i] + span[i] for i in range(n))
-        return end + 0.3 * sum(start[i] for i in long) / len(long), end, start, key
-
-    def late(start):
-        s = fit(ordered([-start[i] - span[i] for i in range(n)], bwd, seq[::-1]), bwd, back)
-        return [-s[i] - span[i] for i in range(n)]
-
-    def move(key, i, by):
-        todo = [(i, key[i] + by)]
-        key[i] = max(key[i], key[i] + by)
-        while todo:
-            i, at = todo.pop()
-            if key[i] > at:
-                key[i] = at
-                todo += [(j, at - 1e-2) for j in fwd[i]]
-
-    seq = sequence(pre)
-    long = [i for i in range(n) if ops[i]["cost"] > 800 and ops[i]["q"] in "vs"]
-    alike = {}
-    for o in ops:
-        alike.setdefault(o["name"], []).append(o["i"])
-    tail = [0.0] * n
-    for i in seq[::-1]:
-        tail[i] = max([span[i]] + [tail[k] + fwd[k][i] for k in bwd[i]])
-    dice = np.random.default_rng(seed).random((passes, 3, 7)).tolist()
-    now = best = early(late(early([-x for x in tail])[2]))
-    for k, d in enumerate(dice):
-        if d[0][0] < 0.05:
-            key = late(now[2])
-        else:
-            key = list(now[3]) if d[0][1] < 0.7 else [now[2][i] for i in range(n)]
-            for a in d[:(1, 1, 2, 3)[int(4 * d[1][0])]]:
-                i = long[int(a[2] * len(long))] if a[3] < 0.3 else int(a[2] * n)
-                for j in alike[ops[i]["name"]] if a[4] < 0.4 else [i]:
-                    move(key, j, (600, 2000, 6000)[int(3 * a[5])] * (2 * a[6] - 1) * abs(2 * a[6] - 1))
-        new = early(key)
-        if new[0] < now[0] - (5 + 120.0 * (1 - k / passes)) * math.log(d[2][0]):
-            now = new
-            if new[1] < best[1]:
-                best = new
-    end, start = best[1:3]
-    order = sorted(range(n), key=lambda i: (start[i], i))
-    waits, last = [dict(e) for e in pre], {}
-    for i in order:
-        for b in banks[i]:
-            for q, j in last.setdefault(b, {}).items():
-                if q != ops[i]["q"]:
-                    waits[i][j] = True
-            last[b][ops[i]["q"]] = i
-    return order, waits, start, end
 
 
 def fit(seq, lags, uses, tail=None, limit=None, old=None):
@@ -738,7 +597,7 @@ def fit(seq, lags, uses, tail=None, limit=None, old=None):
     return seq, start, marks
 
 
-def schedule(ops, pre, passes, seed, heat=100.0):
+def schedule(ops, pre, stages, seed):
     n = len(ops)
     span = [o["cost"] + o["lat"] for o in ops]
     banks = [sorted(set(bank(r) for r in o["reads"] + o["writes"] if bank(r))) for o in ops]
@@ -782,6 +641,17 @@ def schedule(ops, pre, passes, seed, heat=100.0):
                 key[i] = at
                 todo += [(j, at + sign * 1e-2) for j, d in lags[i]]
 
+    def tight(start):
+        ends = {(res, round(start[i] + off + m)): i for i in range(n) for res, off, m, who in ahead[i]}
+        i, out = max(range(n), key=lambda i: start[i] + span[i]), []
+        while i is not None:
+            out.append(i)
+            got = [j for j, d in fwd[i] if abs(start[j] + d - start[i]) < 1]
+            got += [ends[res, round(start[i] + off)] for res, off, m, who in ahead[i] if (res, round(start[i] + off)) in ends]
+            got = [j for j in got if start[j] < start[i]]
+            i = got[-1] if got else None
+        return out
+
     seq = sequence(pre)
     long = [i for i in range(n) if ops[i]["cost"] > 800 and ops[i]["q"] in "vs"]
     alike = {}
@@ -790,23 +660,28 @@ def schedule(ops, pre, passes, seed, heat=100.0):
     tail = [0.0] * n
     for i in seq[::-1]:
         tail[i] = max([span[i]] + [tail[k] + d + span[i] - span[k] for k, d in bwd[i]])
-    dice = np.random.default_rng(seed).random((passes, 3, 7)).tolist()
-    now = best = early(late(early(mend([-x for x in tail], fwd, seq))[2][1]))
-    for k, d in enumerate(dice):
-        if d[0][0] < 0.03:
-            key = late(now[2][1])
-        else:
-            key = list(now[3]) if d[0][1] < 0.8 else mend(list(now[2][1]), fwd, seq)
-            for a in d[:(1, 1, 2, 3)[int(4 * d[1][0])]]:
-                i = long[int(a[2] * len(long))] if a[3] < 0.3 else int(a[2] * n)
-                for j in alike[ops[i]["name"]] if a[4] < 0.3 else [i]:
-                    move(key, j, (600, 2000, 6000)[int(3 * a[5])] * (2 * a[6] - 1) * abs(2 * a[6] - 1))
-        more = -(5 + heat * (1 - k / passes)) * math.log(d[2][0])
-        new = early(key, now[1] + more + 300, now[2])
-        if new and new[0] < now[0] + more:
-            now = new
-            if new[1] < best[1]:
-                best = new
+    rng = np.random.default_rng(seed)
+    best = early(late(early(mend([-x for x in tail], fwd, seq))[2][1]))
+    for passes, heat in stages:
+        now = best
+        hot = tight(now[2][1])
+        for k, d in enumerate(rng.random((passes, 3, 7)).tolist()):
+            if d[0][0] < 0.03:
+                key = late(now[2][1])
+            else:
+                key = list(now[3]) if d[0][1] < 0.8 else mend(list(now[2][1]), fwd, seq)
+                for a in d[:(1, 1, 2, 3)[int(4 * d[1][0])]]:
+                    i = long[int(a[2] * len(long))] if a[3] < 0.15 else int(a[2] * n) if a[3] < 0.35 else hot[int(a[2] * len(hot))]
+                    for j in alike[ops[i]["name"]] if a[4] < 0.3 else [i]:
+                        move(key, j, (600, 2000, 6000)[int(3 * a[5])] * (2 * a[6] - 1) * abs(2 * a[6] - 1))
+            more = -(5 + heat * (1 - k / passes)) * math.log(d[2][0])
+            new = early(key, now[1] + more + 300, now[2])
+            if new and new[0] < now[0] + more:
+                now = new
+                if k % 4 == 0:
+                    hot = tight(now[2][1])
+                if new[1] < best[1]:
+                    best = new
     end, start = best[1], best[2][1]
     order = sorted(range(n), key=lambda i: (start[i], i))
     waits, last = [dict(e) for e in pre], {}
@@ -819,49 +694,31 @@ def schedule(ops, pre, passes, seed, heat=100.0):
     return order, waits, start, end
 
 
-HALVES = ((0, 64), (64, 128))
-WHOLE = ((0, 128),)
-S_TURN = "sAG_1@1536 sx_0@0 sx_0@1024 sLg_0@0 sLg_0@1024 sLg_1@0 sLg_1@1024 sAy_0@0 sAy_0@1024 sAy_1@0 sAy_1@1024 sAy_1@1536"
-V_TURN = "vDG_0@0 vDG_0@1024 vJu_0@0 vJu_1@0 vx_1@0 vDy_0@0 vDy_0@1024 vDy_1@0 vDy_1@1024 vDy_1@1536"
-OPT = {"turns": ((V_TURN,), (S_TURN, V_TURN), (S_TURN, V_TURN, "vI@2 vL@1")),
-       "ge": (("64v 64v", "64s 64v"), ("64v 64v", "64s 64s"), ("64v 64v", "64s 64s")), "gk": (WHOLE, WHOLE), "rg": (1, 0),
-       "xe": (("64s 64s", "64v 64v"),) * 3, "le": (("64s 64s", "64s 64s"),) * 3, "yk": (HALVES, ((0, 64), (64, 96), (96, 128))), "ry": (0, 0),
-       "sk": (WHOLE, ((0, 96), (96, 128))),
-       "emu": "s", "emh": "g", "eu": "v", "jh": "g", "jf": "g", "nu": "v", "sign": "s", "nrx": "s", "qt": "gss", "ui": "vss", "oeu": "g", "fold": ((1, 1), (1, 1), (1, 2)), "ju16": "v", "lo16": "ggv", "icv": "s", "lcv": "gs",
-       "split": (1, 1, 0), "apart": (0, 0, 1), "zx": (("V" * 12 + "S" * 4,) * 2, ("g" * 13 + "v" * 3, "g" * 16), ("g" * 13 + "v" * 3, "g" * 16))}
 PLAN = {}
 
 
-def plan(opt, passes=28000, seed=2):
-    ops = build(opt)
-    pre = edges(ops)
-    order, waits, start, end = schedule(ops, pre, passes, seed)
-    return ops, order, waits, start, end
+def plan(stages=((27000, 100.0), (20000, 50.0)), seed=9):
+    ops = build()
+    return (ops,) + schedule(ops, edges(ops), stages, seed)
 
 
 def helper(core, T, topo):
     return [c for c in topo.cores_of(core) if c not in T.cores and topo.die(c) == topo.die(core)][0]
 
 
-def spare(core, T, topo):
-    near = topo.engines(core, helper(core, T, topo))
-    far = topo.engines(core, T.cores[(T.rank_of(core) + 1) % len(T.cores)])
-    use = near
-    return sum(1 << e for e in use), len(use)
-
-
 def hand_back(g, core, owner, T, topo):
     rid, pid, _e = topo.addr(owner)
     folds = [PLAN["ops"][i]["calls"][0] for i in PLAN["order"] if PLAN["ops"][i]["kind"] == "fold"]
     for out, a, b, k in folds:
-        g.wait_ge(T.sem["fa%d" % k], spare(owner, T, topo)[1])
-        g.remote_dma(T[out[0]][:, out[1]:out[2]], T[out[0]][:, out[1]:out[2]], T.sem["fb%d" % k], T.sem["loc"], pid, rid, topo.mask(core, owner))
+        g.wait_ge(T.sem["fa%d" % k], len(topo.engines(owner, core)))
+        piece = T[out[0]][:, out[1]:out[2]]
+        g.remote_dma(piece, piece, T.sem["fb%d" % k], T.sem["loc"], pid, rid, topo.mask(core, owner))
     g.wait_ge(T.sem["loc"], len(folds) * len(topo.engines(core, owner)))
 
 
 def rank_program(g, core, T, topo):
     if "ops" not in PLAN:
-        PLAN["ops"], PLAN["order"], PLAN["waits"] = plan(OPT)[:3]
+        PLAN["ops"], PLAN["order"], PLAN["waits"] = plan()[:3]
     rank = T.rank_of(core)
     if rank is None:
         for owner in T.cores:
@@ -872,6 +729,8 @@ def rank_program(g, core, T, topo):
     n = len(T.cores)
     queue = {"v": g.vector, "s": g.scalar, "t": g.tensor, "g": g, "y": g.sync}
     qsem = {"v": "qv", "s": "qs", "t": "qt", "g": "qg"}
+    vector = {"tensor_copy": g.vector.tensor_copy, "tensor_scalar": g.vector.tensor_scalar, "tensor_tensor": g.vector.tensor_tensor,
+              "tensor_tensor_scan": g.vector.tensor_tensor_scan, "memset": g.vector.memset}
     count = {}
     seen = {q: {} for q in queue}
     done = {}
@@ -894,7 +753,7 @@ def rank_program(g, core, T, topo):
         q, eng, k = o["q"], queue[o["q"]], o["kind"]
         known = seen[q]
         for j in sorted(pre[i], key=lambda j: -place[j]):
-            if not pre[i][j]:
+            if not pre[i][j] and j not in o["clash"]:
                 continue
             sem, val, kn = done[j]
             if known.get(sem, 0) < val:
@@ -903,9 +762,7 @@ def rank_program(g, core, T, topo):
                     known[s] = max(known.get(s, 0), kn[s])
                 known[sem] = max(known.get(sem, 0), val)
         if k == "dma":
-            out, in_ = o["calls"][0]
-            out = ap(out) if isinstance(out, tuple) else T[out][:]
-            in_ = ap(in_) if isinstance(in_, tuple) else T[in_][:]
+            out, in_ = [ap(x) if isinstance(x, tuple) else T[x][:] for x in o["calls"][0]]
             eng.dma_start(out, in_).then_inc(T.sem[o["sem"]], 16)
             done[i] = (o["sem"], 16, dict(known))
             count[o["sem"]] = 16
@@ -923,10 +780,10 @@ def rank_program(g, core, T, topo):
             out, a, b, f = o["calls"][0]
             relay = helper(core, T, topo)
             rid, pid, _e = topo.addr(relay)
-            mask, m = spare(core, T, topo)
-            g.remote_dma_fused([RemoteDMATransfer(dst_ids=[DstId(rid=rid, pnc=pid)], dma_engine_mask=mask, remote_sem=T.sem["fa%d" % f],
-                                                  srcs=[ap(a), ap(b)], dsts=[ap(out)], alu_op=2)], local_sem=T.sem["loc"])
-            count["loc"] = count.get("loc", 0) + m
+            g.remote_dma_fused([RemoteDMATransfer(dst_ids=[DstId(rid=rid, pnc=pid)], dma_engine_mask=topo.mask(core, relay),
+                                                  remote_sem=T.sem["fa%d" % f], srcs=[ap(a), ap(b)], dsts=[ap(out)], alu_op=2)],
+                               local_sem=T.sem["loc"])
+            count["loc"] = count.get("loc", 0) + len(topo.engines(core, relay))
             done[i] = ("fb%d" % f, len(topo.engines(relay, core)), dict(known))
             continue
         sem = qsem[q]
@@ -934,33 +791,16 @@ def rank_program(g, core, T, topo):
             if k == "matmul":
                 ins = g.tensor.matmul(ap(c[0]), ap(c[1]), ap(c[2]), bool(c[3]), bool(c[4]))
             elif k == "activation":
-                kw = {}
-                if c[3] is not None:
-                    kw["bias"] = arg(c[3])
-                if c[4] is not None:
-                    kw["scale"] = arg(c[4])
+                kw = {name: arg(x) for name, x in zip(("bias", "scale", "accum_out"), c[3:]) if x is not None}
                 ins = g.scalar.activation(ap(c[0]), ap(c[1]), c[2], **kw)
+            elif k == "iota" and DTYPE[c[0][0]] == "int32":
+                ins = g.iota(ap(c[0]), c[1], c[2], c[3])
             elif k == "iota":
-                if DTYPE[c[0][0]] == "int32":
-                    ins = g.iota(ap(c[0]), c[1], c[2], c[3])
-                else:
-                    ins = g.iota(ap(c[0]), c[1], c[2], c[3], allow_small_or_imprecise_dtypes=True)
+                ins = g.iota(ap(c[0]), c[1], c[2], c[3], allow_small_or_imprecise_dtypes=True)
             elif k == "select":
                 ins = g.affine_select(ap(c[0]), ap(c[1]), c[2], A.is_equal, 0.0, c[3], c[4])
             else:
-                x = [arg(y) for y in c]
-                if k == "tensor_copy":
-                    ins = g.vector.tensor_copy(*x)
-                elif k == "tensor_scalar":
-                    ins = g.vector.tensor_scalar(*x)
-                elif k == "tensor_tensor":
-                    ins = g.vector.tensor_tensor(*x)
-                elif k == "tensor_tensor_scan":
-                    ins = g.vector.tensor_tensor_scan(*x)
-                elif k == "tensor_reduce":
-                    ins = g.vector.tensor_reduce(x[0], x[1], AxisListType.X, x[3])
-                else:
-                    ins = g.vector.memset(*x)
+                ins = vector[k](*[arg(x) for x in c])
             ins.then_inc(T.sem[sem], 1)
             count[sem] = count.get(sem, 0) + 1
         kn = dict(known)

@@ -4,11 +4,34 @@ from concourse.bass import DstId, RemoteDMATransfer
 from concourse.mybir import AluOpType as A, ActivationFunctionType as F
 
 BIG = 1.0e9
-CYC, GAT, SCA, WAKE, FIX, SFIX, TCYC = 0.8333, 1.56, 3.8, 130.0, 20.0, 80.0, 0.5
-DLAT, DRATE, RLAT, FLAT0, FLAT1, RCOST = 1600.0, 200.0, 3800.0, 3500.0, 3.0, 500.0
+TIMES = dict(CYC=0.8333, GAT=1.56, SCA=3.8, WAKE=130.0, FIX=20.0, SFIX=80.0, TCYC=0.5, DLAT=1600.0, DRATE=200.0, RLAT=3900.0, FLAT0=3500.0,
+             FLAT1=3.0, RCOST=500.0)
+WAKE = TIMES["WAKE"]
+CASES = ({}, dict(CYC=0.92, TCYC=0.5, RLAT=4200.0), dict(CYC=1.05, TCYC=0.63, WAKE=160.0), dict(CYC=1.0, TCYC=0.6, GAT=1.15, SCA=4.5, RLAT=4500.0),
+         dict(CYC=1.0, TCYC=0.6, GAT=1.95, SCA=2.5, WAKE=180.0, DRATE=260.0),
+         dict(CYC=1.0, TCYC=0.6, RLAT=5800.0, FLAT0=4800.0, RCOST=850.0, SCA=5.2),
+         dict(CYC=1.1, TCYC=0.66, GAT=1.3, DRATE=140.0, FLAT1=4.5, WAKE=100.0))
 SCRATCH = {}
 TWO = ("bfloat16", "float16", "uint16")
-SEG = (0, 16, 48, 96)
+DUMP = 176
+SEG = (0, 17, 50, 99)
+BW = 164
+UP = 192.0
+HALVES = ((0, 64), (64, 128))
+LAST = ((0, 64), (64, 96), (96, 128))
+CFG = dict(
+    packed=(False, False, False),
+    x=(((0, 128, "s"),), ((0, 64, "v"), (64, 128, "v"))),
+    l=(((0, 64, "s"), (64, 128, "s")), ((0, 64, "s"), (64, 128, "s"))),
+    x0=(((0, 96, "s"), (96, 128, "v")), ((0, 64, "v"), (64, 128, "s"))),
+    l2=(((0, 64, "s"), (64, 128, "s")), ((0, 32, "v"), (32, 64, "s"), (64, 128, "s"))),
+    y=((0, 64, "v"), (64, 128, "v"), (128, 192, "v"), (192, 256, "s")),
+    relu="vvvv",
+    cuts=(((0, 128),), ((0, 128),)),
+    wide=((0, 0), (0, 0), (0, 0)),
+    casts=(1, 1, 1), folds=((1, 2), (1, 2), (2, 2)), zs=1, r="ss", nu="vv", emu="ss", eu="vv", Ju="sv",
+    sub=("b0", "b6", "b4", "b5"), ch="ssv", g=(((0, 128),), HALVES), UH="s", QT="ssv", uu="vvv", oE="sss", oJ="ssv", J16="ssv", zl="s",
+    emi="vv", zn="sv", z0="VVVVVVVVVvvvvsss", harden=(6000, 0.15), scan=(1024, 1024, 512), rows=16, late=(0, 0, 0), WT="sv", copy=0.02, alike=0.4, aim=0.6, mean=0.3)
 
 
 def _buf(name, cols, dtype, where="sbuf"):
@@ -17,35 +40,33 @@ def _buf(name, cols, dtype, where="sbuf"):
 
 _B, _H, _F, _I, _U = "bfloat16", "float16", "float32", "int32", "uint16"
 for _n, _c, _d in (
-        ("xb", 2048, _B), ("G", 1088, _B), ("ixi", 1024, _I), ("I", 1088, _F), ("lki", 2048, _I), ("L", 2112, _F),
-        ("wti", 1, _I), ("hki", 2, _I), ("thi", 2, _I),
+        ("xb", 2048, _B), ("G", DUMP + 1024, _B), ("ixi", 1024, _I), ("I", DUMP + 1024, _F), ("lki", 2048, _I), ("XL", DUMP + 2048, _F),
+        ("L", DUMP + 2048, _F), ("wti", 1, _I), ("hki", 2, _I), ("thi", 2, _I),
         ("z0", 256, _B), ("z1", 256, _B), ("z2", 256, _B), ("z3", 256, _B),
-        ("zs0", 256, _B), ("zs1", 256, _B), ("zs2", 256, _B), ("zt", 256, _B),
-        ("pI", 1, _I), ("p16i", 1, _I), ("pgi", 1, _I), ("pf", 1, _F), ("p16", 1, _F), ("pg", 1, _F), ("colA", 1, _F), ("colB", 1, _F),
-        ("k15", 1, _F), ("wf", 1, _F), ("hI", 4, _I), ("hf", 4, _F), ("tf", 2, _F), ("q2i", 1, _I), ("bI", 1, _I), ("pk1", 1, _F),
-        ("pk2", 1, _F), ("pk4", 1, _F), ("m15", 1, _F), ("acol", 1, _F), ("dI", 144, _B), ("gI", 128, _B), ("g8I", 16, _I),
-        ("rI", 128, _B), ("dg4", 128, _B), ("duI", 16, _I), ("r15I", 128, _B), ("slI", 16, _B), ("qrel", 160, _B), ("dcol", 160, _B),
-        ("SM", 320, _B), ("IW", 136, _H), ("IB", 136, _B), ("In", 128, _H), ("I1n", 128, _H), ("I2n", 128, _H), ("Ih", 128, _H),
-        ("Ic", 128, _H), ("BHn", 128, _H), ("BBn", 128, _B), ("BLK", 16, _B), ("BKn", 16, _B), ("BK2", 16, _B), ("BL1", 8, _B),
-        ("BL2", 8, _B), ("Q16", 8, _H), ("MK", 128, _H), ("SEL", 2048, _H), ("EN", 2048, _B), ("MR", 2048, _B), ("CD", 128, _H),
-        ("CS", 256, _H), ("ON64", 128, _H), ("ONn", 128, _H), ("ONk", 128, _H), ("MMIN", 128, _F), ("MMAX", 128, _F), ("OFFR", 8, _U),
-        ("OF15", 8, _U), ("OFF2", 8, _U), ("PK", 4, _U), ("DUE", 16, _F), ("DUn", 16, _H), ("DUJ", 16, _F), ("RPJ", 128, _H),
-        ("TS", 320, _H), ("RPK", 128, _H), ("SLW", 16, _H), ("E2", 320, _H), ("EC", 640, _H), ("TR", 320, _H), ("dg0", 128, _H),
-        ("dg1", 128, _H), ("dg2", 128, _H), ("dg3", 128, _H), ("W8", 8, _B), ("ZQ", 528, _H), ("PM_0", 128, _H), ("PM_1", 128, _H),
-        ("PQ_0", 128, _H), ("PQ_1", 128, _H),
-        ("ui", 16, _I), ("uu", 16, _I), ("UQ", 64, _I), ("UH", 66, _H), ("RLu", 128, _H), ("q1", 256, _H), ("q2", 256, _H),
-        ("emu", 256, _U), ("emh", 256, _H), ("Nc", 1, _F), ("Nb", 1, _F), ("Ncx", 9, _F), ("Nbx", 9, _F), ("zx0", 4096, _B),
-        ("zx1", 4096, _B), ("zT", 128, _B), ("eu", 16, _U), ("Jf", 256, _F), ("Jh", 256, _H), ("Y", 256, _H), ("AdE", 640, _B),
-        ("msE", 640, _B), ("aE", 16, _F), ("tE", 16, _F), ("oE", 16, _F), ("oEu", 16, _U), ("dz", 256, _B), ("tg", 256, _B),
-        ("le", 256, _B), ("cs", 256, _B), ("nrx", 256, _H), ("sm", 256, _I), ("SJ", 32, _I), ("QT", 64, _H), ("RL", 256, _H),
-        ("WT", 512, _H), ("AdJ", 640, _B), ("msJ", 640, _B), ("aJ", 24, _F), ("tJ", 32, _F), ("oJ", 16, _F), ("oJu", 16, _U),
-        ("Ju16", 16, _U), ("fT", 256, _H), ("ch", 256, _F), ("tmp", 256, _F), ("Lold", 256, _F), ("Lo16", 256, _H), ("mk", 256, _F),
-        ("t2", 256, _F)):
+        ("zs0", 256, _B), ("zs1", 256, _B), ("zs2", 256, _B), ("zt", 256, _B), ("zr", 256, _B),
+        ("pI", 6, _I), ("pf", 5, _F), ("p32", 1, _F), ("colA", 1, _F), ("colB", 1, _F),
+        ("colC", 1, _F), ("k15", 1, _F), ("hI", 3, _I), ("hf", 3, _F), ("tf", 2, _F), ("OFF0", 8, _U),
+        ("pk1", 1, _F), ("pk2", 1, _F), ("m15", 1, _F), ("acol", 1, _F), ("dI", 144, _B), ("gI", 128, _B), ("g8I", 16, _I),
+        ("rI", 128, _B), ("dg4", 128, _B), ("r15I", 128, _B), ("slI", 16, _B), ("qrel", BW, _B), ("dcol", BW, _B), ("dl", BW, _B),
+        ("SM", 2 * BW, _B), ("IW", 136, _H), ("IB", 136, _B), ("IBn", 128, _B), ("I64", 128, _B), ("In", 128, _H), ("I2n", 128, _H),
+        ("Ih", 128, _H), ("Ic", 128, _H), ("BHn", 128, _H), ("BBn", 128, _B), ("BLK", 24, _B), ("BKn", 16, _B), ("BK2", 16, _B),
+        ("BL1", 8, _B), ("BL2", 8, _B), ("MK", 128, _H), ("EN", 512, _B), ("SEL", 2048, _H), ("MR", 1024, _B), ("CD", 256, _H),
+        ("CS", 256, _H), ("ON64", 128, _H), ("ONf", 128, _F), ("UPn", 128, _B), ("SK", 256, _F), ("MMIN", 128, _B), ("MMAX", 128, _B),
+        ("Nc", 1, _F), ("CB", 256, _H), ("vj", 256, _H),
+        ("OFFR", 8, _U), ("OF15", 8, _U), ("OFF2", 8, _U), ("PK", 4, _U), ("RPJ", 128, _H), ("RPK", 128, _H), ("SLW", 16, _H),
+        ("EE", 6 * BW, _H), ("TT", 4 * BW, _H), ("dg0", 128, _H), ("dg1", 128, _H), ("dg2", 128, _H), ("W8", 16, _B), ("ZQ", 528, _H),
+        ("PM_0", 128, _H), ("PM_1", 128, _H), ("PQ_0", 128, _H), ("PQ_1", 128, _H),
+        ("ui", 16, _I), ("uu", 16, _I), ("UQ", 64, _I), ("UH", 66, _H), ("RLu", 128, _H), ("q2", 256, _H), ("emi", 256, _I),
+        ("emu", 256, _U), ("emh", 256, _H), ("Nx", 2, _F), ("zx0", 4096, _B), ("zx1", 4096, _B), ("zT", 128, _B), ("eu", 16, _U),
+        ("Jf", 256, _F), ("Jh", 256, _H), ("Y", 256, _H), ("AdE", 4 * BW, _F), ("msE", 4 * BW, _F), ("oEu", 16, _U), ("dz", 256, _B),
+        ("tg", 256, _B), ("rd", 256, _B), ("Lh", 256, _H), ("le", 256, _B), ("cs", 256, _B), ("nrx", 256, _H), ("sm", 256, _I),
+        ("SJ", 32, _I), ("QT", 64, _H), ("RL", 256, _H), ("WT", 512, _H), ("AdJ", 4 * BW, _F), ("msJ", 4 * BW, _F), ("oJu", 32, _U),
+        ("Ju16", 16, _U), ("fT", 256, _H), ("ch", 256, _F), ("tmp", 256, _F), ("Lold", 256, _F), ("mk", 256, _F), ("t2", 256, _F)):
     _buf(_n, _c, _d)
 for _h in "01":
-    for _n, _c, _d in (("DG", 2048, _B), ("AG", 2048, _B), ("x", 2064, _B), ("Lg", 2048, _H), ("mx", 2048, _B), ("Dy", 2048, _B),
-                       ("Ay", 2048, _B), ("km", 128, _I), ("ej", 8, _I), ("ME", 128, _H), ("Ju", 128, _U), ("nu", 128, _U),
-                       ("M0", 2048, _B), ("M1", 2048, _B), ("M2", 2048, _B)):
+    for _n, _c, _d in (("DG", 2048, _B), ("AG", 2048, _B), ("x", 2064, _B), ("XG", 2064, _F), ("Lg", 2048, _H), ("mx", 2048, _B),
+                       ("Dy", 2048, _B), ("Ay", 2048, _B), ("km", 128, _I), ("ej", 8, _I), ("ME", 128, _H), ("Ju", 128, _U),
+                       ("nu", 128, _U), ("M0", 2048, _B), ("M1", 2048, _B), ("M2", 2048, _B)):
         _buf(_n + "_" + _h, _c, _d)
 for _b in range(8):
     _buf("b%d" % _b, 512, _F, "psum")
@@ -60,24 +81,25 @@ for _n in sorted(SCRATCH):
     else:
         PLACE[_n] = (_n, 0)
 DTYPE = {_n: SCRATCH[_n][2] for _n in SCRATCH}
+COLS = {_n: SCRATCH[_n][1][1] for _n in SCRATCH}
 for _n in list(SCRATCH):
     if PLACE[_n][0] != _n:
         del SCRATCH[_n]
 for _d in _pack:
     _buf("k_" + _d, _pack[_d], _d)
-SEMAPHORES = (["qv", "qs", "qt", "qg", "loc"] + ["arr%d" % i for i in range(6)] + [s + str(i) for s in ("fa", "fb") for i in range(10)]
-              + ["d%d" % i for i in range(15)])
+SEMAPHORES = (["qv", "qs", "qt", "qg", "loc"] + ["arr%d" % i for i in range(6)] + [s + str(i) for s in ("fa", "fb") for i in range(24)]
+              + ["d%d" % i for i in range(40)])
 
-LOADS = "<yz0@0 <yG@0 <yixi@0 <yxb@0 <ylki@0 <ylki@1024 <ylki@1536"
-S_TURN = ("sDG_1@0 sDG_1@1024 sAG_1@0 sAG_1@512 sAG_1@1024 sAG_1@1536 sx_0@0 sx_0@1024 sLg_0@0 sLg_0@1024 sLg_1@0 sLg_1@1024 "
-          "sAy_0@0 sAy_0@1024 sAy_1@0 sAy_1@1024 sAy_1@1536")
-V_TURN = "vDG_0@0 vDG_0@1024 vJu_0@0 vJu_1@0 vx_1@0 vDy_0@0 vDy_0@1024 vDy_1@0 vDy_1@1024 vDy_1@1536"
-Z_TURN = "vx_1@0 vmx_0@0 vx_1@1024 vmx_1@0 vDy_0@0"
-TURNS = ((LOADS, S_TURN, V_TURN, Z_TURN), (S_TURN, V_TURN, Z_TURN),
-         (S_TURN, V_TURN + " vmx_1@0", "vI@2 vL@1", "vzs2@0 vzs2@128 vI@3"))
-HALVES = ((0, 64), (64, 128))
-LAST = ((0, 64), (64, 96), (96, 128))
-FOLDS = ((1, 2), (1, 2), (2, 2))
+LOADS = "<yz0@0 <yG@176 <yixi@0 <yxb@0 <ylki@0 <ylki@1024 <ylki@1536"
+S_TURN = ("sDG_1@0 sDG_1@1024 sAG_1@0 sAG_1@512 sAG_1@1024 sAG_1@1536 sx_0@0 sLg_0@0 sLg_0@1024 sLg_1@1024 sLg_1@0 "
+          "sy1@1024")
+V_TURN = "vDG_0@0 veu@0 vkm_1@0 vx_1@0 vDy_0@0 vDy_0@1024 vDy_1@0"
+Z_TURN = "vx_1@0 vmx_0@0 vmx_0@1024 vx_1@1024 vmx_1@0 vmx_1@1024 vdz@0 vzs0@128 vzs1@128 vDy_0@0"
+FIRST = (S_TURN.replace("sLg_0@0", "sx_1@1024 sLg_0@0").replace("sLg_1@0", "sLg_1@512"),
+         V_TURN.replace("vx_1@0 vDy_0@0", "vx_0@1536 vx_1@0 vmx_0@0 vmx_0@1024 vmx_1@0 vmx_1@1024 vzs0@128 vLg_1@0 vDy_0@0"))
+TURNS = ((LOADS,) + FIRST, (S_TURN, V_TURN, Z_TURN),
+         (S_TURN, V_TURN, "vx_1@0 vx_1@1024 vDy_0@0", "vDy_1@0 vAy_1@0 vsm@0", "vI@0 vch@128", "vI@2 vL@1", "sAdE@0 sLg_1@0",
+          "sAdE@328 sLg_1@0", "sy1@1024 sAy_1@1024 sAy_1@1536 snrx@0") + tuple("vAy_1@0 vmx_1@%d" % c for c in range(0, 2048, 512)))
 
 
 def R(buf, a=0, b=None, step=1, p=128, p0=0):
@@ -106,13 +128,19 @@ def ind(win, off):
     return IndOp((win, off))
 
 
-def build():
+def build(case={}):
     ops, now = [], [-1]
+    CYC, GAT, SCA, _w, FIX, SFIX, TCYC, DLAT, DRATE, RLAT, FLAT0, FLAT1, RCOST = [case.get(x, TIMES[x]) for x in TIMES]
 
     def add(q, kind, calls, reads, writes, cost, lat=0.0, **kw):
         r = (writes or reads)[0]
         ops.append(dict(q=q, kind=kind, calls=calls, reads=reads, writes=writes, cost=cost, lat=lat, i=len(ops), t=now[0],
                         name="%s%s@%d" % (q, r[0], r[1]), **kw))
+
+    def join():
+        o = ops.pop()
+        for part in ("calls", "reads", "writes", "cost"):
+            ops[-1][part] = ops[-1][part] + o[part]
 
     def flat(x):
         if isinstance(x, IndOp):
@@ -142,19 +170,23 @@ def build():
     def select(out, in_, pattern, base, cm):
         add("g", "select", [(out, in_, pattern, base, cm)], [in_], [out], 170 + 2 * width(out) * CYC)
 
-    def C(eng, out, in_):
-        if eng == "v":
-            V("tensor_copy", out, in_)
-        elif eng == "s":
-            S(out, in_, F.Copy)
-        else:
+    def C(eng, out, in_, by=None, plus=None):
+        if eng == "s":
+            S(out, in_, F.Copy, plus, by)
+        elif eng == "g":
             select(out, in_, [[0, width(out)]], 0, 0)
+        elif by is not None:
+            V("tensor_scalar", out, in_, by, plus or 0.0, A.mult, A.add)
+        elif plus is not None:
+            V("tensor_scalar", out, in_, plus, None, A.add)
+        else:
+            V("tensor_copy", out, in_)
 
     def P(items):
         c = 0.0
         rd, wr = [], []
         for o, l, r, a, b in items:
-            c += max(min(64, width(l)), width(r)) * TCYC + 5
+            c += max(min(64, width(l)), width(r)) * TCYC * (4 if DTYPE[l[0]] == _F else 1) + 5
             for x in (l, r):
                 if x not in rd:
                     rd.append(x)
@@ -168,335 +200,428 @@ def build():
     def iota(out, pattern, base, cm):
         add("g", "iota", [(out, pattern, base, cm)], [], [out], 130 + 2 * width(out) * CYC)
 
-    def dma(q, out, in_, nbytes, sem):
+    def dma(q, out, in_, nbytes):
         rd = [in_] if isinstance(in_, tuple) else []
         wr = [out] if isinstance(out, tuple) else []
-        add(q, "dma", [(out, in_)], rd, wr, 60, DLAT + nbytes * 128 / DRATE, sem=sem, hold=nbytes * 128 / DRATE if nbytes > 32 else 0)
+        add(q, "dma", [(out, in_)], rd, wr, 60, DLAT + nbytes * 128 / DRATE,
+            sem="d%d" % sum(o["kind"] == "dma" for o in ops), hold=nbytes * 128 / DRATE if nbytes > 32 else 0)
 
     def fill(out, value):
-        S(out, R("ZQ", 400, 400 + width(out)), F.Copy, value)
+        S(out, R("ZQ", 400, 400 + width(out), 1, out[4], out[5]), F.Copy, value)
 
-    dma("y", R("z0", 0, 128), R("zc", 128, 256), 256, "d0")
-    dma("s", R("z0", 128, 256), R("zc", 0, 128), 256, "d12")
-    dma("s", R("wti", 0, 1), "wt", 4, "d1")
-    dma("s", R("hki", 0, 2), "hk", 8, "d2")
-    dma("y", R("G", 0, 1024), "gi", 2048, "d3")
-    dma("y", R("ixi", 0, 1024), "ix", 4096, "d4")
-    dma("y", R("xb", 0, 2048), "xc", 4096, "d5")
-    dma("s", R("thi", 0, 2), "th", 8, "d6")
-    dma("y", R("lki", 0, 1024), R("lk", 0, 1024), 4096, "d7")
-    dma("y", R("lki", 1024, 1536), R("lk", 1024, 1536), 2048, "d11")
-    dma("y", R("lki", 1536, 2048), R("lk", 1536, 2048), 2048, "d14")
+    tab = lambda buf, n, a=0: R(buf, DUMP + a, DUMP + n)
+    dma("y", R("z0", 0, 128), R("zc", 128, 256), 256)
+    dma("s", R("z0", 128, 256), R("zc", 0, 128), 256)
+    dma("s", R("wti", 0, 1), "wt", 4)
+    dma("s", R("hki", 0, 2), "hk", 8)
+    dma("y", tab("G", 1024), "gi", 2048)
+    dma("y", R("ixi", 0, 1024), "ix", 4096)
+    dma("y", R("xb", 0, 2048), "xc", 4096)
+    dma("s", R("thi", 0, 2), "th", 8)
+    dma("y", R("lki", 0, 1024), R("lk", 0, 1024), 4096)
+    dma("y", R("lki", 1024, 1536), R("lk", 1024, 1536), 2048)
+    dma("y", R("lki", 1536, 2048), R("lk", 1536, 2048), 2048)
     iota(R("pI", 0, 1), [[0, 1]], 0, 1)
     iota(R("g8I", 0, 16), [[0, 2], [1, 8]], 0, 0)
     iota(R("dI", 0, 144), [[1, 144]], 0, -1)
     iota(R("gI", 0, 128), [[1, 8], [0, 16]], 0, 0)
     iota(R("rI", 0, 128), [[0, 8], [1, 16]], 0, 0)
     iota(R("r15I", 0, 128), [[0, 8], [-1, 16]], 15, 0)
-    iota(R("duI", 0, 16), [[0, 4], [-16, 4]], 0, 0)
     iota(R("dg4", 0, 128), [[4, 8], [0, 16]], 0, -1)
     iota(R("slI", 0, 16), [[1, 2], [4, 8]], 0, -1)
     for q in range(4):
         a, n = SEG[q], 16 * (q + 1)
-        iota(R("qrel", a, a + n), [[0, n]], q, 0)
+        iota(R("qrel", a, a + n + 1), [[0, n + 1]], q, 0)
         iota(R("dcol", a, a + n), [[1, n]], -16 * q, 0)
-        iota(R("SM", a, a + n), [[-1, n]], 1, 0)
+        if q % 2:
+            iota(R("dcol", a - 1, a + n + 1, n + 1), [[0, 2]], 0, 0)
+        iota(R("SM", a, a + n), [[-4096, n]], 4096, 0)
+        iota(R("SM", a + n, a + n + 1), [[0, 1]], 16 * q, 1)
     for a in range(0, 2048, 512):
-        V("memset", R("MR", a, a + 512), 1.0)
-        select(R("SEL", a, a + 512), R("MR", a, a + 512), [[-256, 4], [-16, 8], [255, 16]], -2 * a, 1)
-        select(R("EN", a, a + 512), R("MR", a, a + 512), [[1, 32], [0, 16]], a // 16, -1)
-    c1 = lambda b: R(b, 0, 1)
+        if a < 1024:
+            V("memset", R("MR", a, a + 512), 1.0)
+        select(R("SEL", a, a + 512), R("MR", 0, 512), [[-256, 4], [-16, 8], [255, 16]], -2 * a, 1)
+    for a, b, e in CFG["y"]:
+        if e == "s":
+            iota(R("Dy_%d" % (a // 128), 16 * (a % 128), 16 * (a % 128 + b - a)), [[0, 16 * (b - a)]], -int(UP), 0)
+    COL = ("pf", "pg", "p16", "p4", "b4")
+    c1 = lambda b: R("pf", COL.index(b)) if b in COL else R(b, 0, 1)
     ts, tt, tc, scan = "tensor_scalar", "tensor_tensor", "tensor_copy", "tensor_tensor_scan"
     I16, IB, ISH = R("IW", 4, 132), R("IB", 4, 132), R("IW", 5, 133)
-    In, I1n, I2n = R("In", 0, 128), R("I1n", 0, 128), R("I2n", 0, 128)
-    V("memset", R("MR", 0, 2048, 16), 0.0)
-    V(ts, c1("pgi"), c1("pI"), 4, None, A.arith_shift_right)
-    V(tc, c1("pg"), c1("pgi"))
-    V(tc, c1("wf"), c1("wti"))
-    V(ts, R("W8", 0, 8), R("g8I", 0, 8), c1("pg"), c1("wf"), A.is_equal, A.mult)
-    for j, (col, bits) in enumerate(((0, 31), (0, 992), (1, 63), (1, 1984))):
+    In, I2n = R("In", 0, 128), R("I2n", 0, 128)
+    Q16 = R("ZQ", 72, 80)
+    V("memset", R("MR", 0, 1024, 16), 0.0)
+    V(ts, R("pI", 1), c1("pI"), 4, None, A.arith_shift_right)
+    V(ts, R("pI", 2), c1("pI"), 15, None, A.bitwise_and)
+    V(ts, R("pI", 3), c1("pI"), 3, None, A.bitwise_and)
+    V(ts, R("pI", 4), c1("pI"), 2, 3, A.arith_shift_right, A.bitwise_and)
+    V(tc, R("pf", 0, 5), R("pI", 0, 5))
+    iota(R("EN", 0, 512), [[1, 32], [0, 16]], 0, 0)
+    V(ts, R("pI", 5), c1("pI"), 31, None, A.bitwise_and)
+    V(tc, c1("p32"), R("pI", 5))
+    V(ts, R("EN", 0, 512), R("EN", 0, 512), c1("p32"), None, A.is_equal)
+    for name, by, plus in (("OFF0", 0.0, None), ("OFFR", None, None), ("OF15", 16.0, 15.0), ("OFF2", 2.0, None)):
+        C("s", R(name, 0, 8), R("g8I", 0, 8), by, plus)
+    V(ts, R("BLK", 8, 24), R("g8I", 0, 16), c1("pg"), None, A.is_equal)
+    S(R("BLK", 0, 8), R("BLK", 8, 16), F.Copy, None, 32768.0)
+    V(tt, R("W8", 0, 16), ind(c1("wti"), c1("OFF0")), R("BLK", 8, 24), A.mult)
+    for j, (col, bits) in enumerate(((0, 1023), (1, 63), (1, 1984))):
         V(ts, R("hI", j, j + 1), R("hki", col, col + 1), bits, None, A.bitwise_and)
-    V(tc, R("hf", 0, 4), R("hI", 0, 4))
+    V(tc, R("hf", 0, 3), R("hI", 0, 3))
     V("memset", R("ZQ", 0, 528), 0.0)
     V(ts, R("ZQ", 72, 80), R("g8I", 0, 8), c1("pg"), None, A.is_equal)
     V(ts, R("ZQ", 200, 208), R("g8I", 0, 8), c1("pg"), -0.0625, A.is_equal, A.mult)
-    fill(R("ZQ", 320, 321), 1088.0)
     fill(R("ZQ", 392, 393), 2176.0)
     fill(R("UH", 64, 66), 1024.0)
     V(ts, R("BHn", 0, 128), R("gI", 0, 128), c1("pg"), -1.0, A.is_equal, A.mult)
-    V(ts, c1("p16i"), c1("pI"), 15, None, A.bitwise_and)
-    V(tc, c1("p16"), c1("p16i"))
-    V(tc, c1("pf"), c1("pI"))
     V(ts, R("IW", 0, 136), R("dI", 0, 136), 4.0, None, A.is_equal)
-    V(ts, R("BLK", 0, 8), R("g8I", 0, 8), c1("pg"), 32768.0, A.is_equal, A.mult)
-    V(ts, R("BLK", 8, 16), R("g8I", 0, 8), c1("pg"), None, A.is_equal)
-    V(ts, R("Q16", 0, 8), R("g8I", 0, 8), c1("pg"), None, A.is_equal)
     V(ts, R("MK", 0, 128), R("rI", 0, 128), c1("p16"), None, A.is_equal)
-    V(tc, R("OFFR", 0, 8), R("g8I", 0, 8))
     V(ts, c1("colA"), c1("pf"), 64.0, 0.5, A.is_ge, A.mult)
     V(ts, c1("colB"), c1("pf"), 64.0, -4096.0, A.is_lt, A.mult)
+    V(ts, c1("colC"), c1("pf"), 64.0, -8 * 16 * UP - 4096.0, A.is_lt, A.mult)
     fill(R("ON64", 0, 128), 64.0)
-    V(ts, R("CD", 0, 128), R("rI", 0, 128), c1("colA"), c1("colB"), A.mult, A.add)
+    for h, col in enumerate(("colC", "colB")):
+        V(ts, R("CD", 128 * h, 128 * h + 128), R("rI", 0, 128), c1("colA"), c1(col), A.mult, A.add)
     V(ts, R("MMIN", 0, 128), R("rI", 0, 128), 0.0, BIG, A.is_equal, A.mult)
-    for name, by in ((In, -1.0), (I1n, -1024.0)):
-        V(ts, name, R("dI", 0, 128), 0.0, by, A.is_equal, A.mult)
-    for name, by in ((I2n, -2048.0), (R("Ih", 0, 128), 0.5), (R("Ic", 0, 128), 1.0 / 128)):
+    V(ts, In, R("dI", 0, 128), 0.0, -1.0, A.is_equal, A.mult)
+    for name, by in ((I2n, -2048.0), (R("Ih", 0, 128), 0.5), (R("Ic", 0, 128), 1.0 / 128), (R("IBn", 0, 128), -1.0)):
         S(name, I16, F.Copy, None, by)
+    if any(CFG["packed"]):
+        for name in ("I64", "SK"):
+            S(R(name, 0, 128), I16, F.Copy, None, 65536.0)
+        S(R("SK", 128, 256), R("BHn", 0, 128), F.Copy)
 
-    def factors(j, name, square, const):
-        for i in (2 * j, 2 * j + 1):
-            V(ts, R("dg%d" % i, 0, 128), I16, R("hf", i, i + 1), None, A.mult)
+    def factors(j, name, rows):
         for h in (0, 1):
             o = R("b%d" % (4 + h), 128 * j, 128 * j + 128, 1, 65)
-            rows = ((72 - 8 * h, R("dg%d" % (2 * j), 0, 128)), (24 - 8 * h, R("dg%d" % (2 * j + 1), 0, 128)),
-                    (200 - square - 8 * h, R("BHn", 0, 128)), (const - 64, I16))
-            group([(o, R("ZQ", a, a + 65), r) for a, r in rows])
+            group([(o, R("ZQ", a - s * h, a - s * h + 65), r) for a, s, r in rows])
             S(R(name + str(h), 0, 128, 1, 65), o, F.Copy)
-    factors(0, "PM_", 32, 320)
-    factors(1, "PQ_", 16, 392)
-    C("s", R("I", 0, 1024), R("ixi", 0, 1024))
-    for e, a, b in (("g", 0, 1024), ("g", 1024, 1536), ("s", 1536, 2048)):
-        C(e, R("L", a, b), R("lki", a, b))
+    for i in range(3):
+        V(ts, R("dg%d" % i, 0, 128), I16, R("hf", i, i + 1), None, A.mult)
+    factors(0, "PM_", ((72, 8, R("dg0", 0, 128)), (168, 8, R("BHn", 0, 128))))
+    factors(1, "PQ_", ((72, 8, R("dg1", 0, 128)), (24, 8, R("dg2", 0, 128)), (184, 8, R("BHn", 0, 128)), (328, 0, I16)))
+    C("g", tab("I", 1024), R("ixi", 0, 1024))
     V(ts, R("IB", 0, 136), R("dI", 0, 136), 4.0, None, A.is_equal)
     V(ts, R("BBn", 0, 128), R("gI", 0, 128), c1("pg"), -1.0, A.is_equal, A.mult)
     S(R("BL1", 0, 8), R("BLK", 8, 16), F.Copy, None, -1.0)
     S(R("BL2", 0, 8), R("BLK", 8, 16), F.Copy, None, 2.0)
-    fill(R("x_0", 2048, 2064), 0.0)
-    fill(R("x_1", 2048, 2064), 0.0)
-    V(ts, R("CS", 0, 128), R("r15I", 0, 128), c1("colA"), c1("colB"), A.mult, A.add)
+    for buf in ("x_0", "x_1") + (("XG_0", "XG_1") if any(CFG["packed"]) else ()):
+        fill(R(buf, 2048, 2064), UP)
+    V(ts, R("CS", 0, 128), R("r15I", 0, 128), c1("colA"), c1("colC"), A.mult, A.add)
+    fill(R("CS", 15, 128, 16, 64), -4096.0)
     V(ts, R("MMAX", 0, 128), R("rI", 0, 128), 0.0, -BIG, A.is_equal, A.mult)
     V(tc, R("tf", 0, 2), R("thi", 0, 2))
     DOWN = -0.5 + 2.0 ** -12
-    fill(R("ONn", 0, 128), -0.5)
-    fill(R("ONk", 0, 128), -0.5 / 1024)
-    fill(R("b0", 32, 33), DOWN)
+    fill(R("ONf", 0, 128), -1.0 / 32)
+    fill(R("UPn", 0, 128), -UP)
     V(ts, c1("m15"), c1("p16"), 15.0, -1.0 / 64, A.is_lt, A.mult)
-    V(ts, c1("acol"), c1("tf"), 1.5, c1("m15"), A.add, A.mult)
-    V(ts, c1("acol"), c1("acol"), 1.0 / 64, None, A.add)
-    V(ts, R("CS", 128, 256), I16, c1("acol"), None, A.mult)
-    V(ts, c1("q2i"), c1("pI"), 3, None, A.bitwise_and)
-    V(ts, c1("bI"), c1("p16i"), 2, None, A.arith_shift_right)
-    V(ts, c1("pk1"), c1("q2i"), 8.0, 8.0, A.mult, A.add)
-    V(ts, c1("pk2"), c1("q2i"), 2.0, c1("pk1"), A.add, A.mult)
-    V(ts, c1("pk4"), c1("bI"), 160.0, c1("pk2"), A.mult, A.add)
-    V(ts, R("PK", 0, 1), c1("pk4"), -1.0, None, A.add)
-    V(ts, R("DUn", 0, 16), R("duI", 0, 16), c1("p16"), None, A.subtract)
-    V(ts, R("DUE", 0, 16), R("DUn", 0, 16), -1.0, 1024.0, A.mult, A.add)
-    V(ts, c1("k15"), c1("p16"), -1.0, 15.0, A.mult, A.add)
-    V(ts, R("DUJ", 0, 16), R("DUn", 0, 16), -1.0, 2048.0, A.mult, A.add)
+    V(ts, c1("acol"), c1("tf"), c1("m15"), None, A.mult)
+    for h in (0, 1):
+        V(ts, R("CB", 128 * h, 128 * h + 128), I16, R("tf", 1), -1.0 / 64, A.mult, A.mult)
+    V(ts, R("CS", 128, 256), I16, c1("acol"), -16 * UP / (64 * 128), A.mult, A.add)
+    V(ts, c1("pk1"), c1("p4"), 8.0, 25.0, A.mult, A.add)
+    V(ts, c1("pk2"), c1("p4"), c1("pk1"), 16.0, A.mult, A.add)
+    V(ts, R("PK", 0, 1), c1("b4"), float(BW), c1("pk2"), A.mult, A.add)
+    V(ts, R("PK", 2, 3), R("PK", 0, 1), 2.0 * BW - 1, None, A.min)
+    C("s", c1("k15"), c1("p16"), -1.0, 15.0)
     V(ts, R("RPJ", 0, 128), R("dg4", 0, 128), 0.0, -1.0, A.is_equal, A.mult)
     V(ts, R("RPK", 0, 128), R("dg4", 0, 128), -2.0, None, A.is_equal)
     V(ts, R("SLW", 0, 16), R("slI", 0, 16), 0.0, None, A.is_equal)
-    V(ts, R("OF15", 0, 8), R("g8I", 0, 8), 16.0, 15.0, A.mult, A.add)
+    V(ts, R("dl", 0, BW), R("dcol", 0, BW), c1("pf"), -1.0, A.subtract, A.max)
+    for b in range(6):
+        V(ts, R("EE", BW * b, BW * b + BW), R("qrel", 0, BW), 4.0 * (b if b < 2 else b - 2), c1("pg" if b < 2 else "pf"), A.add, A.is_equal)
     for b in range(2):
-        V(ts, R("E2", 160 * b, 160 * b + 160), R("qrel", 0, 160), 4.0 * b, c1("pg"), A.add, A.is_equal)
-        V(ts, R("TR", 160 * b, 160 * b + 160), R("dcol", 0, 160), c1("pf"), 16384.0, A.is_ge, A.mult)
-        V(ts, R("TS", 160 * b, 160 * b + 160), R("dcol", 0, 160), c1("pf"), -20480.0, A.is_equal, A.mult)
-    for b in range(4):
-        V(ts, R("EC", 160 * b, 160 * b + 160), R("qrel", 0, 160), 4.0 * b, c1("pf"), A.add, A.is_equal)
-    V(tc, R("SM", 160, 320), R("SM", 0, 160))
+        for c in (2 * b, 2 * b + 1):
+            C("v", R("TT", BW * c, BW * c + BW), R("dl", 0, BW), *((2048.0, 2048.0), (-4096.0, -2048.0))[b])
+    for q in range(4):
+        a = SEG[q] + 16 * (q + 1)
+        C("s", R("EE", a, 6 * BW, BW), R("EE", a, 6 * BW, BW), 1.0 / 4096)
+        fill(R("TT", a, 4 * BW, BW), DUMP / 4096)
+    V(tc, R("SM", BW, 2 * BW), R("SM", 0, BW))
     fill(R("QT", 1, 64, 2), 0.0)
     S(R("BKn", 0, 16), R("BLK", 0, 16), F.Copy, None, -1.0)
     S(R("BK2", 0, 16), R("BLK", 0, 16), F.Copy, None, 2.0)
-    V(ts, R("PK", 2, 3), c1("pk4"), -1.0, 319.0, A.add, A.min)
-    fill(R("aJ", 16, 24), 0.0)
-    V(ts, R("OFF2", 0, 8), R("g8I", 0, 8), 2.0, None, A.mult)
 
-    def keys(K, n, m, a, con, payload, cuts, d=None):
+    def keys(K, at, n, m, a, con, payload, cuts, d, alone):
         def sums(src, by, lo, hi, last):
-            P([(R(K, k, n, 16, hi, lo), R(src, 16 * lo + k, 16 * hi, 16), R(by, 0, n // 16), False, last and k == m - 1) for k in range(m)])
-        pay = (R(K, 0, 128), payload, I16, False, bool(d))
-        P([(R(K, 0, n), R("ON64", 0, 128), R(con, 0, n), True, False)] + ([] if d else [pay]))
+            P([(R(K, at + k, at + n, 16, hi, lo), R(src, 16 * lo + k, 16 * hi, 16), R(by, 0, n // 16), False, last and k == m - 1)
+               for k in range(m)])
+            ops[-1]["name"] = "t" + src
+        pay = (R(K, at, at + 128), payload, I16, False, bool(d))
+        P([(R(K, at, at + n), R("ON64", 0, 128), con, alone, False)] + ([] if d else [pay]))
         for lo, hi in cuts:
             if d:
                 sums(d, "BKn", lo, hi, False)
             sums(a, "BK2" if d else "BLK", lo, hi, not d)
         if d:
             P([pay])
+            ops[-1]["writes"] = [R(K, at, at + n)]
 
     def earlier(h, own, spread, pick, row, p, Ad, ms, links):
-        D = "b%d" % (4 + h)
-        items = [(R(D, 0, 320), R("MK", 0, 128, 1, 16), R(c, 0, 320, 1, 16), c == "TR", False) for c in (("TR", "TS") if links else ("TR",))]
-        rows = [(160 * b + SEG[q], 16 * (q + 1), 64 * b) for b in (0, 1) for q in range(4)]
-        P(items + [(R(D, a, a + n), pick, R(row, 128 * h + l, 128 * h + l + n, 1, p), False, False) for a, n, l in rows])
+        D, W = "b%d" % (4 + h), 2 * BW
+        rows = [(BW * b + SEG[q], 16 * (q + 1), 64 * b) for b in (0, 1) for q in range(4)]
+        P([(R(D, 0, W), R("MK", 0, 128, 1, 16), R("TT", W * links, W * links + W, 1, 16), True, False)] +
+          [(R(D, a, a + n), pick, R(row, 128 * h + l, 128 * h + l + n, 1, p), False, False) for a, n, l in rows])
+        ops[-1]["name"] = "t%s%d" % (Ad, h)
         if links:
             P([(R(D, a, a + n), R("nrx", 128 * h, 128 * h + 128), R("I2n", l, l + n), False, False) for a, n, l in rows])
-        P([(R(D, 0, 320), own, spread, False, True)])
-        S(R(Ad, 320 * h, 320 * h + 320), R(D, 0, 320), F.Abs, 2048.0 if links else None)
-        V(scan, R(ms, 320 * h, 320 * h + 320), R("SM", 0, 320), R(Ad, 320 * h, 320 * h + 320), 0.0, A.max, A.min)
+        P([(R(D, 0, W), own, spread, False, True)])
+        S(R(Ad, W * h, W * h + W), R(D, 0, W), F.Abs, None, 4096.0)
+        V(scan, R(ms, W * h, W * h + W), R("SM", 0, W), R(Ad, W * h, W * h + W), 0.0, A.max, A.min)
 
-    def scatter(table, n, off, a, b):
+    def scatter(table, n, off, a, b, far=8):
         for k in (1, 0, 3, 2):
-            V(tt, ind(R(table, 0, n), R(off, 4 * k, 4 * k + 4)), R(a, 64 * k, 64 * k + 64), R(b, 64 * k, 64 * k + 64), A.add)
+            o = far * (k // 2) + 4 * (k % 2)
+            V(tt, ind(R(table, 0, DUMP + n), R(off, o, o + 4)), R(a, 64 * k, 64 * k + 64), R(b, 64 * k, 64 * k + 64), A.add)
             ops[-1]["name"] = "v%s@%d" % (table, k)
+
+    def repack(out, src, op):
+        for c in range(0, 2048, 512):
+            group([(R("b6", 0, 512), R("I64", 0, 128), R("xb", c, c + 512))])
+            V(tt, tab(out, c + 512, c), R(src[0], src[1] + c, src[1] + c + 512), R("b6", 0, 512), op)
 
     RLu = R("RLu", 0, 128, 1, 65)
     for t in range(3):
         now[0] = t
+        packed = CFG["packed"][t]
         z, zx = "z%d" % t, "zx%d" % (t % 2)
         half = lambda buf, h, at=0: R(buf, at + 128 * h, at + 128 * h + 128)
-        P([(R("b0", 8 * h, 8 * h + 8), half(z, h), R("W8", 0, 8), True, True) for h in (0, 1)])
+        up = lambda h: half(z if t else "zt", h)
+
+        def far(h, x):
+            o = half(FB[h], h) if t == 2 else R("b1", 0, 256)
+            P([(o, R("ON64", 0, 128), R("CB", 0, width(o)), True, False)] * (t == 2 or h == 0) +
+              [(half(FB[h], h), up(h), R("BBn", 0, 128), False, False)])
+            P([(R(FB[h], 128 * h + k, 128 * h + 128, 16), R(x, k, 2048, 16), R("BL1", 0, 8), False, False) for k in range(16)])
+        FB = ("b1", "b0" if t == 2 else "b1")
+        for h in (0, 1):
+            group([(R("b0", 8 * h, 8 * h + 8), l, R("W8", 0, 8)) for l in ([R("UPn", 0, 128)] if t else []) + [half(z, h)]])
         C("s" if t else "v", R("ui", 0, 16), R("b0", 0, 16))
         V(ts, R("ui", 0, 16), R("ui", 0, 16), 4095, None, A.bitwise_and)
-        V(tt, R("uu", 0, 16), R("ui", 0, 16), R("ui", 0, 16), A.mult)
+        if CFG["uu"][t] == "s":
+            S(R("uu", 0, 16), R("ui", 0, 16), F.Square)
+        else:
+            V(tt, R("uu", 0, 16), R("ui", 0, 16), R("ui", 0, 16), A.mult)
         V(ts, R("UQ", 0, 16), R("ui", 0, 16), 2047, None, A.bitwise_and)
         V(ts, R("UQ", 48, 64), R("ui", 0, 16), 31, None, A.bitwise_and)
         V(ts, R("UQ", 16, 32), R("uu", 0, 16), 4, 2047, A.arith_shift_right, A.bitwise_and)
         V(ts, R("UQ", 32, 48), R("uu", 0, 16), 5, 1023, A.arith_shift_right, A.bitwise_and)
-        C("s" if t else "v", R("UH", 0, 64), R("UQ", 0, 64))
+        C(CFG["UH"] if t else "v", R("UH", 0, 64), R("UQ", 0, 64))
         group([(R("b0", 128, 256, 1, 65), R("UH", 0, 65), I16)])
         S(RLu, R("b0", 128, 256, 1, 65), F.Copy)
         P([(half("b0", h, 256), R("PM_%d" % h, 0, 128, 1, 65), RLu, True, True) for h in (0, 1)])
-        S(R("q1", 0, 256), R("b0", 256, 512), F.Identity if t else F.Copy, c1("Nb") if t else DOWN, 1.0 / 1024)
-        P([(R("b3", 256, 512), I1n, R("q1", 0, 256), True, False)] +
-          [(half("b3", h, 256), R("PM_%d" % h, 0, 128, 1, 65), RLu, False, h == 1) for h in (0, 1)])
-        S(R("emu", 0, 256), R("b3", 256, 512), F.Identity if t else F.Copy, c1("Nc") if t else None)
-        C("g", R("emh", 0, 256), R("emu", 0, 256))
+        for h in (0, 1):
+            if t and CFG["emi"][h] == "s":
+                S(half("emi", h), half("b0", h, 256), F.Identity, c1("Nc"))
+            elif t:
+                V(ts, half("emi", h), half("b0", h, 256), R("b0", 16), R("b0", 17), A.add, A.add)
+                ops[-1]["name"] = "vsum%d" % h
+            else:
+                C("vs"[h], half("emi", h), half("b0", h, 256))
+            V(ts, half("emi", h), half("emi", h), 1023, None, A.bitwise_and)
+            C(CFG["emu"][h], half("emu", h), half("emi", h))
+        C("g", R("emh", 0, 256), R("emi", 0, 256))
         if t == 0:
-            for m in range(16):
-                C("v" if m < 11 else "s", R(zx, m, 4096, 16), R(z, 0, 256))
+            C("v", R("zt", 0, 256), R(z, 0, 256), None, UP)
+            for m, e in enumerate(CFG["z0"]):
+                if e in "vs":
+                    C(e, R(zx, m, 4096, 16), R("zt", 0, 256))
+                else:
+                    C(e.lower(), R(zx, m, 2048, 16), half("zt", 0))
+                    C("g", R(zx, 2048 + m, 4096, 16), half("zt", 1))
         else:
             for h in (0, 1):
                 for m in range(16):
-                    C("s" if h == 0 and m >= 14 else "g", R(zx, 2048 * h + m, 2048 * h + 2048, 16), half(z, h))
+                    C("s" if h == 0 and m >= 16 - CFG["zs"] else "g", R(zx, 2048 * h + m, 2048 * h + 2048, 16), half(z, h))
+                    if m % 2 and ops[-1]["q"] == "g":
+                        join()
+        if t == 1:
+            C("v", R("zr", 0, 256), R(z, 0, 256), None, -UP)
         for h in (0, 1):
-            H, K = "_%d" % h, "b%d" % (2 + h)
-            if h == 1:
+            H = "_%d" % h
+            if h == 1 and t:
                 group([(R("b0", 128, 256), half(z, h), IB)])
                 S(R("zT", 0, 128), R("b0", 128, 256), F.Copy, None, -1.0)
-            for a, b in HALVES:
-                got, d = ind(R("G", 0, 1024), R("emu", 128 * h + a, 128 * h + b)), R("DG" + H, 16 * a, 16 * b)
+            for a, b in CFG["g"][h]:
+                got, d = ind(tab("G", 1024), R("emu", 128 * h + a, 128 * h + b)), R("DG" + H, 16 * a, 16 * b)
                 if h == 0:
                     V(tt, d, got, R(zx, 16 * a, 16 * b), A.subtract)
-                    V(ts, R("AG" + H, 16 * a, 16 * b), d, 0.0, None, A.max)
+                    V(ts, R("AG" + H, 16 * a, 16 * b), d, -UP, UP, A.max, A.add)
                 else:
                     S(d, got, F.Copy)
                     for c in range(16 * a, 16 * b, 512):
-                        o = R("b%d" % (4 + c // 512 % 2), 0, 512)
-                        group([(o, IB, R("DG" + H, c, c + 512)), (o, R("zT", 0, 128), R("EN", c, c + 512))])
-                        S(R("AG" + H, c, c + 512), o, F.Abs)
-            keys(K, 128, 16, "AG" + H, "CD", half("emh", h), ((0, 128),), None if h else "DG_0")
-            V(scan, R("km" + H, 0, 128), R("MMIN", 0, 128), R(K, 0, 128), 0.0, A.add, A.min)
+                        o, l = R(CFG["sub"][c // 512], 0, 512), c // 16
+                        P([(o, R("zT", 0, 128, 1, l + 32, l), R("EN", 0, 512, 1, l + 32, l), True, False) if t else
+                           (o, R("IBn", 0, 128), R(zx, 2048 + c, 2048 + c + 512), True, False)])
+                        P([(o, IB, R("DG" + H, c, c + 512), False, True)])
+                        S(R("AG" + H, c, c + 512), o, F.Abs, UP)
+            keys("b%d" % (2 + h), 0, 128, 16, "AG" + H, half("CD", h), half("emh", h), ((0, 128),), None if h else "DG_0", True)
+            V(scan, R("km" + H, 0, 128), R("MMIN", 0, 128), R("b%d" % (2 + h), 0, 128), 0.0, A.add, A.min)
             V(ts, R("ej" + H, 0, 8), R("km" + H, 15, 128, 16), 1023, None, A.bitwise_and)
             V(tt, R("ME" + H, 0, 128), ind(R("ej" + H, 0, 8), R("OFFR", 0, 8)), R("MK", 0, 128), A.mult)
-            group([(R("b7", 8 * h, 8 * h + 8), R("ME" + H, 0, 128), R("Q16", 0, 8))])
-            V(tc, R("eu", 8 * h, 8 * h + 8), R("b7", 8 * h, 8 * h + 8))
-            V(tc, R("Ju" + H, 0, 128), ind(R("I", 0, 1024), R("eu", 8 * h, 8 * h + 8)))
+            group([(R("b7", 8 * h, 8 * h + 8), R("ME" + H, 0, 128), Q16)])
+            C(CFG["eu"][h], R("eu", 8 * h, 8 * h + 8), R("b7", 8 * h, 8 * h + 8))
+            C(CFG["Ju"][h], R("Ju" + H, 0, 128), ind(tab("I", 1024) if t else R("ixi", 0, 1024), R("eu", 8 * h, 8 * h + 8)))
             C("g", half("Jh", h), R("Ju" + H, 0, 128))
             group([(half("b7", h, 256), R("ME" + H, 0, 128), I16)])
-        P([(half("b0", h, 256), R("PQ_%d" % h, 0, 128, 1, 65), RLu, True, True) for h in (0, 1)])
-        S(R("q2", 0, 256), R("b0", 256, 512), F.Copy, DOWN, 1.0 / 2048)
-        for h in (0, 1):
-            H = "_%d" % h
-            for a, b in HALVES:
-                C("sv"[h], R("x" + H, 16 * a, 16 * b), ind(R("xb", 0, 2048), R("Ju" + H, a, b)))
-            for a, b in HALVES:
-                S(R("Lg" + H, 16 * a, 16 * b), ind(R("L", 0, 2048), R("Ju" + H, a, b)), F.Copy)
-                o = R("b6", 128 * h + a, 128 * h + b)
-                group([(o, R("SEL", 128 * k, 128 * k + 128), R("Lg" + H, 16 * a + k, 16 * b, 16)) for k in range(16)])
-                V(tc, R("nu" + H, a, b), o)
-            for a, b in (HALVES, LAST)[h]:
-                d = R("Dy" + H, 16 * a, 16 * b)
-                V(tt, d, ind(R("xb", 0, 2048), R("nu" + H, a, b)), R("x" + H, 16 * a + 1, 16 * b + 1), A.subtract)
-                S(R("Ay" + H, 16 * a, 16 * b), d, F.Abs)
-            w = 2048 if t < 2 else 512
-            for c in range(0, 2048, w):
-                V(scan, R("mx" + H, c, c + w), R("MR", c, c + w), R("x" + H, c, c + w), 0.0, A.mult, A.max)
-            o = half("b0", h, 256)
-            group([(o, IB, half(z, h)), (o, IB, R("mx" + H, 15, 2048, 16))])
-            S(half("zt", h), o, F.Copy, 127.75, 0.5)
-            V(ts, half("zs%d" % t, h), half("zt", h), -128.0, None, A.add)
-            add("g", "remote", [(t, 128 * h, 128 * h + 128, "arr%d" % (2 * t + h))], [half("zs%d" % t, h)], [half("z%d" % (t + 1), h)], RCOST, RLAT)
-        V(tt, R("aE", 0, 16), R("b7", 0, 16), R("DUE", 0, 16), A.subtract)
-        S(R("Y", 0, 256), R("b7", 256, 512), F.Copy)
-        for h in (0, 1):
-            earlier(h, R("ME_%d" % h, 0, 128), R("E2", 0, 320), R("BHn", 0, 128), "Y", 128, "AdE", "msE", False)
-        V(tt, R("tE", 0, 16), ind(R("msE", 0, 640), R("PK", 0, 1)), R("aE", 0, 16), A.mult)
-        V(tt, R("oE", 0, 16), R("tE", 0, 16), R("DUE", 0, 16), A.add)
-        C("g", R("oEu", 0, 16), R("oE", 0, 16))
-        if t < 2:
-            V(tt, R("dz", 0, 256), ind(R("G", 0, 1024), R("eu", 0, 16)), R(z, 0, 256), A.subtract)
+        P([(half("b6", h, 256), R("PQ_%d" % h, 0, 128, 1, 65), RLu, True, True) for h in (0, 1)])
+        S(R("q2", 0, 256), R("b6", 256, 512), F.Copy, DOWN, 1.0 / 2048)
+        if t == 0 and any(CFG["packed"]):
+            repack("XL", ("lki", 0), A.add)
+        elif t == 0:
+            for a in (0, 1024):
+                C("g", tab("L", a + 1024, a), R("lki", a, a + 1024))
+        if t == 2 and packed:
+            repack("L", ("XL", DUMP), A.subtract)
         C("g", R("Jf", 0, 256), R("Jh", 0, 256))
         VJ = R("b2", 256, 512)
-        P([(VJ, I1n, R("q2", 0, 256), True, False), (VJ, I1n, R("q2", 0, 256), False, False)] +
+        P([(VJ, I2n, R("q2", 0, 256), True, False)] +
           [(half("b2", h, 256), R("PQ_%d" % h, 0, 128, 1, 65), RLu, False, False) for h in (0, 1)] +
           [(VJ, In, R("Jh", 0, 256), False, True)])
+        S(R("Y", 0, 256), R("b7", 256, 512), F.Copy)
+        def winners():
+            for h in (0, 1):
+                earlier(h, R("ME_%d" % h, 0, 128), R("EE", 0, 2 * BW), R("BHn", 0, 128), "Y", 128, "AdE", "msE", 0)
+            C(CFG["oE"][t], R("oEu", 0, 16), ind(R("msE", 0, 4 * BW), R("PK", 0, 1)))
+        if not CFG["late"][t]:
+            winners()
+        raw = "zr" if t else z
+        if t < 2:
+            V(tt, R("dz", 0, 256), ind(tab("G", 1024), R("eu", 0, 16)), R(raw, 0, 256), A.subtract)
+        for h in (0, 1):
+            H, K = "_%d" % h, "b%d" % (2 + h)
+            X = ("XG" if packed else "x") + H
+            for a, b, e in CFG["x" if t else "x0"][h]:
+                C(e, R(X, 16 * a, 16 * b), ind(R("xb", 0, 2048), R("Ju" + H, a, b)), None, UP)
+            if packed:
+                w = 2048 // CFG["casts"][t]
+                for c in range(0, 2048, w):
+                    dma("g", R("x" + H, c, c + w), R(X, c, c + w), 2 * w)
+                P([(R(K, 256 + k, 512, 16), R(X, k, 2048, 16), R("SK", k, 256, 16), k == 0, False) for k in range(16)])
+                C(CFG["r"][h], half("rd", h), R(K, 256, 384))
+                V(tt, half("Lh", h), R(K, 256, 384), half("rd", h), A.subtract)
+                group([(half("b6", h), half("Lh", h), I16)])
+                ops[-1]["name"] = "tnu%d" % h
+                C(CFG["nu"][h], R("nu" + H, 0, 128), half("b6", h))
+            else:
+                for a, b, e in CFG["l" if t else "l2"][h]:
+                    C(e, R("Lg" + H, 16 * a, 16 * b), ind(tab("L", 2048) if t else R("lki", 0, 2048), R("Ju" + H, a, b)))
+                for a, b in HALVES:
+                    o = R("b6", 128 * h + a, 128 * h + b)
+                    group([(o, R("SEL", 128 * k, 128 * k + 128), R("Lg" + H, 16 * a + k, 16 * b, 16)) for k in range(16)])
+                    C(CFG["nu"][h], R("nu" + H, a, b), o)
+                C("g", half("Lh", h), R("nu" + H, 0, 128))
+            far(h, "x_%d" % h)
+            for (a, b, e), e2 in zip(CFG["y"], CFG["relu"]):
+                if a // 128 != h:
+                    continue
+                a, b = a - 128 * h, b - 128 * h
+                got = ind(R("xb", 0, 2048), R("nu" + H, a, b))
+                if e == "v":
+                    d = R("Dy" + H, 16 * a, 16 * b)
+                    V(tt, d, got, R(X, 16 * a + 1, 16 * b + 1), A.subtract)
+                    if e2 == "v":
+                        V(ts, R("Ay" + H, 16 * a, 16 * b), d, -UP, UP, A.max, A.add)
+                    else:
+                        S(R("Ay" + H, 16 * a, 16 * b), d, F.Relu, UP)
+                else:
+                    S(R("AG" + H, 16 * a, 16 * b), got, F.Copy)
+                    ops[-1]["name"] = "sy%d@%d" % (h, 16 * a)
+                    for c in range(16 * a, 16 * b, 512):
+                        o = R("b%d" % (4 + c // 512 % 2), 0, 512)
+                        P([(o, R("IBn", 0, 128), R("x" + H, c + 1, c + 513), True, False)])
+                        P([(o, IB, R("AG" + H, c, c + 512), False, True)])
+                        S(R("Ay" + H, c, c + 512), o, F.Abs, UP / 2, 0.5)
+            w = CFG["scan"][t]
+            for c in range(0, 2048, w):
+                V(scan, R("mx" + H, c, c + w), R("MR", 0, w), R(X if CFG["wide"][t][h] else "x" + H, c, c + w), 0.0, A.mult, A.max)
+            o = half("b0" if t < 2 else "b6", h, 256)
+            group([(o, IB, half(z, h)), (o, IB, R("mx" + H, 15, 2048, 16))])
+            if t < 2:
+                C(CFG["zn"][h], half("zs%d" % t, h), o, 0.5, -0.25 + (0 if t else UP / 2))
+            else:
+                S(half("zt", h), o, F.Copy, -0.25, 0.5)
+                C(CFG["zl"], half("zs2", h), half("zt", h), None, -UP)
+            add("g", "remote", [(t, 128 * h, 128 * h + 128, "arr%d" % (2 * t + h))], [half("zs%d" % t, h)], [half("z%d" % (t + 1), h)], RCOST, RLAT)
+        if CFG["late"][t]:
+            winners()
         for h in (0, 1):
             K = "b%d" % (2 + h)
-            keys(K, 256, 15, "Ay_%d" % h, "CS", half("Jh", h), (((0, 128),), ((0, 96), (96, 128)))[h])
-            S(half("le", h), R(K, 128, 256), F.Sign)
+            keys(K, 0, 256, 15, "Ay_%d" % h, R("CS", 0, 256), half("Jh", h), CFG["cuts"][h], "Dy_%d" % h, True)
+            S(half("le", h), R(K, 128, 256), F.Sign, -0.5)
             V(scan, half("cs", h), R("MR", 0, 128), half("le", h), 0.0, A.mult, A.add)
-            S(half("nrx", h), ind(half("cs", h), R("OF15", 0, 8)), F.Sign, 7.0)
+            S(half("nrx", h), ind(half("cs", h), R("OF15", 0, 8)), F.Sign, 9.0, None, R("Nx", h, h + 1) if t < 2 else None)
             if t < 2:
                 group([(half("b6", h), R("ON64", 0, 128), R("Ic", 0, 128)), (half("b6", h), half("nrx", h), R("Ih", 0, 128))])
                 V(tt, half("tg", h), half("b6", h), half("dz", h), A.mult)
             V(scan, half("sm", h), R("MMAX", 0, 128), R(K, 0, 128), 0.0, A.add, A.max)
         if t < 2:
-            for a, by in ((24, "ONk"), (16, "ONn")):
-                group([(R("b0", a, a + 8), R(by, 0, 128), R("nrx", 128 * h, 128 * h + 128, 16)) for h in (0, 1)])
-            for out, a, b in (("Nb", 24, 33), ("Nc", 16, 24)):
-                S(R(out + "x", 0, b - a), R("b0", a, b), F.Copy, None, None, c1(out))
-            scatter("G", 1088, "oEu", "tg", z)
-        P([(R("b1", 0, 256), R("ZQ", 400, 528), R("Jh", 0, 256), True, False)] +
-          [(half("b1", h), half(z, h), R("BBn", 0, 128), False, False) for h in (0, 1)])
+            for h in (0, 1):
+                group([(R("b0", 16 + h), R("ONf", 0, 128), R("Nx", h))])
+            scatter("G", 1024, "oEu", "tg", raw)
         for h in (0, 1):
-            w = 2048 // FOLDS[t][h]
+            w = 2048 // CFG["folds"][t][h]
             for c in range(0, 2048, w):
                 M, X, Z = R("M%d_%d" % (t, h), c, c + w), R("x_%d" % h, c, c + w), R(zx, 2048 * h + c, 2048 * h + c + w)
                 add("g", "fold", [(M, X, Z, sum(o["kind"] == "fold" for o in ops))], [X, Z], [M], RCOST, FLAT0 + FLAT1 * w)
-        for src, by in (("x_%d", "BL1"), ("M%d_%%d" % t, "BL2")):
-            for h in (0, 1):
-                P([(R("b1", 128 * h + k, 128 * h + 128, 16), R(src % h, k, 2048, 16), R(by, 0, 8), False, by == "BL2" and h == 1 and k == 15)
-                   for k in range(16)])
-        S(R("fT", 0, 256), R("b1", 0, 256), F.Copy)
         for h in (0, 1):
-            group([(half("b1", h, 256), half("fT", h), I16), (half("b1", h, 256), half("nrx", h), I2n)])
-        for a, b in ((0, 256),) if t < 2 else ((0, 128), (128, 256)):
-            V(ts, R("ch", a, b), R("b1", 256 + a, 256 + b), 2048.0, R("tf", 1, 2), A.add, A.is_gt)
-            V(tt, R("tmp", a, b), R("ch", a, b), R("b2", 256 + a, 256 + b), A.mult)
-        scatter("I", 1088, "oEu", "tmp", "Jf")
+            P([(R(FB[h], 128 * h + k, 128 * h + 128, 16), R("M%d_%d" % (t, h), k, 2048, 16), R("BL2", 0, 8), False, t == 2 and k == 15)
+               for k in range(16)])
+            if t == 2:
+                S(half("fT", h), half(FB[h], h), F.Copy)
+                group([(half("b1", h, 256), half("fT", h), I16), (half("b1", h, 256), half("nrx", h), I2n)])
+                V(ts, half("ch", h), half("b1", h, 256), -2047.5, None, A.is_gt)
+                V(tt, half("tmp", h), half("ch", h), half("b2", h, 256), A.mult)
+        if t < 2:
+            P([(half("b1", h), I2n, half("nrx", h), False, h == 1) for h in (0, 1)])
+            S(R("fT", 0, 256), R("b1", 0, 256), F.Sign, 2047.5)
+            for h in (0, 1):
+                group([(half("b1", h, 256), R("ON64", 0, 128), R("Ic", 0, 128)), (half("b1", h, 256), half("fT", h), R("Ih", 0, 128))])
+            S(R("vj", 0, 256), VJ, F.Copy)
+            V(tt, R("tmp", 0, 256), R("b1", 256, 512), R("vj", 0, 256), A.mult)
+
+        scatter("I", 1024, "oEu", "tmp", "Jf")
         if t == 2:
-            dma("y", "yi", R("I", 0, 1024), 4096, "d8")
+            dma("y", "yi", tab("I", 1024), 4096)
+        table = "XL" if t < 2 and any(CFG["packed"]) else "L"
         for h0, h1 in ((0, 2),) if t < 2 else ((0, 1), (1, 2)):
-            n, a, b = 8 * (h1 - h0), 128 * h0, 128 * h1
+            a, b = 128 * h0, 128 * h1
             V(ts, R("SJ", 16 * h0, 16 * h1, 2), R("sm", a + 15, b, 16), 2047, None, A.bitwise_and)
             V(ts, R("SJ", 16 * h0 + 1, 16 * h1, 2), R("sm", a + 15, b, 16), 11, 15, A.arith_shift_right, A.bitwise_and)
-            C("s" if t < 2 else "v", R("QT", 32 * h0, 32 * h1, 2), R("SJ", 16 * h0, 16 * h1))
+            C(CFG["QT"][t], R("QT", 32 * h0, 32 * h1, 2), R("SJ", 16 * h0, 16 * h1))
             P([(R("b7", 256 + 128 * h, 384 + 128 * h, 1, 32), R("QT", 32 * h, 32 * h + 32), I16, True, True) for h in range(h0, h1)])
             RL = R("RL", a, b, 1, 32)
             S(RL, R("b7", 256 + a, 256 + b, 1, 32), F.Copy)
             o = R("b7", 48 + 8 * h0, 48 + 8 * h1)
-            if t == 2:
-                WJ, spread = R("WT", 256 * h0, 256 * h0 + 128), [R("E2", 0, 320)]
+            if t == 2 and CFG["WT"][h0] == "s":
+                WJ, spread = R("WT", a, b, 1, 8), [R("EE", 2 * BW, 4 * BW, 1, 8)]
+                P([(R("b7", 64 + r, 192, 16, 8), R("RL", a + r, b, 16, 32), R("SLW", 0, 8, 1, 32), True, True) for r in range(16)])
+                S(WJ, R("b7", 64, 192, 1, 8), F.Copy)
+                group([(o, WJ, R("IW", 4, 12, 1, 8))])
+            elif t == 2:
+                WJ, spread = R("WT", 256 * h0, 256 * h0 + 128), [R("EE", 0, 2 * BW)]
                 V(tt, WJ, ind(R("SJ", 16 * h0, 16 * h1), R("OFF2", 0, 8)), R("MK", 0, 128), A.mult)
-                group([(o, WJ, R("Q16", 0, 8))])
+                group([(o, WJ, Q16)])
             else:
-                WJ, spread = R("WT", 0, 128, 1, 16), [R("EC", 320 * h, 320 * h + 320, 1, 16) for h in (0, 1)]
+                WJ, spread = R("WT", 0, 128, 1, 16), [R("EE", 2 * BW * (h + 1), 2 * BW * (h + 2), 1, 16) for h in (0, 1)]
                 P([(R("b7", 64 + r, 192, 16, 16), R("RL", r, 256, 16, 32), R("SLW", 0, 8, 1, 32), True, True) for r in range(16)])
                 S(WJ, R("b7", 64, 192, 1, 16), F.Copy)
                 group([(o, WJ, R("IW", 4, 20, 1, 16))])
-            V(tt, R("aJ", 8 * h0, 8 * h1), o, R("DUJ", 8 * h0, 8 * h1), A.subtract)
-            V(tc, R("Ju16", 8 * h0, 8 * h1), o)
+            C(CFG["J16"][t], R("Ju16", 8 * h0, 8 * h1), o)
             for h in range(h0, h1):
-                earlier(h, WJ, spread[h - h0], R("RPJ", 0, 128, 1, 32), "RL", 32, "AdJ", "msJ", True)
+                earlier(h, WJ, spread[h - h0], R("RPJ", 0, 128, 1, 32), "RL", 32, "AdJ", "msJ", 1)
             pk = 2 if t == 2 else 0
-            V(tt, R("tJ", 16 * h0, 16 * h0 + 16), ind(R("msJ", 320 * h0, 320 * h1), R("PK", pk, pk + 1)), R("aJ", 8 * h0, 8 * h0 + 16), A.mult)
-            V(tt, R("oJ", 8 * h0, 8 * h1), R("tJ", 16 * h0, 16 * h0 + n), R("DUJ", 8 * h0, 8 * h1), A.add)
-            V(tc, R("oJu", 8 * h0, 8 * h1), R("oJ", 8 * h0, 8 * h1))
-            S(R("Lold", a, b), ind(R("L", 0, 2048), R("Ju16", 8 * h0, 8 * h1)), F.Copy)
-            group([(R("b6", 256 + a, 256 + b), R("RPK", 0, 128, 1, 32), RL)])
-            V(ts, R("mk", a, b), R("b6", 256 + a, 256 + b), c1("k15"), None, A.is_equal)
-            if t == 2:
-                group([(R("b6", a, b), ISH, R("Jh", a, b))])
-                V(tt, R("b6", a, b), R("b6", a, b), R("Lold", a, b), A.subtract)
-            else:
-                C("g", R("Lo16", a, b), R("Lold", a, b))
-                group([(R("b6", a, b), ISH, R("Jh", a, b)), (R("b6", a, b), In, R("Lo16", a, b))])
-            V(tt, R("t2", a, b), R("b6", a, b), R("mk", a, b), A.mult)
-        scatter("L", 2112, "oJu", "t2", "Lold")
-    dma("y", R("yz", 0, 128), R("z3", 128, 256), 256, "d9")
-    dma("y", R("yz", 128, 256), R("z3", 0, 128), 256, "d13")
-    dma("y", "yl", R("L", 0, 2048), 8192, "d10")
+            C(CFG["oJ"][t], R("oJu", 16 * h0, 16 * h0 + 16), ind(R("msJ", 2 * BW * h0, 2 * BW * h1), R("PK", pk, pk + 1)))
+            S(R("Lold", a, b), ind(tab(table, 2048), R("Ju16", 8 * h0, 8 * h1)), F.Copy)
+            group([(R("b7", 256 + a, 256 + b), R("RPK", 0, 128, 1, 32), RL)])
+            V(ts, R("mk", a, b), R("b7", 256 + a, 256 + b), c1("k15"), None, A.is_equal)
+            o = R("b1", 256 + a, 256 + b) if t < 2 else R("b6", a, b)
+            group([(o, ISH, R("Jh", a, b)), (o, In, R("Lh", a, b))])
+            V(tt, R("t2", a, b), o, R("mk", a, b), A.mult)
+        scatter(table, 2048, "oJu", "t2", "Lold", 8 if t < 2 else 16)
+    dma("y", R("yz", 0, 128), R("z3", 128, 256), 256)
+    dma("y", R("yz", 128, 256), R("z3", 0, 128), 256)
+    dma("y", "yl", tab("L", 2048), 8192 * CFG["rows"] // 16)
     return ops
 
 
@@ -524,7 +649,8 @@ def edges(ops):
     where = {(o["t"], o["name"]): o["i"] for o in ops}
     for t in range(3):
         for turn in TURNS[t]:
-            got = [where[t - w.count("<"), w.strip("<")] for w in turn.split()]
+            got = [where.get((t - w.count("<"), w.strip("<"))) for w in turn.split()]
+            got = [i for i in got if i is not None]
             for j, i in zip(got, got[1:]):
                 pre[i].setdefault(j, False)
     return pre
@@ -546,55 +672,148 @@ def sequence(pre):
     return seq
 
 
-def before(taken, s):
-    lo, hi = 0, len(taken)
-    while lo < hi:
-        mid = (lo + hi) // 2
-        if taken[mid][0] < s:
-            lo = mid + 1
-        else:
-            hi = mid
-    return lo
-
-
 def fit(seq, lags, uses, tail=None, limit=None, old=None):
     n, k0 = len(seq), 0
     if old:
         while k0 < n and seq[k0] == old[0][k0]:
             k0 += 1
-        k0 = min(k0, n - 1) // 32 * 32
-        start, marks = list(old[1]), old[2][:k0 // 32]
-        busy = [list(x) for x in old[2][k0 // 32]]
+        start, busy = list(old[1]), [[x for x in taken if x[3] < k0] for taken in old[2]]
     else:
-        start, marks, busy = [0.0] * n, [], [[] for _ in range(16)]
+        start, busy = [0.0] * n, [[(-2.0, -1.0, -1, -1)] * 2 for _ in range(14)]
     for k in range(k0, n):
-        if k % 32 == 0:
-            marks.append([list(x) for x in busy])
         i, s = seq[k], 0.0
         for j, d in lags[i]:
-            if start[j] + d > s:
-                s = start[j] + d
+            d += start[j]
+            if d > s:
+                s = d
+        mine = uses[i]
+        res, off, m, who = mine[0]
+        taken = busy[res]
+        if not mine[1:] and taken[-1][1] <= s + off:
+            if limit and s + tail[i] > limit:
+                return None
+            start[i] = s
+            taken.append((s + off, s + off + m, who, k))
+            continue
         moved = True
         while moved:
             moved = False
-            for res, off, m, who in uses[i]:
-                taken = busy[res]
-                if taken and taken[-1][1] > s + off:
-                    for a, b, other in taken[max(0, before(taken, s + off) - 2):]:
-                        if a >= s + off + m - 1e-6:
+            for res, off, m, who in mine:
+                taken, at = busy[res], s + off
+                if taken[-1][1] > at:
+                    p = -1
+                    while taken[p][0] >= at:
+                        p -= 1
+                    for a, b, other, _k in taken[p - 1:]:
+                        if a >= at + m - 1e-6:
                             break
-                        if s + off < b - 1e-6 and who != other:
-                            s, moved = b - off, len(uses[i]) > 1
+                        if at < b - 1e-6 and who != other:
+                            at, moved = b, mine[1:]
+                    s = at - off
         if limit and s + tail[i] > limit:
             return None
         start[i] = s
-        for res, off, m, who in uses[i]:
-            taken = busy[res]
-            if not taken or taken[-1][0] <= s + off:
-                taken.append((s + off, s + off + m, who))
+        for res, off, m, who in mine:
+            taken, at = busy[res], s + off
+            if taken[-1][0] <= at:
+                taken.append((at, at + m, who, k))
             else:
-                taken.insert(before(taken, s + off), (s + off, s + off + m, who))
-    return seq, start, marks
+                p = -1
+                while taken[p - 1][0] > at:
+                    p -= 1
+                taken.insert(p, (at, at + m, who, k))
+    return seq, start, busy
+
+
+def harden(way, arcs, banks, rng, passes, heat):
+    n, cases = len(way), []
+    succ, before = [[] for _ in range(n)], [[] for _ in range(n)]
+    for j, i in arcs:
+        succ[j].append(i)
+        before[i].append(j)
+    for case in CASES:
+        ops, wake = build(case), case.get("WAKE", WAKE)
+        queue = ["vstgy".index(o["q"]) for o in ops]
+        span = [o["cost"] + o["lat"] for o in ops]
+        rows = []
+        for i, o in enumerate(ops):
+            own = [(queue[i], o["cost"])] + [(6 + 3 * int(b[1]) + queue[i], o["cost"] + wake) for b in banks[i]]
+            rows.append(([(j, span[j] + wake if arcs[j, i] else ops[j]["cost"]) for j in before[i]],
+                         [queue[i]] + [6 + 3 * int(b[1]) + q for b in banks[i] for q in (0, 1, 2) if q != queue[i]], own,
+                         o.get("hold"), span[i]))
+        cases.append(rows)
+    final = [i for i in range(n) if not succ[i]]
+
+    def replay(rows, way, a, old):
+        a = a // 16 * 16
+        head, why, marks = list(old[0]), list(old[1]), old[2][:a // 16]
+        free, last = list(old[2][a // 16][0]), list(old[2][a // 16][1])
+        for k in range(a, n):
+            if k % 16 == 0:
+                marks.append((tuple(free), tuple(last)))
+            i = way[k]
+            lags, rival, own, hold, span = rows[i]
+            s, by = 0.0, None
+            for j, d in lags:
+                d += head[j]
+                if d > s:
+                    s, by = d, j
+            for r in rival:
+                if free[r] > s:
+                    s, by = free[r], ~last[r]
+            if hold:
+                if free[5] + hold - span > s:
+                    s, by = free[5] + hold - span, ~last[5]
+                free[5], last[5] = s + span, i
+            head[i], why[i] = s, by
+            for r, m in own:
+                free[r], last[r] = s + m, i
+        end = max(final, key=lambda i: head[i] + rows[i][4])
+        return head, why, marks, head[end] + rows[end][4], end
+
+    def held(got):
+        i, out = got[4], []
+        while i is not None:
+            j = got[1][i]
+            if j is not None and j < 0:
+                j = ~j
+                out.append((j, i))
+            i = j
+        return out
+
+    now = [replay(rows, way, 0, ([0.0] * n, [None] * n, [((0.0,) * 30, (0,) * 30)])) for rows in cases]
+    base = [got[3] for got in now]
+    at, hot = {i: k for k, i in enumerate(way)}, [held(got) for got in now]
+    mean = 1.0
+    best = (mean, list(way), base)
+    for k, d in enumerate(rng.random((passes, 5)).tolist()):
+        pairs = hot[int(d[0] * len(hot))]
+        j, i = pairs[int(d[1] * len(pairs))]
+        a, b = at[j], at[i] + 1
+        part = way[a:b]
+        group, near, ends = ({i}, before, part[::-1]) if d[3] < 0.5 else ({j}, succ, part)
+        for x in ends:
+            if x in group:
+                group.update(near[x])
+        if i in group and j in group:
+            continue
+        part = [x for x in part if (x in group) == (d[3] < 0.5)] + [x for x in part if (x in group) != (d[3] < 0.5)]
+        trial, new, total = way[:a] + part + way[b:], [], 0.0
+        room = len(cases) * (mean - (0.05 + heat * (1 - k / passes)) * 1e-3 * math.log(d[4]))
+        for rows, old, was in zip(cases, now, base):
+            new.append(replay(rows, trial, a, old))
+            total += new[-1][3] / was
+            if total + 0.985 * sum(x[3] / y for x, y in zip(now[len(new):], base[len(new):])) > room:
+                break
+        else:
+            if total <= room:
+                way, now, mean = trial, new, total / len(cases)
+                at.update((x, a + p) for p, x in enumerate(part))
+                hot = [held(got) for got in now]
+                if mean < best[0]:
+                    best = (mean, list(way), [x[3] for x in now])
+    PLAN["ends"] = base, best[2]
+    return best[1]
 
 
 def schedule(ops, pre, stages, seed):
@@ -611,7 +830,7 @@ def schedule(ops, pre, stages, seed):
     for i, o in enumerate(ops):
         u = [(8 + "vstgy".index(o["q"]), 0.0, o["cost"], i)] + [(int(b[1]), 0.0, o["cost"] + WAKE, o["q"]) for b in banks[i]]
         if o.get("hold"):
-            u.append((13, o["cost"] + DLAT, o["hold"], i))
+            u.append((13, span[i] - o["hold"], o["hold"], i))
         ahead.append(u)
         back.append([(res, span[i] - off - m, m, who) for res, off, m, who in u])
 
@@ -623,10 +842,10 @@ def schedule(ops, pre, stages, seed):
         return key
 
     def early(key, limit=None, old=None):
-        got = fit(sorted(range(n), key=lambda i: key[i]), fwd, ahead, tail, limit, old)
+        got = fit(np.argsort(key, kind="stable").tolist(), fwd, ahead, tail, limit, old)
         if got:
-            end = max(s + w for s, w in zip(got[1], span))
-            return end + 0.3 * sum(got[1][i] for i in long) / len(long), end, got, key
+            end = max(got[1][i] + span[i] for i in final)
+            return end + CFG["mean"] * sum(got[1][i] for i in long) / len(long), end, got, key
 
     def late(start):
         key = mend([-start[i] - span[i] for i in range(n)], bwd, seq[::-1])
@@ -641,18 +860,41 @@ def schedule(ops, pre, stages, seed):
                 key[i] = at
                 todo += [(j, at + sign * 1e-2) for j, d in lags[i]]
 
-    def tight(start):
+    def tight(start, pick):
         ends = {(res, round(start[i] + off + m)): i for i in range(n) for res, off, m, who in ahead[i]}
-        i, out = max(range(n), key=lambda i: start[i] + span[i]), []
+        i, out, arcs = max(range(n), key=lambda i: start[i] + span[i]), [], []
         while i is not None:
             out.append(i)
             got = [j for j, d in fwd[i] if abs(start[j] + d - start[i]) < 1]
-            got += [ends[res, round(start[i] + off)] for res, off, m, who in ahead[i] if (res, round(start[i] + off)) in ends]
-            got = [j for j in got if start[j] < start[i]]
-            i = got[-1] if got else None
-        return out
+            held = [ends[res, round(start[i] + off)] for res, off, m, who in ahead[i] if (res, round(start[i] + off)) in ends]
+            held = [j for j in held if start[j] < start[i] and j not in pre[i]]
+            if held and not got:
+                arcs.append((held[-1], i))
+            got = [j for j in got + held if start[j] < start[i]]
+            i = got[int(pick * len(got))] if got else None
+        return out, arcs
+
+    def swap(key, j, i, a):
+        same = alike[ops[j]["name"]], alike[ops[i]["name"]]
+        every = a[4] < CFG["alike"] and ops[i]["t"] == ops[j]["t"] and len(same[0]) == len(same[1])
+        for j, i in zip(*same) if every else [(j, i)]:
+            if key[j] < key[i] and a[5] < 0.5:
+                move(key, i, key[j] - key[i] - 1 - 300 * a[6])
+            elif key[j] < key[i]:
+                move(key, j, key[i] - key[j] + 1 + 300 * a[6])
+
+    def copy(start, t, u, a, w):
+        key, zero = list(start), [start[i] for i in alike["vDG_0@0"]]
+        for same in alike.values():
+            here, there = [i for i in same if ops[i]["t"] == t], [i for i in same if ops[i]["t"] == u]
+            if len(here) == len(there):
+                for i, j in zip(here, there):
+                    if a - 4000 <= start[i] - zero[t] < a - 4000 + w:
+                        key[j] = start[i] - zero[t] + zero[u]
+        return mend(key, fwd, seq)
 
     seq = sequence(pre)
+    final = [i for i in range(n) if not bwd[i]]
     long = [i for i in range(n) if ops[i]["cost"] > 800 and ops[i]["q"] in "vs"]
     alike = {}
     for o in ops:
@@ -664,26 +906,33 @@ def schedule(ops, pre, stages, seed):
     best = early(late(early(mend([-x for x in tail], fwd, seq))[2][1]))
     for passes, heat in stages:
         now = best
-        hot = tight(now[2][1])
+        hot, arcs = tight(now[2][1], 0.99)
         for k, d in enumerate(rng.random((passes, 3, 7)).tolist()):
             if d[0][0] < 0.03:
                 key = late(now[2][1])
+            elif d[0][0] < 0.03 + CFG["copy"]:
+                key = copy(now[2][1], int(3 * d[1][1]), int(3 * d[1][2]), 30000 * d[1][3], 4000 + 20000 * d[1][4])
             else:
                 key = list(now[3]) if d[0][1] < 0.8 else mend(list(now[2][1]), fwd, seq)
                 for a in d[:(1, 1, 2, 3)[int(4 * d[1][0])]]:
+                    if a[1] < CFG["aim"] and arcs:
+                        swap(key, *arcs[int(a[2] * len(arcs))], a)
+                        continue
                     i = long[int(a[2] * len(long))] if a[3] < 0.15 else int(a[2] * n) if a[3] < 0.35 else hot[int(a[2] * len(hot))]
-                    for j in alike[ops[i]["name"]] if a[4] < 0.3 else [i]:
+                    for j in alike[ops[i]["name"]] if a[4] < CFG["alike"] else [i]:
                         move(key, j, (600, 2000, 6000)[int(3 * a[5])] * (2 * a[6] - 1) * abs(2 * a[6] - 1))
             more = -(5 + heat * (1 - k / passes)) * math.log(d[2][0])
             new = early(key, now[1] + more + 300, now[2])
             if new and new[0] < now[0] + more:
                 now = new
-                if k % 4 == 0:
-                    hot = tight(now[2][1])
+                if d[2][2] < 0.5:
+                    hot, arcs = tight(now[2][1], d[2][1])
                 if new[1] < best[1]:
                     best = new
     end, start = best[1], best[2][1]
-    order = sorted(range(n), key=lambda i: (start[i], i))
+    place = {i: k for k, i in enumerate(seq)}
+    order = sorted(range(n), key=lambda i: (start[i], place[i]))
+    order = harden(order, {(j, i): pre[i][j] for i in range(n) for j, d in fwd[i]}, banks, rng, *CFG["harden"])
     waits, last = [dict(e) for e in pre], {}
     for i in order:
         for b in banks[i]:
@@ -697,7 +946,7 @@ def schedule(ops, pre, stages, seed):
 PLAN = {}
 
 
-def plan(stages=((27000, 100.0), (20000, 50.0)), seed=9):
+def plan(stages=((24000, 100.0), (26000, 60.0), (22000, 35.0)), seed=4):
     ops = build()
     return (ops,) + schedule(ops, edges(ops), stages, seed)
 

import math
import numpy as np
from concourse.bass import DstId, RemoteDMATransfer
from concourse.mybir import AluOpType as A, ActivationFunctionType as F

BIG = 1.0e9
TIMES = dict(CYC=0.8333, GAT=1.56, SCA=3.8, WAKE=130.0, FIX=20.0, SFIX=80.0, TCYC=0.5, DLAT=1600.0, DRATE=200.0, RLAT=3900.0, FLAT0=3500.0,
             FLAT1=3.0, RCOST=500.0)
WAKE = TIMES["WAKE"]
CASES = ({}, dict(CYC=0.92, TCYC=0.5, RLAT=4200.0), dict(CYC=1.05, TCYC=0.63, WAKE=160.0), dict(CYC=1.0, TCYC=0.6, GAT=1.15, SCA=4.5, RLAT=4500.0),
         dict(CYC=1.0, TCYC=0.6, GAT=1.95, SCA=2.5, WAKE=180.0, DRATE=260.0),
         dict(CYC=1.0, TCYC=0.6, RLAT=5800.0, FLAT0=4800.0, RCOST=850.0, SCA=5.2),
         dict(CYC=1.1, TCYC=0.66, GAT=1.3, DRATE=140.0, FLAT1=4.5, WAKE=100.0))
SCRATCH = {}
TWO = ("bfloat16", "float16", "uint16")
DUMP = 176
SEG = (0, 17, 50, 99)
BW = 164
UP = 192.0
HALVES = ((0, 64), (64, 128))
LAST = ((0, 64), (64, 96), (96, 128))
CFG = dict(
    packed=(False, False, False),
    x=(((0, 128, "s"),), ((0, 64, "v"), (64, 128, "v"))),
    l=(((0, 64, "s"), (64, 128, "s")), ((0, 64, "s"), (64, 128, "s"))),
    x0=(((0, 96, "s"), (96, 128, "v")), ((0, 64, "v"), (64, 128, "s"))),
    l2=(((0, 64, "s"), (64, 128, "s")), ((0, 32, "v"), (32, 64, "s"), (64, 128, "s"))),
    y=((0, 64, "v"), (64, 128, "v"), (128, 192, "v"), (192, 256, "s")),
    relu="vvvv",
    cuts=(((0, 128),), ((0, 128),)),
    wide=((0, 0), (0, 0), (0, 0)),
    casts=(1, 1, 1), folds=((1, 2), (1, 2), (2, 2)), zs=1, r="ss", nu="vv", emu="ss", eu="vv", Ju="sv",
    sub=("b0", "b6", "b4", "b5"), ch="ssv", g=(((0, 128),), HALVES), UH="s", QT="ssv", uu="vvv", oE="sss", oJ="ssv", J16="ssv", zl="s",
    emi="vv", zn="sv", z0="VVVVVVVVVvvvvsss", harden=(6000, 0.15), scan=(1024, 1024, 512), rows=16, late=(0, 0, 0), WT="sv", copy=0.02, alike=0.4, aim=0.6, mean=0.3)


def _buf(name, cols, dtype, where="sbuf"):
    SCRATCH[name] = (where, [128, cols], dtype)


_B, _H, _F, _I, _U = "bfloat16", "float16", "float32", "int32", "uint16"
for _n, _c, _d in (
        ("xb", 2048, _B), ("G", DUMP + 1024, _B), ("ixi", 1024, _I), ("I", DUMP + 1024, _F), ("lki", 2048, _I), ("XL", DUMP + 2048, _F),
        ("L", DUMP + 2048, _F), ("wti", 1, _I), ("hki", 2, _I), ("thi", 2, _I),
        ("z0", 256, _B), ("z1", 256, _B), ("z2", 256, _B), ("z3", 256, _B),
        ("zs0", 256, _B), ("zs1", 256, _B), ("zs2", 256, _B), ("zt", 256, _B), ("zr", 256, _B),
        ("pI", 6, _I), ("pf", 5, _F), ("p32", 1, _F), ("colA", 1, _F), ("colB", 1, _F),
        ("colC", 1, _F), ("k15", 1, _F), ("hI", 3, _I), ("hf", 3, _F), ("tf", 2, _F), ("OFF0", 8, _U),
        ("pk1", 1, _F), ("pk2", 1, _F), ("m15", 1, _F), ("acol", 1, _F), ("dI", 144, _B), ("gI", 128, _B), ("g8I", 16, _I),
        ("rI", 128, _B), ("dg4", 128, _B), ("r15I", 128, _B), ("slI", 16, _B), ("qrel", BW, _B), ("dcol", BW, _B), ("dl", BW, _B),
        ("SM", 2 * BW, _B), ("IW", 136, _H), ("IB", 136, _B), ("IBn", 128, _B), ("I64", 128, _B), ("In", 128, _H), ("I2n", 128, _H),
        ("Ih", 128, _H), ("Ic", 128, _H), ("BHn", 128, _H), ("BBn", 128, _B), ("BLK", 24, _B), ("BKn", 16, _B), ("BK2", 16, _B),
        ("BL1", 8, _B), ("BL2", 8, _B), ("MK", 128, _H), ("EN", 512, _B), ("SEL", 2048, _H), ("MR", 1024, _B), ("CD", 256, _H),
        ("CS", 256, _H), ("ON64", 128, _H), ("ONf", 128, _F), ("UPn", 128, _B), ("SK", 256, _F), ("MMIN", 128, _B), ("MMAX", 128, _B),
        ("Nc", 1, _F), ("CB", 256, _H), ("vj", 256, _H),
        ("OFFR", 8, _U), ("OF15", 8, _U), ("OFF2", 8, _U), ("PK", 4, _U), ("RPJ", 128, _H), ("RPK", 128, _H), ("SLW", 16, _H),
        ("EE", 6 * BW, _H), ("TT", 4 * BW, _H), ("dg0", 128, _H), ("dg1", 128, _H), ("dg2", 128, _H), ("W8", 16, _B), ("ZQ", 528, _H),
        ("PM_0", 128, _H), ("PM_1", 128, _H), ("PQ_0", 128, _H), ("PQ_1", 128, _H),
        ("ui", 16, _I), ("uu", 16, _I), ("UQ", 64, _I), ("UH", 66, _H), ("RLu", 128, _H), ("q2", 256, _H), ("emi", 256, _I),
        ("emu", 256, _U), ("emh", 256, _H), ("Nx", 2, _F), ("zx0", 4096, _B), ("zx1", 4096, _B), ("zT", 128, _B), ("eu", 16, _U),
        ("Jf", 256, _F), ("Jh", 256, _H), ("Y", 256, _H), ("AdE", 4 * BW, _F), ("msE", 4 * BW, _F), ("oEu", 16, _U), ("dz", 256, _B),
        ("tg", 256, _B), ("rd", 256, _B), ("Lh", 256, _H), ("le", 256, _B), ("cs", 256, _B), ("nrx", 256, _H), ("sm", 256, _I),
        ("SJ", 32, _I), ("QT", 64, _H), ("RL", 256, _H), ("WT", 512, _H), ("AdJ", 4 * BW, _F), ("msJ", 4 * BW, _F), ("oJu", 32, _U),
        ("Ju16", 16, _U), ("fT", 256, _H), ("ch", 256, _F), ("tmp", 256, _F), ("Lold", 256, _F), ("mk", 256, _F), ("t2", 256, _F)):
    _buf(_n, _c, _d)
for _h in "01":
    for _n, _c, _d in (("DG", 2048, _B), ("AG", 2048, _B), ("x", 2064, _B), ("XG", 2064, _F), ("Lg", 2048, _H), ("mx", 2048, _B),
                       ("Dy", 2048, _B), ("Ay", 2048, _B), ("km", 128, _I), ("ej", 8, _I), ("ME", 128, _H), ("Ju", 128, _U),
                       ("nu", 128, _U), ("M0", 2048, _B), ("M1", 2048, _B), ("M2", 2048, _B)):
        _buf(_n + "_" + _h, _c, _d)
for _b in range(8):
    _buf("b%d" % _b, 512, _F, "psum")
PLACE = {_n: (_n, 0) for _n in ("lk", "zc", "yz")}
_pack = {}
for _n in sorted(SCRATCH):
    _w, _s, _d = SCRATCH[_n]
    if _w == "sbuf" and _n not in ("G", "I", "ixi", "z0", "z1", "z2", "z3", "zs0", "zs1", "zs2") and _s[1] < 2000:
        _o = _pack.get(_d, 0)
        PLACE[_n] = ("k_" + _d, _o)
        _pack[_d] = _o + (_s[1] + 31) // 32 * 32
    else:
        PLACE[_n] = (_n, 0)
DTYPE = {_n: SCRATCH[_n][2] for _n in SCRATCH}
COLS = {_n: SCRATCH[_n][1][1] for _n in SCRATCH}
for _n in list(SCRATCH):
    if PLACE[_n][0] != _n:
        del SCRATCH[_n]
for _d in _pack:
    _buf("k_" + _d, _pack[_d], _d)
SEMAPHORES = (["qv", "qs", "qt", "qg", "loc"] + ["arr%d" % i for i in range(6)] + [s + str(i) for s in ("fa", "fb") for i in range(24)]
              + ["d%d" % i for i in range(40)])

LOADS = "<yz0@0 <yG@176 <yixi@0 <yxb@0 <ylki@0 <ylki@1024 <ylki@1536"
S_TURN = ("sDG_1@0 sDG_1@1024 sAG_1@0 sAG_1@512 sAG_1@1024 sAG_1@1536 sx_0@0 sLg_0@0 sLg_0@1024 sLg_1@1024 sLg_1@0 "
          "sy1@1024")
V_TURN = "vDG_0@0 veu@0 vkm_1@0 vx_1@0 vDy_0@0 vDy_0@1024 vDy_1@0"
Z_TURN = "vx_1@0 vmx_0@0 vmx_0@1024 vx_1@1024 vmx_1@0 vmx_1@1024 vdz@0 vzs0@128 vzs1@128 vDy_0@0"
FIRST = (S_TURN.replace("sLg_0@0", "sx_1@1024 sLg_0@0").replace("sLg_1@0", "sLg_1@512"),
         V_TURN.replace("vx_1@0 vDy_0@0", "vx_0@1536 vx_1@0 vmx_0@0 vmx_0@1024 vmx_1@0 vmx_1@1024 vzs0@128 vLg_1@0 vDy_0@0"))
TURNS = ((LOADS,) + FIRST, (S_TURN, V_TURN, Z_TURN),
         (S_TURN, V_TURN, "vx_1@0 vx_1@1024 vDy_0@0", "vDy_1@0 vAy_1@0 vsm@0", "vI@0 vch@128", "vI@2 vL@1", "sAdE@0 sLg_1@0",
          "sAdE@328 sLg_1@0", "sy1@1024 sAy_1@1024 sAy_1@1536 snrx@0") + tuple("vAy_1@0 vmx_1@%d" % c for c in range(0, 2048, 512)))


def R(buf, a=0, b=None, step=1, p=128, p0=0):
    return (buf, a, a + 1 if b is None else b, step, p, p0)


def width(r):
    return (r[2] - r[1] + r[3] - 1) // r[3]


def clash(r, s):
    if r[0] != s[0] or r[1] >= s[2] or s[1] >= r[2]:
        return False
    return not (r[3] == s[3] and r[3] > 1 and (r[1] - s[1]) % r[3] != 0)


def bank(r):
    return r[0] if r[0][0] == "b" and len(r[0]) == 2 and r[0][1].isdigit() else None


class IndOp(tuple):
    pass


def ind(win, off):
    return IndOp((win, off))


def build(case={}):
    ops, now = [], [-1]
    CYC, GAT, SCA, _w, FIX, SFIX, TCYC, DLAT, DRATE, RLAT, FLAT0, FLAT1, RCOST = [case.get(x, TIMES[x]) for x in TIMES]

    def add(q, kind, calls, reads, writes, cost, lat=0.0, **kw):
        r = (writes or reads)[0]
        ops.append(dict(q=q, kind=kind, calls=calls, reads=reads, writes=writes, cost=cost, lat=lat, i=len(ops), t=now[0],
                        name="%s%s@%d" % (q, r[0], r[1]), **kw))

    def join():
        o = ops.pop()
        for part in ("calls", "reads", "writes", "cost"):
            ops[-1][part] = ops[-1][part] + o[part]

    def flat(x):
        if isinstance(x, IndOp):
            return [x[0], x[1]]
        return [x] if isinstance(x, tuple) else []

    def V(name, out, *args):
        full = [x for x in args if isinstance(x, tuple)]
        rd = [y for x in full for y in flat(x)]
        if isinstance(out, IndOp):
            rd = rd + [out[1]]
            c = 50 + width(out[1]) * 16 * SCA * CYC
        elif any(isinstance(x, IndOp) for x in full):
            c = 50 + width(out) * GAT * CYC
        elif name == "tensor_tensor":
            c = max(64.0, width(out) * (1.0 if any(bank(x) for x in full) else 2.0)) * CYC + FIX
        else:
            half = all(DTYPE[r[0]] in TWO for r in [out] + [x for x in full if width(x) > 1])
            c = max(64.0, width(out) * (0.5 if half else 1.0)) * CYC + FIX
        add("v", name, [(out,) + args], rd, flat(out)[:1], c)

    def S(out, in_, func, bias=None, scale=None, total=None):
        c = SFIX + width(out) * CYC * (GAT if isinstance(in_, IndOp) else 1.0) + (20 if total else 0)
        rd = flat(in_) + [x for x in (bias, scale) if isinstance(x, tuple)]
        add("s", "activation", [(out, in_, func, bias, scale, total)], rd, [out] + flat(total), c)

    def select(out, in_, pattern, base, cm):
        add("g", "select", [(out, in_, pattern, base, cm)], [in_], [out], 170 + 2 * width(out) * CYC)

    def C(eng, out, in_, by=None, plus=None):
        if eng == "s":
            S(out, in_, F.Copy, plus, by)
        elif eng == "g":
            select(out, in_, [[0, width(out)]], 0, 0)
        elif by is not None:
            V("tensor_scalar", out, in_, by, plus or 0.0, A.mult, A.add)
        elif plus is not None:
            V("tensor_scalar", out, in_, plus, None, A.add)
        else:
            V("tensor_copy", out, in_)

    def P(items):
        c = 0.0
        rd, wr = [], []
        for o, l, r, a, b in items:
            c += max(min(64, width(l)), width(r)) * TCYC * (4 if DTYPE[l[0]] == _F else 1) + 5
            for x in (l, r):
                if x not in rd:
                    rd.append(x)
            if o not in wr:
                wr.append(o)
        add("t", "matmul", items, rd, wr, c)

    def group(items):
        P([(o, l, r, i == 0, i == len(items) - 1) for i, (o, l, r) in enumerate(items)])

    def iota(out, pattern, base, cm):
        add("g", "iota", [(out, pattern, base, cm)], [], [out], 130 + 2 * width(out) * CYC)

    def dma(q, out, in_, nbytes):
        rd = [in_] if isinstance(in_, tuple) else []
        wr = [out] if isinstance(out, tuple) else []
        add(q, "dma", [(out, in_)], rd, wr, 60, DLAT + nbytes * 128 / DRATE,
            sem="d%d" % sum(o["kind"] == "dma" for o in ops), hold=nbytes * 128 / DRATE if nbytes > 32 else 0)

    def fill(out, value):
        S(out, R("ZQ", 400, 400 + width(out), 1, out[4], out[5]), F.Copy, value)

    tab = lambda buf, n, a=0: R(buf, DUMP + a, DUMP + n)
    dma("y", R("z0", 0, 128), R("zc", 128, 256), 256)
    dma("s", R("z0", 128, 256), R("zc", 0, 128), 256)
    dma("s", R("wti", 0, 1), "wt", 4)
    dma("s", R("hki", 0, 2), "hk", 8)
    dma("y", tab("G", 1024), "gi", 2048)
    dma("y", R("ixi", 0, 1024), "ix", 4096)
    dma("y", R("xb", 0, 2048), "xc", 4096)
    dma("s", R("thi", 0, 2), "th", 8)
    dma("y", R("lki", 0, 1024), R("lk", 0, 1024), 4096)
    dma("y", R("lki", 1024, 1536), R("lk", 1024, 1536), 2048)
    dma("y", R("lki", 1536, 2048), R("lk", 1536, 2048), 2048)
    iota(R("pI", 0, 1), [[0, 1]], 0, 1)
    iota(R("g8I", 0, 16), [[0, 2], [1, 8]], 0, 0)
    iota(R("dI", 0, 144), [[1, 144]], 0, -1)
    iota(R("gI", 0, 128), [[1, 8], [0, 16]], 0, 0)
    iota(R("rI", 0, 128), [[0, 8], [1, 16]], 0, 0)
    iota(R("r15I", 0, 128), [[0, 8], [-1, 16]], 15, 0)
    iota(R("dg4", 0, 128), [[4, 8], [0, 16]], 0, -1)
    iota(R("slI", 0, 16), [[1, 2], [4, 8]], 0, -1)
    for q in range(4):
        a, n = SEG[q], 16 * (q + 1)
        iota(R("qrel", a, a + n + 1), [[0, n + 1]], q, 0)
        iota(R("dcol", a, a + n), [[1, n]], -16 * q, 0)
        if q % 2:
            iota(R("dcol", a - 1, a + n + 1, n + 1), [[0, 2]], 0, 0)
        iota(R("SM", a, a + n), [[-4096, n]], 4096, 0)
        iota(R("SM", a + n, a + n + 1), [[0, 1]], 16 * q, 1)
    for a in range(0, 2048, 512):
        if a < 1024:
            V("memset", R("MR", a, a + 512), 1.0)
        select(R("SEL", a, a + 512), R("MR", 0, 512), [[-256, 4], [-16, 8], [255, 16]], -2 * a, 1)
    for a, b, e in CFG["y"]:
        if e == "s":
            iota(R("Dy_%d" % (a // 128), 16 * (a % 128), 16 * (a % 128 + b - a)), [[0, 16 * (b - a)]], -int(UP), 0)
    COL = ("pf", "pg", "p16", "p4", "b4")
    c1 = lambda b: R("pf", COL.index(b)) if b in COL else R(b, 0, 1)
    ts, tt, tc, scan = "tensor_scalar", "tensor_tensor", "tensor_copy", "tensor_tensor_scan"
    I16, IB, ISH = R("IW", 4, 132), R("IB", 4, 132), R("IW", 5, 133)
    In, I2n = R("In", 0, 128), R("I2n", 0, 128)
    Q16 = R("ZQ", 72, 80)
    V("memset", R("MR", 0, 1024, 16), 0.0)
    V(ts, R("pI", 1), c1("pI"), 4, None, A.arith_shift_right)
    V(ts, R("pI", 2), c1("pI"), 15, None, A.bitwise_and)
    V(ts, R("pI", 3), c1("pI"), 3, None, A.bitwise_and)
    V(ts, R("pI", 4), c1("pI"), 2, 3, A.arith_shift_right, A.bitwise_and)
    V(tc, R("pf", 0, 5), R("pI", 0, 5))
    iota(R("EN", 0, 512), [[1, 32], [0, 16]], 0, 0)
    V(ts, R("pI", 5), c1("pI"), 31, None, A.bitwise_and)
    V(tc, c1("p32"), R("pI", 5))
    V(ts, R("EN", 0, 512), R("EN", 0, 512), c1("p32"), None, A.is_equal)
    for name, by, plus in (("OFF0", 0.0, None), ("OFFR", None, None), ("OF15", 16.0, 15.0), ("OFF2", 2.0, None)):
        C("s", R(name, 0, 8), R("g8I", 0, 8), by, plus)
    V(ts, R("BLK", 8, 24), R("g8I", 0, 16), c1("pg"), None, A.is_equal)
    S(R("BLK", 0, 8), R("BLK", 8, 16), F.Copy, None, 32768.0)
    V(tt, R("W8", 0, 16), ind(c1("wti"), c1("OFF0")), R("BLK", 8, 24), A.mult)
    for j, (col, bits) in enumerate(((0, 1023), (1, 63), (1, 1984))):
        V(ts, R("hI", j, j + 1), R("hki", col, col + 1), bits, None, A.bitwise_and)
    V(tc, R("hf", 0, 3), R("hI", 0, 3))
    V("memset", R("ZQ", 0, 528), 0.0)
    V(ts, R("ZQ", 72, 80), R("g8I", 0, 8), c1("pg"), None, A.is_equal)
    V(ts, R("ZQ", 200, 208), R("g8I", 0, 8), c1("pg"), -0.0625, A.is_equal, A.mult)
    fill(R("ZQ", 392, 393), 2176.0)
    fill(R("UH", 64, 66), 1024.0)
    V(ts, R("BHn", 0, 128), R("gI", 0, 128), c1("pg"), -1.0, A.is_equal, A.mult)
    V(ts, R("IW", 0, 136), R("dI", 0, 136), 4.0, None, A.is_equal)
    V(ts, R("MK", 0, 128), R("rI", 0, 128), c1("p16"), None, A.is_equal)
    V(ts, c1("colA"), c1("pf"), 64.0, 0.5, A.is_ge, A.mult)
    V(ts, c1("colB"), c1("pf"), 64.0, -4096.0, A.is_lt, A.mult)
    V(ts, c1("colC"), c1("pf"), 64.0, -8 * 16 * UP - 4096.0, A.is_lt, A.mult)
    fill(R("ON64", 0, 128), 64.0)
    for h, col in enumerate(("colC", "colB")):
        V(ts, R("CD", 128 * h, 128 * h + 128), R("rI", 0, 128), c1("colA"), c1(col), A.mult, A.add)
    V(ts, R("MMIN", 0, 128), R("rI", 0, 128), 0.0, BIG, A.is_equal, A.mult)
    V(ts, In, R("dI", 0, 128), 0.0, -1.0, A.is_equal, A.mult)
    for name, by in ((I2n, -2048.0), (R("Ih", 0, 128), 0.5), (R("Ic", 0, 128), 1.0 / 128), (R("IBn", 0, 128), -1.0)):
        S(name, I16, F.Copy, None, by)
    if any(CFG["packed"]):
        for name in ("I64", "SK"):
            S(R(name, 0, 128), I16, F.Copy, None, 65536.0)
        S(R("SK", 128, 256), R("BHn", 0, 128), F.Copy)

    def factors(j, name, rows):
        for h in (0, 1):
            o = R("b%d" % (4 + h), 128 * j, 128 * j + 128, 1, 65)
            group([(o, R("ZQ", a - s * h, a - s * h + 65), r) for a, s, r in rows])
            S(R(name + str(h), 0, 128, 1, 65), o, F.Copy)
    for i in range(3):
        V(ts, R("dg%d" % i, 0, 128), I16, R("hf", i, i + 1), None, A.mult)
    factors(0, "PM_", ((72, 8, R("dg0", 0, 128)), (168, 8, R("BHn", 0, 128))))
    factors(1, "PQ_", ((72, 8, R("dg1", 0, 128)), (24, 8, R("dg2", 0, 128)), (184, 8, R("BHn", 0, 128)), (328, 0, I16)))
    C("g", tab("I", 1024), R("ixi", 0, 1024))
    V(ts, R("IB", 0, 136), R("dI", 0, 136), 4.0, None, A.is_equal)
    V(ts, R("BBn", 0, 128), R("gI", 0, 128), c1("pg"), -1.0, A.is_equal, A.mult)
    S(R("BL1", 0, 8), R("BLK", 8, 16), F.Copy, None, -1.0)
    S(R("BL2", 0, 8), R("BLK", 8, 16), F.Copy, None, 2.0)
    for buf in ("x_0", "x_1") + (("XG_0", "XG_1") if any(CFG["packed"]) else ()):
        fill(R(buf, 2048, 2064), UP)
    V(ts, R("CS", 0, 128), R("r15I", 0, 128), c1("colA"), c1("colC"), A.mult, A.add)
    fill(R("CS", 15, 128, 16, 64), -4096.0)
    V(ts, R("MMAX", 0, 128), R("rI", 0, 128), 0.0, -BIG, A.is_equal, A.mult)
    V(tc, R("tf", 0, 2), R("thi", 0, 2))
    DOWN = -0.5 + 2.0 ** -12
    fill(R("ONf", 0, 128), -1.0 / 32)
    fill(R("UPn", 0, 128), -UP)
    V(ts, c1("m15"), c1("p16"), 15.0, -1.0 / 64, A.is_lt, A.mult)
    V(ts, c1("acol"), c1("tf"), c1("m15"), None, A.mult)
    for h in (0, 1):
        V(ts, R("CB", 128 * h, 128 * h + 128), I16, R("tf", 1), -1.0 / 64, A.mult, A.mult)
    V(ts, R("CS", 128, 256), I16, c1("acol"), -16 * UP / (64 * 128), A.mult, A.add)
    V(ts, c1("pk1"), c1("p4"), 8.0, 25.0, A.mult, A.add)
    V(ts, c1("pk2"), c1("p4"), c1("pk1"), 16.0, A.mult, A.add)
    V(ts, R("PK", 0, 1), c1("b4"), float(BW), c1("pk2"), A.mult, A.add)
    V(ts, R("PK", 2, 3), R("PK", 0, 1), 2.0 * BW - 1, None, A.min)
    C("s", c1("k15"), c1("p16"), -1.0, 15.0)
    V(ts, R("RPJ", 0, 128), R("dg4", 0, 128), 0.0, -1.0, A.is_equal, A.mult)
    V(ts, R("RPK", 0, 128), R("dg4", 0, 128), -2.0, None, A.is_equal)
    V(ts, R("SLW", 0, 16), R("slI", 0, 16), 0.0, None, A.is_equal)
    V(ts, R("dl", 0, BW), R("dcol", 0, BW), c1("pf"), -1.0, A.subtract, A.max)
    for b in range(6):
        V(ts, R("EE", BW * b, BW * b + BW), R("qrel", 0, BW), 4.0 * (b if b < 2 else b - 2), c1("pg" if b < 2 else "pf"), A.add, A.is_equal)
    for b in range(2):
        for c in (2 * b, 2 * b + 1):
            C("v", R("TT", BW * c, BW * c + BW), R("dl", 0, BW), *((2048.0, 2048.0), (-4096.0, -2048.0))[b])
    for q in range(4):
        a = SEG[q] + 16 * (q + 1)
        C("s", R("EE", a, 6 * BW, BW), R("EE", a, 6 * BW, BW), 1.0 / 4096)
        fill(R("TT", a, 4 * BW, BW), DUMP / 4096)
    V(tc, R("SM", BW, 2 * BW), R("SM", 0, BW))
    fill(R("QT", 1, 64, 2), 0.0)
    S(R("BKn", 0, 16), R("BLK", 0, 16), F.Copy, None, -1.0)
    S(R("BK2", 0, 16), R("BLK", 0, 16), F.Copy, None, 2.0)

    def keys(K, at, n, m, a, con, payload, cuts, d, alone):
        def sums(src, by, lo, hi, last):
            P([(R(K, at + k, at + n, 16, hi, lo), R(src, 16 * lo + k, 16 * hi, 16), R(by, 0, n // 16), False, last and k == m - 1)
               for k in range(m)])
            ops[-1]["name"] = "t" + src
        pay = (R(K, at, at + 128), payload, I16, False, bool(d))
        P([(R(K, at, at + n), R("ON64", 0, 128), con, alone, False)] + ([] if d else [pay]))
        for lo, hi in cuts:
            if d:
                sums(d, "BKn", lo, hi, False)
            sums(a, "BK2" if d else "BLK", lo, hi, not d)
        if d:
            P([pay])
            ops[-1]["writes"] = [R(K, at, at + n)]

    def earlier(h, own, spread, pick, row, p, Ad, ms, links):
        D, W = "b%d" % (4 + h), 2 * BW
        rows = [(BW * b + SEG[q], 16 * (q + 1), 64 * b) for b in (0, 1) for q in range(4)]
        P([(R(D, 0, W), R("MK", 0, 128, 1, 16), R("TT", W * links, W * links + W, 1, 16), True, False)] +
          [(R(D, a, a + n), pick, R(row, 128 * h + l, 128 * h + l + n, 1, p), False, False) for a, n, l in rows])
        ops[-1]["name"] = "t%s%d" % (Ad, h)
        if links:
            P([(R(D, a, a + n), R("nrx", 128 * h, 128 * h + 128), R("I2n", l, l + n), False, False) for a, n, l in rows])
        P([(R(D, 0, W), own, spread, False, True)])
        S(R(Ad, W * h, W * h + W), R(D, 0, W), F.Abs, None, 4096.0)
        V(scan, R(ms, W * h, W * h + W), R("SM", 0, W), R(Ad, W * h, W * h + W), 0.0, A.max, A.min)

    def scatter(table, n, off, a, b, far=8):
        for k in (1, 0, 3, 2):
            o = far * (k // 2) + 4 * (k % 2)
            V(tt, ind(R(table, 0, DUMP + n), R(off, o, o + 4)), R(a, 64 * k, 64 * k + 64), R(b, 64 * k, 64 * k + 64), A.add)
            ops[-1]["name"] = "v%s@%d" % (table, k)

    def repack(out, src, op):
        for c in range(0, 2048, 512):
            group([(R("b6", 0, 512), R("I64", 0, 128), R("xb", c, c + 512))])
            V(tt, tab(out, c + 512, c), R(src[0], src[1] + c, src[1] + c + 512), R("b6", 0, 512), op)

    RLu = R("RLu", 0, 128, 1, 65)
    for t in range(3):
        now[0] = t
        packed = CFG["packed"][t]
        z, zx = "z%d" % t, "zx%d" % (t % 2)
        half = lambda buf, h, at=0: R(buf, at + 128 * h, at + 128 * h + 128)
        up = lambda h: half(z if t else "zt", h)

        def far(h, x):
            o = half(FB[h], h) if t == 2 else R("b1", 0, 256)
            P([(o, R("ON64", 0, 128), R("CB", 0, width(o)), True, False)] * (t == 2 or h == 0) +
              [(half(FB[h], h), up(h), R("BBn", 0, 128), False, False)])
            P([(R(FB[h], 128 * h + k, 128 * h + 128, 16), R(x, k, 2048, 16), R("BL1", 0, 8), False, False) for k in range(16)])
        FB = ("b1", "b0" if t == 2 else "b1")
        for h in (0, 1):
            group([(R("b0", 8 * h, 8 * h + 8), l, R("W8", 0, 8)) for l in ([R("UPn", 0, 128)] if t else []) + [half(z, h)]])
        C("s" if t else "v", R("ui", 0, 16), R("b0", 0, 16))
        V(ts, R("ui", 0, 16), R("ui", 0, 16), 4095, None, A.bitwise_and)
        if CFG["uu"][t] == "s":
            S(R("uu", 0, 16), R("ui", 0, 16), F.Square)
        else:
            V(tt, R("uu", 0, 16), R("ui", 0, 16), R("ui", 0, 16), A.mult)
        V(ts, R("UQ", 0, 16), R("ui", 0, 16), 2047, None, A.bitwise_and)
        V(ts, R("UQ", 48, 64), R("ui", 0, 16), 31, None, A.bitwise_and)
        V(ts, R("UQ", 16, 32), R("uu", 0, 16), 4, 2047, A.arith_shift_right, A.bitwise_and)
        V(ts, R("UQ", 32, 48), R("uu", 0, 16), 5, 1023, A.arith_shift_right, A.bitwise_and)
        C(CFG["UH"] if t else "v", R("UH", 0, 64), R("UQ", 0, 64))
        group([(R("b0", 128, 256, 1, 65), R("UH", 0, 65), I16)])
        S(RLu, R("b0", 128, 256, 1, 65), F.Copy)
        P([(half("b0", h, 256), R("PM_%d" % h, 0, 128, 1, 65), RLu, True, True) for h in (0, 1)])
        for h in (0, 1):
            if t and CFG["emi"][h] == "s":
                S(half("emi", h), half("b0", h, 256), F.Identity, c1("Nc"))
            elif t:
                V(ts, half("emi", h), half("b0", h, 256), R("b0", 16), R("b0", 17), A.add, A.add)
                ops[-1]["name"] = "vsum%d" % h
            else:
                C("vs"[h], half("emi", h), half("b0", h, 256))
            V(ts, half("emi", h), half("emi", h), 1023, None, A.bitwise_and)
            C(CFG["emu"][h], half("emu", h), half("emi", h))
        C("g", R("emh", 0, 256), R("emi", 0, 256))
        if t == 0:
            C("v", R("zt", 0, 256), R(z, 0, 256), None, UP)
            for m, e in enumerate(CFG["z0"]):
                if e in "vs":
                    C(e, R(zx, m, 4096, 16), R("zt", 0, 256))
                else:
                    C(e.lower(), R(zx, m, 2048, 16), half("zt", 0))
                    C("g", R(zx, 2048 + m, 4096, 16), half("zt", 1))
        else:
            for h in (0, 1):
                for m in range(16):
                    C("s" if h == 0 and m >= 16 - CFG["zs"] else "g", R(zx, 2048 * h + m, 2048 * h + 2048, 16), half(z, h))
                    if m % 2 and ops[-1]["q"] == "g":
                        join()
        if t == 1:
            C("v", R("zr", 0, 256), R(z, 0, 256), None, -UP)
        for h in (0, 1):
            H = "_%d" % h
            if h == 1 and t:
                group([(R("b0", 128, 256), half(z, h), IB)])
                S(R("zT", 0, 128), R("b0", 128, 256), F.Copy, None, -1.0)
            for a, b in CFG["g"][h]:
                got, d = ind(tab("G", 1024), R("emu", 128 * h + a, 128 * h + b)), R("DG" + H, 16 * a, 16 * b)
                if h == 0:
                    V(tt, d, got, R(zx, 16 * a, 16 * b), A.subtract)
                    V(ts, R("AG" + H, 16 * a, 16 * b), d, -UP, UP, A.max, A.add)
                else:
                    S(d, got, F.Copy)
                    for c in range(16 * a, 16 * b, 512):
                        o, l = R(CFG["sub"][c // 512], 0, 512), c // 16
                        P([(o, R("zT", 0, 128, 1, l + 32, l), R("EN", 0, 512, 1, l + 32, l), True, False) if t else
                           (o, R("IBn", 0, 128), R(zx, 2048 + c, 2048 + c + 512), True, False)])
                        P([(o, IB, R("DG" + H, c, c + 512), False, True)])
                        S(R("AG" + H, c, c + 512), o, F.Abs, UP)
            keys("b%d" % (2 + h), 0, 128, 16, "AG" + H, half("CD", h), half("emh", h), ((0, 128),), None if h else "DG_0", True)
            V(scan, R("km" + H, 0, 128), R("MMIN", 0, 128), R("b%d" % (2 + h), 0, 128), 0.0, A.add, A.min)
            V(ts, R("ej" + H, 0, 8), R("km" + H, 15, 128, 16), 1023, None, A.bitwise_and)
            V(tt, R("ME" + H, 0, 128), ind(R("ej" + H, 0, 8), R("OFFR", 0, 8)), R("MK", 0, 128), A.mult)
            group([(R("b7", 8 * h, 8 * h + 8), R("ME" + H, 0, 128), Q16)])
            C(CFG["eu"][h], R("eu", 8 * h, 8 * h + 8), R("b7", 8 * h, 8 * h + 8))
            C(CFG["Ju"][h], R("Ju" + H, 0, 128), ind(tab("I", 1024) if t else R("ixi", 0, 1024), R("eu", 8 * h, 8 * h + 8)))
            C("g", half("Jh", h), R("Ju" + H, 0, 128))
            group([(half("b7", h, 256), R("ME" + H, 0, 128), I16)])
        P([(half("b6", h, 256), R("PQ_%d" % h, 0, 128, 1, 65), RLu, True, True) for h in (0, 1)])
        S(R("q2", 0, 256), R("b6", 256, 512), F.Copy, DOWN, 1.0 / 2048)
        if t == 0 and any(CFG["packed"]):
            repack("XL", ("lki", 0), A.add)
        elif t == 0:
            for a in (0, 1024):
                C("g", tab("L", a + 1024, a), R("lki", a, a + 1024))
        if t == 2 and packed:
            repack("L", ("XL", DUMP), A.subtract)
        C("g", R("Jf", 0, 256), R("Jh", 0, 256))
        VJ = R("b2", 256, 512)
        P([(VJ, I2n, R("q2", 0, 256), True, False)] +
          [(half("b2", h, 256), R("PQ_%d" % h, 0, 128, 1, 65), RLu, False, False) for h in (0, 1)] +
          [(VJ, In, R("Jh", 0, 256), False, True)])
        S(R("Y", 0, 256), R("b7", 256, 512), F.Copy)
        def winners():
            for h in (0, 1):
                earlier(h, R("ME_%d" % h, 0, 128), R("EE", 0, 2 * BW), R("BHn", 0, 128), "Y", 128, "AdE", "msE", 0)
            C(CFG["oE"][t], R("oEu", 0, 16), ind(R("msE", 0, 4 * BW), R("PK", 0, 1)))
        if not CFG["late"][t]:
            winners()
        raw = "zr" if t else z
        if t < 2:
            V(tt, R("dz", 0, 256), ind(tab("G", 1024), R("eu", 0, 16)), R(raw, 0, 256), A.subtract)
        for h in (0, 1):
            H, K = "_%d" % h, "b%d" % (2 + h)
            X = ("XG" if packed else "x") + H
            for a, b, e in CFG["x" if t else "x0"][h]:
                C(e, R(X, 16 * a, 16 * b), ind(R("xb", 0, 2048), R("Ju" + H, a, b)), None, UP)
            if packed:
                w = 2048 // CFG["casts"][t]
                for c in range(0, 2048, w):
                    dma("g", R("x" + H, c, c + w), R(X, c, c + w), 2 * w)
                P([(R(K, 256 + k, 512, 16), R(X, k, 2048, 16), R("SK", k, 256, 16), k == 0, False) for k in range(16)])
                C(CFG["r"][h], half("rd", h), R(K, 256, 384))
                V(tt, half("Lh", h), R(K, 256, 384), half("rd", h), A.subtract)
                group([(half("b6", h), half("Lh", h), I16)])
                ops[-1]["name"] = "tnu%d" % h
                C(CFG["nu"][h], R("nu" + H, 0, 128), half("b6", h))
            else:
                for a, b, e in CFG["l" if t else "l2"][h]:
                    C(e, R("Lg" + H, 16 * a, 16 * b), ind(tab("L", 2048) if t else R("lki", 0, 2048), R("Ju" + H, a, b)))
                for a, b in HALVES:
                    o = R("b6", 128 * h + a, 128 * h + b)
                    group([(o, R("SEL", 128 * k, 128 * k + 128), R("Lg" + H, 16 * a + k, 16 * b, 16)) for k in range(16)])
                    C(CFG["nu"][h], R("nu" + H, a, b), o)
                C("g", half("Lh", h), R("nu" + H, 0, 128))
            far(h, "x_%d" % h)
            for (a, b, e), e2 in zip(CFG["y"], CFG["relu"]):
                if a // 128 != h:
                    continue
                a, b = a - 128 * h, b - 128 * h
                got = ind(R("xb", 0, 2048), R("nu" + H, a, b))
                if e == "v":
                    d = R("Dy" + H, 16 * a, 16 * b)
                    V(tt, d, got, R(X, 16 * a + 1, 16 * b + 1), A.subtract)
                    if e2 == "v":
                        V(ts, R("Ay" + H, 16 * a, 16 * b), d, -UP, UP, A.max, A.add)
                    else:
                        S(R("Ay" + H, 16 * a, 16 * b), d, F.Relu, UP)
                else:
                    S(R("AG" + H, 16 * a, 16 * b), got, F.Copy)
                    ops[-1]["name"] = "sy%d@%d" % (h, 16 * a)
                    for c in range(16 * a, 16 * b, 512):
                        o = R("b%d" % (4 + c // 512 % 2), 0, 512)
                        P([(o, R("IBn", 0, 128), R("x" + H, c + 1, c + 513), True, False)])
                        P([(o, IB, R("AG" + H, c, c + 512), False, True)])
                        S(R("Ay" + H, c, c + 512), o, F.Abs, UP / 2, 0.5)
            w = CFG["scan"][t]
            for c in range(0, 2048, w):
                V(scan, R("mx" + H, c, c + w), R("MR", 0, w), R(X if CFG["wide"][t][h] else "x" + H, c, c + w), 0.0, A.mult, A.max)
            o = half("b0" if t < 2 else "b6", h, 256)
            group([(o, IB, half(z, h)), (o, IB, R("mx" + H, 15, 2048, 16))])
            if t < 2:
                C(CFG["zn"][h], half("zs%d" % t, h), o, 0.5, -0.25 + (0 if t else UP / 2))
            else:
                S(half("zt", h), o, F.Copy, -0.25, 0.5)
                C(CFG["zl"], half("zs2", h), half("zt", h), None, -UP)
            add("g", "remote", [(t, 128 * h, 128 * h + 128, "arr%d" % (2 * t + h))], [half("zs%d" % t, h)], [half("z%d" % (t + 1), h)], RCOST, RLAT)
        if CFG["late"][t]:
            winners()
        for h in (0, 1):
            K = "b%d" % (2 + h)
            keys(K, 0, 256, 15, "Ay_%d" % h, R("CS", 0, 256), half("Jh", h), CFG["cuts"][h], "Dy_%d" % h, True)
            S(half("le", h), R(K, 128, 256), F.Sign, -0.5)
            V(scan, half("cs", h), R("MR", 0, 128), half("le", h), 0.0, A.mult, A.add)
            S(half("nrx", h), ind(half("cs", h), R("OF15", 0, 8)), F.Sign, 9.0, None, R("Nx", h, h + 1) if t < 2 else None)
            if t < 2:
                group([(half("b6", h), R("ON64", 0, 128), R("Ic", 0, 128)), (half("b6", h), half("nrx", h), R("Ih", 0, 128))])
                V(tt, half("tg", h), half("b6", h), half("dz", h), A.mult)
            V(scan, half("sm", h), R("MMAX", 0, 128), R(K, 0, 128), 0.0, A.add, A.max)
        if t < 2:
            for h in (0, 1):
                group([(R("b0", 16 + h), R("ONf", 0, 128), R("Nx", h))])
            scatter("G", 1024, "oEu", "tg", raw)
        for h in (0, 1):
            w = 2048 // CFG["folds"][t][h]
            for c in range(0, 2048, w):
                M, X, Z = R("M%d_%d" % (t, h), c, c + w), R("x_%d" % h, c, c + w), R(zx, 2048 * h + c, 2048 * h + c + w)
                add("g", "fold", [(M, X, Z, sum(o["kind"] == "fold" for o in ops))], [X, Z], [M], RCOST, FLAT0 + FLAT1 * w)
        for h in (0, 1):
            P([(R(FB[h], 128 * h + k, 128 * h + 128, 16), R("M%d_%d" % (t, h), k, 2048, 16), R("BL2", 0, 8), False, t == 2 and k == 15)
               for k in range(16)])
            if t == 2:
                S(half("fT", h), half(FB[h], h), F.Copy)
                group([(half("b1", h, 256), half("fT", h), I16), (half("b1", h, 256), half("nrx", h), I2n)])
                V(ts, half("ch", h), half("b1", h, 256), -2047.5, None, A.is_gt)
                V(tt, half("tmp", h), half("ch", h), half("b2", h, 256), A.mult)
        if t < 2:
            P([(half("b1", h), I2n, half("nrx", h), False, h == 1) for h in (0, 1)])
            S(R("fT", 0, 256), R("b1", 0, 256), F.Sign, 2047.5)
            for h in (0, 1):
                group([(half("b1", h, 256), R("ON64", 0, 128), R("Ic", 0, 128)), (half("b1", h, 256), half("fT", h), R("Ih", 0, 128))])
            S(R("vj", 0, 256), VJ, F.Copy)
            V(tt, R("tmp", 0, 256), R("b1", 256, 512), R("vj", 0, 256), A.mult)

        scatter("I", 1024, "oEu", "tmp", "Jf")
        if t == 2:
            dma("y", "yi", tab("I", 1024), 4096)
        table = "XL" if t < 2 and any(CFG["packed"]) else "L"
        for h0, h1 in ((0, 2),) if t < 2 else ((0, 1), (1, 2)):
            a, b = 128 * h0, 128 * h1
            V(ts, R("SJ", 16 * h0, 16 * h1, 2), R("sm", a + 15, b, 16), 2047, None, A.bitwise_and)
            V(ts, R("SJ", 16 * h0 + 1, 16 * h1, 2), R("sm", a + 15, b, 16), 11, 15, A.arith_shift_right, A.bitwise_and)
            C(CFG["QT"][t], R("QT", 32 * h0, 32 * h1, 2), R("SJ", 16 * h0, 16 * h1))
            P([(R("b7", 256 + 128 * h, 384 + 128 * h, 1, 32), R("QT", 32 * h, 32 * h + 32), I16, True, True) for h in range(h0, h1)])
            RL = R("RL", a, b, 1, 32)
            S(RL, R("b7", 256 + a, 256 + b, 1, 32), F.Copy)
            o = R("b7", 48 + 8 * h0, 48 + 8 * h1)
            if t == 2 and CFG["WT"][h0] == "s":
                WJ, spread = R("WT", a, b, 1, 8), [R("EE", 2 * BW, 4 * BW, 1, 8)]
                P([(R("b7", 64 + r, 192, 16, 8), R("RL", a + r, b, 16, 32), R("SLW", 0, 8, 1, 32), True, True) for r in range(16)])
                S(WJ, R("b7", 64, 192, 1, 8), F.Copy)
                group([(o, WJ, R("IW", 4, 12, 1, 8))])
            elif t == 2:
                WJ, spread = R("WT", 256 * h0, 256 * h0 + 128), [R("EE", 0, 2 * BW)]
                V(tt, WJ, ind(R("SJ", 16 * h0, 16 * h1), R("OFF2", 0, 8)), R("MK", 0, 128), A.mult)
                group([(o, WJ, Q16)])
            else:
                WJ, spread = R("WT", 0, 128, 1, 16), [R("EE", 2 * BW * (h + 1), 2 * BW * (h + 2), 1, 16) for h in (0, 1)]
                P([(R("b7", 64 + r, 192, 16, 16), R("RL", r, 256, 16, 32), R("SLW", 0, 8, 1, 32), True, True) for r in range(16)])
                S(WJ, R("b7", 64, 192, 1, 16), F.Copy)
                group([(o, WJ, R("IW", 4, 20, 1, 16))])
            C(CFG["J16"][t], R("Ju16", 8 * h0, 8 * h1), o)
            for h in range(h0, h1):
                earlier(h, WJ, spread[h - h0], R("RPJ", 0, 128, 1, 32), "RL", 32, "AdJ", "msJ", 1)
            pk = 2 if t == 2 else 0
            C(CFG["oJ"][t], R("oJu", 16 * h0, 16 * h0 + 16), ind(R("msJ", 2 * BW * h0, 2 * BW * h1), R("PK", pk, pk + 1)))
            S(R("Lold", a, b), ind(tab(table, 2048), R("Ju16", 8 * h0, 8 * h1)), F.Copy)
            group([(R("b7", 256 + a, 256 + b), R("RPK", 0, 128, 1, 32), RL)])
            V(ts, R("mk", a, b), R("b7", 256 + a, 256 + b), c1("k15"), None, A.is_equal)
            o = R("b1", 256 + a, 256 + b) if t < 2 else R("b6", a, b)
            group([(o, ISH, R("Jh", a, b)), (o, In, R("Lh", a, b))])
            V(tt, R("t2", a, b), o, R("mk", a, b), A.mult)
        scatter(table, 2048, "oJu", "t2", "Lold", 8 if t < 2 else 16)
    dma("y", R("yz", 0, 128), R("z3", 128, 256), 256)
    dma("y", R("yz", 128, 256), R("z3", 0, 128), 256)
    dma("y", "yl", tab("L", 2048), 8192 * CFG["rows"] // 16)
    return ops


SPAN = ("b1", "b2", "b3", "b4", "b5")


def edges(ops):
    touched, pre = {}, []
    for o in ops:
        e = {}
        for w, rs in ((True, o["writes"]), (False, o["reads"])):
            for r in rs:
                for (j, s, sw) in touched.get(r[0], []):
                    same = ops[j]["q"] == o["q"]
                    if same and o["q"] == "t" and bank(r):
                        if r[0] in SPAN or clash(r, s):
                            e.setdefault(j, False)
                    elif (w or sw) and clash(r, s):
                        e[j] = e.get(j, False) or bool(not same or sw or ops[j]["lat"] > 0)
        o["clash"] = set(e) if o["q"] != "t" else set()
        pre.append(e)
        for w, rs in ((True, o["writes"]), (False, o["reads"])):
            for r in rs:
                touched.setdefault(r[0], []).append((o["i"], r, w))
    where = {(o["t"], o["name"]): o["i"] for o in ops}
    for t in range(3):
        for turn in TURNS[t]:
            got = [where.get((t - w.count("<"), w.strip("<"))) for w in turn.split()]
            got = [i for i in got if i is not None]
            for j, i in zip(got, got[1:]):
                pre[i].setdefault(j, False)
    return pre


def sequence(pre):
    seq, seen = [], set()
    for i in range(len(pre)):
        todo = [i]
        while todo:
            left = [j for j in pre[todo[-1]] if j not in seen]
            if left:
                todo.append(left[0])
            elif todo[-1] not in seen:
                seen.add(todo[-1])
                seq.append(todo.pop())
            else:
                todo.pop()
    return seq


def fit(seq, lags, uses, tail=None, limit=None, old=None):
    n, k0 = len(seq), 0
    if old:
        while k0 < n and seq[k0] == old[0][k0]:
            k0 += 1
        start, busy = list(old[1]), [[x for x in taken if x[3] < k0] for taken in old[2]]
    else:
        start, busy = [0.0] * n, [[(-2.0, -1.0, -1, -1)] * 2 for _ in range(14)]
    for k in range(k0, n):
        i, s = seq[k], 0.0
        for j, d in lags[i]:
            d += start[j]
            if d > s:
                s = d
        mine = uses[i]
        res, off, m, who = mine[0]
        taken = busy[res]
        if not mine[1:] and taken[-1][1] <= s + off:
            if limit and s + tail[i] > limit:
                return None
            start[i] = s
            taken.append((s + off, s + off + m, who, k))
            continue
        moved = True
        while moved:
            moved = False
            for res, off, m, who in mine:
                taken, at = busy[res], s + off
                if taken[-1][1] > at:
                    p = -1
                    while taken[p][0] >= at:
                        p -= 1
                    for a, b, other, _k in taken[p - 1:]:
                        if a >= at + m - 1e-6:
                            break
                        if at < b - 1e-6 and who != other:
                            at, moved = b, mine[1:]
                    s = at - off
        if limit and s + tail[i] > limit:
            return None
        start[i] = s
        for res, off, m, who in mine:
            taken, at = busy[res], s + off
            if taken[-1][0] <= at:
                taken.append((at, at + m, who, k))
            else:
                p = -1
                while taken[p - 1][0] > at:
                    p -= 1
                taken.insert(p, (at, at + m, who, k))
    return seq, start, busy


def harden(way, arcs, banks, rng, passes, heat):
    n, cases = len(way), []
    succ, before = [[] for _ in range(n)], [[] for _ in range(n)]
    for j, i in arcs:
        succ[j].append(i)
        before[i].append(j)
    for case in CASES:
        ops, wake = build(case), case.get("WAKE", WAKE)
        queue = ["vstgy".index(o["q"]) for o in ops]
        span = [o["cost"] + o["lat"] for o in ops]
        rows = []
        for i, o in enumerate(ops):
            own = [(queue[i], o["cost"])] + [(6 + 3 * int(b[1]) + queue[i], o["cost"] + wake) for b in banks[i]]
            rows.append(([(j, span[j] + wake if arcs[j, i] else ops[j]["cost"]) for j in before[i]],
                         [queue[i]] + [6 + 3 * int(b[1]) + q for b in banks[i] for q in (0, 1, 2) if q != queue[i]], own,
                         o.get("hold"), span[i]))
        cases.append(rows)
    final = [i for i in range(n) if not succ[i]]

    def replay(rows, way, a, old):
        a = a // 16 * 16
        head, why, marks = list(old[0]), list(old[1]), old[2][:a // 16]
        free, last = list(old[2][a // 16][0]), list(old[2][a // 16][1])
        for k in range(a, n):
            if k % 16 == 0:
                marks.append((tuple(free), tuple(last)))
            i = way[k]
            lags, rival, own, hold, span = rows[i]
            s, by = 0.0, None
            for j, d in lags:
                d += head[j]
                if d > s:
                    s, by = d, j
            for r in rival:
                if free[r] > s:
                    s, by = free[r], ~last[r]
            if hold:
                if free[5] + hold - span > s:
                    s, by = free[5] + hold - span, ~last[5]
                free[5], last[5] = s + span, i
            head[i], why[i] = s, by
            for r, m in own:
                free[r], last[r] = s + m, i
        end = max(final, key=lambda i: head[i] + rows[i][4])
        return head, why, marks, head[end] + rows[end][4], end

    def held(got):
        i, out = got[4], []
        while i is not None:
            j = got[1][i]
            if j is not None and j < 0:
                j = ~j
                out.append((j, i))
            i = j
        return out

    now = [replay(rows, way, 0, ([0.0] * n, [None] * n, [((0.0,) * 30, (0,) * 30)])) for rows in cases]
    base = [got[3] for got in now]
    at, hot = {i: k for k, i in enumerate(way)}, [held(got) for got in now]
    mean = 1.0
    best = (mean, list(way), base)
    for k, d in enumerate(rng.random((passes, 5)).tolist()):
        pairs = hot[int(d[0] * len(hot))]
        j, i = pairs[int(d[1] * len(pairs))]
        a, b = at[j], at[i] + 1
        part = way[a:b]
        group, near, ends = ({i}, before, part[::-1]) if d[3] < 0.5 else ({j}, succ, part)
        for x in ends:
            if x in group:
                group.update(near[x])
        if i in group and j in group:
            continue
        part = [x for x in part if (x in group) == (d[3] < 0.5)] + [x for x in part if (x in group) != (d[3] < 0.5)]
        trial, new, total = way[:a] + part + way[b:], [], 0.0
        room = len(cases) * (mean - (0.05 + heat * (1 - k / passes)) * 1e-3 * math.log(d[4]))
        for rows, old, was in zip(cases, now, base):
            new.append(replay(rows, trial, a, old))
            total += new[-1][3] / was
            if total + 0.985 * sum(x[3] / y for x, y in zip(now[len(new):], base[len(new):])) > room:
                break
        else:
            if total <= room:
                way, now, mean = trial, new, total / len(cases)
                at.update((x, a + p) for p, x in enumerate(part))
                hot = [held(got) for got in now]
                if mean < best[0]:
                    best = (mean, list(way), [x[3] for x in now])
    PLAN["ends"] = base, best[2]
    return best[1]


def schedule(ops, pre, stages, seed):
    n = len(ops)
    span = [o["cost"] + o["lat"] for o in ops]
    banks = [sorted(set(bank(r) for r in o["reads"] + o["writes"] if bank(r))) for o in ops]
    lag = [{j: (span[j] + WAKE if w else ops[j]["cost"]) for j, w in pre[i].items()} for i in range(n)]
    fwd = [[(j, d) for j, d in lag[i].items() if not any(lag[k].get(j, -1e9) + e >= d for k, e in lag[i].items())] for i in range(n)]
    bwd = [[] for _ in range(n)]
    for i in range(n):
        for j, d in fwd[i]:
            bwd[j].append((i, d - span[j] + span[i]))
    ahead, back = [], []
    for i, o in enumerate(ops):
        u = [(8 + "vstgy".index(o["q"]), 0.0, o["cost"], i)] + [(int(b[1]), 0.0, o["cost"] + WAKE, o["q"]) for b in banks[i]]
        if o.get("hold"):
            u.append((13, span[i] - o["hold"], o["hold"], i))
        ahead.append(u)
        back.append([(res, span[i] - off - m, m, who) for res, off, m, who in u])

    def mend(key, lags, way):
        for i in way:
            for j, d in lags[i]:
                if key[j] >= key[i]:
                    key[i] = key[j] + 1e-3
        return key

    def early(key, limit=None, old=None):
        got = fit(np.argsort(key, kind="stable").tolist(), fwd, ahead, tail, limit, old)
        if got:
            end = max(got[1][i] + span[i] for i in final)
            return end + CFG["mean"] * sum(got[1][i] for i in long) / len(long), end, got, key

    def late(start):
        key = mend([-start[i] - span[i] for i in range(n)], bwd, seq[::-1])
        s = fit(sorted(range(n), key=lambda i: key[i]), bwd, back)[1]
        return mend([-s[i] - span[i] for i in range(n)], fwd, seq)

    def move(key, i, by):
        todo, sign, lags = [(i, key[i] + by)], (1 if by > 0 else -1), (bwd if by > 0 else fwd)
        while todo:
            i, at = todo.pop()
            if sign * key[i] < sign * at:
                key[i] = at
                todo += [(j, at + sign * 1e-2) for j, d in lags[i]]

    def tight(start, pick):
        ends = {(res, round(start[i] + off + m)): i for i in range(n) for res, off, m, who in ahead[i]}
        i, out, arcs = max(range(n), key=lambda i: start[i] + span[i]), [], []
        while i is not None:
            out.append(i)
            got = [j for j, d in fwd[i] if abs(start[j] + d - start[i]) < 1]
            held = [ends[res, round(start[i] + off)] for res, off, m, who in ahead[i] if (res, round(start[i] + off)) in ends]
            held = [j for j in held if start[j] < start[i] and j not in pre[i]]
            if held and not got:
                arcs.append((held[-1], i))
            got = [j for j in got + held if start[j] < start[i]]
            i = got[int(pick * len(got))] if got else None
        return out, arcs

    def swap(key, j, i, a):
        same = alike[ops[j]["name"]], alike[ops[i]["name"]]
        every = a[4] < CFG["alike"] and ops[i]["t"] == ops[j]["t"] and len(same[0]) == len(same[1])
        for j, i in zip(*same) if every else [(j, i)]:
            if key[j] < key[i] and a[5] < 0.5:
                move(key, i, key[j] - key[i] - 1 - 300 * a[6])
            elif key[j] < key[i]:
                move(key, j, key[i] - key[j] + 1 + 300 * a[6])

    def copy(start, t, u, a, w):
        key, zero = list(start), [start[i] for i in alike["vDG_0@0"]]
        for same in alike.values():
            here, there = [i for i in same if ops[i]["t"] == t], [i for i in same if ops[i]["t"] == u]
            if len(here) == len(there):
                for i, j in zip(here, there):
                    if a - 4000 <= start[i] - zero[t] < a - 4000 + w:
                        key[j] = start[i] - zero[t] + zero[u]
        return mend(key, fwd, seq)

    seq = sequence(pre)
    final = [i for i in range(n) if not bwd[i]]
    long = [i for i in range(n) if ops[i]["cost"] > 800 and ops[i]["q"] in "vs"]
    alike = {}
    for o in ops:
        alike.setdefault(o["name"], []).append(o["i"])
    tail = [0.0] * n
    for i in seq[::-1]:
        tail[i] = max([span[i]] + [tail[k] + d + span[i] - span[k] for k, d in bwd[i]])
    rng = np.random.default_rng(seed)
    best = early(late(early(mend([-x for x in tail], fwd, seq))[2][1]))
    for passes, heat in stages:
        now = best
        hot, arcs = tight(now[2][1], 0.99)
        for k, d in enumerate(rng.random((passes, 3, 7)).tolist()):
            if d[0][0] < 0.03:
                key = late(now[2][1])
            elif d[0][0] < 0.03 + CFG["copy"]:
                key = copy(now[2][1], int(3 * d[1][1]), int(3 * d[1][2]), 30000 * d[1][3], 4000 + 20000 * d[1][4])
            else:
                key = list(now[3]) if d[0][1] < 0.8 else mend(list(now[2][1]), fwd, seq)
                for a in d[:(1, 1, 2, 3)[int(4 * d[1][0])]]:
                    if a[1] < CFG["aim"] and arcs:
                        swap(key, *arcs[int(a[2] * len(arcs))], a)
                        continue
                    i = long[int(a[2] * len(long))] if a[3] < 0.15 else int(a[2] * n) if a[3] < 0.35 else hot[int(a[2] * len(hot))]
                    for j in alike[ops[i]["name"]] if a[4] < CFG["alike"] else [i]:
                        move(key, j, (600, 2000, 6000)[int(3 * a[5])] * (2 * a[6] - 1) * abs(2 * a[6] - 1))
            more = -(5 + heat * (1 - k / passes)) * math.log(d[2][0])
            new = early(key, now[1] + more + 300, now[2])
            if new and new[0] < now[0] + more:
                now = new
                if d[2][2] < 0.5:
                    hot, arcs = tight(now[2][1], d[2][1])
                if new[1] < best[1]:
                    best = new
    end, start = best[1], best[2][1]
    place = {i: k for k, i in enumerate(seq)}
    order = sorted(range(n), key=lambda i: (start[i], place[i]))
    order = harden(order, {(j, i): pre[i][j] for i in range(n) for j, d in fwd[i]}, banks, rng, *CFG["harden"])
    waits, last = [dict(e) for e in pre], {}
    for i in order:
        for b in banks[i]:
            for q, j in last.setdefault(b, {}).items():
                if q != ops[i]["q"]:
                    waits[i][j] = True
            last[b][ops[i]["q"]] = i
    return order, waits, start, end


PLAN = {}


def plan(stages=((24000, 100.0), (26000, 60.0), (22000, 35.0)), seed=4):
    ops = build()
    return (ops,) + schedule(ops, edges(ops), stages, seed)


def helper(core, T, topo):
    return [c for c in topo.cores_of(core) if c not in T.cores and topo.die(c) == topo.die(core)][0]


def hand_back(g, core, owner, T, topo):
    rid, pid, _e = topo.addr(owner)
    folds = [PLAN["ops"][i]["calls"][0] for i in PLAN["order"] if PLAN["ops"][i]["kind"] == "fold"]
    for out, a, b, k in folds:
        g.wait_ge(T.sem["fa%d" % k], len(topo.engines(owner, core)))
        piece = T[out[0]][:, out[1]:out[2]]
        g.remote_dma(piece, piece, T.sem["fb%d" % k], T.sem["loc"], pid, rid, topo.mask(core, owner))
    g.wait_ge(T.sem["loc"], len(folds) * len(topo.engines(core, owner)))


def rank_program(g, core, T, topo):
    if "ops" not in PLAN:
        PLAN["ops"], PLAN["order"], PLAN["waits"] = plan()[:3]
    rank = T.rank_of(core)
    if rank is None:
        for owner in T.cores:
            if helper(owner, T, topo) == core:
                hand_back(g, core, owner, T, topo)
        return
    ops, pre = PLAN["ops"], PLAN["waits"]
    n = len(T.cores)
    queue = {"v": g.vector, "s": g.scalar, "t": g.tensor, "g": g, "y": g.sync}
    qsem = {"v": "qv", "s": "qs", "t": "qt", "g": "qg"}
    vector = {"tensor_copy": g.vector.tensor_copy, "tensor_scalar": g.vector.tensor_scalar, "tensor_tensor": g.vector.tensor_tensor,
              "tensor_tensor_scan": g.vector.tensor_tensor_scan, "memset": g.vector.memset}
    count = {}
    seen = {q: {} for q in queue}
    done = {}

    def ap(r):
        if isinstance(r, IndOp):
            return ap(r[0]).indirect(ap(r[1]))
        name, off = PLACE[r[0]]
        a, b, st, p, p0 = r[1] + off, r[2] + off, r[3], r[4], r[5]
        if st == 1:
            return T[name][:, a:b] if p - p0 == 128 else T[name][p0:p, a:b]
        return T[name][:, a:b:st] if p - p0 == 128 else T[name][p0:p, a:b:st]

    def arg(x):
        return ap(x) if isinstance(x, tuple) else x

    place = {i: k for k, i in enumerate(PLAN["order"])}
    for i in PLAN["order"]:
        o = ops[i]
        q, eng, k = o["q"], queue[o["q"]], o["kind"]
        known = seen[q]
        for j in sorted(pre[i], key=lambda j: -place[j]):
            if not pre[i][j] and j not in o["clash"]:
                continue
            sem, val, kn = done[j]
            if known.get(sem, 0) < val:
                eng.wait_ge(T.sem[sem], val)
                for s in kn:
                    known[s] = max(known.get(s, 0), kn[s])
                known[sem] = max(known.get(sem, 0), val)
        if k == "dma":
            out, in_ = [ap(x) if isinstance(x, tuple) else T[x][:] for x in o["calls"][0]]
            eng.dma_start(out, in_).then_inc(T.sem[o["sem"]], 16)
            done[i] = (o["sem"], 16, dict(known))
            count[o["sem"]] = 16
            continue
        if k == "remote":
            t, a, b, sem = o["calls"][0]
            step = 1 if t < 2 else 2
            dst, src = T.cores[(rank + step) % n], T.cores[(rank - step) % n]
            rid, pid, _e = topo.addr(dst)
            g.remote_dma(T["z%d" % (t + 1)][:, a:b], T["zs%d" % t][:, a:b], T.sem[sem], T.sem["loc"], pid, rid, topo.mask(core, dst))
            count["loc"] = count.get("loc", 0) + len(topo.engines(core, dst))
            done[i] = (sem, len(topo.engines(src, core)), {})
            continue
        if k == "fold":
            out, a, b, f = o["calls"][0]
            relay = helper(core, T, topo)
            rid, pid, _e = topo.addr(relay)
            g.remote_dma_fused([RemoteDMATransfer(dst_ids=[DstId(rid=rid, pnc=pid)], dma_engine_mask=topo.mask(core, relay),
                                                  remote_sem=T.sem["fa%d" % f], srcs=[ap(a), ap(b)], dsts=[ap(out)], alu_op=2)],
                               local_sem=T.sem["loc"])
            count["loc"] = count.get("loc", 0) + len(topo.engines(core, relay))
            done[i] = ("fb%d" % f, len(topo.engines(relay, core)), dict(known))
            continue
        sem = qsem[q]
        for c in o["calls"]:
            if k == "matmul":
                ins = g.tensor.matmul(ap(c[0]), ap(c[1]), ap(c[2]), bool(c[3]), bool(c[4]))
            elif k == "activation":
                kw = {name: arg(x) for name, x in zip(("bias", "scale", "accum_out"), c[3:]) if x is not None}
                ins = g.scalar.activation(ap(c[0]), ap(c[1]), c[2], **kw)
            elif k == "iota" and DTYPE[c[0][0]] == "int32":
                ins = g.iota(ap(c[0]), c[1], c[2], c[3])
            elif k == "iota":
                ins = g.iota(ap(c[0]), c[1], c[2], c[3], allow_small_or_imprecise_dtypes=True)
            elif k == "select":
                ins = g.affine_select(ap(c[0]), ap(c[1]), c[2], A.is_equal, 0.0, c[3], c[4])
            else:
                ins = vector[k](*[arg(x) for x in c])
            ins.then_inc(T.sem[sem], 1)
            count[sem] = count.get(sem, 0) + 1
        kn = dict(known)
        kn[sem] = count[sem]
        done[i] = (sem, count[sem], kn)
    for sem in sorted(count):
        g.wait_ge(T.sem[sem], count[sem])
